import numpy as np
import ml_dtypes


def mxq(x, axis, fmt="e4m3"):
    dtype, down = {"e4m3": (ml_dtypes.float8_e4m3fn, 7), "e5m2": (ml_dtypes.float8_e5m2, 14)}[fmt]
    v = np.moveaxis(np.asarray(x, np.float32).astype(ml_dtypes.bfloat16).astype(np.float64), axis, -1)
    blocks = v.reshape(v.shape[:-1] + (-1, 32))
    amax = np.abs(blocks).max(-1, keepdims=True)
    byte = np.maximum(np.where(amax > 0, np.frexp(amax)[1] - 1 + 127, 0) - down, 1)
    scale = np.exp2(byte - 127.0)
    codes = (blocks / scale).astype(np.float32).astype(dtype).astype(np.float64)
    return np.moveaxis((codes * scale).reshape(v.shape), -1, axis)


WIDE = False


def mx_kscale(k):
    if not WIDE:
        return np.ones(k)
    levels = np.array([10, -10, 5, -5, 0])
    if k % 512:
        return np.exp2(np.random.permutation(np.resize(levels, k // 32))).repeat(32)
    a = np.empty((k // 512, 16))
    for p in range(k // 512):
        a[p, :8] = np.random.permutation(np.resize(levels, 8))
        for g in range(8):
            far = levels[np.abs(levels - a[p, g]) >= 10]
            a[p, g + 8] = far[np.random.randint(len(far))]
    return np.exp2(a.ravel()).repeat(32)


BF16 = ml_dtypes.bfloat16


def bf(x):
    return np.asarray(x, np.float32).astype(BF16)


def f64(x):
    return np.asarray(x).astype(np.float64)


N, M, L = 128, 4096, 4096


def draw0():
    u, t = mx_kscale(M), mx_kscale(L)
    return {"s": bf(3.0 / np.sqrt(L) * np.random.standard_normal((N, L))),
            "z": bf(2.0 / np.sqrt(L) * np.random.standard_normal((M, L)) / u[:, None]),
            "kgain": bf(1.5 / np.sqrt(M) * np.random.standard_normal((N, M)) * u[None, :]),
            "g": bf((1.0 + 0.2 * np.random.standard_normal(L)) * t),
            "d": bf(np.random.uniform(0.5, 2.0, L) / (t * t)),
            "r": bf(np.random.uniform(1.0, 3.0, M) / (u * u))}


def weighted_gram(left, right):
    return left @ right.T


def core(s, z, kgain, g, d, r):
    k = f64(kgain)
    kq = mxq(k, 1, "e4m3")
    kz = kq @ mxq(f64(z), 0, "e4m3")
    w = (f64(s) - kz) * f64(g)[None, :]
    wd = w * f64(d)[None, :]
    j = weighted_gram(mxq(wd, 1, "e4m3"), mxq(w, 1, "e4m3"))
    kr = k * f64(r)[None, :]
    q = weighted_gram(mxq(kr, 1, "e4m3"), kq)
    return j + q


def e4m3fn_bytes(y):
    return np.clip(np.asarray(y, np.float64), -448.0, 448.0).astype(np.float32).astype(ml_dtypes.float8_e4m3fn).view(np.uint8)


def e4m3fn_values(b):
    return np.asarray(b, np.uint8).view(ml_dtypes.float8_e4m3fn).astype(np.float64)


def setup_inputs():
    d = draw0()
    x0 = np.asarray(d['z']).astype(np.float64)
    s = (np.max(np.abs(x0), axis=(1,), keepdims=True) / 448.0).astype(np.float32)
    out = {}
    for k, v in d.items():
        if k == 'z':
            out['z_bytes'] = e4m3fn_bytes(x0 / s.astype(np.float64))
            out['z_scale'] = s
        else:
            out[k] = v
    return out


def reference(s, z_bytes, z_scale, kgain, g, d, r):
    return core(s, e4m3fn_values(z_bytes) * z_scale.astype(np.float64), kgain, g, d, r)

@@ -1,0 +1,479 @@
+from contextlib import ExitStack
+
+import concourse.mybir as mybir
+from concourse.masks import make_identity
+
+N, M, L = 128, 4096, 4096
+FLOPS = 2 * N * M * L + 4 * N * N * L
+
+F32 = mybir.dt.float32
+BF16 = mybir.dt.bfloat16
+U32 = mybir.dt.uint32
+U8 = mybir.dt.uint8
+F8 = mybir.dt.float8_e4m3fn
+FP8X4 = mybir.dt.float8_e4m3fn_x4
+MULT = mybir.AluOpType.mult
+SUB = mybir.AluOpType.subtract
+COPY = mybir.ActivationFunctionType.Copy
+
+P = 128
+KP = M // 512
+CHUNKS = [512, 1024, 1024, 1024, 512]
+WMAX = 1024
+
+
+def tile_josephkalmanupdate_w_kernel(tc, s, z_bytes, z_scale, kgain, g, d, r, out):
+    nc = tc.nc
+    with ExitStack() as ctx:
+        keep = ctx.enter_context(tc.tile_pool(name="keep", bufs=1))
+        bpool = ctx.enter_context(tc.tile_pool(name="bpool", bufs=6))
+        work = ctx.enter_context(tc.tile_pool(name="work", bufs=3))
+        cpool = ctx.enter_context(tc.tile_pool(name="cpool", bufs=2))
+        epool = ctx.enter_context(tc.tile_pool(name="epool", bufs=2))
+        psum = ctx.enter_context(tc.psum_pool(name="psum", bufs=1))
+
+        units = []
+        l0 = 0
+        for c, w in enumerate(CHUNKS):
+            for gp in range(KP):
+                units.append((c, gp, l0, w))
+            l0 += w
+        nu = len(units)
+        SPLIT = {}
+
+        ident = keep.tile([P, P], F32, name="ident")
+        identb = keep.tile([P, P], BF16, name="identb")
+        zs = keep.tile([P, KP, 4], F32, name="zs")
+        rt = keep.tile([P, KP, 4], BF16, name="rt")
+        gdraw = keep.tile([P, 512], BF16, name="gdraw")
+        gdperm = keep.tile([P, 4, P], BF16, name="gdperm")
+        gT = keep.tile([P, 8, 4], F32, name="gT")
+        dT = keep.tile([P, 8, 4], F32, name="dT")
+        gdT = keep.tile([P, 8, 4], F32, name="gdT")
+        kg = keep.tile([P, M], BF16, name="kg")
+        kT = keep.tile([P, KP, P * 4], BF16, name="kT", align_bytes=64)
+        krT = keep.tile([P, KP, P * 4], BF16, name="krT", align_bytes=64)
+        kq = keep.tile([P, KP, P], U32, name="kq", align_bytes=64)
+        kqs = keep.tile([P, KP, P], U8, name="kqs", align_bytes=64)
+        krq = keep.tile([P, KP, P], U32, name="krq", align_bytes=64)
+        krqs = keep.tile([P, KP, P], U8, name="krqs", align_bytes=64)
+        sraw = keep.tile([P, L], BF16, name="sraw")
+        sperm = {}
+        sT = keep.tile([P, 8, 4, P], BF16, name="sT")
+
+        qj = psum.tile([P, P], F32, name="qj", tag="qj", bufs=1)
+
+        zb = {}
+        planes = {}
+        pairs = {}
+        il = {}
+        codes = {}
+        kz = {}
+        ep = {}
+
+        def load(u):
+            c, gp, lo, w = units[u]
+            t_ = bpool.tile([P, 4, WMAX], U8, name="zb", tag="zb", bufs=6)
+            nc.sync.dma_start(
+                out=t_[:, :, 0:w],
+                in_=z_bytes[512 * gp : 512 * (gp + 1), lo : lo + w].rearrange("(p t) w -> p t w", t=4),
+            )
+            zb[u] = t_
+
+        def widen_e(u):
+            c, gp, lo, w = units[u]
+            a0 = SPLIT.get(u, 0)
+            p_ = work.tile([P, 2, WMAX * 2], BF16, name="pairs", tag="pairs", bufs=2, align_bytes=64)
+            pairs[u] = p_
+            for t in range(4):
+                nc.vector.tensor_scalar(
+                    out=p_[:, t // 2, 32 * a0 : 2 * w].rearrange("p (l e) -> p e l", e=2)[:, t % 2],
+                    in0=zb[u][:, t, 16 * a0 : w].bitcast(F8),
+                    scalar1=zs[:, gp, t : t + 1],
+                    scalar2=None,
+                    op0=MULT,
+                )
+
+        def il_alloc(u):
+            il[u] = work.tile([P, 4 * WMAX], BF16, name="il", tag="il", bufs=4, align_bytes=64)
+
+        def word(u, eng):
+            c, gp, l_, w = units[u]
+            a0 = SPLIT.get(u, 0)
+            f = nc.scalar.copy if eng == "S" else nc.vector.tensor_copy
+            f(
+                out=il[u][:, 0 : 4 * w]
+                .bitcast(F32)
+                .rearrange("p (T A i u) -> p A T i u", T=4, i=4, u=2)[:, a0:],
+                in_=pairs[u][:]
+                .rearrange("p u x -> p (u x)")
+                .bitcast(F32)
+                .rearrange("p (u l) -> p l u", u=2)[:, 16 * a0 : w, :]
+                .rearrange("p (A T i) u -> p A T i u", T=4, i=4),
+            )
+
+        def d_widen(u, t):
+            c, gp, lo, w = units[u]
+            n = 16 * SPLIT[u] if u in SPLIT else w
+            if t == 0:
+                planes[u] = work.tile([P, 4, WMAX], BF16, name="planes", tag="planes", bufs=2, align_bytes=64)
+            nc.scalar.activation(
+                out=planes[u][:, t, 0:n], in_=zb[u][:, t, 0:n].bitcast(F8), func=COPY, scale=zs[:, gp, t : t + 1]
+            )
+
+        def d_inter(u, b):
+            c, gp, lo, w = units[u]
+            n = SPLIT[u] if u in SPLIT else w // 16
+            if u in SPLIT:
+                if b:
+                    return
+                lo_a, hi_a = 0, n
+            else:
+                if b % 2:
+                    return
+                lo_a, hi_a = n * b // 4, n * (b + 2) // 4
+            nc.scalar.copy(
+                out=il[u][:, 0 : 4 * w].rearrange("p (T A i t) -> p A T i t", T=4, i=4, t=4)[:, lo_a:hi_a],
+                in_=planes[u][:, :, 0 : 16 * n]
+                .rearrange("p t l -> p l t")[:, 16 * lo_a : 16 * hi_a, :]
+                .rearrange("p (A T i) t -> p A T i t", T=4, i=4),
+            )
+
+        def p_inter(u, b):
+            c, gp, lo, w = units[u]
+            ps = psum.tile([P, 2, 512], BF16, name="tp", tag="tp", bufs=4)
+            view = planes[u][:, :, 0:w].rearrange("p t (A T i) -> p T A i t", T=4, i=4)
+            for x in range(2):
+                j = 2 * b + x
+                nc.tensor.matmul(
+                    ps[:, x, :].rearrange("p (A i t) -> p A i t", i=4, t=4),
+                    lhsT=identb[:],
+                    rhs=view[:, j // 2, 32 * (j % 2) : 32 * (j % 2) + 32],
+                    start=True,
+                    stop=True,
+                )
+            nc.scalar.copy(out=il[u][:, 1024 * b : 1024 * (b + 1)], in_=ps[:].rearrange("p x n -> p (x n)"))
+
+        def quant(u):
+            c, gp, lo, w = units[u]
+            if c not in codes:
+                codes[c] = (
+                    cpool.tile([P, KP, WMAX], U32, name="zc", tag="zc", bufs=2, align_bytes=64),
+                    cpool.tile([P, KP, WMAX], U8, name="zsc", tag="zsc", bufs=2, align_bytes=64),
+                )
+            cd, sc = codes[c]
+            nc.vector.quantize_mx(
+                out=cd[:, gp, 0:w].bitcast(FP8X4), scales=sc[:, gp, 0:w], in_=il[u][:, 0 : 4 * w]
+            )
+
+        def kzpass(c, h, T, gp, dst, first=0, final=KP - 1):
+            cd, sc = codes[c]
+            w = CHUNKS[c]
+            c0 = T * (w // 4) + 128 * h
+            nc.tensor.matmul_mx(
+                out=dst,
+                lhsT=cd[:, gp, c0 : c0 + 128].bitcast(FP8X4),
+                lhsT_scale=sc[:, gp, c0 : c0 + 128],
+                rhs=kq[:, gp, :].bitcast(FP8X4),
+                rhs_scale=kqs[:, gp, :],
+                start=(gp == first),
+                stop=(gp == final),
+            )
+
+        def kzall(c):
+            for h in range(CHUNKS[c] // 512):
+                b_ = psum.tile([P, 4, P], F32, name="kz", tag="kz", bufs=3)
+                kz[(c, h)] = b_
+                for T in range(4):
+                    for gp in range(KP):
+                        kzpass(c, h, T, gp, b_[:, T, :])
+
+        def hh0(c):
+            return sum(CHUNKS[:c]) // 512
+
+        def e_alloc(c):
+            nh = CHUNKS[c] // 512
+            ep[c] = dict(
+                t1=epool.tile([P, 2, 512], F32, name="t1", tag="t1", bufs=1),
+                w=epool.tile([P, 2, 512], BF16, name="w", tag="w", bufs=1, align_bytes=64),
+                wd=epool.tile([P, 2, 512], BF16, name="wd", tag="wd", bufs=1, align_bytes=64),
+                wq=epool.tile([P, 2, P], U32, name="wq", tag="wq", bufs=2, align_bytes=64),
+                wqs=epool.tile([P, 2, P], U8, name="wqs", tag="wqs", bufs=2, align_bytes=64),
+                wdq=epool.tile([P, 2, P], U32, name="wdq", tag="wdq", bufs=2, align_bytes=64),
+                wdqs=epool.tile([P, 2, P], U8, name="wdqs", tag="wdqs", bufs=2, align_bytes=64),
+            )
+
+        def e_t1(c, h):
+            if h == 0:
+                e_alloc(c)
+            hh = hh0(c) + h
+            nc.vector.tensor_tensor(
+                out=ep[c]["t1"][:, h, :].rearrange("p (n T) -> p n T", T=4),
+                in0=sT[:, hh, :, :].rearrange("p T n -> p n T"),
+                in1=kz[(c, h)][:].rearrange("p T n -> p n T"),
+                op=SUB,
+            )
+
+        def e_mul(c, key, gain):
+            nh = CHUNKS[c] // 512
+            nc.vector.tensor_tensor(
+                out=ep[c][key][:, 0:nh, :].rearrange("p h (n T) -> p h n T", T=4),
+                in0=ep[c]["t1"][:, 0:nh, :].rearrange("p h (T n) -> p h n T" if c == len(CHUNKS) - 1 else "p h (n T) -> p h n T", T=4),
+                in1=gain[:, hh0(c) : hh0(c) + nh, :].unsqueeze(2).to_broadcast([P, nh, P, 4]),
+                op=MULT,
+            )
+
+        def e_q(c, key):
+            nh = CHUNKS[c] // 512
+            e = ep[c]
+            nc.vector.quantize_mx(
+                out=e[key + "q"][:, 0:nh, :].rearrange("p h n -> p (h n)").bitcast(FP8X4),
+                scales=e[key + "qs"][:, 0:nh, :].rearrange("p h n -> p (h n)"),
+                in_=e[key][:, 0:nh, :].rearrange("p h x -> p (h x)"),
+            )
+
+        def e_j(c):
+            e = ep[c]
+            for h in range(CHUNKS[c] // 512):
+                nc.tensor.matmul_mx(
+                    out=qj[:],
+                    lhsT=e["wdq"][:, h, :].bitcast(FP8X4),
+                    lhsT_scale=e["wdqs"][:, h, :],
+                    rhs=e["wq"][:, h, :].bitcast(FP8X4),
+                    rhs_scale=e["wqs"][:, h, :],
+                    start=False,
+                    stop=(hh0(c) + h == 7),
+                )
+
+        def tp_f32():
+            return psum.tile([P, 2, 2, P], F32, name="tp", tag="tp", bufs=4)
+
+        def k_turn(q):
+            ps = tp_f32()
+            words = kg[:].bitcast(F32)
+            for j in range(2):
+                for u in range(2):
+                    b0 = 256 * (2 * q + j)
+                    nc.tensor.transpose(ps[:, j, u, :], words[:, b0 + u : b0 + 256 : 2], ident[:])
+            nc.scalar.copy(
+                out=kT[:, 2 * q : 2 * q + 2, :].bitcast(F32).rearrange("p j (n u) -> p j n u", u=2),
+                in_=ps[:].rearrange("p j u n -> p j n u"),
+            )
+
+        def k_q(q):
+            a, b = 4 * q, 4 * q + 4
+            nc.vector.quantize_mx(
+                out=kq[:, a:b, :].rearrange("p g n -> p (g n)").bitcast(FP8X4),
+                scales=kqs[:, a:b, :].rearrange("p g n -> p (g n)"),
+                in_=kT[:, a:b, :].rearrange("p g x -> p (g x)"),
+            )
+
+        def kr_mul(q):
+            a, b = 4 * q, 4 * q + 4
+            nc.vector.tensor_tensor(
+                out=krT[:, a:b, :].rearrange("p g (n t) -> p g n t", t=4),
+                in0=kT[:, a:b, :].rearrange("p g (n t) -> p g n t", t=4),
+                in1=rt[:, a:b, :].unsqueeze(2).to_broadcast([P, 4, P, 4]),
+                op=MULT,
+            )
+
+        def kr_q(q):
+            a, b = 4 * q, 4 * q + 4
+            nc.vector.quantize_mx(
+                out=krq[:, a:b, :].rearrange("p g n -> p (g n)").bitcast(FP8X4),
+                scales=krqs[:, a:b, :].rearrange("p g n -> p (g n)"),
+                in_=krT[:, a:b, :].rearrange("p g x -> p (g x)"),
+            )
+
+        def q_all():
+            for gp in range(KP):
+                nc.tensor.matmul_mx(
+                    out=qj[:],
+                    lhsT=krq[:, gp, :].bitcast(FP8X4),
+                    lhsT_scale=krqs[:, gp, :],
+                    rhs=kq[:, gp, :].bitcast(FP8X4),
+                    rhs_scale=kqs[:, gp, :],
+                    start=(gp == 0),
+                    stop=False,
+                )
+
+        def s_perm(q):
+            sperm[q] = epool.tile([P, 4, P], BF16, name="sperm", tag="sperm", bufs=2)
+            nc.scalar.copy(
+                out=sperm[q][:].rearrange("p T (A i) -> p T A i", i=4),
+                in_=sraw[:, 512 * q : 512 * (q + 1)].rearrange("p (A T i) -> p T A i", T=4, i=4),
+            )
+
+        def s_turn(q):
+            ps = psum.tile([P, 4, P], BF16, name="tp", tag="tp", bufs=4)
+            for T in range(4):
+                nc.tensor.transpose(ps[:, T, :], sperm[q][:, T, :], identb[:])
+            nc.scalar.copy(out=sT[:, q, :, :], in_=ps[:])
+
+        def gd_perm():
+            nc.vector.tensor_copy(
+                out=gdperm[:].rearrange("p T (A i) -> p T A i", i=4),
+                in_=gdraw[:].rearrange("p (A T i) -> p T A i", T=4, i=4),
+            )
+
+        def gd_prep():
+            ps = psum.tile([P, 4, P], BF16, name="tp", tag="tp", bufs=4)
+            for T in range(4):
+                nc.tensor.transpose(ps[:, T, :], gdperm[:, T, :], identb[:])
+            nc.vector.tensor_copy(out=gT[:].rearrange("p h T -> p T h"), in_=ps[:, :, 0:8])
+            nc.vector.tensor_copy(out=dT[:].rearrange("p h T -> p T h"), in_=ps[:, :, 8:16])
+            nc.vector.tensor_tensor(out=gdT[:], in0=gT[:], in1=dT[:], op=MULT)
+
+        DSET = (1, 5)
+        esteps = [u for u in range(nu) if u % 8 not in DSET]
+        dunits = [u for u in range(nu) if u % 8 in DSET]
+        PSET = (13, 21, 29)
+        SPLIT.update({15: 16, 23: 16, 31: 16})
+        ns = len(esteps)
+        tasks = {}
+
+        def at(step, fn, *args):
+            tasks.setdefault(step, []).append((fn, args))
+
+        at(2, k_turn, 0)
+        at(2, k_turn, 1)
+        at(3, k_turn, 2)
+        at(3, k_turn, 3)
+        at(5, gd_perm)
+        at(6, gd_prep)
+        at(4, k_q, 0)
+        at(4, k_q, 1)
+        at(6, kr_mul, 0)
+        at(6, kr_mul, 1)
+        at(7, kr_q, 0)
+        at(7, kr_q, 1)
+        at(7, q_all)
+        for c, w in enumerate(CHUNKS):
+            end = 6 * (c + 1) - 1
+            for h in range(w // 512):
+                k = 5 if c == 0 else end - 8 if c == len(CHUNKS) - 1 else end - 3 + h
+                at(k, s_perm, hh0(c) + h)
+                at(k + 1, s_turn, hh0(c) + h)
+            if c < len(CHUNKS) - 1:
+                k = end + (5 if c == len(CHUNKS) - 2 else 4)
+                for h in range(w // 512):
+                    at(k, e_t1, c, h)
+                at(k + 1, e_mul, c, "w", gT)
+                at(k + 2, e_mul, c, "wd", gdT)
+                at(k + 2, e_q, c, "w")
+                at(k + 3, e_q, c, "wd")
+                at(k + 3, e_j, c)
+
+        with tc.manual_schedule():
+            zsv = z_scale.rearrange("(g p t) o -> p g (t o)", p=P, t=4)
+            nc.scalar.dma_start(out=zs[:, 0:2, :], in_=zsv[:, 0:2, :])
+            nc.scalar.dma_start(out=zs[:, 2:8, :], in_=zsv[:, 2:8, :])
+            order = []
+            for k in range(ns):
+                if k % 3 == 0:
+                    order += [esteps[k], dunits[k // 3]]
+                else:
+                    order += [esteps[k]]
+            nload = 0
+
+            nc.gpsimd.memset(gdraw[:], 0.0)
+            make_identity(nc, ident[:])
+            nc.gpsimd.tensor_copy(out=identb[:], in_=ident[:])
+
+            def small():
+                nc.sync.dma_start(out=rt[:], in_=r.rearrange("(g p t) -> p g t", p=P, t=4))
+                nc.sync.dma_start(out=gdraw[0:8, :], in_=g.rearrange("(h x) -> h x", h=8))
+                nc.sync.dma_start(out=gdraw[8:16, :], in_=d.rearrange("(h x) -> h x", h=8))
+
+            def s_load(a, b):
+                nc.sync.dma_start(out=sraw[:, a:b], in_=s[:, a:b])
+
+            def k_load(a, b):
+                nc.sync.dma_start(out=kg[:, a:b], in_=kgain[:, a:b])
+
+            extra = {
+                4: [(k_load, (0, 2048))],
+                5: [(k_load, (2048, 4096))],
+                6: [(small, ())],
+                7: [(s_load, (0, 1536))],
+                9: [(s_load, (1536, 4096))],
+            }
+
+            def load_next(n):
+                load(order[n])
+                for fn, args in extra.get(n + 1, []):
+                    fn(*args)
+
+            for n in range(5):
+                load_next(n)
+            nload = 5
+
+            last = len(CHUNKS) - 1
+            fin = []
+            done = {}
+
+            def quantized(u):
+                quant(u)
+                c, gp, lo, w = units[u]
+                done.setdefault(c, []).append(gp)
+                seq = done[c]
+                if c < last:
+                    if len(seq) == KP:
+                        kzall(c)
+                else:
+                    if len(seq) == 1:
+                        for T in range(4):
+                            fin.append(psum.tile([P, P], F32, name="tp", tag="tp", bufs=4))
+                    for T in range(4):
+                        kzpass(c, 0, T, gp, fin[T][:], first=seq[0], final=gp if len(seq) == KP else -1)
+
+            for k in range(ns + 1):
+                while nload < len(order) and nload < k + k // 3 + 6:
+                    load_next(nload)
+                    nload += 1
+                if k < ns:
+                    il_alloc(esteps[k])
+                    widen_e(esteps[k])
+                if k >= 1:
+                    word(esteps[k - 1], "V" if k == ns else "S")
+                if k < ns:
+                    dd = dunits[k // 3]
+                    if k % 3 == 0:
+                        il_alloc(dd)
+                        for t in range(4 if dd in PSET else 3):
+                            d_widen(dd, t)
+                    elif k % 3 == 1:
+                        if dd not in PSET:
+                            d_widen(dd, 3)
+                        for x in (0, 1):
+                            p_inter(dd, x) if dd in PSET else d_inter(dd, x)
+                    else:
+                        for x in (2, 3):
+                            p_inter(dd, x) if dd in PSET else d_inter(dd, x)
+                    if esteps[k] in SPLIT:
+                        for t in range(4):
+                            d_widen(esteps[k], t)
+                        for T in range(4):
+                            d_inter(esteps[k], T)
+                for fn, args in tasks.get(k, []):
+                    fn(*args)
+                if k >= 1 and k % 3 == 0:
+                    quantized(dunits[k // 3 - 1])
+                if k >= 1:
+                    quantized(esteps[k - 1])
+            for k in sorted(x for x in tasks if x > ns):
+                for fn, args in tasks[k]:
+                    fn(*args)
+            e_alloc(last)
+            for T in range(4):
+                nc.vector.tensor_tensor(
+                    out=ep[last]["t1"][:, 0, 128 * T : 128 * (T + 1)], in0=sT[:, 7, T, :], in1=fin[T][:], op=SUB
+                )
+            e_mul(last, "wd", gdT)
+            e_mul(last, "w", gT)
+            e_q(last, "wd")
+            e_q(last, "w")
+            e_j(last)
+            res = epool.tile([P, P], F32, name="res", tag="res", bufs=1)
+            nc.vector.tensor_copy(out=res[:], in_=qj[:])
+            nc.sync.dma_start(out=out, in_=res[:])

@@ -13,243 +13,177 @@ U8 = mybir.dt.uint8
 F8 = mybir.dt.float8_e4m3fn
 FP8X4 = mybir.dt.float8_e4m3fn_x4
 MULT = mybir.AluOpType.mult
-SUB = mybir.AluOpType.subtract
 COPY = mybir.ActivationFunctionType.Copy
 
 P = 128
-KP = M // 512
-CHUNKS = [512, 1024, 1024, 1024, 512]
-WMAX = 1024
+PASSES = M // 512
+W = 1024
+BLK = 512
+CHUNKS = L // W
+PAIR_PASSES = (0, 2, 3, 4, 6, 7)
+PLANE_PASSES = (1, 5)
+STEPS = CHUNKS * len(PAIR_PASSES)
+LAG = 2
 
 
 def tile_josephkalmanupdate_w_kernel(tc, s, z_bytes, z_scale, kgain, g, d, r, out):
     nc = tc.nc
     with ExitStack() as ctx:
         keep = ctx.enter_context(tc.tile_pool(name="keep", bufs=1))
-        bpool = ctx.enter_context(tc.tile_pool(name="bpool", bufs=6))
-        work = ctx.enter_context(tc.tile_pool(name="work", bufs=3))
-        cpool = ctx.enter_context(tc.tile_pool(name="cpool", bufs=2))
-        epool = ctx.enter_context(tc.tile_pool(name="epool", bufs=2))
+        work = ctx.enter_context(tc.tile_pool(name="work", bufs=1))
         psum = ctx.enter_context(tc.psum_pool(name="psum", bufs=1))
-
-        units = []
-        l0 = 0
-        for c, w in enumerate(CHUNKS):
-            for gp in range(KP):
-                units.append((c, gp, l0, w))
-            l0 += w
-        nu = len(units)
-        SPLIT = {}
 
         ident = keep.tile([P, P], F32, name="ident")
         identb = keep.tile([P, P], BF16, name="identb")
-        zs = keep.tile([P, KP, 4], F32, name="zs")
-        rt = keep.tile([P, KP, 4], BF16, name="rt")
-        gdraw = keep.tile([P, 512], BF16, name="gdraw")
-        gdperm = keep.tile([P, 4, P], BF16, name="gdperm")
-        gT = keep.tile([P, 8, 4], F32, name="gT")
-        dT = keep.tile([P, 8, 4], F32, name="dT")
-        gdT = keep.tile([P, 8, 4], F32, name="gdT")
+        zs = keep.tile([P, PASSES, 4], F32, name="zs")
+        rt = keep.tile([P, PASSES, 4], BF16, name="rt")
+        gt = keep.tile([P, 8, 4], BF16, name="gt")
+        dt_ = keep.tile([P, 8, 4], BF16, name="dtile")
+        gdt = keep.tile([P, 8, 4], F32, name="gdt")
         kg = keep.tile([P, M], BF16, name="kg")
-        kT = keep.tile([P, KP, P * 4], BF16, name="kT", align_bytes=64)
-        krT = keep.tile([P, KP, P * 4], BF16, name="krT", align_bytes=64)
-        kq = keep.tile([P, KP, P], U32, name="kq", align_bytes=64)
-        kqs = keep.tile([P, KP, P], U8, name="kqs", align_bytes=64)
-        krq = keep.tile([P, KP, P], U32, name="krq", align_bytes=64)
-        krqs = keep.tile([P, KP, P], U8, name="krqs", align_bytes=64)
+        kT = keep.tile([P, PASSES, P * 4], BF16, name="kT", align_bytes=64)
+        krT = keep.tile([P, PASSES, P * 4], BF16, name="krT", align_bytes=64)
+        kq = keep.tile([P, PASSES, P], U32, name="kq", align_bytes=64)
+        kqs = keep.tile([P, PASSES, P], U8, name="kqs", align_bytes=64)
+        krq = keep.tile([P, PASSES, P], U32, name="krq", align_bytes=64)
+        krqs = keep.tile([P, PASSES, P], U8, name="krqs", align_bytes=64)
         sraw = keep.tile([P, L], BF16, name="sraw")
-        sperm = {}
-        sT = keep.tile([P, 8, 4, P], BF16, name="sT")
-
         qj = psum.tile([P, P], F32, name="qj", tag="qj", bufs=1)
 
-        zb = {}
-        planes = {}
-        pairs = {}
-        il = {}
-        codes = {}
-        kz = {}
-        ep = {}
+        pair_units = [(c, gp) for c in range(CHUNKS) for gp in PAIR_PASSES]
+        plane_units = [(c, gp) for c in range(CHUNKS) for gp in PLANE_PASSES]
 
-        def load(u):
-            c, gp, lo, w = units[u]
-            t_ = bpool.tile([P, 4, WMAX], U8, name="zb", tag="zb", bufs=6)
-            nc.sync.dma_start(
-                out=t_[:, :, 0:w],
-                in_=z_bytes[512 * gp : 512 * (gp + 1), lo : lo + w].rearrange("(p t) w -> p t w", t=4),
-            )
-            zb[u] = t_
+        zb, pairs, planes, il, codes, kz, turned, ep = {}, {}, {}, {}, {}, {}, {}, {}
+        passes_done = {}
 
-        def widen_e(u):
-            c, gp, lo, w = units[u]
-            a0 = SPLIT.get(u, 0)
-            p_ = work.tile([P, 2, WMAX * 2], BF16, name="pairs", tag="pairs", bufs=2, align_bytes=64)
-            pairs[u] = p_
+        def load(u, t0=0, t1=4):
+            c, gp = u
+            if t0 == 0:
+                zb[u] = work.tile([P, 4, W], U8, name="zb", tag="zb", bufs=7)
+            rows = z_bytes[512 * gp : 512 * (gp + 1), W * c : W * (c + 1)].rearrange("(p t) w -> p t w", t=4)
+            nc.sync.dma_start(out=zb[u][:, t0:t1, :], in_=rows[:, t0:t1, :])
+
+        def widen_pairs(u, lo=0, hi=W):
+            if lo == 0:
+                pairs[u] = work.tile([P, 2, 2 * W], BF16, name="pairs", tag="pairs", bufs=3, align_bytes=64)
             for t in range(4):
                 nc.vector.tensor_scalar(
-                    out=p_[:, t // 2, 32 * a0 : 2 * w].rearrange("p (l e) -> p e l", e=2)[:, t % 2],
-                    in0=zb[u][:, t, 16 * a0 : w].bitcast(F8),
-                    scalar1=zs[:, gp, t : t + 1],
+                    out=pairs[u][:, t // 2, 2 * lo : 2 * hi].rearrange("p (l e) -> p e l", e=2)[:, t % 2],
+                    in0=zb[u][:, t, lo:hi].bitcast(F8),
+                    scalar1=zs[:, u[1], t : t + 1],
                     scalar2=None,
                     op0=MULT,
                 )
 
-        def il_alloc(u):
-            il[u] = work.tile([P, 4 * WMAX], BF16, name="il", tag="il", bufs=4, align_bytes=64)
-
-        def word(u, eng):
-            c, gp, l_, w = units[u]
-            a0 = SPLIT.get(u, 0)
-            f = nc.scalar.copy if eng == "S" else nc.vector.tensor_copy
-            f(
-                out=il[u][:, 0 : 4 * w]
-                .bitcast(F32)
-                .rearrange("p (T A i u) -> p A T i u", T=4, i=4, u=2)[:, a0:],
-                in_=pairs[u][:]
-                .rearrange("p u x -> p (u x)")
-                .bitcast(F32)
-                .rearrange("p (u l) -> p l u", u=2)[:, 16 * a0 : w, :]
-                .rearrange("p (A T i) u -> p A T i u", T=4, i=4),
-            )
-
-        def d_widen(u, t):
-            c, gp, lo, w = units[u]
-            n = 16 * SPLIT[u] if u in SPLIT else w
-            if t == 0:
-                planes[u] = work.tile([P, 4, WMAX], BF16, name="planes", tag="planes", bufs=2, align_bytes=64)
-            nc.scalar.activation(
-                out=planes[u][:, t, 0:n], in_=zb[u][:, t, 0:n].bitcast(F8), func=COPY, scale=zs[:, gp, t : t + 1]
-            )
-
-        def d_inter(u, b):
-            c, gp, lo, w = units[u]
-            n = SPLIT[u] if u in SPLIT else w // 16
-            if u in SPLIT:
-                if b:
-                    return
-                lo_a, hi_a = 0, n
-            else:
-                if b % 2:
-                    return
-                lo_a, hi_a = n * b // 4, n * (b + 2) // 4
+        def join(u, lo=0, hi=W):
+            if lo == 0:
+                il[u] = work.tile([P, 4 * W], BF16, name="il", tag="il", bufs=4, align_bytes=64)
             nc.scalar.copy(
-                out=il[u][:, 0 : 4 * w].rearrange("p (T A i t) -> p A T i t", T=4, i=4, t=4)[:, lo_a:hi_a],
-                in_=planes[u][:, :, 0 : 16 * n]
-                .rearrange("p t l -> p l t")[:, 16 * lo_a : 16 * hi_a, :]
-                .rearrange("p (A T i) t -> p A T i t", T=4, i=4),
+                out=il[u][:, 4 * lo : 4 * hi].bitcast(F32).rearrange("p (l u) -> p l u", u=2),
+                in_=pairs[u][:].rearrange("p u x -> p (u x)").bitcast(F32).rearrange("p (u l) -> p l u", u=2)[:, lo:hi, :],
             )
 
-        def p_inter(u, b):
-            c, gp, lo, w = units[u]
-            ps = psum.tile([P, 2, 512], BF16, name="tp", tag="tp", bufs=4)
-            view = planes[u][:, :, 0:w].rearrange("p t (A T i) -> p T A i t", T=4, i=4)
+        def widen_plane(u, t):
+            if t == 0:
+                planes[u] = work.tile([P, 4, W], BF16, name="planes", tag="planes", bufs=2, align_bytes=64)
+                il[u] = work.tile([P, 4 * W], BF16, name="il_s", tag="il_s", bufs=2, align_bytes=64)
+            nc.scalar.activation(
+                out=planes[u][:, t, :], in_=zb[u][:, t, :].bitcast(F8), func=COPY, scale=zs[:, u[1], t : t + 1]
+            )
+
+        def interleave(u, lo, hi):
+            nc.scalar.copy(
+                out=il[u][:, 4 * lo : 4 * hi].rearrange("p (l t) -> p l t", t=4),
+                in_=planes[u][:, :, lo:hi].rearrange("p t l -> p l t"),
+            )
+
+        def pe_interleave(u, lo):
+            ps = psum.tile([P, 2, 512], BF16, name="tp", tag="tp", bufs=3)
             for x in range(2):
-                j = 2 * b + x
                 nc.tensor.matmul(
-                    ps[:, x, :].rearrange("p (A i t) -> p A i t", i=4, t=4),
+                    ps[:, x, :].rearrange("p (l t) -> p l t", t=4),
                     lhsT=identb[:],
-                    rhs=view[:, j // 2, 32 * (j % 2) : 32 * (j % 2) + 32],
+                    rhs=planes[u][:, :, lo + P * x : lo + P * (x + 1)].rearrange("p t l -> p l t"),
                     start=True,
                     stop=True,
                 )
-            nc.scalar.copy(out=il[u][:, 1024 * b : 1024 * (b + 1)], in_=ps[:].rearrange("p x n -> p (x n)"))
+            return ps
 
-        def quant(u):
-            c, gp, lo, w = units[u]
-            if c not in codes:
-                codes[c] = (
-                    cpool.tile([P, KP, WMAX], U32, name="zc", tag="zc", bufs=2, align_bytes=64),
-                    cpool.tile([P, KP, WMAX], U8, name="zsc", tag="zsc", bufs=2, align_bytes=64),
+        def pe_interleave_out(u, lo, ps):
+            nc.scalar.copy(
+                out=il[u][:, 4 * lo : 4 * lo + 1024].bitcast(F32), in_=ps[:].rearrange("p x n -> p (x n)").bitcast(F32)
+            )
+
+        def quant(u, lo=0, hi=W):
+            if lo == 0:
+                codes[u] = (
+                    work.tile([P, W], U32, name="zc", tag="zc", bufs=3, align_bytes=64),
+                    work.tile([P, W], U8, name="zsc", tag="zsc", bufs=3, align_bytes=64),
                 )
-            cd, sc = codes[c]
-            nc.vector.quantize_mx(
-                out=cd[:, gp, 0:w].bitcast(FP8X4), scales=sc[:, gp, 0:w], in_=il[u][:, 0 : 4 * w]
-            )
+            cd, sc = codes[u]
+            nc.vector.quantize_mx(out=cd[:, lo:hi].bitcast(FP8X4), scales=sc[:, lo:hi], in_=il[u][:, 4 * lo : 4 * hi])
 
-        def kzpass(c, h, T, gp, dst, first=0, final=KP - 1):
-            cd, sc = codes[c]
-            w = CHUNKS[c]
-            c0 = T * (w // 4) + 128 * h
-            nc.tensor.matmul_mx(
-                out=dst,
-                lhsT=cd[:, gp, c0 : c0 + 128].bitcast(FP8X4),
-                lhsT_scale=sc[:, gp, c0 : c0 + 128],
-                rhs=kq[:, gp, :].bitcast(FP8X4),
-                rhs_scale=kqs[:, gp, :],
-                start=(gp == first),
-                stop=(gp == final),
-            )
-
-        def kzall(c):
-            for h in range(CHUNKS[c] // 512):
-                b_ = psum.tile([P, 4, P], F32, name="kz", tag="kz", bufs=3)
-                kz[(c, h)] = b_
-                for T in range(4):
-                    for gp in range(KP):
-                        kzpass(c, h, T, gp, b_[:, T, :])
-
-        def hh0(c):
-            return sum(CHUNKS[:c]) // 512
-
-        def e_alloc(c):
-            nh = CHUNKS[c] // 512
-            ep[c] = dict(
-                t1=epool.tile([P, 2, 512], F32, name="t1", tag="t1", bufs=1),
-                w=epool.tile([P, 2, 512], BF16, name="w", tag="w", bufs=1, align_bytes=64),
-                wd=epool.tile([P, 2, 512], BF16, name="wd", tag="wd", bufs=1, align_bytes=64),
-                wq=epool.tile([P, 2, P], U32, name="wq", tag="wq", bufs=2, align_bytes=64),
-                wqs=epool.tile([P, 2, P], U8, name="wqs", tag="wqs", bufs=2, align_bytes=64),
-                wdq=epool.tile([P, 2, P], U32, name="wdq", tag="wdq", bufs=2, align_bytes=64),
-                wdqs=epool.tile([P, 2, P], U8, name="wdqs", tag="wdqs", bufs=2, align_bytes=64),
-            )
-
-        def e_t1(c, h):
-            if h == 0:
-                e_alloc(c)
-            hh = hh0(c) + h
-            nc.vector.tensor_tensor(
-                out=ep[c]["t1"][:, h, :].rearrange("p (n T) -> p n T", T=4),
-                in0=sT[:, hh, :, :].rearrange("p T n -> p n T"),
-                in1=kz[(c, h)][:].rearrange("p T n -> p n T"),
-                op=SUB,
-            )
-
-        def e_mul(c, key, gain):
-            nh = CHUNKS[c] // 512
-            nc.vector.tensor_tensor(
-                out=ep[c][key][:, 0:nh, :].rearrange("p h (n T) -> p h n T", T=4),
-                in0=ep[c]["t1"][:, 0:nh, :].rearrange("p h (T n) -> p h n T" if c == len(CHUNKS) - 1 else "p h (n T) -> p h n T", T=4),
-                in1=gain[:, hh0(c) : hh0(c) + nh, :].unsqueeze(2).to_broadcast([P, nh, P, 4]),
-                op=MULT,
-            )
-
-        def e_q(c, key):
-            nh = CHUNKS[c] // 512
-            e = ep[c]
-            nc.vector.quantize_mx(
-                out=e[key + "q"][:, 0:nh, :].rearrange("p h n -> p (h n)").bitcast(FP8X4),
-                scales=e[key + "qs"][:, 0:nh, :].rearrange("p h n -> p (h n)"),
-                in_=e[key][:, 0:nh, :].rearrange("p h x -> p (h x)"),
-            )
-
-        def e_j(c):
-            e = ep[c]
-            for h in range(CHUNKS[c] // 512):
+        def kz_pass(u, lo=0, hi=W):
+            c, gp = u
+            cd, sc = codes[u]
+            for col in range(lo, hi, BLK):
+                h = (W * c + col) // BLK
+                if h not in kz:
+                    kz[h] = psum.tile([P, BLK], F32, name="kz", tag="kz", bufs=4)
+                n_done = passes_done.get(h, 0)
+                passes_done[h] = n_done + 1
                 nc.tensor.matmul_mx(
-                    out=qj[:],
-                    lhsT=e["wdq"][:, h, :].bitcast(FP8X4),
-                    lhsT_scale=e["wdqs"][:, h, :],
-                    rhs=e["wq"][:, h, :].bitcast(FP8X4),
-                    rhs_scale=e["wqs"][:, h, :],
-                    start=False,
-                    stop=(hh0(c) + h == 7),
+                    out=kz[h][:],
+                    lhsT=kq[:, gp, :].bitcast(FP8X4),
+                    lhsT_scale=kqs[:, gp, :],
+                    rhs=cd[:, col : col + BLK].bitcast(FP8X4),
+                    rhs_scale=sc[:, col : col + BLK],
+                    start=(n_done == 0),
+                    stop=(n_done == PASSES - 1),
                 )
 
-        def tp_f32():
-            return psum.tile([P, 2, 2, P], F32, name="tp", tag="tp", bufs=4)
+        def residual(h):
+            nk = work.tile([P, 4, P], F32, name="nk", tag="nk", bufs=2)
+            nc.scalar.activation(out=nk[:], in_=kz[h][:].rearrange("n (p t) -> n t p", t=4), func=COPY, scale=-1.0)
+            tr = psum.tile([P, P, 4], F32, name="tp", tag="tp", bufs=3)
+            turned[h] = tr
+            for t in range(4):
+                nc.tensor.matmul(
+                    tr[:, :, t], lhsT=sraw[:, BLK * h + t : BLK * (h + 1) : 4], rhs=identb[:], start=True, stop=False
+                )
+                nc.tensor.matmul(tr[:, :, t], lhsT=nk[:, t, :], rhs=ident[:], is_transpose=True, start=False, stop=True)
+
+        def gains(h):
+            ww = work.tile([P, 2, BLK], BF16, name="ww", tag="ww", bufs=3, align_bytes=64)
+            ep[h] = ww
+            for i, gain in enumerate((gt, gdt)):
+                nc.vector.tensor_tensor(
+                    out=ww[:, i, :].rearrange("p (n t) -> p n t", t=4),
+                    in0=turned[h][:],
+                    in1=gain[:, h, :].unsqueeze(1).to_broadcast([P, P, 4]),
+                    op=MULT,
+                )
+
+        def gram(h):
+            wq = work.tile([P, 2, P], U32, name="wq", tag="wq", bufs=2, align_bytes=64)
+            wqs = work.tile([P, 2, P], U8, name="wqs", tag="wqs", bufs=2, align_bytes=64)
+            nc.vector.quantize_mx(
+                out=wq[:].rearrange("p i n -> p (i n)").bitcast(FP8X4),
+                scales=wqs[:].rearrange("p i n -> p (i n)"),
+                in_=ep[h][:].rearrange("p i x -> p (i x)"),
+            )
+            nc.tensor.matmul_mx(
+                out=qj[:],
+                lhsT=wq[:, 1, :].bitcast(FP8X4),
+                lhsT_scale=wqs[:, 1, :],
+                rhs=wq[:, 0, :].bitcast(FP8X4),
+                rhs_scale=wqs[:, 0, :],
+                start=False,
+                stop=(h == L // BLK - 1),
+            )
 
         def k_turn(q):
-            ps = tp_f32()
+            ps = psum.tile([P, 2, 2, P], F32, name="tp", tag="tp", bufs=3)
             words = kg[:].bitcast(F32)
             for j in range(2):
                 for u in range(2):
@@ -260,33 +194,23 @@ def tile_josephkalmanupdate_w_kernel(tc, s, z_bytes, z_scale, kgain, g, d, r, ou
                 in_=ps[:].rearrange("p j u n -> p j n u"),
             )
 
-        def k_q(q):
-            a, b = 4 * q, 4 * q + 4
+        def k_quant(src, cd, sc):
             nc.vector.quantize_mx(
-                out=kq[:, a:b, :].rearrange("p g n -> p (g n)").bitcast(FP8X4),
-                scales=kqs[:, a:b, :].rearrange("p g n -> p (g n)"),
-                in_=kT[:, a:b, :].rearrange("p g x -> p (g x)"),
+                out=cd[:].rearrange("p g n -> p (g n)").bitcast(FP8X4),
+                scales=sc[:].rearrange("p g n -> p (g n)"),
+                in_=src[:].rearrange("p g x -> p (g x)"),
             )
 
-        def kr_mul(q):
-            a, b = 4 * q, 4 * q + 4
+        def kr_mul(a, b):
             nc.vector.tensor_tensor(
                 out=krT[:, a:b, :].rearrange("p g (n t) -> p g n t", t=4),
                 in0=kT[:, a:b, :].rearrange("p g (n t) -> p g n t", t=4),
-                in1=rt[:, a:b, :].unsqueeze(2).to_broadcast([P, 4, P, 4]),
+                in1=rt[:, a:b, :].unsqueeze(2).to_broadcast([P, b - a, P, 4]),
                 op=MULT,
             )
 
-        def kr_q(q):
-            a, b = 4 * q, 4 * q + 4
-            nc.vector.quantize_mx(
-                out=krq[:, a:b, :].rearrange("p g n -> p (g n)").bitcast(FP8X4),
-                scales=krqs[:, a:b, :].rearrange("p g n -> p (g n)"),
-                in_=krT[:, a:b, :].rearrange("p g x -> p (g x)"),
-            )
-
-        def q_all():
-            for gp in range(KP):
+        def q_passes():
+            for gp in range(PASSES):
                 nc.tensor.matmul_mx(
                     out=qj[:],
                     lhsT=krq[:, gp, :].bitcast(FP8X4),
@@ -297,183 +221,97 @@ def tile_josephkalmanupdate_w_kernel(tc, s, z_bytes, z_scale, kgain, g, d, r, ou
                     stop=False,
                 )
 
-        def s_perm(q):
-            sperm[q] = epool.tile([P, 4, P], BF16, name="sperm", tag="sperm", bufs=2)
-            nc.scalar.copy(
-                out=sperm[q][:].rearrange("p T (A i) -> p T A i", i=4),
-                in_=sraw[:, 512 * q : 512 * (q + 1)].rearrange("p (A T i) -> p T A i", T=4, i=4),
-            )
-
-        def s_turn(q):
-            ps = psum.tile([P, 4, P], BF16, name="tp", tag="tp", bufs=4)
-            for T in range(4):
-                nc.tensor.transpose(ps[:, T, :], sperm[q][:, T, :], identb[:])
-            nc.scalar.copy(out=sT[:, q, :, :], in_=ps[:])
-
-        def gd_perm():
-            nc.vector.tensor_copy(
-                out=gdperm[:].rearrange("p T (A i) -> p T A i", i=4),
-                in_=gdraw[:].rearrange("p (A T i) -> p T A i", T=4, i=4),
-            )
-
-        def gd_prep():
-            ps = psum.tile([P, 4, P], BF16, name="tp", tag="tp", bufs=4)
-            for T in range(4):
-                nc.tensor.transpose(ps[:, T, :], gdperm[:, T, :], identb[:])
-            nc.vector.tensor_copy(out=gT[:].rearrange("p h T -> p T h"), in_=ps[:, :, 0:8])
-            nc.vector.tensor_copy(out=dT[:].rearrange("p h T -> p T h"), in_=ps[:, :, 8:16])
-            nc.vector.tensor_tensor(out=gdT[:], in0=gT[:], in1=dT[:], op=MULT)
-
-        DSET = (1, 5)
-        esteps = [u for u in range(nu) if u % 8 not in DSET]
-        dunits = [u for u in range(nu) if u % 8 in DSET]
-        PSET = (13, 21, 29)
-        SPLIT.update({15: 16, 23: 16, 31: 16})
-        ns = len(esteps)
-        tasks = {}
-
-        def at(step, fn, *args):
-            tasks.setdefault(step, []).append((fn, args))
-
-        at(2, k_turn, 0)
-        at(2, k_turn, 1)
-        at(3, k_turn, 2)
-        at(3, k_turn, 3)
-        at(5, gd_perm)
-        at(6, gd_prep)
-        at(4, k_q, 0)
-        at(4, k_q, 1)
-        at(6, kr_mul, 0)
-        at(6, kr_mul, 1)
-        at(7, kr_q, 0)
-        at(7, kr_q, 1)
-        at(7, q_all)
-        for c, w in enumerate(CHUNKS):
-            end = 6 * (c + 1) - 1
-            for h in range(w // 512):
-                k = 5 if c == 0 else end - 8 if c == len(CHUNKS) - 1 else end - 3 + h
-                at(k, s_perm, hh0(c) + h)
-                at(k + 1, s_turn, hh0(c) + h)
-            if c < len(CHUNKS) - 1:
-                k = end + (5 if c == len(CHUNKS) - 2 else 4)
-                for h in range(w // 512):
-                    at(k, e_t1, c, h)
-                at(k + 1, e_mul, c, "w", gT)
-                at(k + 2, e_mul, c, "wd", gdT)
-                at(k + 2, e_q, c, "w")
-                at(k + 3, e_q, c, "wd")
-                at(k + 3, e_j, c)
-
         with tc.manual_schedule():
             zsv = z_scale.rearrange("(g p t) o -> p g (t o)", p=P, t=4)
             nc.scalar.dma_start(out=zs[:, 0:2, :], in_=zsv[:, 0:2, :])
             nc.scalar.dma_start(out=zs[:, 2:8, :], in_=zsv[:, 2:8, :])
-            order = []
-            for k in range(ns):
-                if k % 3 == 0:
-                    order += [esteps[k], dunits[k // 3]]
-                else:
-                    order += [esteps[k]]
-            nload = 0
-
-            nc.gpsimd.memset(gdraw[:], 0.0)
             make_identity(nc, ident[:])
             nc.gpsimd.tensor_copy(out=identb[:], in_=ident[:])
 
-            def small():
-                nc.sync.dma_start(out=rt[:], in_=r.rearrange("(g p t) -> p g t", p=P, t=4))
-                nc.sync.dma_start(out=gdraw[0:8, :], in_=g.rearrange("(h x) -> h x", h=8))
-                nc.sync.dma_start(out=gdraw[8:16, :], in_=d.rearrange("(h x) -> h x", h=8))
+            order = []
+            for k in range(STEPS):
+                order.append(pair_units[k])
+                if k % 3 == 0:
+                    order.append(plane_units[k // 3])
+            for t0 in (0, 2):
+                load(order[0], t0, t0 + 2)
+                load(order[1], t0, t0 + 2)
+            load(order[2])
+            nc.sync.dma_start(out=kg[:, 0:2048], in_=kgain[:, 0:2048])
+            nc.sync.dma_start(out=kg[:, 2048:4096], in_=kgain[:, 2048:4096])
+            load(order[3])
+            nc.sync.dma_start(out=rt[:], in_=r.rearrange("(g p t) -> p g t", p=P, t=4))
+            load(order[4])
+            load(order[5])
+            nc.sync.dma_start(out=gt[:], in_=g.rearrange("(h p t) -> p h t", p=P, t=4))
+            nc.sync.dma_start(out=dt_[:], in_=d.rearrange("(h p t) -> p h t", p=P, t=4))
+            load(order[6])
+            nc.sync.dma_start(out=sraw[:], in_=s)
+            nload = 7
 
-            def s_load(a, b):
-                nc.sync.dma_start(out=sraw[:, a:b], in_=s[:, a:b])
-
-            def k_load(a, b):
-                nc.sync.dma_start(out=kg[:, a:b], in_=kgain[:, a:b])
-
-            extra = {
-                4: [(k_load, (0, 2048))],
-                5: [(k_load, (2048, 4096))],
-                6: [(small, ())],
-                7: [(s_load, (0, 1536))],
-                9: [(s_load, (1536, 4096))],
-            }
-
-            def load_next(n):
-                load(order[n])
-                for fn, args in extra.get(n + 1, []):
-                    fn(*args)
-
-            for n in range(5):
-                load_next(n)
-            nload = 5
-
-            last = len(CHUNKS) - 1
-            fin = []
-            done = {}
-
-            def quantized(u):
-                quant(u)
-                c, gp, lo, w = units[u]
-                done.setdefault(c, []).append(gp)
-                seq = done[c]
-                if c < last:
-                    if len(seq) == KP:
-                        kzall(c)
-                else:
-                    if len(seq) == 1:
-                        for T in range(4):
-                            fin.append(psum.tile([P, P], F32, name="tp", tag="tp", bufs=4))
-                    for T in range(4):
-                        kzpass(c, 0, T, gp, fin[T][:], first=seq[0], final=gp if len(seq) == KP else -1)
-
-            for k in range(ns + 1):
+            K_READY = 2
+            for k in range(STEPS):
+                last = k == STEPS - 1
                 while nload < len(order) and nload < k + k // 3 + 6:
-                    load_next(nload)
+                    load(order[nload])
                     nload += 1
-                if k < ns:
-                    il_alloc(esteps[k])
-                    widen_e(esteps[k])
                 if k >= 1:
-                    word(esteps[k - 1], "V" if k == ns else "S")
-                if k < ns:
-                    dd = dunits[k // 3]
-                    if k % 3 == 0:
-                        il_alloc(dd)
-                        for t in range(4 if dd in PSET else 3):
-                            d_widen(dd, t)
-                    elif k % 3 == 1:
-                        if dd not in PSET:
-                            d_widen(dd, 3)
-                        for x in (0, 1):
-                            p_inter(dd, x) if dd in PSET else d_inter(dd, x)
-                    else:
-                        for x in (2, 3):
-                            p_inter(dd, x) if dd in PSET else d_inter(dd, x)
-                    if esteps[k] in SPLIT:
-                        for t in range(4):
-                            d_widen(esteps[k], t)
-                        for T in range(4):
-                            d_inter(esteps[k], T)
-                for fn, args in tasks.get(k, []):
-                    fn(*args)
-                if k >= 1 and k % 3 == 0:
-                    quantized(dunits[k // 3 - 1])
-                if k >= 1:
-                    quantized(esteps[k - 1])
-            for k in sorted(x for x in tasks if x > ns):
-                for fn, args in tasks[k]:
-                    fn(*args)
-            e_alloc(last)
-            for T in range(4):
-                nc.vector.tensor_tensor(
-                    out=ep[last]["t1"][:, 0, 128 * T : 128 * (T + 1)], in0=sT[:, 7, T, :], in1=fin[T][:], op=SUB
-                )
-            e_mul(last, "wd", gdT)
-            e_mul(last, "w", gT)
-            e_q(last, "wd")
-            e_q(last, "w")
-            e_j(last)
-            res = epool.tile([P, P], F32, name="res", tag="res", bufs=1)
+                    join(pair_units[k - 1])
+                pu = plane_units[k // 3]
+                if k % 3 == 0:
+                    for t in range(3):
+                        widen_plane(pu, t)
+                elif k % 3 == 1:
+                    widen_plane(pu, 3)
+                    interleave(pu, 0, 256)
+                else:
+                    interleave(pu, 256, 768)
+                    pe_interleave_out(pu, 768, via_pe)
+                if k == K_READY - 1:
+                    for q in range(4):
+                        k_turn(q)
+                if k % 3 == 1:
+                    via_pe = pe_interleave(pu, 768)
+                closing = k - 6 - LAG
+                if closing >= 0 and closing % 6 < 2:
+                    residual(2 * (closing // 6) + closing % 6)
+                if not last:
+                    widen_pairs(pair_units[k])
+                else:
+                    for lo in (0, BLK):
+                        widen_pairs(pair_units[k], lo, lo + BLK)
+                        join(pair_units[k], lo, lo + BLK)
+                if k == K_READY:
+                    k_quant(kT, kq, kqs)
+                if k in (K_READY, K_READY + 1):
+                    kr_mul(4 * (k - K_READY), 4 * (k - K_READY + 1))
+                if k == K_READY + 2:
+                    k_quant(krT, krq, krqs)
+                    nc.vector.tensor_tensor(out=gdt[:], in0=gt[:], in1=dt_[:], op=MULT)
+                    q_passes()
+                if closing >= 2 and (closing - 2) % 6 < 2:
+                    gram(2 * ((closing - 2) // 6) + (closing - 2) % 6)
+                if closing >= 1 and (closing - 1) % 6 < 2:
+                    gains(2 * ((closing - 1) // 6) + (closing - 1) % 6)
+                ready = []
+                if k >= 3 and k % 3 == 0:
+                    ready.append(plane_units[k // 3 - 1])
+                if k >= LAG:
+                    ready.append(pair_units[k - LAG])
+                for u in ready:
+                    quant(u)
+                    kz_pass(u)
+
+            rest = [plane_units[-1]] + pair_units[STEPS - LAG :]
+            for lo in (0, BLK):
+                for u in rest:
+                    quant(u, lo, lo + BLK)
+                    kz_pass(u, lo, lo + BLK)
+                residual(6 + lo // BLK)
+            gains(6)
+            gains(7)
+            gram(6)
+            gram(7)
+            res = work.tile([P, P], F32, name="res", tag="res", bufs=1)
             nc.vector.tensor_copy(out=res[:], in_=qj[:])
             nc.sync.dma_start(out=out, in_=res[:])

@@ -20,10 +20,8 @@ PASSES = M // 512
 W = 1024
 BLK = 512
 CHUNKS = L // W
-PAIR_PASSES = (0, 2, 3, 4, 6, 7)
-PLANE_PASSES = (1, 5)
-STEPS = CHUNKS * len(PAIR_PASSES)
 LAG = 2
+QUARTER = 256
 
 
 def tile_josephkalmanupdate_w_kernel(tc, s, z_bytes, z_scale, kgain, g, d, r, out):
@@ -50,84 +48,86 @@ def tile_josephkalmanupdate_w_kernel(tc, s, z_bytes, z_scale, kgain, g, d, r, ou
         sraw = keep.tile([P, L], BF16, name="sraw")
         qj = psum.tile([P, P], F32, name="qj", tag="qj", bufs=1)
 
-        pair_units = [(c, gp) for c in range(CHUNKS) for gp in PAIR_PASSES]
-        plane_units = [(c, gp) for c in range(CHUNKS) for gp in PLANE_PASSES]
+        groups = [(c, g0, 0, W) for c in range(CHUNKS) for g0 in (0, 4)]
+        groups = groups[:-1] + [(CHUNKS - 1, 4, 0, BLK), (CHUNKS - 1, 4, BLK, W)]
+        pair_units = [(c, g0 + i, lo, hi) for c, g0, lo, hi in groups for i in (0, 2, 3)]
+        plane_units = [(c, g0 + 1, lo, hi) for c, g0, lo, hi in groups]
+        steps = len(pair_units)
 
-        zb, pairs, planes, il, codes, kz, turned, ep = {}, {}, {}, {}, {}, {}, {}, {}
+        zb, pairs, planes, il, kz, turned, ep = {}, {}, {}, {}, {}, {}, {}
         passes_done = {}
 
-        def load(u, t0=0, t1=4):
-            c, gp = u
-            if t0 == 0:
-                zb[u] = work.tile([P, 4, W], U8, name="zb", tag="zb", bufs=7)
+        def load(c, gp, ts=slice(0, 4)):
+            if ts.start == 0:
+                zb[c, gp] = work.tile([P, 4, W], U8, name="zb", tag="zb", bufs=7)
             rows = z_bytes[512 * gp : 512 * (gp + 1), W * c : W * (c + 1)].rearrange("(p t) w -> p t w", t=4)
-            nc.sync.dma_start(out=zb[u][:, t0:t1, :], in_=rows[:, t0:t1, :])
+            nc.sync.dma_start(out=zb[c, gp][:, ts, :], in_=rows[:, ts, :])
 
-        def widen_pairs(u, lo=0, hi=W):
-            if lo == 0:
-                pairs[u] = work.tile([P, 2, 2 * W], BF16, name="pairs", tag="pairs", bufs=3, align_bytes=64)
-            for t in range(4):
+        def widen_pairs(u):
+            c, gp, lo, hi = u
+            pairs[u] = work.tile([P, 2, 2 * W], BF16, name="pairs", tag="pairs", bufs=3, align_bytes=64)
+            for t in (0, 2, 1, 3):
                 nc.vector.tensor_scalar(
-                    out=pairs[u][:, t // 2, 2 * lo : 2 * hi].rearrange("p (l e) -> p e l", e=2)[:, t % 2],
-                    in0=zb[u][:, t, lo:hi].bitcast(F8),
-                    scalar1=zs[:, u[1], t : t + 1],
+                    out=pairs[u][:, t // 2, 0 : 2 * (hi - lo)].rearrange("p (l e) -> p e l", e=2)[:, t % 2],
+                    in0=zb[c, gp][:, t, lo:hi].bitcast(F8),
+                    scalar1=zs[:, gp, t : t + 1],
                     scalar2=None,
                     op0=MULT,
                 )
 
-        def join(u, lo=0, hi=W):
-            if lo == 0:
-                il[u] = work.tile([P, 4 * W], BF16, name="il", tag="il", bufs=4, align_bytes=64)
-            nc.scalar.copy(
-                out=il[u][:, 4 * lo : 4 * hi].bitcast(F32).rearrange("p (l u) -> p l u", u=2),
-                in_=pairs[u][:].rearrange("p u x -> p (u x)").bitcast(F32).rearrange("p (u l) -> p l u", u=2)[:, lo:hi, :],
+        def join(u, copy):
+            w = u[3] - u[2]
+            il[u] = work.tile([P, 4 * W], BF16, name="il", tag="il", bufs=4, align_bytes=64)
+            copy(
+                out=il[u][:, 0 : 4 * w].bitcast(F32).rearrange("p (l u) -> p l u", u=2),
+                in_=pairs[u][:].rearrange("p u x -> p (u x)").bitcast(F32).rearrange("p (u l) -> p l u", u=2)[:, 0:w, :],
             )
 
         def widen_plane(u, t):
+            c, gp, lo, hi = u
             if t == 0:
                 planes[u] = work.tile([P, 4, W], BF16, name="planes", tag="planes", bufs=2, align_bytes=64)
                 il[u] = work.tile([P, 4 * W], BF16, name="il_s", tag="il_s", bufs=2, align_bytes=64)
             nc.scalar.activation(
-                out=planes[u][:, t, :], in_=zb[u][:, t, :].bitcast(F8), func=COPY, scale=zs[:, u[1], t : t + 1]
+                out=planes[u][:, t, 0 : hi - lo],
+                in_=zb[c, gp][:, t, lo:hi].bitcast(F8),
+                func=COPY,
+                scale=zs[:, gp, t : t + 1],
             )
 
-        def interleave(u, lo, hi):
+        def interleave(u, a, b):
             nc.scalar.copy(
-                out=il[u][:, 4 * lo : 4 * hi].rearrange("p (l t) -> p l t", t=4),
-                in_=planes[u][:, :, lo:hi].rearrange("p t l -> p l t"),
+                out=il[u][:, 4 * a : 4 * b].rearrange("p (l t) -> p l t", t=4),
+                in_=planes[u][:, :, a:b].rearrange("p t l -> p l t"),
             )
 
-        def pe_interleave(u, lo):
+        def pe_interleave(u, a):
             ps = psum.tile([P, 2, 512], BF16, name="tp", tag="tp", bufs=3)
             for x in range(2):
                 nc.tensor.matmul(
                     ps[:, x, :].rearrange("p (l t) -> p l t", t=4),
                     lhsT=identb[:],
-                    rhs=planes[u][:, :, lo + P * x : lo + P * (x + 1)].rearrange("p t l -> p l t"),
+                    rhs=planes[u][:, :, a + P * x : a + P * (x + 1)].rearrange("p t l -> p l t"),
                     start=True,
                     stop=True,
                 )
             return ps
 
-        def pe_interleave_out(u, lo, ps):
+        def pe_interleave_out(u, a, ps):
             nc.scalar.copy(
-                out=il[u][:, 4 * lo : 4 * lo + 1024].bitcast(F32), in_=ps[:].rearrange("p x n -> p (x n)").bitcast(F32)
+                out=il[u][:, 4 * a : 4 * (a + QUARTER)].bitcast(F32),
+                in_=ps[:].rearrange("p x n -> p (x n)").bitcast(F32),
             )
 
-        def quant(u, lo=0, hi=W):
-            if lo == 0:
-                codes[u] = (
-                    work.tile([P, W], U32, name="zc", tag="zc", bufs=3, align_bytes=64),
-                    work.tile([P, W], U8, name="zsc", tag="zsc", bufs=3, align_bytes=64),
-                )
-            cd, sc = codes[u]
-            nc.vector.quantize_mx(out=cd[:, lo:hi].bitcast(FP8X4), scales=sc[:, lo:hi], in_=il[u][:, 4 * lo : 4 * hi])
-
-        def kz_pass(u, lo=0, hi=W):
-            c, gp = u
-            cd, sc = codes[u]
-            for col in range(lo, hi, BLK):
-                h = (W * c + col) // BLK
+        def quant_and_multiply(u):
+            c, gp, lo, hi = u
+            w = hi - lo
+            cd = work.tile([P, W], U32, name="zc", tag="zc", bufs=3, align_bytes=64)
+            sc = work.tile([P, W], U8, name="zsc", tag="zsc", bufs=3, align_bytes=64)
+            nc.vector.quantize_mx(out=cd[:, 0:w].bitcast(FP8X4), scales=sc[:, 0:w], in_=il[u][:, 0 : 4 * w])
+            closed = []
+            for col in range(0, w, BLK):
+                h = (W * c + lo + col) // BLK
                 if h not in kz:
                     kz[h] = psum.tile([P, BLK], F32, name="kz", tag="kz", bufs=4)
                 n_done = passes_done.get(h, 0)
@@ -141,17 +141,28 @@ def tile_josephkalmanupdate_w_kernel(tc, s, z_bytes, z_scale, kgain, g, d, r, ou
                     start=(n_done == 0),
                     stop=(n_done == PASSES - 1),
                 )
+                if n_done == PASSES - 1:
+                    closed.append(h)
+            return closed
+
+        def s_turn(h):
+            turned[h] = psum.tile([P, P, 4], F32, name="tp", tag="tp", bufs=3)
+            for t in range(4):
+                nc.tensor.matmul(
+                    turned[h][:, :, t],
+                    lhsT=sraw[:, BLK * h + t : BLK * (h + 1) : 4],
+                    rhs=identb[:],
+                    start=(t == 0),
+                    stop=False,
+                )
 
         def residual(h):
             nk = work.tile([P, 4, P], F32, name="nk", tag="nk", bufs=2)
             nc.scalar.activation(out=nk[:], in_=kz[h][:].rearrange("n (p t) -> n t p", t=4), func=COPY, scale=-1.0)
-            tr = psum.tile([P, P, 4], F32, name="tp", tag="tp", bufs=3)
-            turned[h] = tr
             for t in range(4):
                 nc.tensor.matmul(
-                    tr[:, :, t], lhsT=sraw[:, BLK * h + t : BLK * (h + 1) : 4], rhs=identb[:], start=True, stop=False
+                    turned[h][:, :, t], lhsT=nk[:, t, :], rhs=ident[:], is_transpose=True, start=False, stop=(t == 3)
                 )
-                nc.tensor.matmul(tr[:, :, t], lhsT=nk[:, t, :], rhs=ident[:], is_transpose=True, start=False, stop=True)
 
         def gains(h):
             ww = work.tile([P, 2, BLK], BF16, name="ww", tag="ww", bufs=3, align_bytes=64)
@@ -178,7 +189,7 @@ def tile_josephkalmanupdate_w_kernel(tc, s, z_bytes, z_scale, kgain, g, d, r, ou
                 lhsT_scale=wqs[:, 1, :],
                 rhs=wq[:, 0, :].bitcast(FP8X4),
                 rhs_scale=wqs[:, 0, :],
-                start=False,
+                start=(h == 0),
                 stop=(h == L // BLK - 1),
             )
 
@@ -217,7 +228,7 @@ def tile_josephkalmanupdate_w_kernel(tc, s, z_bytes, z_scale, kgain, g, d, r, ou
                     lhsT_scale=krqs[:, gp, :],
                     rhs=kq[:, gp, :].bitcast(FP8X4),
                     rhs_scale=kqs[:, gp, :],
-                    start=(gp == 0),
+                    start=False,
                     stop=False,
                 )
 
@@ -228,90 +239,90 @@ def tile_josephkalmanupdate_w_kernel(tc, s, z_bytes, z_scale, kgain, g, d, r, ou
             make_identity(nc, ident[:])
             nc.gpsimd.tensor_copy(out=identb[:], in_=ident[:])
 
-            order = []
-            for k in range(STEPS):
-                order.append(pair_units[k])
-                if k % 3 == 0:
-                    order.append(plane_units[k // 3])
-            for t0 in (0, 2):
-                load(order[0], t0, t0 + 2)
-                load(order[1], t0, t0 + 2)
-            load(order[2])
+            order = [(c, gp) for c in range(CHUNKS) for gp in range(PASSES)]
+            for half in range(2):
+                load(*order[0], slice(half, 4, 2))
+                load(*order[1], slice(2 * half, 2 * half + 2))
+            load(*order[2])
             nc.sync.dma_start(out=kg[:, 0:2048], in_=kgain[:, 0:2048])
             nc.sync.dma_start(out=kg[:, 2048:4096], in_=kgain[:, 2048:4096])
-            load(order[3])
+            load(*order[3])
             nc.sync.dma_start(out=rt[:], in_=r.rearrange("(g p t) -> p g t", p=P, t=4))
-            load(order[4])
-            load(order[5])
+            load(*order[4])
+            load(*order[5])
             nc.sync.dma_start(out=gt[:], in_=g.rearrange("(h p t) -> p h t", p=P, t=4))
             nc.sync.dma_start(out=dt_[:], in_=d.rearrange("(h p t) -> p h t", p=P, t=4))
-            load(order[6])
+            load(*order[6])
             nc.sync.dma_start(out=sraw[:], in_=s)
             nload = 7
 
             K_READY = 2
-            for k in range(STEPS):
-                last = k == STEPS - 1
+            last_blocks = (L // BLK - 2, L // BLK - 1)
+            turn_at, gains_at, gram_at = {}, {}, {}
+            for k in range(steps):
                 while nload < len(order) and nload < k + k // 3 + 6:
-                    load(order[nload])
+                    load(*order[nload])
                     nload += 1
-                if k >= 1:
-                    join(pair_units[k - 1])
                 pu = plane_units[k // 3]
+                by_pe = pu[3] - pu[2] - QUARTER
+                if k % 3 == 1:
+                    widen_plane(pu, 3)
+                if k >= 1:
+                    join(pair_units[k - 1], nc.scalar.copy)
                 if k % 3 == 0:
                     for t in range(3):
                         widen_plane(pu, t)
                 elif k % 3 == 1:
-                    widen_plane(pu, 3)
-                    interleave(pu, 0, 256)
+                    if by_pe > QUARTER:
+                        interleave(pu, 0, QUARTER)
                 else:
-                    interleave(pu, 256, 768)
-                    pe_interleave_out(pu, 768, via_pe)
+                    interleave(pu, QUARTER if by_pe > QUARTER else 0, by_pe)
+                    pe_interleave_out(pu, by_pe, via_pe)
                 if k == K_READY - 1:
                     for q in range(4):
                         k_turn(q)
                 if k % 3 == 1:
-                    via_pe = pe_interleave(pu, 768)
-                closing = k - 6 - LAG
-                if closing >= 0 and closing % 6 < 2:
-                    residual(2 * (closing // 6) + closing % 6)
-                if not last:
-                    widen_pairs(pair_units[k])
-                else:
-                    for lo in (0, BLK):
-                        widen_pairs(pair_units[k], lo, lo + BLK)
-                        join(pair_units[k], lo, lo + BLK)
+                    via_pe = pe_interleave(pu, by_pe)
+                if k == steps - 2:
+                    for h in last_blocks:
+                        s_turn(h)
+                if k in turn_at:
+                    s_turn(turn_at[k])
+                    residual(turn_at[k])
+                widen_pairs(pair_units[k])
                 if k == K_READY:
                     k_quant(kT, kq, kqs)
-                if k in (K_READY, K_READY + 1):
-                    kr_mul(4 * (k - K_READY), 4 * (k - K_READY + 1))
+                    kr_mul(0, 4)
                 if k == K_READY + 2:
-                    k_quant(krT, krq, krqs)
                     nc.vector.tensor_tensor(out=gdt[:], in0=gt[:], in1=dt_[:], op=MULT)
-                    q_passes()
-                if closing >= 2 and (closing - 2) % 6 < 2:
-                    gram(2 * ((closing - 2) // 6) + (closing - 2) % 6)
-                if closing >= 1 and (closing - 1) % 6 < 2:
-                    gains(2 * ((closing - 1) // 6) + (closing - 1) % 6)
+                if k in gram_at:
+                    gram(gram_at[k])
+                if k in gains_at:
+                    gains(gains_at[k])
                 ready = []
                 if k >= 3 and k % 3 == 0:
                     ready.append(plane_units[k // 3 - 1])
                 if k >= LAG:
                     ready.append(pair_units[k - LAG])
                 for u in ready:
-                    quant(u)
-                    kz_pass(u)
+                    for i, h in enumerate(quant_and_multiply(u)):
+                        if h not in last_blocks:
+                            turn_at[k + 1 + i] = h
+                            gains_at[k + 3 + i] = h
+                            gram_at[k + 4 + i] = h
 
-            rest = [plane_units[-1]] + pair_units[STEPS - LAG :]
-            for lo in (0, BLK):
-                for u in rest:
-                    quant(u, lo, lo + BLK)
-                    kz_pass(u, lo, lo + BLK)
-                residual(6 + lo // BLK)
-            gains(6)
-            gains(7)
-            gram(6)
-            gram(7)
+            residual(last_blocks[0])
+            join(pair_units[-1], nc.vector.tensor_copy)
+            for u in [plane_units[-1]] + pair_units[steps - LAG :]:
+                quant_and_multiply(u)
+            residual(last_blocks[1])
+            kr_mul(4, 8)
+            gains(last_blocks[0])
+            k_quant(krT, krq, krqs)
+            q_passes()
+            gram(last_blocks[0])
+            gains(last_blocks[1])
+            gram(last_blocks[1])
             res = work.tile([P, P], F32, name="res", tag="res", bufs=1)
             nc.vector.tensor_copy(out=res[:], in_=qj[:])
             nc.sync.dma_start(out=out, in_=res[:])

@@ -54,7 +54,7 @@ def tile_josephkalmanupdate_w_kernel(tc, s, z_bytes, z_scale, kgain, g, d, r, ou
         plane_units = [(c, g0 + 1, lo, hi) for c, g0, lo, hi in groups]
         steps = len(pair_units)
 
-        zb, pairs, planes, il, kz, turned, ep = {}, {}, {}, {}, {}, {}, {}
+        zb, pairs, planes, il, codes, kz, nk, turned, ep = {}, {}, {}, {}, {}, {}, {}, {}, {}
         passes_done = {}
 
         def load(c, gp, ts=slice(0, 4)):
@@ -97,8 +97,8 @@ def tile_josephkalmanupdate_w_kernel(tc, s, z_bytes, z_scale, kgain, g, d, r, ou
 
         def interleave(u, a, b):
             nc.scalar.copy(
-                out=il[u][:, 4 * a : 4 * b].rearrange("p (l t) -> p l t", t=4),
-                in_=planes[u][:, :, a:b].rearrange("p t l -> p l t"),
+                out=il[u][:, 4 * a : 4 * b].rearrange("p (c i t) -> p c t i", i=4, t=4),
+                in_=planes[u][:, :, a:b].rearrange("p t (c i) -> p c t i", i=4),
             )
 
         def pe_interleave(u, a):
@@ -119,14 +119,18 @@ def tile_josephkalmanupdate_w_kernel(tc, s, z_bytes, z_scale, kgain, g, d, r, ou
                 in_=ps[:].rearrange("p x n -> p (x n)").bitcast(F32),
             )
 
-        def quant_and_multiply(u):
-            c, gp, lo, hi = u
-            w = hi - lo
-            cd = work.tile([P, W], U32, name="zc", tag="zc", bufs=3, align_bytes=64)
-            sc = work.tile([P, W], U8, name="zsc", tag="zsc", bufs=3, align_bytes=64)
+        def quant(u):
+            w = u[3] - u[2]
+            cd = work.tile([P, W], U32, name="zc", tag="zc", bufs=4, align_bytes=64)
+            sc = work.tile([P, W], U8, name="zsc", tag="zsc", bufs=4, align_bytes=64)
             nc.vector.quantize_mx(out=cd[:, 0:w].bitcast(FP8X4), scales=sc[:, 0:w], in_=il[u][:, 0 : 4 * w])
+            codes[u] = (cd, sc)
+
+        def multiply(u):
+            c, gp, lo, hi = u
+            cd, sc = codes[u]
             closed = []
-            for col in range(0, w, BLK):
+            for col in range(0, hi - lo, BLK):
                 h = (W * c + lo + col) // BLK
                 if h not in kz:
                     kz[h] = psum.tile([P, BLK], F32, name="kz", tag="kz", bufs=4)
@@ -156,12 +160,14 @@ def tile_josephkalmanupdate_w_kernel(tc, s, z_bytes, z_scale, kgain, g, d, r, ou
                     stop=False,
                 )
 
-        def residual(h):
-            nk = work.tile([P, 4, P], F32, name="nk", tag="nk", bufs=2)
-            nc.scalar.activation(out=nk[:], in_=kz[h][:].rearrange("n (p t) -> n t p", t=4), func=COPY, scale=-1.0)
+        def kz_out(h):
+            nk[h] = work.tile([P, 4, P], F32, name="nk", tag="nk", bufs=2)
+            nc.scalar.activation(out=nk[h][:], in_=kz[h][:].rearrange("n (p t) -> n t p", t=4), func=COPY, scale=-1.0)
+
+        def kz_turn(h):
             for t in range(4):
                 nc.tensor.matmul(
-                    turned[h][:, :, t], lhsT=nk[:, t, :], rhs=ident[:], is_transpose=True, start=False, stop=(t == 3)
+                    turned[h][:, :, t], lhsT=nk[h][:, t, :], rhs=ident[:], is_transpose=True, start=False, stop=(t == 3)
                 )
 
         def gains(h):
@@ -244,9 +250,9 @@ def tile_josephkalmanupdate_w_kernel(tc, s, z_bytes, z_scale, kgain, g, d, r, ou
                 load(*order[0], slice(half, 4, 2))
                 load(*order[1], slice(2 * half, 2 * half + 2))
             load(*order[2])
+            load(*order[3])
             nc.sync.dma_start(out=kg[:, 0:2048], in_=kgain[:, 0:2048])
             nc.sync.dma_start(out=kg[:, 2048:4096], in_=kgain[:, 2048:4096])
-            load(*order[3])
             nc.sync.dma_start(out=rt[:], in_=r.rearrange("(g p t) -> p g t", p=P, t=4))
             load(*order[4])
             load(*order[5])
@@ -256,9 +262,10 @@ def tile_josephkalmanupdate_w_kernel(tc, s, z_bytes, z_scale, kgain, g, d, r, ou
             nc.sync.dma_start(out=sraw[:], in_=s)
             nload = 7
 
-            K_READY = 2
+            K_READY = LAG
+            KR_AT = [LAG]
             last_blocks = (L // BLK - 2, L // BLK - 1)
-            turn_at, gains_at, gram_at = {}, {}, {}
+            out_at, turn_at, gains_at, gram_at = {}, {}, {}, {}
             for k in range(steps):
                 while nload < len(order) and nload < k + k // 3 + 6:
                     load(*order[nload])
@@ -278,7 +285,7 @@ def tile_josephkalmanupdate_w_kernel(tc, s, z_bytes, z_scale, kgain, g, d, r, ou
                 else:
                     interleave(pu, QUARTER if by_pe > QUARTER else 0, by_pe)
                     pe_interleave_out(pu, by_pe, via_pe)
-                if k == K_READY - 1:
+                if k == 1:
                     for q in range(4):
                         k_turn(q)
                 if k % 3 == 1:
@@ -288,41 +295,54 @@ def tile_josephkalmanupdate_w_kernel(tc, s, z_bytes, z_scale, kgain, g, d, r, ou
                         s_turn(h)
                 if k in turn_at:
                     s_turn(turn_at[k])
-                    residual(turn_at[k])
+                    kz_turn(turn_at[k])
+                if k in out_at:
+                    kz_out(out_at[k])
                 widen_pairs(pair_units[k])
-                if k == K_READY:
-                    k_quant(kT, kq, kqs)
-                    kr_mul(0, 4)
                 if k == K_READY + 2:
                     nc.vector.tensor_tensor(out=gdt[:], in0=gt[:], in1=dt_[:], op=MULT)
+                if k in KR_AT:
+                    kr_mul(4 * KR_AT.index(k), 4 * KR_AT.index(k) + 4)
                 if k in gram_at:
                     gram(gram_at[k])
                 if k in gains_at:
                     gains(gains_at[k])
                 ready = []
-                if k >= 3 and k % 3 == 0:
-                    ready.append(plane_units[k // 3 - 1])
+                if k >= LAG + 1 and (k - LAG - 1) % 3 == 0 and k >= 3:
+                    ready.append(plane_units[(k - LAG - 1) // 3])
                 if k >= LAG:
                     ready.append(pair_units[k - LAG])
                 for u in ready:
-                    for i, h in enumerate(quant_and_multiply(u)):
+                    quant(u)
+                    if k == K_READY:
+                        k_quant(kT, kq, kqs)
+                    for i, h in enumerate(multiply(u)):
                         if h not in last_blocks:
-                            turn_at[k + 1 + i] = h
-                            gains_at[k + 3 + i] = h
-                            gram_at[k + 4 + i] = h
+                            out_at[k + 1 + i] = h
+                            turn_at[k + 2 + i] = h
+                            gains_at[k + 4 + i] = h
+                            gram_at[k + 5 + i] = h
 
-            residual(last_blocks[0])
+            kz_out(last_blocks[0])
             join(pair_units[-1], nc.vector.tensor_copy)
-            for u in [plane_units[-1]] + pair_units[steps - LAG :]:
-                quant_and_multiply(u)
-            residual(last_blocks[1])
+            for u in pair_units[steps - LAG :] + [plane_units[-1]]:
+                quant(u)
+                multiply(u)
+            kz_out(last_blocks[1])
+            for h in last_blocks:
+                kz_turn(h)
             kr_mul(4, 8)
-            gains(last_blocks[0])
+            for k in range(steps, steps + 4):
+                if k in gram_at:
+                    gram(gram_at[k])
+                if k in gains_at:
+                    gains(gains_at[k])
             k_quant(krT, krq, krqs)
             q_passes()
-            gram(last_blocks[0])
-            gains(last_blocks[1])
-            gram(last_blocks[1])
+            for h in last_blocks:
+                gains(h)
+            for h in last_blocks:
+                gram(h)
             res = work.tile([P, P], F32, name="res", tag="res", bufs=1)
             nc.vector.tensor_copy(out=res[:], in_=qj[:])
             nc.sync.dma_start(out=out, in_=res[:])

@@ -21,6 +21,7 @@ W = 1024
 BLK = 512
 CHUNKS = L // W
 LAG = 2
+EXTRA = 256
 QUARTER = 256
 
 
@@ -38,6 +39,7 @@ def tile_josephkalmanupdate_w_kernel(tc, s, z_bytes, z_scale, kgain, g, d, r, ou
         gt = keep.tile([P, 8, 4], BF16, name="gt")
         dt_ = keep.tile([P, 8, 4], BF16, name="dtile")
         gdt = keep.tile([P, 8, 4], F32, name="gdt")
+        gt32 = keep.tile([P, 8, 4], F32, name="gt32")
         kg = keep.tile([P, M], BF16, name="kg")
         kT = keep.tile([P, PASSES, P * 4], BF16, name="kT", align_bytes=64)
         krT = keep.tile([P, PASSES, P * 4], BF16, name="krT", align_bytes=64)
@@ -53,6 +55,10 @@ def tile_josephkalmanupdate_w_kernel(tc, s, z_bytes, z_scale, kgain, g, d, r, ou
         pair_units = [(c, g0 + i, lo, hi) for c, g0, lo, hi in groups for i in (0, 2, 3)]
         plane_units = [(c, g0 + 1, lo, hi) for c, g0, lo, hi in groups]
         steps = len(pair_units)
+        shared = [pair_units[-4]]
+
+        def pair_width(u):
+            return u[3] - u[2] - (EXTRA if u in shared else 0)
 
         zb, pairs, planes, il, codes, kz, nk, turned, ep = {}, {}, {}, {}, {}, {}, {}, {}, {}
         passes_done = {}
@@ -65,6 +71,7 @@ def tile_josephkalmanupdate_w_kernel(tc, s, z_bytes, z_scale, kgain, g, d, r, ou
 
         def widen_pairs(u):
             c, gp, lo, hi = u
+            hi = lo + pair_width(u)
             pairs[u] = work.tile([P, 2, 2 * W], BF16, name="pairs", tag="pairs", bufs=3, align_bytes=64)
             for t in (0, 2, 1, 3):
                 nc.vector.tensor_scalar(
@@ -76,7 +83,7 @@ def tile_josephkalmanupdate_w_kernel(tc, s, z_bytes, z_scale, kgain, g, d, r, ou
                 )
 
         def join(u, copy):
-            w = u[3] - u[2]
+            w = pair_width(u)
             il[u] = work.tile([P, 4 * W], BF16, name="il", tag="il", bufs=4, align_bytes=64)
             copy(
                 out=il[u][:, 0 : 4 * w].bitcast(F32).rearrange("p (l u) -> p l u", u=2),
@@ -86,7 +93,7 @@ def tile_josephkalmanupdate_w_kernel(tc, s, z_bytes, z_scale, kgain, g, d, r, ou
         def widen_plane(u, t):
             c, gp, lo, hi = u
             if t == 0:
-                planes[u] = work.tile([P, 4, W], BF16, name="planes", tag="planes", bufs=2, align_bytes=64)
+                planes[u] = work.tile([P, 4, W], BF16, name="planes", tag="planes", bufs=3, align_bytes=64)
                 il[u] = work.tile([P, 4 * W], BF16, name="il_s", tag="il_s", bufs=2, align_bytes=64)
             nc.scalar.activation(
                 out=planes[u][:, t, 0 : hi - lo],
@@ -94,6 +101,17 @@ def tile_josephkalmanupdate_w_kernel(tc, s, z_bytes, z_scale, kgain, g, d, r, ou
                 func=COPY,
                 scale=zs[:, gp, t : t + 1],
             )
+
+        def widen_extra(u):
+            c, gp, lo, hi = u
+            planes[u] = work.tile([P, 4, W], BF16, name="planes", tag="planes", bufs=3, align_bytes=64)
+            for t in range(4):
+                nc.scalar.activation(
+                    out=planes[u][:, t, hi - lo - EXTRA : hi - lo],
+                    in_=zb[c, gp][:, t, hi - EXTRA : hi].bitcast(F8),
+                    func=COPY,
+                    scale=zs[:, gp, t : t + 1],
+                )
 
         def interleave(u, a, b):
             nc.scalar.copy(
@@ -181,6 +199,21 @@ def tile_josephkalmanupdate_w_kernel(tc, s, z_bytes, z_scale, kgain, g, d, r, ou
                     op=MULT,
                 )
 
+        def gains_on_scalar(h):
+            ww = work.tile([P, 2, BLK], BF16, name="ww", tag="ww", bufs=3, align_bytes=64)
+            ep[h] = ww
+            wp = work.tile([P, 2, 4, P], BF16, name="wp", tag="wp", bufs=1)
+            for i, gain in enumerate((gt32, gdt)):
+                for t in range(4):
+                    nc.scalar.activation(
+                        out=wp[:, i, t, :], in_=turned[h][:, :, t], func=COPY, scale=gain[:, h, t : t + 1]
+                    )
+            for i in range(2):
+                nc.scalar.copy(
+                    out=ww[:, i, :].rearrange("p (c j t) -> p c t j", j=4, t=4),
+                    in_=wp[:, i].rearrange("p t (c j) -> p c t j", j=4),
+                )
+
         def gram(h):
             wq = work.tile([P, 2, P], U32, name="wq", tag="wq", bufs=2, align_bytes=64)
             wqs = work.tile([P, 2, P], U8, name="wqs", tag="wqs", bufs=2, align_bytes=64)
@@ -211,11 +244,11 @@ def tile_josephkalmanupdate_w_kernel(tc, s, z_bytes, z_scale, kgain, g, d, r, ou
                 in_=ps[:].rearrange("p j u n -> p j n u"),
             )
 
-        def k_quant(src, cd, sc):
+        def k_quant(src, cd, sc, a=0, b=PASSES):
             nc.vector.quantize_mx(
-                out=cd[:].rearrange("p g n -> p (g n)").bitcast(FP8X4),
-                scales=sc[:].rearrange("p g n -> p (g n)"),
-                in_=src[:].rearrange("p g x -> p (g x)"),
+                out=cd[:, a:b, :].rearrange("p g n -> p (g n)").bitcast(FP8X4),
+                scales=sc[:, a:b, :].rearrange("p g n -> p (g n)"),
+                in_=src[:, a:b, :].rearrange("p g x -> p (g x)"),
             )
 
         def kr_mul(a, b):
@@ -240,16 +273,21 @@ def tile_josephkalmanupdate_w_kernel(tc, s, z_bytes, z_scale, kgain, g, d, r, ou
 
         with tc.manual_schedule():
             zsv = z_scale.rearrange("(g p t) o -> p g (t o)", p=P, t=4)
-            nc.scalar.dma_start(out=zs[:, 0:2, :], in_=zsv[:, 0:2, :])
-            nc.scalar.dma_start(out=zs[:, 2:8, :], in_=zsv[:, 2:8, :])
+            nc.scalar.dma_start(out=zs[:, 0:3, :], in_=zsv[:, 0:3, :])
             make_identity(nc, ident[:])
             nc.gpsimd.tensor_copy(out=identb[:], in_=ident[:])
 
             order = [(c, gp) for c in range(CHUNKS) for gp in range(PASSES)]
+            for pair_rows, plane_rows in (
+                (slice(0, 1), slice(0, 1)),
+                (slice(2, 3), slice(1, 2)),
+                (slice(1, 4, 2), slice(2, 4)),
+            ):
+                load(*order[0], pair_rows)
+                load(*order[1], plane_rows)
             for half in range(2):
-                load(*order[0], slice(half, 4, 2))
-                load(*order[1], slice(2 * half, 2 * half + 2))
-            load(*order[2])
+                load(*order[2], slice(half, 4, 2))
+            nc.sync.dma_start(out=zs[:, 3:8, :], in_=zsv[:, 3:8, :])
             load(*order[3])
             nc.sync.dma_start(out=kg[:, 0:2048], in_=kgain[:, 0:2048])
             nc.sync.dma_start(out=kg[:, 2048:4096], in_=kgain[:, 2048:4096])
@@ -263,7 +301,6 @@ def tile_josephkalmanupdate_w_kernel(tc, s, z_bytes, z_scale, kgain, g, d, r, ou
             nload = 7
 
             K_READY = LAG
-            KR_AT = [LAG]
             last_blocks = (L // BLK - 2, L // BLK - 1)
             out_at, turn_at, gains_at, gram_at = {}, {}, {}, {}
             for k in range(steps):
@@ -276,6 +313,8 @@ def tile_josephkalmanupdate_w_kernel(tc, s, z_bytes, z_scale, kgain, g, d, r, ou
                     widen_plane(pu, 3)
                 if k >= 1:
                     join(pair_units[k - 1], nc.scalar.copy)
+                    if pair_units[k - 1] in shared:
+                        interleave(pair_units[k - 1], pair_width(pair_units[k - 1]), pair_width(pair_units[k - 1]) + EXTRA)
                 if k % 3 == 0:
                     for t in range(3):
                         widen_plane(pu, t)
@@ -285,6 +324,8 @@ def tile_josephkalmanupdate_w_kernel(tc, s, z_bytes, z_scale, kgain, g, d, r, ou
                 else:
                     interleave(pu, QUARTER if by_pe > QUARTER else 0, by_pe)
                     pe_interleave_out(pu, by_pe, via_pe)
+                if pair_units[k] in shared:
+                    widen_extra(pair_units[k])
                 if k == 1:
                     for q in range(4):
                         k_turn(q)
@@ -301,8 +342,7 @@ def tile_josephkalmanupdate_w_kernel(tc, s, z_bytes, z_scale, kgain, g, d, r, ou
                 widen_pairs(pair_units[k])
                 if k == K_READY + 2:
                     nc.vector.tensor_tensor(out=gdt[:], in0=gt[:], in1=dt_[:], op=MULT)
-                if k in KR_AT:
-                    kr_mul(4 * KR_AT.index(k), 4 * KR_AT.index(k) + 4)
+                    nc.vector.tensor_copy(out=gt32[:], in_=gt[:])
                 if k in gram_at:
                     gram(gram_at[k])
                 if k in gains_at:
@@ -331,16 +371,18 @@ def tile_josephkalmanupdate_w_kernel(tc, s, z_bytes, z_scale, kgain, g, d, r, ou
             kz_out(last_blocks[1])
             for h in last_blocks:
                 kz_turn(h)
-            kr_mul(4, 8)
+            gains_on_scalar(last_blocks[0])
+            for a in (0, 4):
+                kr_mul(a, a + 4)
             for k in range(steps, steps + 4):
                 if k in gram_at:
                     gram(gram_at[k])
                 if k in gains_at:
                     gains(gains_at[k])
-            k_quant(krT, krq, krqs)
+            for a in (0, 4):
+                k_quant(krT, krq, krqs, a, a + 4)
             q_passes()
-            for h in last_blocks:
-                gains(h)
+            gains(last_blocks[1])
             for h in last_blocks:
                 gram(h)
             res = work.tile([P, P], F32, name="res", tag="res", bufs=1)

@@ -13,6 +13,7 @@ U8 = mybir.dt.uint8
 F8 = mybir.dt.float8_e4m3fn
 FP8X4 = mybir.dt.float8_e4m3fn_x4
 MULT = mybir.AluOpType.mult
+ADD = mybir.AluOpType.add
 COPY = mybir.ActivationFunctionType.Copy
 
 P = 128
@@ -20,9 +21,9 @@ PASSES = M // 512
 W = 1024
 BLK = 512
 CHUNKS = L // W
-LAG = 2
-EXTRA = 256
-QUARTER = 256
+G_FULL = 896
+G_HALF = 384
+FIRST_PRODUCT = 6
 
 
 def tile_josephkalmanupdate_w_kernel(tc, s, z_bytes, z_scale, kgain, g, d, r, out):
@@ -34,7 +35,9 @@ def tile_josephkalmanupdate_w_kernel(tc, s, z_bytes, z_scale, kgain, g, d, r, ou
 
         ident = keep.tile([P, P], F32, name="ident")
         identb = keep.tile([P, P], BF16, name="identb")
-        zs = keep.tile([P, PASSES, 4], F32, name="zs")
+        zs_sq = keep.tile([P, P], F32, name="zs_sq")
+        zs_t = keep.tile([P, P], F32, name="zs_t")
+        zs = zs_sq[:, 0 : 4 * PASSES].rearrange("p (g t) -> p g t", t=4)
         rt = keep.tile([P, PASSES, 4], BF16, name="rt")
         gt = keep.tile([P, 8, 4], BF16, name="gt")
         dt_ = keep.tile([P, 8, 4], BF16, name="dtile")
@@ -49,52 +52,70 @@ def tile_josephkalmanupdate_w_kernel(tc, s, z_bytes, z_scale, kgain, g, d, r, ou
         krqs = keep.tile([P, PASSES, P], U8, name="krqs", align_bytes=64)
         sraw = keep.tile([P, L], BF16, name="sraw")
         qj = psum.tile([P, P], F32, name="qj", tag="qj", bufs=1)
+        zs_ps = psum.tile([P, P], F32, name="zs_ps", tag="zs_ps", bufs=1)
 
-        groups = [(c, g0, 0, W) for c in range(CHUNKS) for g0 in (0, 4)]
-        groups = groups[:-1] + [(CHUNKS - 1, 4, 0, BLK), (CHUNKS - 1, 4, BLK, W)]
-        pair_units = [(c, g0 + i, lo, hi) for c, g0, lo, hi in groups for i in (0, 2, 3)]
-        plane_units = [(c, g0 + 1, lo, hi) for c, g0, lo, hi in groups]
-        steps = len(pair_units)
-        shared = [pair_units[-4]]
+        ranges = [(c, gp, 0, W) for c in range(CHUNKS) for gp in range(0, PASSES, 2)][:-2]
+        ranges = ranges + [(CHUNKS - 1, gp, lo, lo + BLK) for lo in (0, BLK) for gp in (4, 6)]
+        v_units = ranges
+        g_units = [(c, gp + 1, lo, hi) for c, gp, lo, hi in ranges]
+        steps = len(ranges)
 
-        def pair_width(u):
-            return u[3] - u[2] - (EXTRA if u in shared else 0)
-
-        zb, pairs, planes, il, codes, kz, nk, turned, ep = {}, {}, {}, {}, {}, {}, {}, {}, {}
+        zb, pairs, planes, il, il_s, codes, kz, nk, turned, ep = {}, {}, {}, {}, {}, {}, {}, {}, {}, {}
         passes_done = {}
+        k_ps = []
 
         def load(c, gp, ts=slice(0, 4)):
             if ts.start == 0:
-                zb[c, gp] = work.tile([P, 4, W], U8, name="zb", tag="zb", bufs=7)
+                zb[c, gp] = work.tile([P, 4, W], U8, name="zb", tag="zb", bufs=8)
             rows = z_bytes[512 * gp : 512 * (gp + 1), W * c : W * (c + 1)].rearrange("(p t) w -> p t w", t=4)
             nc.sync.dma_start(out=zb[c, gp][:, ts, :], in_=rows[:, ts, :])
 
         def widen_pairs(u):
             c, gp, lo, hi = u
-            hi = lo + pair_width(u)
-            pairs[u] = work.tile([P, 2, 2 * W], BF16, name="pairs", tag="pairs", bufs=3, align_bytes=64)
+            pairs[u] = work.tile([P, 2, 2 * W], BF16, name="pairs", tag="pairs", bufs=1, align_bytes=64)
             for t in (0, 2, 1, 3):
                 nc.vector.tensor_scalar(
-                    out=pairs[u][:, t // 2, 0 : 2 * (hi - lo)].rearrange("p (l e) -> p e l", e=2)[:, t % 2],
-                    in0=zb[c, gp][:, t, lo:hi].bitcast(F8),
+                    out=pairs[u][:, t // 2, :].rearrange("p (l e) -> p e l", e=2)[:, t % 2],
+                    in0=zb[c, gp][:, t, :].bitcast(F8),
                     scalar1=zs[:, gp, t : t + 1],
                     scalar2=None,
                     op0=MULT,
                 )
 
-        def join(u, copy):
-            w = pair_width(u)
-            il[u] = work.tile([P, 4 * W], BF16, name="il", tag="il", bufs=4, align_bytes=64)
-            copy(
-                out=il[u][:, 0 : 4 * w].bitcast(F32).rearrange("p (l u) -> p l u", u=2),
-                in_=pairs[u][:].rearrange("p u x -> p (u x)").bitcast(F32).rearrange("p (u l) -> p l u", u=2)[:, 0:w, :],
+        def join(u, tag, bufs):
+            il[u] = work.tile([P, 4 * W], BF16, name=tag, tag=tag, bufs=bufs, align_bytes=64)
+            nc.vector.tensor_copy(
+                out=il[u][:].bitcast(F32).rearrange("p (l u) -> p l u", u=2),
+                in_=pairs[u][:].rearrange("p u x -> p (u x)").bitcast(F32).rearrange("p (u l) -> p l u", u=2),
+            )
+
+        def cast(u):
+            c, gp, lo, hi = u
+            planes[u] = work.tile([P, 4, W], BF16, name="raw", tag="raw", bufs=3, align_bytes=64)
+            if hi - lo == W:
+                nc.scalar.copy(
+                    out=planes[u][:].rearrange("p t l -> p (t l)"),
+                    in_=zb[c, gp][:].rearrange("p t l -> p (t l)").bitcast(F8),
+                )
+            else:
+                for t in range(4):
+                    nc.scalar.copy(out=planes[u][:, t, 0 : hi - lo], in_=zb[c, gp][:, t, lo:hi].bitcast(F8))
+
+        def scale_interleave(u):
+            c, gp, lo, hi = u
+            w = hi - lo
+            il[u] = work.tile([P, 4 * W], BF16, name="il_v", tag="il_v", bufs=3, align_bytes=64)
+            nc.vector.tensor_tensor(
+                out=il[u][:, 0 : 4 * w].rearrange("p (c i t) -> p c t i", i=4, t=4),
+                in0=planes[u][:, :, 0:w].rearrange("p t (c i) -> p c t i", i=4),
+                in1=zs_ps[:, 4 * gp : 4 * gp + 4].unsqueeze(1).unsqueeze(3).to_broadcast([P, w // 4, 4, 4]),
+                op=MULT,
             )
 
         def widen_plane(u, t):
             c, gp, lo, hi = u
             if t == 0:
                 planes[u] = work.tile([P, 4, W], BF16, name="planes", tag="planes", bufs=3, align_bytes=64)
-                il[u] = work.tile([P, 4 * W], BF16, name="il_s", tag="il_s", bufs=2, align_bytes=64)
             nc.scalar.activation(
                 out=planes[u][:, t, 0 : hi - lo],
                 in_=zb[c, gp][:, t, lo:hi].bitcast(F8),
@@ -102,47 +123,71 @@ def tile_josephkalmanupdate_w_kernel(tc, s, z_bytes, z_scale, kgain, g, d, r, ou
                 scale=zs[:, gp, t : t + 1],
             )
 
-        def widen_extra(u):
-            c, gp, lo, hi = u
-            planes[u] = work.tile([P, 4, W], BF16, name="planes", tag="planes", bufs=3, align_bytes=64)
-            for t in range(4):
-                nc.scalar.activation(
-                    out=planes[u][:, t, hi - lo - EXTRA : hi - lo],
-                    in_=zb[c, gp][:, t, hi - EXTRA : hi].bitcast(F8),
-                    func=COPY,
-                    scale=zs[:, gp, t : t + 1],
-                )
+        def g_width(u):
+            k = g_units.index(u) + 1
+            if k == steps:
+                return 0
+            if v_units[k][3] - v_units[k][2] < W:
+                return G_HALF
+            return G_FULL if k >= FIRST_PRODUCT else G_FULL - P
 
-        def interleave(u, a, b):
-            nc.scalar.copy(
-                out=il[u][:, 4 * a : 4 * b].rearrange("p (c i t) -> p c t i", i=4, t=4),
-                in_=planes[u][:, :, a:b].rearrange("p t (c i) -> p c t i", i=4),
+        def pe_interleave(u):
+            a = u[3] - u[2] - P
+            ps = psum.tile([P, 512], BF16, name="tp", tag="tp", bufs=1)
+            nc.tensor.matmul(
+                ps[:].rearrange("p (l t) -> p l t", t=4),
+                lhsT=identb[:],
+                rhs=planes[u][:, :, a : a + P].rearrange("p t l -> p l t"),
+                start=True,
+                stop=True,
             )
-
-        def pe_interleave(u, a):
-            ps = psum.tile([P, 2, 512], BF16, name="tp", tag="tp", bufs=3)
-            for x in range(2):
-                nc.tensor.matmul(
-                    ps[:, x, :].rearrange("p (l t) -> p l t", t=4),
-                    lhsT=identb[:],
-                    rhs=planes[u][:, :, a + P * x : a + P * (x + 1)].rearrange("p t l -> p l t"),
-                    start=True,
-                    stop=True,
-                )
             return ps
 
-        def pe_interleave_out(u, a, ps):
-            nc.scalar.copy(
-                out=il[u][:, 4 * a : 4 * (a + QUARTER)].bitcast(F32),
-                in_=ps[:].rearrange("p x n -> p (x n)").bitcast(F32),
+        def interleave_rest(u, ps):
+            a, b = g_width(u), u[3] - u[2] - P
+            il_s[u] = work.tile([P, 4 * (W - G_HALF)], BF16, name="il_s", tag="il_s", bufs=3, align_bytes=64)
+            if b > a:
+                nc.scalar.copy(
+                    out=il_s[u][:, 0 : 4 * (b - a)].rearrange("p (c i t) -> p c t i", i=4, t=4),
+                    in_=planes[u][:, :, a:b].rearrange("p t (c i) -> p c t i", i=4),
+                )
+            nc.scalar.copy(out=il_s[u][:, 4 * (b - a) : 4 * (b - a + P)].bitcast(F32), in_=ps[:].bitcast(F32))
+
+        def quant_range(u, src, a, b):
+            lo, width = a, W
+            while lo < b:
+                if lo + width <= b:
+                    quant(u, src[:, 4 * (lo - a) : 4 * (lo - a + width)], lo, lo + width)
+                    lo = lo + width
+                width = width // 2
+
+        def quant_g(u):
+            w, a = u[3] - u[2], g_width(u)
+            new_codes(u)
+            quant_range(u, il_s[u], a, w)
+            if a:
+                quant_range(u, il[u], 0, a)
+
+        def g_interleave(u):
+            a = g_width(u)
+            il[u] = work.tile([P, 4 * W], BF16, name="il_g", tag="il_g", bufs=1, align_bytes=64)
+            nc.gpsimd.tensor_scalar(
+                out=il[u][:, 0 : 4 * a].rearrange("p (l t) -> p l t", t=4),
+                in0=planes[u][:, :, 0:a].rearrange("p t l -> p l t"),
+                scalar1=1.0,
+                scalar2=0.0,
+                op0=MULT,
+                op1=ADD,
             )
 
-        def quant(u):
-            w = u[3] - u[2]
+        def new_codes(u):
             cd = work.tile([P, W], U32, name="zc", tag="zc", bufs=4, align_bytes=64)
             sc = work.tile([P, W], U8, name="zsc", tag="zsc", bufs=4, align_bytes=64)
-            nc.vector.quantize_mx(out=cd[:, 0:w].bitcast(FP8X4), scales=sc[:, 0:w], in_=il[u][:, 0 : 4 * w])
             codes[u] = (cd, sc)
+
+        def quant(u, src, a, b):
+            cd, sc = codes[u]
+            nc.vector.quantize_mx(out=cd[:, a:b].bitcast(FP8X4), scales=sc[:, a:b], in_=src)
 
         def multiply(u):
             c, gp, lo, hi = u
@@ -167,8 +212,8 @@ def tile_josephkalmanupdate_w_kernel(tc, s, z_bytes, z_scale, kgain, g, d, r, ou
                     closed.append(h)
             return closed
 
-        def s_turn(h):
-            turned[h] = psum.tile([P, P, 4], F32, name="tp", tag="tp", bufs=3)
+        def s_turn(h, tag):
+            turned[h] = psum.tile([P, P, 4], F32, name=tag, tag=tag, bufs=1)
             for t in range(4):
                 nc.tensor.matmul(
                     turned[h][:, :, t],
@@ -188,16 +233,15 @@ def tile_josephkalmanupdate_w_kernel(tc, s, z_bytes, z_scale, kgain, g, d, r, ou
                     turned[h][:, :, t], lhsT=nk[h][:, t, :], rhs=ident[:], is_transpose=True, start=False, stop=(t == 3)
                 )
 
-        def gains(h):
-            ww = work.tile([P, 2, BLK], BF16, name="ww", tag="ww", bufs=3, align_bytes=64)
-            ep[h] = ww
-            for i, gain in enumerate((gt, gdt)):
-                nc.vector.tensor_tensor(
-                    out=ww[:, i, :].rearrange("p (n t) -> p n t", t=4),
-                    in0=turned[h][:],
-                    in1=gain[:, h, :].unsqueeze(1).to_broadcast([P, P, 4]),
-                    op=MULT,
-                )
+        def gain_product(h, i):
+            if i == 0:
+                ep[h] = work.tile([P, 2, BLK], BF16, name="ww", tag="ww", bufs=3, align_bytes=64)
+            nc.vector.tensor_tensor(
+                out=ep[h][:, i, :].rearrange("p (n t) -> p n t", t=4),
+                in0=turned[h][:],
+                in1=(gt, gdt)[i][:, h, :].unsqueeze(1).to_broadcast([P, P, 4]),
+                op=MULT,
+            )
 
         def gains_on_scalar(h):
             ww = work.tile([P, 2, BLK], BF16, name="ww", tag="ww", bufs=3, align_bytes=64)
@@ -233,13 +277,17 @@ def tile_josephkalmanupdate_w_kernel(tc, s, z_bytes, z_scale, kgain, g, d, r, ou
             )
 
         def k_turn(q):
-            ps = psum.tile([P, 2, 2, P], F32, name="tp", tag="tp", bufs=3)
+            ps = psum.tile([P, 2, 2, P], F32, name="kz", tag="kz", bufs=4)
+            k_ps.append(ps)
             words = kg[:].bitcast(F32)
             for j in range(2):
                 for u in range(2):
                     b0 = 256 * (2 * q + j)
                     nc.tensor.transpose(ps[:, j, u, :], words[:, b0 + u : b0 + 256 : 2], ident[:])
-            nc.scalar.copy(
+
+        def k_out(q):
+            ps = k_ps[q]
+            nc.vector.tensor_copy(
                 out=kT[:, 2 * q : 2 * q + 2, :].bitcast(F32).rearrange("p j (n u) -> p j n u", u=2),
                 in_=ps[:].rearrange("p j u n -> p j n u"),
             )
@@ -272,8 +320,8 @@ def tile_josephkalmanupdate_w_kernel(tc, s, z_bytes, z_scale, kgain, g, d, r, ou
                 )
 
         with tc.manual_schedule():
-            zsv = z_scale.rearrange("(g p t) o -> p g (t o)", p=P, t=4)
-            nc.scalar.dma_start(out=zs[:, 0:3, :], in_=zsv[:, 0:3, :])
+            nc.vector.memset(zs_sq[:, 4 * PASSES : P], 0.0)
+            nc.scalar.dma_start(out=zs, in_=z_scale.rearrange("(g p t) o -> p g (t o)", p=P, t=4))
             make_identity(nc, ident[:])
             nc.gpsimd.tensor_copy(out=identb[:], in_=ident[:])
 
@@ -283,106 +331,103 @@ def tile_josephkalmanupdate_w_kernel(tc, s, z_bytes, z_scale, kgain, g, d, r, ou
                 (slice(2, 3), slice(1, 2)),
                 (slice(1, 4, 2), slice(2, 4)),
             ):
-                load(*order[0], pair_rows)
-                load(*order[1], plane_rows)
-            for half in range(2):
-                load(*order[2], slice(half, 4, 2))
-            nc.sync.dma_start(out=zs[:, 3:8, :], in_=zsv[:, 3:8, :])
-            load(*order[3])
+                load(0, 0, pair_rows)
+                load(0, 1, plane_rows)
+            load(0, 2)
+            load(0, 3)
             nc.sync.dma_start(out=kg[:, 0:2048], in_=kgain[:, 0:2048])
             nc.sync.dma_start(out=kg[:, 2048:4096], in_=kgain[:, 2048:4096])
-            nc.sync.dma_start(out=rt[:], in_=r.rearrange("(g p t) -> p g t", p=P, t=4))
-            load(*order[4])
-            load(*order[5])
+            load(0, 4)
+            load(0, 5)
+            load(0, 6)
+            load(0, 7)
             nc.sync.dma_start(out=gt[:], in_=g.rearrange("(h p t) -> p h t", p=P, t=4))
             nc.sync.dma_start(out=dt_[:], in_=d.rearrange("(h p t) -> p h t", p=P, t=4))
-            load(*order[6])
+            nc.sync.dma_start(out=rt[:], in_=r.rearrange("(g p t) -> p g t", p=P, t=4))
             nc.sync.dma_start(out=sraw[:], in_=s)
-            nload = 7
+            nload = 8
 
-            K_READY = LAG
+            def scales_to_psum():
+                once = psum.tile([P, P], F32, name="tp", tag="tp", bufs=1)
+                nc.tensor.transpose(once[:], zs_sq[:], ident[:])
+                nc.scalar.copy(out=zs_t[:], in_=once[:])
+                nc.tensor.transpose(zs_ps[:], zs_t[:], ident[:])
+
             last_blocks = (L // BLK - 2, L // BLK - 1)
-            out_at, turn_at, gains_at, gram_at = {}, {}, {}, {}
+            closed_at, to_turn, products, gram_at = {}, [], [], {}
             for k in range(steps):
-                while nload < len(order) and nload < k + k // 3 + 6:
+                while nload < len(order) and nload < 2 * k + 8:
                     load(*order[nload])
                     nload += 1
-                pu = plane_units[k // 3]
-                by_pe = pu[3] - pu[2] - QUARTER
-                if k % 3 == 1:
-                    widen_plane(pu, 3)
+                uv, ug = v_units[k], g_units[k]
+                w = uv[3] - uv[2]
                 if k >= 1:
-                    join(pair_units[k - 1], nc.scalar.copy)
-                    if pair_units[k - 1] in shared:
-                        interleave(pair_units[k - 1], pair_width(pair_units[k - 1]), pair_width(pair_units[k - 1]) + EXTRA)
-                if k % 3 == 0:
-                    for t in range(3):
-                        widen_plane(pu, t)
-                elif k % 3 == 1:
-                    if by_pe > QUARTER:
-                        interleave(pu, 0, QUARTER)
-                else:
-                    interleave(pu, QUARTER if by_pe > QUARTER else 0, by_pe)
-                    pe_interleave_out(pu, by_pe, via_pe)
-                if pair_units[k] in shared:
-                    widen_extra(pair_units[k])
+                    g_interleave(g_units[k - 1])
                 if k == 1:
                     for q in range(4):
                         k_turn(q)
-                if k % 3 == 1:
-                    via_pe = pe_interleave(pu, by_pe)
-                if k == steps - 2:
-                    for h in last_blocks:
-                        s_turn(h)
-                if k in turn_at:
-                    s_turn(turn_at[k])
-                    kz_turn(turn_at[k])
-                if k in out_at:
-                    kz_out(out_at[k])
-                widen_pairs(pair_units[k])
-                if k == K_READY + 2:
+                for t in range(4):
+                    widen_plane(ug, t)
+                    if t == 1:
+                        if k == 0:
+                            scales_to_psum()
+                        for h in closed_at.get(k - 1, []):
+                            kz_out(h)
+                            to_turn.append(h)
+                ps = pe_interleave(ug)
+                if k + 1 < steps:
+                    cast(v_units[k + 1])
+                interleave_rest(ug, ps)
+                if k == 0:
+                    widen_pairs(uv)
+                    join(uv, "il_g", 1)
+                else:
+                    scale_interleave(uv)
+                if k == 1:
+                    for q in range(4):
+                        k_out(q)
+                if products:
+                    h, i = products.pop(0)
+                    gain_product(h, i)
+                    if i == 1:
+                        gram_at[k + 1] = h
+                if to_turn and not products and to_turn[0] not in last_blocks:
+                    h = to_turn.pop(0)
+                    s_turn(h, "turned")
+                    kz_turn(h)
+                    products = [(h, 0), (h, 1)]
+                if k == steps - 1:
+                    s_turn(last_blocks[1], "turned")
+                if k == 2:
                     nc.vector.tensor_tensor(out=gdt[:], in0=gt[:], in1=dt_[:], op=MULT)
                     nc.vector.tensor_copy(out=gt32[:], in_=gt[:])
                 if k in gram_at:
                     gram(gram_at[k])
-                if k in gains_at:
-                    gains(gains_at[k])
-                ready = []
-                if k >= LAG + 1 and (k - LAG - 1) % 3 == 0 and k >= 3:
-                    ready.append(plane_units[(k - LAG - 1) // 3])
-                if k >= LAG:
-                    ready.append(pair_units[k - LAG])
-                for u in ready:
-                    quant(u)
-                    if k == K_READY:
-                        k_quant(kT, kq, kqs)
-                    for i, h in enumerate(multiply(u)):
-                        if h not in last_blocks:
-                            out_at[k + 1 + i] = h
-                            turn_at[k + 2 + i] = h
-                            gains_at[k + 4 + i] = h
-                            gram_at[k + 5 + i] = h
+                new_codes(uv)
+                quant(uv, il[uv][:, 0 : 4 * w], 0, w)
+                if k == 1:
+                    k_quant(kT, kq, kqs)
+                    multiply(v_units[0])
+                if k >= 1:
+                    multiply(uv)
+                    quant_g(g_units[k - 1])
+                    closed_at[k] = multiply(g_units[k - 1])
 
-            kz_out(last_blocks[0])
-            join(pair_units[-1], nc.vector.tensor_copy)
-            for u in pair_units[steps - LAG :] + [plane_units[-1]]:
-                quant(u)
-                multiply(u)
+            s_turn(last_blocks[0], "tp")
+            quant_g(g_units[-1])
+            multiply(g_units[-1])
+            kz_turn(last_blocks[0])
             kz_out(last_blocks[1])
-            for h in last_blocks:
-                kz_turn(h)
+            kz_turn(last_blocks[1])
             gains_on_scalar(last_blocks[0])
             for a in (0, 4):
                 kr_mul(a, a + 4)
-            for k in range(steps, steps + 4):
-                if k in gram_at:
-                    gram(gram_at[k])
-                if k in gains_at:
-                    gains(gains_at[k])
+            gram(gram_at[steps])
             for a in (0, 4):
                 k_quant(krT, krq, krqs, a, a + 4)
             q_passes()
-            gains(last_blocks[1])
+            for i in range(2):
+                gain_product(last_blocks[1], i)
             for h in last_blocks:
                 gram(h)
             res = work.tile([P, P], F32, name="res", tag="res", bufs=1)

@@ -21,9 +21,11 @@ PASSES = M // 512
 W = 1024
 BLK = 512
 CHUNKS = L // W
-G_FULL = 896
-G_HALF = 384
-FIRST_PRODUCT = 6
+SHORT = (4, 5)
+S_ROWS = {-4: (0,), -3: (1,), -2: (2, 3)}
+S_DONE = (-5, -1)
+S_QUANT = (-4, -1)
+K_OUT = {1: (0, 1), 2: (2,), 3: (3,)}
 
 
 def tile_josephkalmanupdate_w_kernel(tc, s, z_bytes, z_scale, kgain, g, d, r, out):
@@ -54,13 +56,14 @@ def tile_josephkalmanupdate_w_kernel(tc, s, z_bytes, z_scale, kgain, g, d, r, ou
         qj = psum.tile([P, P], F32, name="qj", tag="qj", bufs=1)
         zs_ps = psum.tile([P, P], F32, name="zs_ps", tag="zs_ps", bufs=1)
 
-        ranges = [(c, gp, 0, W) for c in range(CHUNKS) for gp in range(0, PASSES, 2)][:-2]
-        ranges = ranges + [(CHUNKS - 1, gp, lo, lo + BLK) for lo in (0, BLK) for gp in (4, 6)]
-        v_units = ranges
-        g_units = [(c, gp + 1, lo, hi) for c, gp, lo, hi in ranges]
-        steps = len(ranges)
+        whole = [(c, gp, 0, W) for c in range(CHUNKS) for gp in range(PASSES)]
+        c_last = CHUNKS - 1
+        v_units = whole[0:-4:2] + [(c_last, gp, lo, lo + BLK) for lo in (0, BLK) for gp in (4, 6)]
+        g_units = whole[1:-6:2] + [(c_last, gp, lo, lo + BLK) for lo in (0, BLK) for gp in (3, 5)]
+        s_units = [(c_last, PASSES - 1, lo, lo + BLK) for lo in (0, BLK)]
+        steps = len(v_units)
 
-        zb, pairs, planes, il, il_s, codes, kz, nk, turned, ep = {}, {}, {}, {}, {}, {}, {}, {}, {}, {}
+        zb, pairs, planes, il, by_pe, codes, kz, nk, turned, ep = {}, {}, {}, {}, {}, {}, {}, {}, {}, {}
         passes_done = {}
         k_ps = []
 
@@ -73,10 +76,10 @@ def tile_josephkalmanupdate_w_kernel(tc, s, z_bytes, z_scale, kgain, g, d, r, ou
         def widen_pairs(u):
             c, gp, lo, hi = u
             pairs[u] = work.tile([P, 2, 2 * W], BF16, name="pairs", tag="pairs", bufs=1, align_bytes=64)
-            for t in (0, 2, 1, 3):
+            for t, a, b in ((0, 0, W), (2, 0, W), (1, 0, W), (3, 0, BLK), (3, BLK, W)):
                 nc.vector.tensor_scalar(
-                    out=pairs[u][:, t // 2, :].rearrange("p (l e) -> p e l", e=2)[:, t % 2],
-                    in0=zb[c, gp][:, t, :].bitcast(F8),
+                    out=pairs[u][:, t // 2, 2 * a : 2 * b].rearrange("p (l e) -> p e l", e=2)[:, t % 2],
+                    in0=zb[c, gp][:, t, a:b].bitcast(F8),
                     scalar1=zs[:, gp, t : t + 1],
                     scalar2=None,
                     op0=MULT,
@@ -84,38 +87,45 @@ def tile_josephkalmanupdate_w_kernel(tc, s, z_bytes, z_scale, kgain, g, d, r, ou
 
         def join(u, tag, bufs):
             il[u] = work.tile([P, 4 * W], BF16, name=tag, tag=tag, bufs=bufs, align_bytes=64)
-            nc.vector.tensor_copy(
-                out=il[u][:].bitcast(F32).rearrange("p (l u) -> p l u", u=2),
-                in_=pairs[u][:].rearrange("p u x -> p (u x)").bitcast(F32).rearrange("p (u l) -> p l u", u=2),
-            )
+            words = pairs[u][:].rearrange("p u x -> p (u x)").bitcast(F32).rearrange("p (u l) -> p l u", u=2)
+            for a in (0, BLK):
+                nc.vector.tensor_copy(
+                    out=il[u][:, 4 * a : 4 * (a + BLK)].bitcast(F32).rearrange("p (l u) -> p l u", u=2),
+                    in_=words[:, a : a + BLK, :],
+                )
 
         def cast(u):
             c, gp, lo, hi = u
-            planes[u] = work.tile([P, 4, W], BF16, name="raw", tag="raw", bufs=3, align_bytes=64)
-            if hi - lo == W:
+            planes[u] = work.tile([P, 4, W], BF16, name="raw", tag="raw", bufs=2, align_bytes=64)
+            if hi - lo == W and u != v_units[1]:
                 nc.scalar.copy(
                     out=planes[u][:].rearrange("p t l -> p (t l)"),
                     in_=zb[c, gp][:].rearrange("p t l -> p (t l)").bitcast(F8),
                 )
             else:
-                for t in range(4):
-                    nc.scalar.copy(out=planes[u][:, t, 0 : hi - lo], in_=zb[c, gp][:, t, lo:hi].bitcast(F8))
+                for a in range(0, hi - lo, BLK):
+                    for t in range(4):
+                        nc.scalar.copy(
+                            out=planes[u][:, t, a : a + BLK], in_=zb[c, gp][:, t, lo + a : lo + a + BLK].bitcast(F8)
+                        )
 
         def scale_interleave(u):
             c, gp, lo, hi = u
             w = hi - lo
             il[u] = work.tile([P, 4 * W], BF16, name="il_v", tag="il_v", bufs=3, align_bytes=64)
-            nc.vector.tensor_tensor(
-                out=il[u][:, 0 : 4 * w].rearrange("p (c i t) -> p c t i", i=4, t=4),
-                in0=planes[u][:, :, 0:w].rearrange("p t (c i) -> p c t i", i=4),
-                in1=zs_ps[:, 4 * gp : 4 * gp + 4].unsqueeze(1).unsqueeze(3).to_broadcast([P, w // 4, 4, 4]),
-                op=MULT,
-            )
+            part = BLK if u == v_units[1] else w
+            for a in range(0, w, part):
+                nc.vector.tensor_tensor(
+                    out=il[u][:, 4 * a : 4 * (a + part)].rearrange("p (c i t) -> p c t i", i=4, t=4),
+                    in0=planes[u][:, :, a : a + part].rearrange("p t (c i) -> p c t i", i=4),
+                    in1=zs_ps[:, 4 * gp : 4 * gp + 4].unsqueeze(1).unsqueeze(3).to_broadcast([P, part // 4, 4, 4]),
+                    op=MULT,
+                )
 
         def widen_plane(u, t):
             c, gp, lo, hi = u
             if t == 0:
-                planes[u] = work.tile([P, 4, W], BF16, name="planes", tag="planes", bufs=3, align_bytes=64)
+                planes[u] = work.tile([P, 4, W], BF16, name="planes", tag="planes", bufs=4, align_bytes=64)
             nc.scalar.activation(
                 out=planes[u][:, t, 0 : hi - lo],
                 in_=zb[c, gp][:, t, lo:hi].bitcast(F8),
@@ -124,49 +134,30 @@ def tile_josephkalmanupdate_w_kernel(tc, s, z_bytes, z_scale, kgain, g, d, r, ou
             )
 
         def g_width(u):
-            k = g_units.index(u) + 1
-            if k == steps:
+            if u in s_units:
                 return 0
-            if v_units[k][3] - v_units[k][2] < W:
-                return G_HALF
-            return G_FULL if k >= FIRST_PRODUCT else G_FULL - P
+            w = u[3] - u[2] - P
+            return w - P if g_units.index(u) + 1 in SHORT else w
 
-        def pe_interleave(u):
+        def pe_interleave(u, tag, bufs):
             a = u[3] - u[2] - P
-            ps = psum.tile([P, 512], BF16, name="tp", tag="tp", bufs=1)
+            by_pe[u] = psum.tile([P, 512], BF16, name=tag, tag=tag, bufs=bufs)
             nc.tensor.matmul(
-                ps[:].rearrange("p (l t) -> p l t", t=4),
+                by_pe[u][:].rearrange("p (l t) -> p l t", t=4),
                 lhsT=identb[:],
                 rhs=planes[u][:, :, a : a + P].rearrange("p t l -> p l t"),
                 start=True,
                 stop=True,
             )
-            return ps
 
-        def interleave_rest(u, ps):
+        def interleave_rest(u):
             a, b = g_width(u), u[3] - u[2] - P
-            il_s[u] = work.tile([P, 4 * (W - G_HALF)], BF16, name="il_s", tag="il_s", bufs=3, align_bytes=64)
             if b > a:
                 nc.scalar.copy(
-                    out=il_s[u][:, 0 : 4 * (b - a)].rearrange("p (c i t) -> p c t i", i=4, t=4),
+                    out=il[u][:, 4 * a : 4 * b].rearrange("p (c i t) -> p c t i", i=4, t=4),
                     in_=planes[u][:, :, a:b].rearrange("p t (c i) -> p c t i", i=4),
                 )
-            nc.scalar.copy(out=il_s[u][:, 4 * (b - a) : 4 * (b - a + P)].bitcast(F32), in_=ps[:].bitcast(F32))
-
-        def quant_range(u, src, a, b):
-            lo, width = a, W
-            while lo < b:
-                if lo + width <= b:
-                    quant(u, src[:, 4 * (lo - a) : 4 * (lo - a + width)], lo, lo + width)
-                    lo = lo + width
-                width = width // 2
-
-        def quant_g(u):
-            w, a = u[3] - u[2], g_width(u)
-            new_codes(u)
-            quant_range(u, il_s[u], a, w)
-            if a:
-                quant_range(u, il[u], 0, a)
+            nc.scalar.copy(out=il[u][:, 4 * b : 4 * (b + P)].bitcast(F32), in_=by_pe[u][:].bitcast(F32))
 
         def g_interleave(u):
             a = g_width(u)
@@ -180,14 +171,14 @@ def tile_josephkalmanupdate_w_kernel(tc, s, z_bytes, z_scale, kgain, g, d, r, ou
                 op1=ADD,
             )
 
-        def new_codes(u):
-            cd = work.tile([P, W], U32, name="zc", tag="zc", bufs=4, align_bytes=64)
-            sc = work.tile([P, W], U8, name="zsc", tag="zsc", bufs=4, align_bytes=64)
+        def quant(u, parts=1):
+            w = u[3] - u[2]
+            cd = work.tile([P, W], U32, name="zc", tag="zc", bufs=5, align_bytes=64)
+            sc = work.tile([P, W], U8, name="zsc", tag="zsc", bufs=5, align_bytes=64)
             codes[u] = (cd, sc)
-
-        def quant(u, src, a, b):
-            cd, sc = codes[u]
-            nc.vector.quantize_mx(out=cd[:, a:b].bitcast(FP8X4), scales=sc[:, a:b], in_=src)
+            for a in range(0, w, w // parts):
+                b = a + w // parts
+                nc.vector.quantize_mx(out=cd[:, a:b].bitcast(FP8X4), scales=sc[:, a:b], in_=il[u][:, 4 * a : 4 * b])
 
         def multiply(u):
             c, gp, lo, hi = u
@@ -212,8 +203,8 @@ def tile_josephkalmanupdate_w_kernel(tc, s, z_bytes, z_scale, kgain, g, d, r, ou
                     closed.append(h)
             return closed
 
-        def s_turn(h, tag):
-            turned[h] = psum.tile([P, P, 4], F32, name=tag, tag=tag, bufs=1)
+        def s_turn(h, tag, bufs):
+            turned[h] = psum.tile([P, P, 4], F32, name=tag, tag=tag, bufs=bufs)
             for t in range(4):
                 nc.tensor.matmul(
                     turned[h][:, :, t],
@@ -321,7 +312,8 @@ def tile_josephkalmanupdate_w_kernel(tc, s, z_bytes, z_scale, kgain, g, d, r, ou
 
         with tc.manual_schedule():
             nc.vector.memset(zs_sq[:, 4 * PASSES : P], 0.0)
-            nc.scalar.dma_start(out=zs, in_=z_scale.rearrange("(g p t) o -> p g (t o)", p=P, t=4))
+            zsv = z_scale.rearrange("(g p t) o -> p g (t o)", p=P, t=4)
+            nc.scalar.dma_start(out=zs[:, 0:2, :], in_=zsv[:, 0:2, :])
             make_identity(nc, ident[:])
             nc.gpsimd.tensor_copy(out=identb[:], in_=ident[:])
 
@@ -333,6 +325,7 @@ def tile_josephkalmanupdate_w_kernel(tc, s, z_bytes, z_scale, kgain, g, d, r, ou
             ):
                 load(0, 0, pair_rows)
                 load(0, 1, plane_rows)
+            nc.sync.dma_start(out=zs[:, 2:PASSES, :], in_=zsv[:, 2:PASSES, :])
             load(0, 2)
             load(0, 3)
             nc.sync.dma_start(out=kg[:, 0:2048], in_=kgain[:, 0:2048])
@@ -359,33 +352,50 @@ def tile_josephkalmanupdate_w_kernel(tc, s, z_bytes, z_scale, kgain, g, d, r, ou
                 while nload < len(order) and nload < 2 * k + 8:
                     load(*order[nload])
                     nload += 1
-                uv, ug = v_units[k], g_units[k]
-                w = uv[3] - uv[2]
+                uv = v_units[k]
                 if k >= 1:
                     g_interleave(g_units[k - 1])
                 if k == 1:
                     for q in range(4):
                         k_turn(q)
-                for t in range(4):
-                    widen_plane(ug, t)
-                    if t == 1:
-                        if k == 0:
-                            scales_to_psum()
-                        for h in closed_at.get(k - 1, []):
-                            kz_out(h)
-                            to_turn.append(h)
-                ps = pe_interleave(ug)
-                if k + 1 < steps:
+                if k - steps == S_DONE[0]:
+                    for t in range(4):
+                        widen_plane(s_units[0], t)
+                if k < len(g_units):
+                    ug = g_units[k]
+                    for t in range(4):
+                        widen_plane(ug, t)
+                        if t == 1 and k >= 1:
+                            interleave_rest(g_units[k - 1])
+                    if k == 0:
+                        scales_to_psum()
+                    pe_interleave(ug, "tp", 1)
                     cast(v_units[k + 1])
-                interleave_rest(ug, ps)
+                else:
+                    interleave_rest(g_units[k - 1])
+                for h in closed_at.get(k - 1, []):
+                    kz_out(h)
+                    to_turn.append(h)
+                for t in S_ROWS.get(k - steps, ()):
+                    widen_plane(s_units[1], t)
+                if k - steps in S_DONE:
+                    us = s_units[S_DONE.index(k - steps)]
+                    pe_interleave(us, "kz", 4)
+                    il[us] = work.tile([P, 4 * BLK], BF16, name="il_s", tag="il_s", bufs=2, align_bytes=64)
+                    interleave_rest(us)
+                if k == steps - 1:
+                    s_turn(last_blocks[0], "kz", 4)
+                    kz_turn(last_blocks[0])
+                    s_turn(last_blocks[1], "tp", 1)
+                    gains_on_scalar(last_blocks[0])
                 if k == 0:
                     widen_pairs(uv)
                     join(uv, "il_g", 1)
-                else:
-                    scale_interleave(uv)
-                if k == 1:
-                    for q in range(4):
-                        k_out(q)
+                    quant(uv, 2)
+                    continue
+                scale_interleave(uv)
+                for q in K_OUT.get(k, ()):
+                    k_out(q)
                 if products:
                     h, i = products.pop(0)
                     gain_product(h, i)
@@ -393,43 +403,39 @@ def tile_josephkalmanupdate_w_kernel(tc, s, z_bytes, z_scale, kgain, g, d, r, ou
                         gram_at[k + 1] = h
                 if to_turn and not products and to_turn[0] not in last_blocks:
                     h = to_turn.pop(0)
-                    s_turn(h, "turned")
+                    s_turn(h, "turned", 1)
                     kz_turn(h)
                     products = [(h, 0), (h, 1)]
-                if k == steps - 1:
-                    s_turn(last_blocks[1], "turned")
                 if k == 2:
                     nc.vector.tensor_tensor(out=gdt[:], in0=gt[:], in1=dt_[:], op=MULT)
                     nc.vector.tensor_copy(out=gt32[:], in_=gt[:])
                 if k in gram_at:
                     gram(gram_at[k])
-                new_codes(uv)
-                quant(uv, il[uv][:, 0 : 4 * w], 0, w)
-                if k == 1:
-                    k_quant(kT, kq, kqs)
-                    multiply(v_units[0])
-                if k >= 1:
-                    multiply(uv)
-                    quant_g(g_units[k - 1])
-                    closed_at[k] = multiply(g_units[k - 1])
+                ready = [uv, g_units[k - 1]]
+                if k - steps in S_QUANT:
+                    ready.insert(1, s_units[S_QUANT.index(k - steps)])
+                closed_at[k] = []
+                for u in ready:
+                    quant(u)
+                    if u == uv:
+                        for q in K_OUT.get(k, ()):
+                            k_quant(kT, kq, kqs, 2 * q, 2 * q + 2)
+                        if k == 1:
+                            multiply(v_units[0])
+                    closed_at[k] = closed_at[k] + multiply(u)
 
-            s_turn(last_blocks[0], "tp")
-            quant_g(g_units[-1])
-            multiply(g_units[-1])
-            kz_turn(last_blocks[0])
             kz_out(last_blocks[1])
             kz_turn(last_blocks[1])
-            gains_on_scalar(last_blocks[0])
             for a in (0, 4):
                 kr_mul(a, a + 4)
             gram(gram_at[steps])
+            gram(last_blocks[0])
             for a in (0, 4):
                 k_quant(krT, krq, krqs, a, a + 4)
             q_passes()
             for i in range(2):
                 gain_product(last_blocks[1], i)
-            for h in last_blocks:
-                gram(h)
+            gram(last_blocks[1])
             res = work.tile([P, P], F32, name="res", tag="res", bufs=1)
             nc.vector.tensor_copy(out=res[:], in_=qj[:])
             nc.sync.dma_start(out=out, in_=res[:])

@@ -21,7 +21,6 @@ PASSES = M // 512
 W = 1024
 BLK = 512
 CHUNKS = L // W
-SHORT = (4, 5)
 S_ROWS = {-4: (0,), -3: (1,), -2: (2, 3)}
 S_DONE = (-5, -1)
 S_QUANT = (-4, -1)
@@ -62,16 +61,18 @@ def tile_josephkalmanupdate_w_kernel(tc, s, z_bytes, z_scale, kgain, g, d, r, ou
         g_units = whole[1:-6:2] + [(c_last, gp, lo, lo + BLK) for lo in (0, BLK) for gp in (3, 5)]
         s_units = [(c_last, PASSES - 1, lo, lo + BLK) for lo in (0, BLK)]
         steps = len(v_units)
+        first_halves = [(0, 2, lo, lo + BLK) for lo in (0, BLK)]
 
         zb, pairs, planes, il, by_pe, codes, kz, nk, turned, ep = {}, {}, {}, {}, {}, {}, {}, {}, {}, {}
         passes_done = {}
         k_ps = []
 
-        def load(c, gp, ts=slice(0, 4)):
+        def load(u, ts=slice(0, 4)):
+            c, gp, lo, hi = u
             if ts.start == 0:
-                zb[c, gp] = work.tile([P, 4, W], U8, name="zb", tag="zb", bufs=8)
-            rows = z_bytes[512 * gp : 512 * (gp + 1), W * c : W * (c + 1)].rearrange("(p t) w -> p t w", t=4)
-            nc.sync.dma_start(out=zb[c, gp][:, ts, :], in_=rows[:, ts, :])
+                zb[u] = work.tile([P, 4, hi - lo], U8, name="zb", tag="zb", bufs=9)
+            rows = z_bytes[512 * gp : 512 * (gp + 1), W * c + lo : W * c + hi].rearrange("(p t) w -> p t w", t=4)
+            nc.sync.dma_start(out=zb[u][:, ts, :], in_=rows[:, ts, :])
 
         def widen_pairs(u):
             c, gp, lo, hi = u
@@ -79,7 +80,7 @@ def tile_josephkalmanupdate_w_kernel(tc, s, z_bytes, z_scale, kgain, g, d, r, ou
             for t, a, b in ((0, 0, W), (2, 0, W), (1, 0, W), (3, 0, BLK), (3, BLK, W)):
                 nc.vector.tensor_scalar(
                     out=pairs[u][:, t // 2, 2 * a : 2 * b].rearrange("p (l e) -> p e l", e=2)[:, t % 2],
-                    in0=zb[c, gp][:, t, a:b].bitcast(F8),
+                    in0=zb[u][:, t, a:b].bitcast(F8),
                     scalar1=zs[:, gp, t : t + 1],
                     scalar2=None,
                     op0=MULT,
@@ -95,30 +96,20 @@ def tile_josephkalmanupdate_w_kernel(tc, s, z_bytes, z_scale, kgain, g, d, r, ou
                 )
 
         def cast(u):
-            c, gp, lo, hi = u
-            planes[u] = work.tile([P, 4, W], BF16, name="raw", tag="raw", bufs=2, align_bytes=64)
-            if hi - lo == W and u != v_units[1]:
-                nc.scalar.copy(
-                    out=planes[u][:].rearrange("p t l -> p (t l)"),
-                    in_=zb[c, gp][:].rearrange("p t l -> p (t l)").bitcast(F8),
-                )
-            else:
-                for a in range(0, hi - lo, BLK):
-                    for t in range(4):
-                        nc.scalar.copy(
-                            out=planes[u][:, t, a : a + BLK], in_=zb[c, gp][:, t, lo + a : lo + a + BLK].bitcast(F8)
-                        )
+            planes[u] = work.tile([P, 4, u[3] - u[2]], BF16, name="raw", tag="raw", bufs=3, align_bytes=64)
+            nc.scalar.copy(
+                out=planes[u][:].rearrange("p t l -> p (t l)"), in_=zb[u][:].rearrange("p t l -> p (t l)").bitcast(F8)
+            )
 
-        def scale_interleave(u):
+        def scale_interleave(u, parts):
             c, gp, lo, hi = u
-            w = hi - lo
             il[u] = work.tile([P, 4 * W], BF16, name="il_v", tag="il_v", bufs=3, align_bytes=64)
-            part = BLK if u == v_units[1] else w
-            for a in range(0, w, part):
+            for part in parts:
+                a, b = part[2] - lo, part[3] - lo
                 nc.vector.tensor_tensor(
-                    out=il[u][:, 4 * a : 4 * (a + part)].rearrange("p (c i t) -> p c t i", i=4, t=4),
-                    in0=planes[u][:, :, a : a + part].rearrange("p t (c i) -> p c t i", i=4),
-                    in1=zs_ps[:, 4 * gp : 4 * gp + 4].unsqueeze(1).unsqueeze(3).to_broadcast([P, part // 4, 4, 4]),
+                    out=il[u][:, 4 * a : 4 * b].rearrange("p (c i t) -> p c t i", i=4, t=4),
+                    in0=planes[part][:].rearrange("p t (c i) -> p c t i", i=4),
+                    in1=zs_ps[:, 4 * gp : 4 * gp + 4].unsqueeze(1).unsqueeze(3).to_broadcast([P, (b - a) // 4, 4, 4]),
                     op=MULT,
                 )
 
@@ -128,16 +119,13 @@ def tile_josephkalmanupdate_w_kernel(tc, s, z_bytes, z_scale, kgain, g, d, r, ou
                 planes[u] = work.tile([P, 4, W], BF16, name="planes", tag="planes", bufs=4, align_bytes=64)
             nc.scalar.activation(
                 out=planes[u][:, t, 0 : hi - lo],
-                in_=zb[c, gp][:, t, lo:hi].bitcast(F8),
+                in_=zb[u][:, t, :].bitcast(F8),
                 func=COPY,
                 scale=zs[:, gp, t : t + 1],
             )
 
         def g_width(u):
-            if u in s_units:
-                return 0
-            w = u[3] - u[2] - P
-            return w - P if g_units.index(u) + 1 in SHORT else w
+            return 0 if u in s_units else u[3] - u[2] - P
 
         def pe_interleave(u, tag, bufs):
             a = u[3] - u[2] - P
@@ -171,14 +159,15 @@ def tile_josephkalmanupdate_w_kernel(tc, s, z_bytes, z_scale, kgain, g, d, r, ou
                 op1=ADD,
             )
 
-        def quant(u, parts=1):
+        def quant(u, half=None):
             w = u[3] - u[2]
-            cd = work.tile([P, W], U32, name="zc", tag="zc", bufs=5, align_bytes=64)
-            sc = work.tile([P, W], U8, name="zsc", tag="zsc", bufs=5, align_bytes=64)
-            codes[u] = (cd, sc)
-            for a in range(0, w, w // parts):
-                b = a + w // parts
-                nc.vector.quantize_mx(out=cd[:, a:b].bitcast(FP8X4), scales=sc[:, a:b], in_=il[u][:, 4 * a : 4 * b])
+            if half != 1:
+                cd = work.tile([P, W], U32, name="zc", tag="zc", bufs=5, align_bytes=64)
+                sc = work.tile([P, W], U8, name="zsc", tag="zsc", bufs=5, align_bytes=64)
+                codes[u] = (cd, sc)
+            cd, sc = codes[u]
+            a, b = (0, w) if half is None else (half * w // 2, (half + 1) * w // 2)
+            nc.vector.quantize_mx(out=cd[:, a:b].bitcast(FP8X4), scales=sc[:, a:b], in_=il[u][:, 4 * a : 4 * b])
 
         def multiply(u):
             c, gp, lo, hi = u
@@ -217,6 +206,12 @@ def tile_josephkalmanupdate_w_kernel(tc, s, z_bytes, z_scale, kgain, g, d, r, ou
         def kz_out(h):
             nk[h] = work.tile([P, 4, P], F32, name="nk", tag="nk", bufs=2)
             nc.scalar.activation(out=nk[h][:], in_=kz[h][:].rearrange("n (p t) -> n t p", t=4), func=COPY, scale=-1.0)
+
+        def kz_out_on_vector(h):
+            nk[h] = work.tile([P, 4, P], F32, name="nk", tag="nk", bufs=2)
+            nc.vector.tensor_scalar(
+                out=nk[h][:], in0=kz[h][:].rearrange("n (p t) -> n t p", t=4), scalar1=-1.0, scalar2=None, op0=MULT
+            )
 
         def kz_turn(h):
             for t in range(4):
@@ -317,28 +312,32 @@ def tile_josephkalmanupdate_w_kernel(tc, s, z_bytes, z_scale, kgain, g, d, r, ou
             make_identity(nc, ident[:])
             nc.gpsimd.tensor_copy(out=identb[:], in_=ident[:])
 
-            order = [(c, gp) for c in range(CHUNKS) for gp in range(PASSES)]
-            for pair_rows, plane_rows in (
-                (slice(0, 1), slice(0, 1)),
-                (slice(2, 3), slice(1, 2)),
-                (slice(1, 4, 2), slice(2, 4)),
-            ):
-                load(0, 0, pair_rows)
-                load(0, 1, plane_rows)
+            order = []
+            for k in range(steps):
+                if k - steps == S_DONE[0]:
+                    order.append(s_units[0])
+                order = order + g_units[k : k + 1] + v_units[k + 1 : k + 2]
+                if k - steps == min(S_ROWS):
+                    order.append(s_units[1])
+            load(v_units[0], slice(0, 1))
+            load(g_units[0], slice(0, 1))
+            load(v_units[0], slice(2, 3))
+            load(g_units[0], slice(1, 2))
+            load(v_units[0], slice(1, 4, 2))
+            load(g_units[0], slice(2, 4))
             nc.sync.dma_start(out=zs[:, 2:PASSES, :], in_=zsv[:, 2:PASSES, :])
-            load(0, 2)
-            load(0, 3)
+            load(first_halves[0])
+            load(first_halves[1])
+            load(order[2])
             nc.sync.dma_start(out=kg[:, 0:2048], in_=kgain[:, 0:2048])
             nc.sync.dma_start(out=kg[:, 2048:4096], in_=kgain[:, 2048:4096])
-            load(0, 4)
-            load(0, 5)
-            load(0, 6)
-            load(0, 7)
+            for u in order[3:7]:
+                load(u)
             nc.sync.dma_start(out=gt[:], in_=g.rearrange("(h p t) -> p h t", p=P, t=4))
             nc.sync.dma_start(out=dt_[:], in_=d.rearrange("(h p t) -> p h t", p=P, t=4))
             nc.sync.dma_start(out=rt[:], in_=r.rearrange("(g p t) -> p g t", p=P, t=4))
             nc.sync.dma_start(out=sraw[:], in_=s)
-            nload = 8
+            nload = 7
 
             def scales_to_psum():
                 once = psum.tile([P, P], F32, name="tp", tag="tp", bufs=1)
@@ -349,8 +348,8 @@ def tile_josephkalmanupdate_w_kernel(tc, s, z_bytes, z_scale, kgain, g, d, r, ou
             last_blocks = (L // BLK - 2, L // BLK - 1)
             closed_at, to_turn, products, gram_at = {}, [], [], {}
             for k in range(steps):
-                while nload < len(order) and nload < 2 * k + 8:
-                    load(*order[nload])
+                while nload < len(order) and nload < 2 * k + 6:
+                    load(order[nload])
                     nload += 1
                 uv = v_units[k]
                 if k >= 1:
@@ -370,12 +369,14 @@ def tile_josephkalmanupdate_w_kernel(tc, s, z_bytes, z_scale, kgain, g, d, r, ou
                     if k == 0:
                         scales_to_psum()
                     pe_interleave(ug, "tp", 1)
-                    cast(v_units[k + 1])
+                    for u in first_halves if k == 0 else [v_units[k + 1]]:
+                        cast(u)
                 else:
                     interleave_rest(g_units[k - 1])
-                for h in closed_at.get(k - 1, []):
-                    kz_out(h)
-                    to_turn.append(h)
+                fresh = closed_at.get(k - 1, [])
+                if products:
+                    for h in fresh:
+                        kz_out(h)
                 for t in S_ROWS.get(k - steps, ()):
                     widen_plane(s_units[1], t)
                 if k - steps in S_DONE:
@@ -391,9 +392,14 @@ def tile_josephkalmanupdate_w_kernel(tc, s, z_bytes, z_scale, kgain, g, d, r, ou
                 if k == 0:
                     widen_pairs(uv)
                     join(uv, "il_g", 1)
-                    quant(uv, 2)
+                    quant(uv, 0)
+                    quant(uv, 1)
                     continue
-                scale_interleave(uv)
+                scale_interleave(uv, first_halves if k == 1 else [uv])
+                if not products:
+                    for h in fresh:
+                        kz_out_on_vector(h)
+                to_turn.extend(fresh)
                 for q in K_OUT.get(k, ()):
                     k_out(q)
                 if products:
@@ -411,19 +417,22 @@ def tile_josephkalmanupdate_w_kernel(tc, s, z_bytes, z_scale, kgain, g, d, r, ou
                     nc.vector.tensor_copy(out=gt32[:], in_=gt[:])
                 if k in gram_at:
                     gram(gram_at[k])
-                ready = [uv, g_units[k - 1]]
-                if k - steps in S_QUANT:
-                    ready.insert(1, s_units[S_QUANT.index(k - steps)])
-                closed_at[k] = []
-                for u in ready:
-                    quant(u)
-                    if u == uv:
-                        for q in K_OUT.get(k, ()):
-                            k_quant(kT, kq, kqs, 2 * q, 2 * q + 2)
-                        if k == 1:
-                            multiply(v_units[0])
-                    closed_at[k] = closed_at[k] + multiply(u)
+                ug = g_units[k - 1]
+                quant(uv, 0)
+                for q in K_OUT.get(k, ()):
+                    k_quant(kT, kq, kqs, 2 * q, 2 * q + 2)
+                if k == 1:
+                    multiply(v_units[0])
+                if k - steps == S_QUANT[0]:
+                    quant(s_units[0])
+                    multiply(s_units[0])
+                quant(ug)
+                closed = multiply(ug)
+                quant(uv, 1)
+                closed_at[k] = closed + multiply(uv)
 
+            quant(s_units[1])
+            multiply(s_units[1])
             kz_out(last_blocks[1])
             kz_turn(last_blocks[1])
             for a in (0, 4):

@@ -24,7 +24,6 @@ CHUNKS = L // W
 S_ROWS = {-4: (0,), -3: (1,), -2: (2, 3)}
 S_DONE = (-5, -1)
 S_QUANT = (-4, -1)
-K_OUT = {1: (0, 1), 2: (2,), 3: (3,)}
 
 
 def tile_josephkalmanupdate_w_kernel(tc, s, z_bytes, z_scale, kgain, g, d, r, out):
@@ -207,12 +206,6 @@ def tile_josephkalmanupdate_w_kernel(tc, s, z_bytes, z_scale, kgain, g, d, r, ou
             nk[h] = work.tile([P, 4, P], F32, name="nk", tag="nk", bufs=2)
             nc.scalar.activation(out=nk[h][:], in_=kz[h][:].rearrange("n (p t) -> n t p", t=4), func=COPY, scale=-1.0)
 
-        def kz_out_on_vector(h):
-            nk[h] = work.tile([P, 4, P], F32, name="nk", tag="nk", bufs=2)
-            nc.vector.tensor_scalar(
-                out=nk[h][:], in0=kz[h][:].rearrange("n (p t) -> n t p", t=4), scalar1=-1.0, scalar2=None, op0=MULT
-            )
-
         def kz_turn(h):
             for t in range(4):
                 nc.tensor.matmul(
@@ -244,14 +237,15 @@ def tile_josephkalmanupdate_w_kernel(tc, s, z_bytes, z_scale, kgain, g, d, r, ou
                     in_=wp[:, i].rearrange("p t (c j) -> p c t j", j=4),
                 )
 
-        def gram(h):
+        def gram(h, parts=((0, 2),)):
             wq = work.tile([P, 2, P], U32, name="wq", tag="wq", bufs=2, align_bytes=64)
             wqs = work.tile([P, 2, P], U8, name="wqs", tag="wqs", bufs=2, align_bytes=64)
-            nc.vector.quantize_mx(
-                out=wq[:].rearrange("p i n -> p (i n)").bitcast(FP8X4),
-                scales=wqs[:].rearrange("p i n -> p (i n)"),
-                in_=ep[h][:].rearrange("p i x -> p (i x)"),
-            )
+            for a, b in parts:
+                nc.vector.quantize_mx(
+                    out=wq[:, a:b, :].rearrange("p i n -> p (i n)").bitcast(FP8X4),
+                    scales=wqs[:, a:b, :].rearrange("p i n -> p (i n)"),
+                    in_=ep[h][:, a:b, :].rearrange("p i x -> p (i x)"),
+                )
             nc.tensor.matmul_mx(
                 out=qj[:],
                 lhsT=wq[:, 1, :].bitcast(FP8X4),
@@ -263,7 +257,7 @@ def tile_josephkalmanupdate_w_kernel(tc, s, z_bytes, z_scale, kgain, g, d, r, ou
             )
 
         def k_turn(q):
-            ps = psum.tile([P, 2, 2, P], F32, name="kz", tag="kz", bufs=4)
+            ps = psum.tile([P, 2, 2, P], F32, name="turned", tag="turned", bufs=1)
             k_ps.append(ps)
             words = kg[:].bitcast(F32)
             for j in range(2):
@@ -354,9 +348,8 @@ def tile_josephkalmanupdate_w_kernel(tc, s, z_bytes, z_scale, kgain, g, d, r, ou
                 uv = v_units[k]
                 if k >= 1:
                     g_interleave(g_units[k - 1])
-                if k == 1:
-                    for q in range(4):
-                        k_turn(q)
+                if 1 <= k <= PASSES // 2:
+                    k_turn(k - 1)
                 if k - steps == S_DONE[0]:
                     for t in range(4):
                         widen_plane(s_units[0], t)
@@ -374,9 +367,8 @@ def tile_josephkalmanupdate_w_kernel(tc, s, z_bytes, z_scale, kgain, g, d, r, ou
                 else:
                     interleave_rest(g_units[k - 1])
                 fresh = closed_at.get(k - 1, [])
-                if products:
-                    for h in fresh:
-                        kz_out(h)
+                for h in fresh:
+                    kz_out(h)
                 for t in S_ROWS.get(k - steps, ()):
                     widen_plane(s_units[1], t)
                 if k - steps in S_DONE:
@@ -394,14 +386,12 @@ def tile_josephkalmanupdate_w_kernel(tc, s, z_bytes, z_scale, kgain, g, d, r, ou
                     join(uv, "il_g", 1)
                     quant(uv, 0)
                     quant(uv, 1)
+                    waiting = [uv]
                     continue
                 scale_interleave(uv, first_halves if k == 1 else [uv])
-                if not products:
-                    for h in fresh:
-                        kz_out_on_vector(h)
                 to_turn.extend(fresh)
-                for q in K_OUT.get(k, ()):
-                    k_out(q)
+                if k <= PASSES // 2:
+                    k_out(k - 1)
                 if products:
                     h, i = products.pop(0)
                     gain_product(h, i)
@@ -419,17 +409,19 @@ def tile_josephkalmanupdate_w_kernel(tc, s, z_bytes, z_scale, kgain, g, d, r, ou
                     gram(gram_at[k])
                 ug = g_units[k - 1]
                 quant(uv, 0)
-                for q in K_OUT.get(k, ()):
-                    k_quant(kT, kq, kqs, 2 * q, 2 * q + 2)
-                if k == 1:
-                    multiply(v_units[0])
+                if k <= PASSES // 2:
+                    k_quant(kT, kq, kqs, 2 * k - 2, 2 * k)
                 if k - steps == S_QUANT[0]:
                     quant(s_units[0])
-                    multiply(s_units[0])
+                    waiting.append(s_units[0])
                 quant(ug)
-                closed = multiply(ug)
                 quant(uv, 1)
-                closed_at[k] = closed + multiply(uv)
+                waiting = waiting + [ug, uv]
+                closed_at[k] = []
+                for u in waiting:
+                    if u[1] < 2 * k:
+                        closed_at[k] = closed_at[k] + multiply(u)
+                waiting = [u for u in waiting if u[1] >= 2 * k]
 
             quant(s_units[1])
             multiply(s_units[1])
@@ -444,7 +436,7 @@ def tile_josephkalmanupdate_w_kernel(tc, s, z_bytes, z_scale, kgain, g, d, r, ou
             q_passes()
             for i in range(2):
                 gain_product(last_blocks[1], i)
-            gram(last_blocks[1])
+            gram(last_blocks[1], ((0, 1), (1, 2)))
             res = work.tile([P, P], F32, name="res", tag="res", bufs=1)
             nc.vector.tensor_copy(out=res[:], in_=qj[:])
             nc.sync.dma_start(out=out, in_=res[:])

@@ -17,13 +17,14 @@ ADD = mybir.AluOpType.add
 COPY = mybir.ActivationFunctionType.Copy
 
 P = 128
-PASSES = M // 512
-W = 1024
+K_PASS = 4 * P
+PASSES = M // K_PASS
 BLK = 512
+BLOCKS = L // BLK
+W = 2 * BLK
 CHUNKS = L // W
-S_ROWS = {-4: (0,), -3: (1,), -2: (2, 3)}
-S_DONE = (-5, -1)
-S_QUANT = (-4, -1)
+BY_PE = P
+K_QUARTERS = PASSES // 2
 
 
 def tile_josephkalmanupdate_w_kernel(tc, s, z_bytes, z_scale, kgain, g, d, r, out):
@@ -34,60 +35,63 @@ def tile_josephkalmanupdate_w_kernel(tc, s, z_bytes, z_scale, kgain, g, d, r, ou
         psum = ctx.enter_context(tc.psum_pool(name="psum", bufs=1))
 
         ident = keep.tile([P, P], F32, name="ident")
-        identb = keep.tile([P, P], BF16, name="identb")
-        zs_sq = keep.tile([P, P], F32, name="zs_sq")
-        zs_t = keep.tile([P, P], F32, name="zs_t")
-        zs = zs_sq[:, 0 : 4 * PASSES].rearrange("p (g t) -> p g t", t=4)
-        rt = keep.tile([P, PASSES, 4], BF16, name="rt")
-        gt = keep.tile([P, 8, 4], BF16, name="gt")
-        dt_ = keep.tile([P, 8, 4], BF16, name="dtile")
-        gdt = keep.tile([P, 8, 4], F32, name="gdt")
-        gt32 = keep.tile([P, 8, 4], F32, name="gt32")
-        kg = keep.tile([P, M], BF16, name="kg")
-        kT = keep.tile([P, PASSES, P * 4], BF16, name="kT", align_bytes=64)
-        krT = keep.tile([P, PASSES, P * 4], BF16, name="krT", align_bytes=64)
-        kq = keep.tile([P, PASSES, P], U32, name="kq", align_bytes=64)
-        kqs = keep.tile([P, PASSES, P], U8, name="kqs", align_bytes=64)
-        krq = keep.tile([P, PASSES, P], U32, name="krq", align_bytes=64)
-        krqs = keep.tile([P, PASSES, P], U8, name="krqs", align_bytes=64)
-        sraw = keep.tile([P, L], BF16, name="sraw")
-        qj = psum.tile([P, P], F32, name="qj", tag="qj", bufs=1)
-        zs_ps = psum.tile([P, P], F32, name="zs_ps", tag="zs_ps", bufs=1)
+        ident_bf = keep.tile([P, P], BF16, name="ident_bf")
+        zs = keep.tile([P, PASSES, 4], F32, name="zs")
+        zs_four = keep.tile([P, 4 * PASSES, 4], F32, name="zs_four")
+        zs_turned = keep.tile([P, P], F32, name="zs_turned")
+        r_sb = keep.tile([P, PASSES, 4], BF16, name="r_sb")
+        g_sb = keep.tile([P, BLOCKS, 4], BF16, name="g_sb")
+        d_sb = keep.tile([P, BLOCKS, 4], BF16, name="d_sb")
+        gd_f32 = keep.tile([P, BLOCKS, 4], F32, name="gd_f32")
+        g_f32 = keep.tile([P, BLOCKS, 4], F32, name="g_f32")
+        k_rows = keep.tile([P, M], BF16, name="k_rows")
+        k_il = keep.tile([P, PASSES, 4 * N], BF16, name="k_il", align_bytes=64)
+        kr_il = keep.tile([P, PASSES, 4 * N], BF16, name="kr_il", align_bytes=64)
+        k_codes = keep.tile([P, PASSES, N], U32, name="k_codes", align_bytes=64)
+        k_scales = keep.tile([P, PASSES, N], U8, name="k_scales", align_bytes=64)
+        kr_codes = keep.tile([P, PASSES, N], U32, name="kr_codes", align_bytes=64)
+        kr_scales = keep.tile([P, PASSES, N], U8, name="kr_scales", align_bytes=64)
+        s_rows = keep.tile([P, L], BF16, name="s_rows")
+        jq = psum.tile([P, N], F32, name="jq", tag="jq", bufs=1)
+        zs_psum = psum.tile([P, PASSES, 4, 4], F32, name="zs_psum", tag="zs_psum", bufs=1)
 
         whole = [(c, gp, 0, W) for c in range(CHUNKS) for gp in range(PASSES)]
-        c_last = CHUNKS - 1
-        v_units = whole[0:-4:2] + [(c_last, gp, lo, lo + BLK) for lo in (0, BLK) for gp in (4, 6)]
-        g_units = whole[1:-6:2] + [(c_last, gp, lo, lo + BLK) for lo in (0, BLK) for gp in (3, 5)]
-        s_units = [(c_last, PASSES - 1, lo, lo + BLK) for lo in (0, BLK)]
-        steps = len(v_units)
+        last_chunk = CHUNKS - 1
+        cast_pieces = whole[0:-4:2] + [(last_chunk, gp, lo, lo + BLK) for lo in (0, BLK) for gp in (4, 6)]
+        plane_pieces = whole[1:-6:2] + [(last_chunk, gp, lo, lo + BLK) for lo in (0, BLK) for gp in (3, 5)]
+        scalar_pieces = [(last_chunk, PASSES - 1, lo, lo + BLK) for lo in (0, BLK)]
+        steps = len(cast_pieces)
+        last_wide = steps - 5
         first_halves = [(0, 2, lo, lo + BLK) for lo in (0, BLK)]
 
-        zb, pairs, planes, il, by_pe, codes, kz, nk, turned, ep = {}, {}, {}, {}, {}, {}, {}, {}, {}, {}
+        zb, planes, il, by_pe, codes, kz, neg_kz, turned, w_wd = {}, {}, {}, {}, {}, {}, {}, {}, {}
         passes_done = {}
-        k_ps = []
 
-        def load(u, ts=slice(0, 4)):
+        def width(u):
+            return u[3] - u[2]
+
+        def load(u, rows=slice(0, 4)):
             c, gp, lo, hi = u
-            if ts.start == 0:
+            if rows.start == 0:
                 zb[u] = work.tile([P, 4, hi - lo], U8, name="zb", tag="zb", bufs=9)
-            rows = z_bytes[512 * gp : 512 * (gp + 1), W * c + lo : W * c + hi].rearrange("(p t) w -> p t w", t=4)
-            nc.sync.dma_start(out=zb[u][:, ts, :], in_=rows[:, ts, :])
+            src = z_bytes[K_PASS * gp : K_PASS * (gp + 1), W * c + lo : W * c + hi].rearrange("(p t) w -> p t w", t=4)
+            nc.sync.dma_start(out=zb[u][:, rows, :], in_=src[:, rows, :])
 
-        def widen_pairs(u):
-            c, gp, lo, hi = u
-            pairs[u] = work.tile([P, 2, 2 * W], BF16, name="pairs", tag="pairs", bufs=1, align_bytes=64)
+        def first_piece_pairs(u):
+            pairs = work.tile([P, 2, 2 * W], BF16, name="pairs", tag="pairs", bufs=1, align_bytes=64)
             for t, a, b in ((0, 0, W), (2, 0, W), (1, 0, W), (3, 0, BLK), (3, BLK, W)):
                 nc.vector.tensor_scalar(
-                    out=pairs[u][:, t // 2, 2 * a : 2 * b].rearrange("p (l e) -> p e l", e=2)[:, t % 2],
+                    out=pairs[:, t // 2, 2 * a : 2 * b].rearrange("p (l e) -> p e l", e=2)[:, t % 2],
                     in0=zb[u][:, t, a:b].bitcast(F8),
-                    scalar1=zs[:, gp, t : t + 1],
+                    scalar1=zs[:, u[1], t : t + 1],
                     scalar2=None,
                     op0=MULT,
                 )
+            return pairs
 
-        def join(u, tag, bufs):
-            il[u] = work.tile([P, 4 * W], BF16, name=tag, tag=tag, bufs=bufs, align_bytes=64)
-            words = pairs[u][:].rearrange("p u x -> p (u x)").bitcast(F32).rearrange("p (u l) -> p l u", u=2)
+        def first_piece_join(u, pairs):
+            il[u] = work.tile([P, 4 * W], BF16, name="il_g", tag="il_g", bufs=1, align_bytes=64)
+            words = pairs[:].rearrange("p u x -> p (u x)").bitcast(F32).rearrange("p (u l) -> p l u", u=2)
             for a in (0, BLK):
                 nc.vector.tensor_copy(
                     out=il[u][:, 4 * a : 4 * (a + BLK)].bitcast(F32).rearrange("p (l u) -> p l u", u=2),
@@ -95,59 +99,47 @@ def tile_josephkalmanupdate_w_kernel(tc, s, z_bytes, z_scale, kgain, g, d, r, ou
                 )
 
         def cast(u):
-            planes[u] = work.tile([P, 4, u[3] - u[2]], BF16, name="raw", tag="raw", bufs=3, align_bytes=64)
+            planes[u] = work.tile([P, 4, width(u)], BF16, name="raw", tag="raw", bufs=3, align_bytes=64)
             nc.scalar.copy(
                 out=planes[u][:].rearrange("p t l -> p (t l)"), in_=zb[u][:].rearrange("p t l -> p (t l)").bitcast(F8)
             )
 
         def scale_interleave(u, parts):
-            c, gp, lo, hi = u
+            gp, lo = u[1], u[2]
             il[u] = work.tile([P, 4 * W], BF16, name="il_v", tag="il_v", bufs=3, align_bytes=64)
             for part in parts:
                 a, b = part[2] - lo, part[3] - lo
                 nc.vector.tensor_tensor(
                     out=il[u][:, 4 * a : 4 * b].rearrange("p (c i t) -> p c t i", i=4, t=4),
                     in0=planes[part][:].rearrange("p t (c i) -> p c t i", i=4),
-                    in1=zs_ps[:, 4 * gp : 4 * gp + 4].unsqueeze(1).unsqueeze(3).to_broadcast([P, (b - a) // 4, 4, 4]),
+                    in1=zs_psum[:, gp].unsqueeze(1).to_broadcast([P, (b - a) // 4, 4, 4]),
                     op=MULT,
                 )
 
-        def widen_plane(u, t):
-            c, gp, lo, hi = u
+        def widen_row(u, t):
             if t == 0:
                 planes[u] = work.tile([P, 4, W], BF16, name="planes", tag="planes", bufs=4, align_bytes=64)
             nc.scalar.activation(
-                out=planes[u][:, t, 0 : hi - lo],
-                in_=zb[u][:, t, :].bitcast(F8),
-                func=COPY,
-                scale=zs[:, gp, t : t + 1],
+                out=planes[u][:, t, 0 : width(u)], in_=zb[u][:, t, :].bitcast(F8), func=COPY, scale=zs[:, u[1], t : t + 1]
             )
 
-        def g_width(u):
-            return 0 if u in s_units else u[3] - u[2] - P
-
-        def pe_interleave(u, tag, bufs):
-            a = u[3] - u[2] - P
-            by_pe[u] = psum.tile([P, 512], BF16, name=tag, tag=tag, bufs=bufs)
+        def interleave_on_pe(u, tag, bufs):
+            a = width(u) - BY_PE
+            by_pe[u] = psum.tile([P, 4 * BY_PE], BF16, name=tag, tag=tag, bufs=bufs)
             nc.tensor.matmul(
                 by_pe[u][:].rearrange("p (l t) -> p l t", t=4),
-                lhsT=identb[:],
-                rhs=planes[u][:, :, a : a + P].rearrange("p t l -> p l t"),
+                lhsT=ident_bf[:],
+                rhs=planes[u][:, :, a : a + BY_PE].rearrange("p t l -> p l t"),
                 start=True,
                 stop=True,
             )
 
-        def interleave_rest(u):
-            a, b = g_width(u), u[3] - u[2] - P
-            if b > a:
-                nc.scalar.copy(
-                    out=il[u][:, 4 * a : 4 * b].rearrange("p (c i t) -> p c t i", i=4, t=4),
-                    in_=planes[u][:, :, a:b].rearrange("p t (c i) -> p c t i", i=4),
-                )
-            nc.scalar.copy(out=il[u][:, 4 * b : 4 * (b + P)].bitcast(F32), in_=by_pe[u][:].bitcast(F32))
+        def by_pe_out(u):
+            a = width(u) - BY_PE
+            nc.scalar.copy(out=il[u][:, 4 * a : 4 * width(u)].bitcast(F32), in_=by_pe[u][:].bitcast(F32))
 
-        def g_interleave(u):
-            a = g_width(u)
+        def interleave_on_gpsimd(u):
+            a = width(u) - BY_PE
             il[u] = work.tile([P, 4 * W], BF16, name="il_g", tag="il_g", bufs=1, align_bytes=64)
             nc.gpsimd.tensor_scalar(
                 out=il[u][:, 0 : 4 * a].rearrange("p (l t) -> p l t", t=4),
@@ -158,285 +150,295 @@ def tile_josephkalmanupdate_w_kernel(tc, s, z_bytes, z_scale, kgain, g, d, r, ou
                 op1=ADD,
             )
 
-        def quant(u, half=None):
-            w = u[3] - u[2]
-            if half != 1:
-                cd = work.tile([P, W], U32, name="zc", tag="zc", bufs=5, align_bytes=64)
-                sc = work.tile([P, W], U8, name="zsc", tag="zsc", bufs=5, align_bytes=64)
-                codes[u] = (cd, sc)
-            cd, sc = codes[u]
-            a, b = (0, w) if half is None else (half * w // 2, (half + 1) * w // 2)
-            nc.vector.quantize_mx(out=cd[:, a:b].bitcast(FP8X4), scales=sc[:, a:b], in_=il[u][:, 4 * a : 4 * b])
+        def interleave_on_scalar(u):
+            a = width(u) - BY_PE
+            interleave_on_pe(u, "kz", 4)
+            il[u] = work.tile([P, 4 * BLK], BF16, name="il_s", tag="il_s", bufs=2, align_bytes=64)
+            nc.scalar.copy(
+                out=il[u][:, 0 : 4 * a].rearrange("p (c i t) -> p c t i", i=4, t=4),
+                in_=planes[u][:, :, 0:a].rearrange("p t (c i) -> p c t i", i=4),
+            )
+            by_pe_out(u)
 
-        def multiply(u):
+        def quantise(u, half=None):
+            if half != 1:
+                z_codes = work.tile([P, W], U32, name="z_codes", tag="z_codes", bufs=5, align_bytes=64)
+                z_scales = work.tile([P, W], U8, name="z_scales", tag="z_scales", bufs=5, align_bytes=64)
+                codes[u] = (z_codes, z_scales)
+            z_codes, z_scales = codes[u]
+            a, b = (0, width(u)) if half is None else (half * width(u) // 2, (half + 1) * width(u) // 2)
+            nc.vector.quantize_mx(
+                out=z_codes[:, a:b].bitcast(FP8X4), scales=z_scales[:, a:b], in_=il[u][:, 4 * a : 4 * b]
+            )
+
+        def kz_passes(u):
             c, gp, lo, hi = u
-            cd, sc = codes[u]
-            closed = []
+            z_codes, z_scales = codes[u]
+            complete = []
             for col in range(0, hi - lo, BLK):
                 h = (W * c + lo + col) // BLK
                 if h not in kz:
                     kz[h] = psum.tile([P, BLK], F32, name="kz", tag="kz", bufs=4)
-                n_done = passes_done.get(h, 0)
-                passes_done[h] = n_done + 1
+                done = passes_done.get(h, 0)
+                passes_done[h] = done + 1
                 nc.tensor.matmul_mx(
                     out=kz[h][:],
-                    lhsT=kq[:, gp, :].bitcast(FP8X4),
-                    lhsT_scale=kqs[:, gp, :],
-                    rhs=cd[:, col : col + BLK].bitcast(FP8X4),
-                    rhs_scale=sc[:, col : col + BLK],
-                    start=(n_done == 0),
-                    stop=(n_done == PASSES - 1),
+                    lhsT=k_codes[:, gp, :].bitcast(FP8X4),
+                    lhsT_scale=k_scales[:, gp, :],
+                    rhs=z_codes[:, col : col + BLK].bitcast(FP8X4),
+                    rhs_scale=z_scales[:, col : col + BLK],
+                    start=(done == 0),
+                    stop=(done == PASSES - 1),
                 )
-                if n_done == PASSES - 1:
-                    closed.append(h)
-            return closed
+                if done == PASSES - 1:
+                    complete.append(h)
+            return complete
+
+        def kz_out(h):
+            neg_kz[h] = work.tile([P, 4, P], F32, name="neg_kz", tag="neg_kz", bufs=2)
+            nc.scalar.activation(out=neg_kz[h][:], in_=kz[h][:].rearrange("n (p t) -> n t p", t=4), func=COPY, scale=-1.0)
 
         def s_turn(h, tag, bufs):
-            turned[h] = psum.tile([P, P, 4], F32, name=tag, tag=tag, bufs=bufs)
+            turned[h] = psum.tile([P, N, 4], F32, name=tag, tag=tag, bufs=bufs)
             for t in range(4):
                 nc.tensor.matmul(
                     turned[h][:, :, t],
-                    lhsT=sraw[:, BLK * h + t : BLK * (h + 1) : 4],
-                    rhs=identb[:],
+                    lhsT=s_rows[:, BLK * h + t : BLK * (h + 1) : 4],
+                    rhs=ident_bf[:],
                     start=(t == 0),
                     stop=False,
                 )
 
-        def kz_out(h):
-            nk[h] = work.tile([P, 4, P], F32, name="nk", tag="nk", bufs=2)
-            nc.scalar.activation(out=nk[h][:], in_=kz[h][:].rearrange("n (p t) -> n t p", t=4), func=COPY, scale=-1.0)
-
         def kz_turn(h):
             for t in range(4):
                 nc.tensor.matmul(
-                    turned[h][:, :, t], lhsT=nk[h][:, t, :], rhs=ident[:], is_transpose=True, start=False, stop=(t == 3)
+                    turned[h][:, :, t], lhsT=neg_kz[h][:, t, :], rhs=ident[:], is_transpose=True, start=False, stop=(t == 3)
                 )
 
         def gain_product(h, i):
             if i == 0:
-                ep[h] = work.tile([P, 2, BLK], BF16, name="ww", tag="ww", bufs=3, align_bytes=64)
+                w_wd[h] = work.tile([P, 2, BLK], BF16, name="w_wd", tag="w_wd", bufs=3, align_bytes=64)
             nc.vector.tensor_tensor(
-                out=ep[h][:, i, :].rearrange("p (n t) -> p n t", t=4),
+                out=w_wd[h][:, i, :].rearrange("p (n t) -> p n t", t=4),
                 in0=turned[h][:],
-                in1=(gt, gdt)[i][:, h, :].unsqueeze(1).to_broadcast([P, P, 4]),
+                in1=(g_sb, gd_f32)[i][:, h, :].unsqueeze(1).to_broadcast([P, N, 4]),
                 op=MULT,
             )
 
-        def gains_on_scalar(h):
-            ww = work.tile([P, 2, BLK], BF16, name="ww", tag="ww", bufs=3, align_bytes=64)
-            ep[h] = ww
-            wp = work.tile([P, 2, 4, P], BF16, name="wp", tag="wp", bufs=1)
-            for i, gain in enumerate((gt32, gdt)):
+        def gain_products_on_scalar(h):
+            w_wd[h] = work.tile([P, 2, BLK], BF16, name="w_wd", tag="w_wd", bufs=3, align_bytes=64)
+            by_t = work.tile([P, 2, 4, N], BF16, name="by_t", tag="by_t", bufs=1)
+            for i, gain in enumerate((g_f32, gd_f32)):
                 for t in range(4):
                     nc.scalar.activation(
-                        out=wp[:, i, t, :], in_=turned[h][:, :, t], func=COPY, scale=gain[:, h, t : t + 1]
+                        out=by_t[:, i, t, :], in_=turned[h][:, :, t], func=COPY, scale=gain[:, h, t : t + 1]
                     )
             for i in range(2):
                 nc.scalar.copy(
-                    out=ww[:, i, :].rearrange("p (c j t) -> p c t j", j=4, t=4),
-                    in_=wp[:, i].rearrange("p t (c j) -> p c t j", j=4),
+                    out=w_wd[h][:, i, :].rearrange("p (c j t) -> p c t j", j=4, t=4),
+                    in_=by_t[:, i].rearrange("p t (c j) -> p c t j", j=4),
                 )
 
-        def gram(h, parts=((0, 2),)):
-            wq = work.tile([P, 2, P], U32, name="wq", tag="wq", bufs=2, align_bytes=64)
-            wqs = work.tile([P, 2, P], U8, name="wqs", tag="wqs", bufs=2, align_bytes=64)
+        def j_pass(h, parts=((0, 2),)):
+            w_codes = work.tile([P, 2, N], U32, name="w_codes", tag="w_codes", bufs=2, align_bytes=64)
+            w_scales = work.tile([P, 2, N], U8, name="w_scales", tag="w_scales", bufs=2, align_bytes=64)
             for a, b in parts:
                 nc.vector.quantize_mx(
-                    out=wq[:, a:b, :].rearrange("p i n -> p (i n)").bitcast(FP8X4),
-                    scales=wqs[:, a:b, :].rearrange("p i n -> p (i n)"),
-                    in_=ep[h][:, a:b, :].rearrange("p i x -> p (i x)"),
+                    out=w_codes[:, a:b, :].rearrange("p i n -> p (i n)").bitcast(FP8X4),
+                    scales=w_scales[:, a:b, :].rearrange("p i n -> p (i n)"),
+                    in_=w_wd[h][:, a:b, :].rearrange("p i x -> p (i x)"),
                 )
             nc.tensor.matmul_mx(
-                out=qj[:],
-                lhsT=wq[:, 1, :].bitcast(FP8X4),
-                lhsT_scale=wqs[:, 1, :],
-                rhs=wq[:, 0, :].bitcast(FP8X4),
-                rhs_scale=wqs[:, 0, :],
+                out=jq[:],
+                lhsT=w_codes[:, 1, :].bitcast(FP8X4),
+                lhsT_scale=w_scales[:, 1, :],
+                rhs=w_codes[:, 0, :].bitcast(FP8X4),
+                rhs_scale=w_scales[:, 0, :],
                 start=(h == 0),
-                stop=(h == L // BLK - 1),
+                stop=(h == BLOCKS - 1),
             )
 
         def k_turn(q):
-            ps = psum.tile([P, 2, 2, P], F32, name="turned", tag="turned", bufs=1)
-            k_ps.append(ps)
-            words = kg[:].bitcast(F32)
+            k_bank = psum.tile([P, 2, 2, N], F32, name="turned", tag="turned", bufs=1)
+            words = k_rows[:].bitcast(F32)
             for j in range(2):
                 for u in range(2):
-                    b0 = 256 * (2 * q + j)
-                    nc.tensor.transpose(ps[:, j, u, :], words[:, b0 + u : b0 + 256 : 2], ident[:])
+                    first = K_PASS // 2 * (2 * q + j)
+                    nc.tensor.transpose(k_bank[:, j, u, :], words[:, first + u : first + K_PASS // 2 : 2], ident[:])
+            return k_bank
 
-        def k_out(q):
-            ps = k_ps[q]
+        def k_out(q, k_bank):
             nc.vector.tensor_copy(
-                out=kT[:, 2 * q : 2 * q + 2, :].bitcast(F32).rearrange("p j (n u) -> p j n u", u=2),
-                in_=ps[:].rearrange("p j u n -> p j n u"),
+                out=k_il[:, 2 * q : 2 * q + 2, :].bitcast(F32).rearrange("p j (n u) -> p j n u", u=2),
+                in_=k_bank[:].rearrange("p j u n -> p j n u"),
             )
 
-        def k_quant(src, cd, sc, a=0, b=PASSES):
+        def quantise_k(src, dst_codes, dst_scales, a, b):
             nc.vector.quantize_mx(
-                out=cd[:, a:b, :].rearrange("p g n -> p (g n)").bitcast(FP8X4),
-                scales=sc[:, a:b, :].rearrange("p g n -> p (g n)"),
+                out=dst_codes[:, a:b, :].rearrange("p g n -> p (g n)").bitcast(FP8X4),
+                scales=dst_scales[:, a:b, :].rearrange("p g n -> p (g n)"),
                 in_=src[:, a:b, :].rearrange("p g x -> p (g x)"),
             )
 
-        def kr_mul(a, b):
+        def kr_product(a, b):
             nc.vector.tensor_tensor(
-                out=krT[:, a:b, :].rearrange("p g (n t) -> p g n t", t=4),
-                in0=kT[:, a:b, :].rearrange("p g (n t) -> p g n t", t=4),
-                in1=rt[:, a:b, :].unsqueeze(2).to_broadcast([P, b - a, P, 4]),
+                out=kr_il[:, a:b, :].rearrange("p g (n t) -> p g n t", t=4),
+                in0=k_il[:, a:b, :].rearrange("p g (n t) -> p g n t", t=4),
+                in1=r_sb[:, a:b, :].unsqueeze(2).to_broadcast([P, b - a, N, 4]),
                 op=MULT,
             )
 
         def q_passes():
             for gp in range(PASSES):
                 nc.tensor.matmul_mx(
-                    out=qj[:],
-                    lhsT=krq[:, gp, :].bitcast(FP8X4),
-                    lhsT_scale=krqs[:, gp, :],
-                    rhs=kq[:, gp, :].bitcast(FP8X4),
-                    rhs_scale=kqs[:, gp, :],
+                    out=jq[:],
+                    lhsT=kr_codes[:, gp, :].bitcast(FP8X4),
+                    lhsT_scale=kr_scales[:, gp, :],
+                    rhs=k_codes[:, gp, :].bitcast(FP8X4),
+                    rhs_scale=k_scales[:, gp, :],
                     start=False,
                     stop=False,
                 )
 
+        def scales_to_psum():
+            nc.vector.tensor_copy(
+                out=zs_four[:], in_=zs[:].rearrange("p g t -> p (g t)").unsqueeze(2).to_broadcast([P, 4 * PASSES, 4])
+            )
+            once = psum.tile([P, P], F32, name="by_pe", tag="by_pe", bufs=1)
+            nc.tensor.transpose(once[:], zs_four[:].rearrange("p x i -> p (x i)"), ident[:])
+            nc.scalar.copy(out=zs_turned[:], in_=once[:])
+            nc.tensor.transpose(zs_psum[:].rearrange("p g t i -> p (g t i)"), zs_turned[:], ident[:])
+
         with tc.manual_schedule():
-            nc.vector.memset(zs_sq[:, 4 * PASSES : P], 0.0)
-            zsv = z_scale.rearrange("(g p t) o -> p g (t o)", p=P, t=4)
-            nc.scalar.dma_start(out=zs[:, 0:2, :], in_=zsv[:, 0:2, :])
+            zs_hbm = z_scale.rearrange("(g p t) o -> p g (t o)", p=P, t=4)
+            nc.scalar.dma_start(out=zs[:, 0:2, :], in_=zs_hbm[:, 0:2, :])
             make_identity(nc, ident[:])
-            nc.gpsimd.tensor_copy(out=identb[:], in_=ident[:])
+            nc.gpsimd.tensor_copy(out=ident_bf[:], in_=ident[:])
 
             order = []
             for k in range(steps):
-                if k - steps == S_DONE[0]:
-                    order.append(s_units[0])
-                order = order + g_units[k : k + 1] + v_units[k + 1 : k + 2]
-                if k - steps == min(S_ROWS):
-                    order.append(s_units[1])
-            load(v_units[0], slice(0, 1))
-            load(g_units[0], slice(0, 1))
-            load(v_units[0], slice(2, 3))
-            load(g_units[0], slice(1, 2))
-            load(v_units[0], slice(1, 4, 2))
-            load(g_units[0], slice(2, 4))
-            nc.sync.dma_start(out=zs[:, 2:PASSES, :], in_=zsv[:, 2:PASSES, :])
+                if k == last_wide:
+                    order.append(scalar_pieces[0])
+                order = order + plane_pieces[k : k + 1] + cast_pieces[k + 1 : k + 2]
+                if k == last_wide + 1:
+                    order.append(scalar_pieces[1])
+            for v_rows, s_rows_first in (
+                (slice(0, 1), slice(0, 1)),
+                (slice(2, 3), slice(1, 2)),
+                (slice(1, 4, 2), slice(2, 4)),
+            ):
+                load(cast_pieces[0], v_rows)
+                load(plane_pieces[0], s_rows_first)
+            nc.sync.dma_start(out=zs[:, 2:PASSES, :], in_=zs_hbm[:, 2:PASSES, :])
             load(first_halves[0])
             load(first_halves[1])
             load(order[2])
-            nc.sync.dma_start(out=kg[:, 0:2048], in_=kgain[:, 0:2048])
-            nc.sync.dma_start(out=kg[:, 2048:4096], in_=kgain[:, 2048:4096])
-            for u in order[3:7]:
+            nc.sync.dma_start(out=k_rows[:, 0 : M // 2], in_=kgain[:, 0 : M // 2])
+            nc.sync.dma_start(out=k_rows[:, M // 2 : M], in_=kgain[:, M // 2 : M])
+            loaded = 7
+            for u in order[3:loaded]:
                 load(u)
-            nc.sync.dma_start(out=gt[:], in_=g.rearrange("(h p t) -> p h t", p=P, t=4))
-            nc.sync.dma_start(out=dt_[:], in_=d.rearrange("(h p t) -> p h t", p=P, t=4))
-            nc.sync.dma_start(out=rt[:], in_=r.rearrange("(g p t) -> p g t", p=P, t=4))
-            nc.sync.dma_start(out=sraw[:], in_=s)
-            nload = 7
+            nc.sync.dma_start(out=g_sb[:], in_=g.rearrange("(h p t) -> p h t", p=P, t=4))
+            nc.sync.dma_start(out=d_sb[:], in_=d.rearrange("(h p t) -> p h t", p=P, t=4))
+            nc.sync.dma_start(out=r_sb[:], in_=r.rearrange("(g p t) -> p g t", p=P, t=4))
+            nc.sync.dma_start(out=s_rows[:], in_=s)
 
-            def scales_to_psum():
-                once = psum.tile([P, P], F32, name="tp", tag="tp", bufs=1)
-                nc.tensor.transpose(once[:], zs_sq[:], ident[:])
-                nc.scalar.copy(out=zs_t[:], in_=once[:])
-                nc.tensor.transpose(zs_ps[:], zs_t[:], ident[:])
-
-            last_blocks = (L // BLK - 2, L // BLK - 1)
-            closed_at, to_turn, products, gram_at = {}, [], [], {}
+            late_rows = {last_wide + 1: (0,), last_wide + 2: (1,), last_wide + 3: (2, 3)}
+            complete, to_turn, products, j_due = [], [], [], None
             for k in range(steps):
-                while nload < len(order) and nload < 2 * k + 6:
-                    load(order[nload])
-                    nload += 1
-                uv = v_units[k]
+                while loaded < min(len(order), 2 * k + 6):
+                    load(order[loaded])
+                    loaded += 1
+                piece = cast_pieces[k]
                 if k >= 1:
-                    g_interleave(g_units[k - 1])
-                if 1 <= k <= PASSES // 2:
-                    k_turn(k - 1)
-                if k - steps == S_DONE[0]:
+                    behind = plane_pieces[k - 1]
+                    interleave_on_gpsimd(behind)
+                if 1 <= k <= K_QUARTERS:
+                    k_bank = k_turn(k - 1)
+
+                if k == last_wide:
                     for t in range(4):
-                        widen_plane(s_units[0], t)
-                if k < len(g_units):
-                    ug = g_units[k]
+                        widen_row(scalar_pieces[0], t)
+                if k + 1 < steps:
                     for t in range(4):
-                        widen_plane(ug, t)
+                        widen_row(plane_pieces[k], t)
                         if t == 1 and k >= 1:
-                            interleave_rest(g_units[k - 1])
+                            by_pe_out(behind)
                     if k == 0:
+                        pairs = first_piece_pairs(piece)
                         scales_to_psum()
-                    pe_interleave(ug, "tp", 1)
-                    for u in first_halves if k == 0 else [v_units[k + 1]]:
+                    interleave_on_pe(plane_pieces[k], "by_pe", 1)
+                    for u in first_halves if k == 0 else [cast_pieces[k + 1]]:
                         cast(u)
                 else:
-                    interleave_rest(g_units[k - 1])
-                fresh = closed_at.get(k - 1, [])
-                for h in fresh:
+                    by_pe_out(behind)
+                for h in complete:
                     kz_out(h)
-                for t in S_ROWS.get(k - steps, ()):
-                    widen_plane(s_units[1], t)
-                if k - steps in S_DONE:
-                    us = s_units[S_DONE.index(k - steps)]
-                    pe_interleave(us, "kz", 4)
-                    il[us] = work.tile([P, 4 * BLK], BF16, name="il_s", tag="il_s", bufs=2, align_bytes=64)
-                    interleave_rest(us)
+                for t in late_rows.get(k, ()):
+                    widen_row(scalar_pieces[1], t)
+                if k == last_wide:
+                    interleave_on_scalar(scalar_pieces[0])
                 if k == steps - 1:
-                    s_turn(last_blocks[0], "kz", 4)
-                    kz_turn(last_blocks[0])
-                    s_turn(last_blocks[1], "tp", 1)
-                    gains_on_scalar(last_blocks[0])
+                    interleave_on_scalar(scalar_pieces[1])
+                    s_turn(BLOCKS - 2, "kz", 4)
+                    kz_turn(BLOCKS - 2)
+                    s_turn(BLOCKS - 1, "by_pe", 1)
+                    gain_products_on_scalar(BLOCKS - 2)
+
                 if k == 0:
-                    widen_pairs(uv)
-                    join(uv, "il_g", 1)
-                    quant(uv, 0)
-                    quant(uv, 1)
-                    waiting = [uv]
+                    first_piece_join(piece, pairs)
+                    quantise(piece, 0)
+                    quantise(piece, 1)
+                    waiting = [piece]
                     continue
-                scale_interleave(uv, first_halves if k == 1 else [uv])
-                to_turn.extend(fresh)
-                if k <= PASSES // 2:
-                    k_out(k - 1)
+                scale_interleave(piece, first_halves if k == 1 else [piece])
+                if k <= K_QUARTERS:
+                    k_out(k - 1, k_bank)
+                j_now, j_due = j_due, None
                 if products:
                     h, i = products.pop(0)
                     gain_product(h, i)
                     if i == 1:
-                        gram_at[k + 1] = h
-                if to_turn and not products and to_turn[0] not in last_blocks:
+                        j_due = h
+                to_turn = to_turn + [h for h in complete if h < BLOCKS - 2]
+                if to_turn and not products:
                     h = to_turn.pop(0)
                     s_turn(h, "turned", 1)
                     kz_turn(h)
                     products = [(h, 0), (h, 1)]
-                if k == 2:
-                    nc.vector.tensor_tensor(out=gdt[:], in0=gt[:], in1=dt_[:], op=MULT)
-                    nc.vector.tensor_copy(out=gt32[:], in_=gt[:])
-                if k in gram_at:
-                    gram(gram_at[k])
-                ug = g_units[k - 1]
-                quant(uv, 0)
-                if k <= PASSES // 2:
-                    k_quant(kT, kq, kqs, 2 * k - 2, 2 * k)
-                if k - steps == S_QUANT[0]:
-                    quant(s_units[0])
-                    waiting.append(s_units[0])
-                quant(ug)
-                quant(uv, 1)
-                waiting = waiting + [ug, uv]
-                closed_at[k] = []
+                if k == K_QUARTERS + 1:
+                    nc.vector.tensor_tensor(out=gd_f32[:], in0=g_sb[:], in1=d_sb[:], op=MULT)
+                    nc.vector.tensor_copy(out=g_f32[:], in_=g_sb[:])
+                if j_now is not None:
+                    j_pass(j_now)
+                else:
+                    quantise(piece, 0)
+                if k <= K_QUARTERS:
+                    quantise_k(k_il, k_codes, k_scales, 2 * k - 2, 2 * k)
+                if k == last_wide + 1:
+                    quantise(scalar_pieces[0])
+                    waiting.append(scalar_pieces[0])
+                quantise(behind)
+                quantise(piece, None if j_now is not None else 1)
+                waiting = waiting + [behind, piece]
+                complete = []
                 for u in waiting:
                     if u[1] < 2 * k:
-                        closed_at[k] = closed_at[k] + multiply(u)
+                        complete = complete + kz_passes(u)
                 waiting = [u for u in waiting if u[1] >= 2 * k]
 
-            quant(s_units[1])
-            multiply(s_units[1])
-            kz_out(last_blocks[1])
-            kz_turn(last_blocks[1])
-            for a in (0, 4):
-                kr_mul(a, a + 4)
-            gram(gram_at[steps])
-            gram(last_blocks[0])
-            for a in (0, 4):
-                k_quant(krT, krq, krqs, a, a + 4)
+            quantise(scalar_pieces[1])
+            kz_passes(scalar_pieces[1])
+            kz_out(BLOCKS - 1)
+            kz_turn(BLOCKS - 1)
+            kr_product(0, PASSES)
+            j_pass(j_due)
+            j_pass(BLOCKS - 2)
+            quantise_k(kr_il, kr_codes, kr_scales, 0, PASSES)
             q_passes()
             for i in range(2):
-                gain_product(last_blocks[1], i)
-            gram(last_blocks[1], ((0, 1), (1, 2)))
-            res = work.tile([P, P], F32, name="res", tag="res", bufs=1)
-            nc.vector.tensor_copy(out=res[:], in_=qj[:])
-            nc.sync.dma_start(out=out, in_=res[:])
+                gain_product(BLOCKS - 1, i)
+            j_pass(BLOCKS - 1, ((0, 1), (1, 2)))
+            result = work.tile([P, N], F32, name="result", tag="result", bufs=1)
+            nc.vector.tensor_copy(out=result[:], in_=jq[:])
+            nc.sync.dma_start(out=out, in_=result[:])

@@ -64,6 +64,11 @@ def tile_josephkalmanupdate_w_kernel(tc, s, z_bytes, z_scale, kgain, g, d, r, ou
         last_wide = steps - 5
         first_halves = [(0, 2, lo, lo + BLK) for lo in (0, BLK)]
 
+        narrowed = cast_pieces[K_QUARTERS + 3 : last_wide + 1 : 2]
+        cast_part = {u: (u[0], u[1], u[2], u[3] - BY_PE) for u in narrowed}
+        pe_part = {u: (u[0], u[1], u[3] - BY_PE, u[3]) for u in narrowed}
+        relieved = [plane_pieces[k - 1] for k in range(1, steps) if cast_pieces[k] in narrowed or k == K_QUARTERS + 1]
+
         zb, planes, il, by_pe, codes, kz, neg_kz, turned, w_wd = {}, {}, {}, {}, {}, {}, {}, {}, {}
         passes_done = {}
 
@@ -73,7 +78,7 @@ def tile_josephkalmanupdate_w_kernel(tc, s, z_bytes, z_scale, kgain, g, d, r, ou
         def load(u, rows=slice(0, 4)):
             c, gp, lo, hi = u
             if rows.start == 0:
-                zb[u] = work.tile([P, 4, hi - lo], U8, name="zb", tag="zb", bufs=9)
+                zb[u] = work.tile([P, 4, hi - lo], U8, name="zb", tag="zb", bufs=10)
             src = z_bytes[K_PASS * gp : K_PASS * (gp + 1), W * c + lo : W * c + hi].rearrange("(p t) w -> p t w", t=4)
             nc.sync.dma_start(out=zb[u][:, rows, :], in_=src[:, rows, :])
 
@@ -106,7 +111,6 @@ def tile_josephkalmanupdate_w_kernel(tc, s, z_bytes, z_scale, kgain, g, d, r, ou
 
         def scale_interleave(u, parts):
             gp, lo = u[1], u[2]
-            il[u] = work.tile([P, 4 * W], BF16, name="il_v", tag="il_v", bufs=3, align_bytes=64)
             for part in parts:
                 a, b = part[2] - lo, part[3] - lo
                 nc.vector.tensor_tensor(
@@ -117,7 +121,9 @@ def tile_josephkalmanupdate_w_kernel(tc, s, z_bytes, z_scale, kgain, g, d, r, ou
                 )
 
         def widen_row(u, t):
-            if t == 0:
+            if t == 0 and width(u) == BY_PE:
+                planes[u] = work.tile([P, 4, BY_PE], BF16, name="pe_planes", tag="pe_planes", bufs=1, align_bytes=64)
+            elif t == 0:
                 planes[u] = work.tile([P, 4, W], BF16, name="planes", tag="planes", bufs=4, align_bytes=64)
             nc.scalar.activation(
                 out=planes[u][:, t, 0 : width(u)], in_=zb[u][:, t, :].bitcast(F8), func=COPY, scale=zs[:, u[1], t : t + 1]
@@ -134,16 +140,16 @@ def tile_josephkalmanupdate_w_kernel(tc, s, z_bytes, z_scale, kgain, g, d, r, ou
                 stop=True,
             )
 
-        def by_pe_out(u):
-            a = width(u) - BY_PE
-            nc.scalar.copy(out=il[u][:, 4 * a : 4 * width(u)].bitcast(F32), in_=by_pe[u][:].bitcast(F32))
+        def by_pe_out(u, owner):
+            a = width(owner) - BY_PE
+            nc.scalar.copy(out=il[owner][:, 4 * a : 4 * width(owner)].bitcast(F32), in_=by_pe[u][:].bitcast(F32))
 
         def interleave_on_gpsimd(u):
-            a = width(u) - BY_PE
+            a = width(u) - (BY_PE if u in relieved else 0)
             il[u] = work.tile([P, 4 * W], BF16, name="il_g", tag="il_g", bufs=1, align_bytes=64)
             nc.gpsimd.tensor_scalar(
-                out=il[u][:, 0 : 4 * a].rearrange("p (l t) -> p l t", t=4),
-                in0=planes[u][:, :, 0:a].rearrange("p t l -> p l t"),
+                out=il[u][:, 0 : 4 * a].rearrange("p (c i t) -> p c t i", i=4, t=4),
+                in0=planes[u][:, :, 0:a].rearrange("p t (c i) -> p c t i", i=4),
                 scalar1=1.0,
                 scalar2=0.0,
                 op0=MULT,
@@ -158,7 +164,7 @@ def tile_josephkalmanupdate_w_kernel(tc, s, z_bytes, z_scale, kgain, g, d, r, ou
                 out=il[u][:, 0 : 4 * a].rearrange("p (c i t) -> p c t i", i=4, t=4),
                 in_=planes[u][:, :, 0:a].rearrange("p t (c i) -> p c t i", i=4),
             )
-            by_pe_out(u)
+            by_pe_out(u, u)
 
         def quantise(u, half=None):
             if half != 1:
@@ -194,9 +200,11 @@ def tile_josephkalmanupdate_w_kernel(tc, s, z_bytes, z_scale, kgain, g, d, r, ou
                     complete.append(h)
             return complete
 
-        def kz_out(h):
+        def kz_out(h, parts=((0, 4),)):
             neg_kz[h] = work.tile([P, 4, P], F32, name="neg_kz", tag="neg_kz", bufs=2)
-            nc.scalar.activation(out=neg_kz[h][:], in_=kz[h][:].rearrange("n (p t) -> n t p", t=4), func=COPY, scale=-1.0)
+            src = kz[h][:].rearrange("n (p t) -> n t p", t=4)
+            for a, b in parts:
+                nc.scalar.activation(out=neg_kz[h][:, a:b, :], in_=src[:, a:b, :], func=COPY, scale=-1.0)
 
         def s_turn(h, tag, bufs):
             turned[h] = psum.tile([P, N, 4], F32, name=tag, tag=tag, bufs=bufs)
@@ -319,7 +327,9 @@ def tile_josephkalmanupdate_w_kernel(tc, s, z_bytes, z_scale, kgain, g, d, r, ou
             for k in range(steps):
                 if k == last_wide:
                     order.append(scalar_pieces[0])
-                order = order + plane_pieces[k : k + 1] + cast_pieces[k + 1 : k + 2]
+                order = order + plane_pieces[k : k + 1]
+                for u in cast_pieces[k + 1 : k + 2]:
+                    order = order + ([pe_part[u], cast_part[u]] if u in narrowed else [u])
                 if k == last_wide + 1:
                     order.append(scalar_pieces[1])
             for v_rows, s_rows_first in (
@@ -335,7 +345,7 @@ def tile_josephkalmanupdate_w_kernel(tc, s, z_bytes, z_scale, kgain, g, d, r, ou
             load(order[2])
             nc.sync.dma_start(out=k_rows[:, 0 : M // 2], in_=kgain[:, 0 : M // 2])
             nc.sync.dma_start(out=k_rows[:, M // 2 : M], in_=kgain[:, M // 2 : M])
-            loaded = 7
+            loaded = 8
             for u in order[3:loaded]:
                 load(u)
             nc.sync.dma_start(out=g_sb[:], in_=g.rearrange("(h p t) -> p h t", p=P, t=4))
@@ -346,7 +356,7 @@ def tile_josephkalmanupdate_w_kernel(tc, s, z_bytes, z_scale, kgain, g, d, r, ou
             late_rows = {last_wide + 1: (0,), last_wide + 2: (1,), last_wide + 3: (2, 3)}
             complete, to_turn, products, j_due = [], [], [], None
             for k in range(steps):
-                while loaded < min(len(order), 2 * k + 6):
+                while loaded < min(len(order), 2 * k + k // 2 + 7):
                     load(order[loaded])
                     loaded += 1
                 piece = cast_pieces[k]
@@ -360,28 +370,36 @@ def tile_josephkalmanupdate_w_kernel(tc, s, z_bytes, z_scale, kgain, g, d, r, ou
                     for t in range(4):
                         widen_row(scalar_pieces[0], t)
                 if k + 1 < steps:
+                    ahead = cast_pieces[k + 1]
+                    il[ahead] = work.tile([P, 4 * W], BF16, name="il_v", tag="il_v", bufs=3, align_bytes=64)
                     for t in range(4):
                         widen_row(plane_pieces[k], t)
-                        if t == 1 and k >= 1:
-                            by_pe_out(behind)
+                        if t == 1 and k >= 1 and behind in relieved:
+                            by_pe_out(behind, behind)
                     if k == 0:
                         pairs = first_piece_pairs(piece)
                         scales_to_psum()
-                    interleave_on_pe(plane_pieces[k], "by_pe", 1)
-                    for u in first_halves if k == 0 else [cast_pieces[k + 1]]:
+                    if ahead in narrowed:
+                        for t in range(4):
+                            widen_row(pe_part[ahead], t)
+                        interleave_on_pe(pe_part[ahead], "by_pe", 1)
+                    for u in first_halves if k == 0 else [cast_part.get(ahead, ahead)]:
                         cast(u)
-                else:
-                    by_pe_out(behind)
+                    if ahead in narrowed:
+                        by_pe_out(pe_part[ahead], ahead)
+                    if plane_pieces[k] in relieved:
+                        interleave_on_pe(plane_pieces[k], "by_pe", 1)
                 for h in complete:
                     kz_out(h)
+                if BLOCKS - 2 in complete:
+                    s_turn(BLOCKS - 2, "kz", 4)
+                    kz_turn(BLOCKS - 2)
                 for t in late_rows.get(k, ()):
                     widen_row(scalar_pieces[1], t)
                 if k == last_wide:
                     interleave_on_scalar(scalar_pieces[0])
                 if k == steps - 1:
                     interleave_on_scalar(scalar_pieces[1])
-                    s_turn(BLOCKS - 2, "kz", 4)
-                    kz_turn(BLOCKS - 2)
                     s_turn(BLOCKS - 1, "by_pe", 1)
                     gain_products_on_scalar(BLOCKS - 2)
 
@@ -391,7 +409,7 @@ def tile_josephkalmanupdate_w_kernel(tc, s, z_bytes, z_scale, kgain, g, d, r, ou
                     quantise(piece, 1)
                     waiting = [piece]
                     continue
-                scale_interleave(piece, first_halves if k == 1 else [piece])
+                scale_interleave(piece, first_halves if k == 1 else [cast_part.get(piece, piece)])
                 if k <= K_QUARTERS:
                     k_out(k - 1, k_bank)
                 j_now, j_due = j_due, None
@@ -411,15 +429,14 @@ def tile_josephkalmanupdate_w_kernel(tc, s, z_bytes, z_scale, kgain, g, d, r, ou
                     nc.vector.tensor_copy(out=g_f32[:], in_=g_sb[:])
                 if j_now is not None:
                     j_pass(j_now)
-                else:
-                    quantise(piece, 0)
+                quantise(piece, 0)
                 if k <= K_QUARTERS:
                     quantise_k(k_il, k_codes, k_scales, 2 * k - 2, 2 * k)
                 if k == last_wide + 1:
                     quantise(scalar_pieces[0])
                     waiting.append(scalar_pieces[0])
                 quantise(behind)
-                quantise(piece, None if j_now is not None else 1)
+                quantise(piece, 1)
                 waiting = waiting + [behind, piece]
                 complete = []
                 for u in waiting:
@@ -429,7 +446,7 @@ def tile_josephkalmanupdate_w_kernel(tc, s, z_bytes, z_scale, kgain, g, d, r, ou
 
             quantise(scalar_pieces[1])
             kz_passes(scalar_pieces[1])
-            kz_out(BLOCKS - 1)
+            kz_out(BLOCKS - 1, ((0, 2), (2, 4)))
             kz_turn(BLOCKS - 1)
             kr_product(0, PASSES)
             j_pass(j_due)

@@ -64,7 +64,7 @@ def tile_josephkalmanupdate_w_kernel(tc, s, z_bytes, z_scale, kgain, g, d, r, ou
         last_wide = steps - 5
         first_halves = [(0, 2, lo, lo + BLK) for lo in (0, BLK)]
 
-        narrowed = cast_pieces[K_QUARTERS + 3 : last_wide + 1 : 2]
+        narrowed = [cast_pieces[k] for k in range(3, last_wide + 1, 2) if k != K_QUARTERS + 1]
         cast_part = {u: (u[0], u[1], u[2], u[3] - BY_PE) for u in narrowed}
         pe_part = {u: (u[0], u[1], u[3] - BY_PE, u[3]) for u in narrowed}
         relieved = [plane_pieces[k - 1] for k in range(1, steps) if cast_pieces[k] in narrowed or k == K_QUARTERS + 1]

@@ -67,7 +67,7 @@ def tile_josephkalmanupdate_w_kernel(tc, s, z_bytes, z_scale, kgain, g, d, r, ou
         narrowed = [cast_pieces[k] for k in range(3, last_wide + 1, 2) if k != K_QUARTERS + 1]
         cast_part = {u: (u[0], u[1], u[2], u[3] - BY_PE) for u in narrowed}
         pe_part = {u: (u[0], u[1], u[3] - BY_PE, u[3]) for u in narrowed}
-        relieved = [plane_pieces[k - 1] for k in range(1, steps) if cast_pieces[k] in narrowed or k == K_QUARTERS + 1]
+        relieved = [plane_pieces[k - 1] for k in range(1, steps) if k == K_QUARTERS + 1]
 
         zb, planes, il, by_pe, codes, kz, neg_kz, turned, w_wd = {}, {}, {}, {}, {}, {}, {}, {}, {}
         passes_done = {}

@@ -23,7 +23,7 @@ BLK = 512
 BLOCKS = L // BLK
 W = 2 * BLK
 CHUNKS = L // W
-BY_PE = P
+EDGE = 64
 K_QUARTERS = PASSES // 2
 
 
@@ -53,55 +53,40 @@ def tile_josephkalmanupdate_w_kernel(tc, s, z_bytes, z_scale, kgain, g, d, r, ou
         kr_scales = keep.tile([P, PASSES, N], U8, name="kr_scales", align_bytes=64)
         s_rows = keep.tile([P, L], BF16, name="s_rows")
         jq = psum.tile([P, N], F32, name="jq", tag="jq", bufs=1)
-        zs_psum = psum.tile([P, PASSES, 4, 4], F32, name="zs_psum", tag="zs_psum", bufs=1)
+        factors = psum.tile([P, P + 2 * PASSES], F32, name="factors", tag="factors", bufs=1)
+        zs_psum = factors[:, 0:P].rearrange("p (g t i) -> p g t i", t=4, i=4)
+        r_psum = factors[:, P:].bitcast(BF16).rearrange("p (g t) -> p g t", t=4)
 
-        whole = [(c, gp, 0, W) for c in range(CHUNKS) for gp in range(PASSES)]
         last_chunk = CHUNKS - 1
-        cast_pieces = whole[0:-4:2] + [(last_chunk, gp, lo, lo + BLK) for lo in (0, BLK) for gp in (4, 6)]
-        plane_pieces = whole[1:-6:2] + [(last_chunk, gp, lo, lo + BLK) for lo in (0, BLK) for gp in (3, 5)]
-        scalar_pieces = [(last_chunk, PASSES - 1, lo, lo + BLK) for lo in (0, BLK)]
+        cast_pieces = [(c, gp, 0, W) for c in range(CHUNKS) for gp in range(0, PASSES, 2)][:-2]
+        cast_pieces = cast_pieces + [(last_chunk, gp, lo, lo + BLK) for lo in (0, BLK) for gp in (4, 6)]
+        plane_pieces = [(c, gp + 1, lo, hi) for c, gp, lo, hi in cast_pieces]
         steps = len(cast_pieces)
-        last_wide = steps - 5
-        first_halves = [(0, 2, lo, lo + BLK) for lo in (0, BLK)]
+        first_halves = [(0, 0, lo, lo + BLK) for lo in (0, BLK)]
+        body = {u: (u[0], u[1], u[2], u[3] - EDGE) for u in cast_pieces[1:]}
+        edge = {u: (u[0], u[1], u[3] - EDGE, u[3]) for u in cast_pieces[1:]}
 
-        narrowed = [cast_pieces[k] for k in range(3, last_wide + 1, 2) if k != K_QUARTERS + 1]
-        cast_part = {u: (u[0], u[1], u[2], u[3] - BY_PE) for u in narrowed}
-        pe_part = {u: (u[0], u[1], u[3] - BY_PE, u[3]) for u in narrowed}
-        relieved = [plane_pieces[k - 1] for k in range(1, steps) if k == K_QUARTERS + 1]
-
-        zb, planes, il, by_pe, codes, kz, neg_kz, turned, w_wd = {}, {}, {}, {}, {}, {}, {}, {}, {}
+        zb, planes, il, codes, kz, neg_kz, turned, w_wd = {}, {}, {}, {}, {}, {}, {}, {}
         passes_done = {}
 
         def width(u):
             return u[3] - u[2]
 
-        def load(u, rows=slice(0, 4)):
+        def load(u, tag="zb", bufs=8, rows=slice(0, 4)):
             c, gp, lo, hi = u
             if rows.start == 0:
-                zb[u] = work.tile([P, 4, hi - lo], U8, name="zb", tag="zb", bufs=10)
+                zb[u] = work.tile([P, 4, hi - lo], U8, name=tag, tag=tag, bufs=bufs)
             src = z_bytes[K_PASS * gp : K_PASS * (gp + 1), W * c + lo : W * c + hi].rearrange("(p t) w -> p t w", t=4)
             nc.sync.dma_start(out=zb[u][:, rows, :], in_=src[:, rows, :])
 
-        def first_piece_pairs(u):
-            pairs = work.tile([P, 2, 2 * W], BF16, name="pairs", tag="pairs", bufs=1, align_bytes=64)
-            for t, a, b in ((0, 0, W), (2, 0, W), (1, 0, W), (3, 0, BLK), (3, BLK, W)):
-                nc.vector.tensor_scalar(
-                    out=pairs[:, t // 2, 2 * a : 2 * b].rearrange("p (l e) -> p e l", e=2)[:, t % 2],
-                    in0=zb[u][:, t, a:b].bitcast(F8),
-                    scalar1=zs[:, u[1], t : t + 1],
-                    scalar2=None,
-                    op0=MULT,
-                )
-            return pairs
+        def load_step(k):
+            load(edge[cast_pieces[k]], "zb_edge", 4)
+            load(plane_pieces[k])
+            load(body[cast_pieces[k]])
 
-        def first_piece_join(u, pairs):
-            il[u] = work.tile([P, 4 * W], BF16, name="il_g", tag="il_g", bufs=1, align_bytes=64)
-            words = pairs[:].rearrange("p u x -> p (u x)").bitcast(F32).rearrange("p (u l) -> p l u", u=2)
-            for a in (0, BLK):
-                nc.vector.tensor_copy(
-                    out=il[u][:, 4 * a : 4 * (a + BLK)].bitcast(F32).rearrange("p (l u) -> p l u", u=2),
-                    in_=words[:, a : a + BLK, :],
-                )
+        def load_kgain(q):
+            cols = slice(2 * K_PASS * q, 2 * K_PASS * (q + 1))
+            nc.sync.dma_start(out=k_rows[:, cols], in_=kgain[:, cols])
 
         def cast(u):
             planes[u] = work.tile([P, 4, width(u)], BF16, name="raw", tag="raw", bufs=3, align_bytes=64)
@@ -120,51 +105,43 @@ def tile_josephkalmanupdate_w_kernel(tc, s, z_bytes, z_scale, kgain, g, d, r, ou
                     op=MULT,
                 )
 
+        def plane_tile(u):
+            planes[u] = work.tile([P, 4, W], BF16, name="planes", tag="planes", bufs=3, align_bytes=64)
+
         def widen_row(u, t):
-            if t == 0 and width(u) == BY_PE:
-                planes[u] = work.tile([P, 4, BY_PE], BF16, name="pe_planes", tag="pe_planes", bufs=1, align_bytes=64)
-            elif t == 0:
-                planes[u] = work.tile([P, 4, W], BF16, name="planes", tag="planes", bufs=4, align_bytes=64)
             nc.scalar.activation(
                 out=planes[u][:, t, 0 : width(u)], in_=zb[u][:, t, :].bitcast(F8), func=COPY, scale=zs[:, u[1], t : t + 1]
             )
 
-        def interleave_on_pe(u, tag, bufs):
-            a = width(u) - BY_PE
-            by_pe[u] = psum.tile([P, 4 * BY_PE], BF16, name=tag, tag=tag, bufs=bufs)
+        def widen_row_on_vector(u, t):
+            nc.vector.tensor_scalar(
+                out=planes[u][:, t, :], in0=zb[u][:, t, :].bitcast(F8), scalar1=zs[:, u[1], t : t + 1], scalar2=None, op0=MULT
+            )
+
+        def edge_through_pe(u):
+            planes[u] = work.tile([P, 4, width(u)], BF16, name="edge_planes", tag="edge_planes", bufs=2, align_bytes=64)
+            for t in range(4):
+                widen_row(u, t)
+            by_pe = psum.tile([P, 4 * width(u)], BF16, name="by_pe", tag="by_pe", bufs=1)
             nc.tensor.matmul(
-                by_pe[u][:].rearrange("p (l t) -> p l t", t=4),
+                by_pe[:].rearrange("p (l t) -> p l t", t=4),
                 lhsT=ident_bf[:],
-                rhs=planes[u][:, :, a : a + BY_PE].rearrange("p t l -> p l t"),
+                rhs=planes[u][:].rearrange("p t l -> p l t"),
                 start=True,
                 stop=True,
             )
-
-        def by_pe_out(u, owner):
-            a = width(owner) - BY_PE
-            nc.scalar.copy(out=il[owner][:, 4 * a : 4 * width(owner)].bitcast(F32), in_=by_pe[u][:].bitcast(F32))
+            return by_pe
 
         def interleave_on_gpsimd(u):
-            a = width(u) - (BY_PE if u in relieved else 0)
             il[u] = work.tile([P, 4 * W], BF16, name="il_g", tag="il_g", bufs=1, align_bytes=64)
             nc.gpsimd.tensor_scalar(
-                out=il[u][:, 0 : 4 * a].rearrange("p (c i t) -> p c t i", i=4, t=4),
-                in0=planes[u][:, :, 0:a].rearrange("p t (c i) -> p c t i", i=4),
+                out=il[u][:, 0 : 4 * width(u)].rearrange("p (c i t) -> p c t i", i=4, t=4),
+                in0=planes[u][:, :, 0 : width(u)].rearrange("p t (c i) -> p c t i", i=4),
                 scalar1=1.0,
                 scalar2=0.0,
                 op0=MULT,
                 op1=ADD,
             )
-
-        def interleave_on_scalar(u):
-            a = width(u) - BY_PE
-            interleave_on_pe(u, "kz", 4)
-            il[u] = work.tile([P, 4 * BLK], BF16, name="il_s", tag="il_s", bufs=2, align_bytes=64)
-            nc.scalar.copy(
-                out=il[u][:, 0 : 4 * a].rearrange("p (c i t) -> p c t i", i=4, t=4),
-                in_=planes[u][:, :, 0:a].rearrange("p t (c i) -> p c t i", i=4),
-            )
-            by_pe_out(u, u)
 
         def quantise(u, half=None):
             if half != 1:
@@ -292,7 +269,7 @@ def tile_josephkalmanupdate_w_kernel(tc, s, z_bytes, z_scale, kgain, g, d, r, ou
             nc.vector.tensor_tensor(
                 out=kr_il[:, a:b, :].rearrange("p g (n t) -> p g n t", t=4),
                 in0=k_il[:, a:b, :].rearrange("p g (n t) -> p g n t", t=4),
-                in1=r_sb[:, a:b, :].unsqueeze(2).to_broadcast([P, b - a, N, 4]),
+                in1=r_psum[:, a:b, :].unsqueeze(2).to_broadcast([P, b - a, N, 4]),
                 op=MULT,
             )
 
@@ -312,144 +289,114 @@ def tile_josephkalmanupdate_w_kernel(tc, s, z_bytes, z_scale, kgain, g, d, r, ou
             nc.vector.tensor_copy(
                 out=zs_four[:], in_=zs[:].rearrange("p g t -> p (g t)").unsqueeze(2).to_broadcast([P, 4 * PASSES, 4])
             )
+
+        def scales_turn():
             once = psum.tile([P, P], F32, name="by_pe", tag="by_pe", bufs=1)
             nc.tensor.transpose(once[:], zs_four[:].rearrange("p x i -> p (x i)"), ident[:])
             nc.scalar.copy(out=zs_turned[:], in_=once[:])
-            nc.tensor.transpose(zs_psum[:].rearrange("p g t i -> p (g t i)"), zs_turned[:], ident[:])
+            nc.tensor.transpose(factors[:, 0:P], zs_turned[:], ident[:])
 
         with tc.manual_schedule():
             zs_hbm = z_scale.rearrange("(g p t) o -> p g (t o)", p=P, t=4)
             nc.scalar.dma_start(out=zs[:, 0:2, :], in_=zs_hbm[:, 0:2, :])
+            nc.scalar.dma_start(out=zs[:, 2:PASSES, :], in_=zs_hbm[:, 2:PASSES, :])
             make_identity(nc, ident[:])
             nc.gpsimd.tensor_copy(out=ident_bf[:], in_=ident[:])
 
-            order = []
-            for k in range(steps):
-                if k == last_wide:
-                    order.append(scalar_pieces[0])
-                order = order + plane_pieces[k : k + 1]
-                for u in cast_pieces[k + 1 : k + 2]:
-                    order = order + ([pe_part[u], cast_part[u]] if u in narrowed else [u])
-                if k == last_wide + 1:
-                    order.append(scalar_pieces[1])
-            for v_rows, s_rows_first in (
-                (slice(0, 1), slice(0, 1)),
-                (slice(2, 3), slice(1, 2)),
-                (slice(1, 4, 2), slice(2, 4)),
-            ):
-                load(cast_pieces[0], v_rows)
-                load(plane_pieces[0], s_rows_first)
-            nc.sync.dma_start(out=zs[:, 2:PASSES, :], in_=zs_hbm[:, 2:PASSES, :])
+            load(plane_pieces[0], rows=slice(0, 1))
             load(first_halves[0])
+            load(plane_pieces[0], rows=slice(1, 3))
             load(first_halves[1])
-            load(order[2])
-            nc.sync.dma_start(out=k_rows[:, 0 : M // 2], in_=kgain[:, 0 : M // 2])
-            nc.sync.dma_start(out=k_rows[:, M // 2 : M], in_=kgain[:, M // 2 : M])
-            loaded = 8
-            for u in order[3:loaded]:
-                load(u)
-            nc.sync.dma_start(out=g_sb[:], in_=g.rearrange("(h p t) -> p h t", p=P, t=4))
-            nc.sync.dma_start(out=d_sb[:], in_=d.rearrange("(h p t) -> p h t", p=P, t=4))
-            nc.sync.dma_start(out=r_sb[:], in_=r.rearrange("(g p t) -> p g t", p=P, t=4))
-            nc.sync.dma_start(out=s_rows[:], in_=s)
+            load(plane_pieces[0], rows=slice(3, 4))
+            load(edge[cast_pieces[1]], "zb_edge", 4)
+            load(plane_pieces[1], rows=slice(0, 2))
+            load(plane_pieces[1], rows=slice(2, 4))
+            load_kgain(0)
+            load(body[cast_pieces[1]])
+            load_step(2)
+            load_kgain(1)
 
-            late_rows = {last_wide + 1: (0,), last_wide + 2: (1,), last_wide + 3: (2, 3)}
+            plane_tile(plane_pieces[0])
+            widen_row_on_vector(plane_pieces[0], 0)
+            scales_to_psum()
+            cast(first_halves[0])
+            scales_turn()
+            cast(first_halves[1])
+            for t in range(1, 4):
+                widen_row_on_vector(plane_pieces[0], t)
+            il[cast_pieces[0]] = work.tile([P, 4 * W], BF16, name="il_v", tag="il_v", bufs=3, align_bytes=64)
+
             complete, to_turn, products, j_due = [], [], [], None
             for k in range(steps):
-                while loaded < min(len(order), 2 * k + k // 2 + 7):
-                    load(order[loaded])
-                    loaded += 1
-                piece = cast_pieces[k]
-                if k >= 1:
-                    behind = plane_pieces[k - 1]
-                    interleave_on_gpsimd(behind)
-                if 1 <= k <= K_QUARTERS:
-                    k_bank = k_turn(k - 1)
+                if k + 3 < steps:
+                    load_step(k + 3)
+                if k + 2 < K_QUARTERS:
+                    load_kgain(k + 2)
+                if k == 1:
+                    nc.sync.dma_start(out=r_sb[:], in_=r.rearrange("(g p t) -> p g t", p=P, t=4))
+                    nc.sync.dma_start(out=g_sb[:], in_=g.rearrange("(h p t) -> p h t", p=P, t=4))
+                    nc.sync.dma_start(out=d_sb[:], in_=d.rearrange("(h p t) -> p h t", p=P, t=4))
+                    nc.sync.dma_start(out=s_rows[:], in_=s)
+                piece, beside = cast_pieces[k], plane_pieces[k]
+                interleave_on_gpsimd(beside)
+                if k < K_QUARTERS:
+                    k_bank = k_turn(k)
 
-                if k == last_wide:
-                    for t in range(4):
-                        widen_row(scalar_pieces[0], t)
                 if k + 1 < steps:
                     ahead = cast_pieces[k + 1]
                     il[ahead] = work.tile([P, 4 * W], BF16, name="il_v", tag="il_v", bufs=3, align_bytes=64)
+                    by_pe = edge_through_pe(edge[ahead])
+                    plane_tile(plane_pieces[k + 1])
                     for t in range(4):
-                        widen_row(plane_pieces[k], t)
-                        if t == 1 and k >= 1 and behind in relieved:
-                            by_pe_out(behind, behind)
-                    if k == 0:
-                        pairs = first_piece_pairs(piece)
-                        scales_to_psum()
-                    if ahead in narrowed:
-                        for t in range(4):
-                            widen_row(pe_part[ahead], t)
-                        interleave_on_pe(pe_part[ahead], "by_pe", 1)
-                    for u in first_halves if k == 0 else [cast_part.get(ahead, ahead)]:
-                        cast(u)
-                    if ahead in narrowed:
-                        by_pe_out(pe_part[ahead], ahead)
-                    if plane_pieces[k] in relieved:
-                        interleave_on_pe(plane_pieces[k], "by_pe", 1)
-                for h in complete:
-                    kz_out(h)
-                if BLOCKS - 2 in complete:
-                    s_turn(BLOCKS - 2, "kz", 4)
-                    kz_turn(BLOCKS - 2)
-                for t in late_rows.get(k, ()):
-                    widen_row(scalar_pieces[1], t)
-                if k == last_wide:
-                    interleave_on_scalar(scalar_pieces[0])
-                if k == steps - 1:
-                    interleave_on_scalar(scalar_pieces[1])
-                    s_turn(BLOCKS - 1, "by_pe", 1)
+                        widen_row(plane_pieces[k + 1], t)
+                    cast(body[ahead])
+                    nc.scalar.copy(
+                        out=il[ahead][:, 4 * width(body[ahead]) : 4 * width(ahead)].bitcast(F32), in_=by_pe[:].bitcast(F32)
+                    )
+                else:
+                    s_turn(BLOCKS - 1, "kz", 4)
                     gain_products_on_scalar(BLOCKS - 2)
+                if complete:
+                    h = complete.pop(0)
+                    kz_out(h)
+                    to_turn.append(h)
 
-                if k == 0:
-                    first_piece_join(piece, pairs)
-                    quantise(piece, 0)
-                    quantise(piece, 1)
-                    waiting = [piece]
-                    continue
-                scale_interleave(piece, first_halves if k == 1 else [cast_part.get(piece, piece)])
-                if k <= K_QUARTERS:
-                    k_out(k - 1, k_bank)
+                scale_interleave(piece, first_halves if k == 0 else [body[piece]])
                 j_now, j_due = j_due, None
-                if products:
+                if k < K_QUARTERS:
+                    k_out(k, k_bank)
+                elif products:
                     h, i = products.pop(0)
                     gain_product(h, i)
                     if i == 1:
                         j_due = h
-                to_turn = to_turn + [h for h in complete if h < BLOCKS - 2]
+                else:
+                    kr_done = 0 if k == K_QUARTERS else 2
+                    kr_product(kr_done, kr_done + 2)
+                if k == K_QUARTERS - 1:
+                    nc.tensor.matmul(
+                        factors[:, P:].bitcast(BF16), lhsT=ident_bf[:], rhs=r_sb[:].rearrange("p g t -> p (g t)"), start=True, stop=True
+                    )
                 if to_turn and not products:
                     h = to_turn.pop(0)
                     s_turn(h, "turned", 1)
                     kz_turn(h)
-                    products = [(h, 0), (h, 1)]
-                if k == K_QUARTERS + 1:
-                    nc.vector.tensor_tensor(out=gd_f32[:], in0=g_sb[:], in1=d_sb[:], op=MULT)
-                    nc.vector.tensor_copy(out=g_f32[:], in_=g_sb[:])
+                    products = [(h, 0), (h, 1)] if h < BLOCKS - 2 else []
                 if j_now is not None:
                     j_pass(j_now)
                 quantise(piece, 0)
-                if k <= K_QUARTERS:
-                    quantise_k(k_il, k_codes, k_scales, 2 * k - 2, 2 * k)
-                if k == last_wide + 1:
-                    quantise(scalar_pieces[0])
-                    waiting.append(scalar_pieces[0])
-                quantise(behind)
+                if k < K_QUARTERS:
+                    quantise_k(k_il, k_codes, k_scales, 2 * k, 2 * k + 2)
+                if k == K_QUARTERS:
+                    nc.vector.tensor_tensor(out=gd_f32[:], in0=g_sb[:], in1=d_sb[:], op=MULT)
+                    nc.vector.tensor_copy(out=g_f32[:], in_=g_sb[:])
+                quantise(beside)
                 quantise(piece, 1)
-                waiting = waiting + [behind, piece]
-                complete = []
-                for u in waiting:
-                    if u[1] < 2 * k:
-                        complete = complete + kz_passes(u)
-                waiting = [u for u in waiting if u[1] >= 2 * k]
+                complete = complete + kz_passes(beside) + kz_passes(piece)
 
-            quantise(scalar_pieces[1])
-            kz_passes(scalar_pieces[1])
             kz_out(BLOCKS - 1, ((0, 2), (2, 4)))
             kz_turn(BLOCKS - 1)
-            kr_product(0, PASSES)
-            j_pass(j_due)
+            kr_product(4, PASSES)
             j_pass(BLOCKS - 2)
             quantise_k(kr_il, kr_codes, kr_scales, 0, PASSES)
             q_passes()

@@ -23,7 +23,7 @@ BLK = 512
 BLOCKS = L // BLK
 W = 2 * BLK
 CHUNKS = L // W
-EDGE = 64
+EDGE = 96
 K_QUARTERS = PASSES // 2
 
 

@@ -24,6 +24,9 @@ BLOCKS = L // BLK
 W = 2 * BLK
 CHUNKS = L // W
 EDGE = 96
+EDGE_BESIDE_KZ = 64
+LATE_EDGE = 128
+RELIEF = P
 K_QUARTERS = PASSES // 2
 
 
@@ -63,10 +66,15 @@ def tile_josephkalmanupdate_w_kernel(tc, s, z_bytes, z_scale, kgain, g, d, r, ou
         plane_pieces = [(c, gp + 1, lo, hi) for c, gp, lo, hi in cast_pieces]
         steps = len(cast_pieces)
         first_halves = [(0, 0, lo, lo + BLK) for lo in (0, BLK)]
-        body = {u: (u[0], u[1], u[2], u[3] - EDGE) for u in cast_pieces[1:]}
-        edge = {u: (u[0], u[1], u[3] - EDGE, u[3]) for u in cast_pieces[1:]}
+        edge_width = [0] + [
+            LATE_EDGE if hi - lo < W else EDGE_BESIDE_KZ if k > K_QUARTERS and k % 2 else EDGE
+            for k, (c, gp, lo, hi) in enumerate(cast_pieces)
+        ][1:]
+        relief = [RELIEF if lo else 0 for c, gp, lo, hi in plane_pieces]
+        edges = [(c, gp, lo, lo + x) for (c, gp, lo, hi), x in zip(cast_pieces, edge_width)]
+        bodies = [(c, gp, lo + x, hi) for (c, gp, lo, hi), x in zip(cast_pieces, edge_width)]
 
-        zb, planes, il, codes, kz, neg_kz, turned, w_wd = {}, {}, {}, {}, {}, {}, {}, {}
+        zb, raw, planes, il_v, il_g, codes, kz, neg_kz, turned, w_wd = {}, {}, {}, {}, {}, {}, {}, {}, {}, {}
         passes_done = {}
 
         def width(u):
@@ -80,101 +88,112 @@ def tile_josephkalmanupdate_w_kernel(tc, s, z_bytes, z_scale, kgain, g, d, r, ou
             nc.sync.dma_start(out=zb[u][:, rows, :], in_=src[:, rows, :])
 
         def load_step(k):
-            load(edge[cast_pieces[k]], "zb_edge", 4)
+            load(edges[k], "zb_edge", 4)
             load(plane_pieces[k])
-            load(body[cast_pieces[k]])
+            load(bodies[k])
 
         def load_kgain(q):
             cols = slice(2 * K_PASS * q, 2 * K_PASS * (q + 1))
             nc.sync.dma_start(out=k_rows[:, cols], in_=kgain[:, cols])
 
         def cast(u):
-            planes[u] = work.tile([P, 4, width(u)], BF16, name="raw", tag="raw", bufs=3, align_bytes=64)
+            raw[u] = work.tile([P, 4, width(u)], BF16, name="raw", tag="raw", bufs=3, align_bytes=64)
             nc.scalar.copy(
-                out=planes[u][:].rearrange("p t l -> p (t l)"), in_=zb[u][:].rearrange("p t l -> p (t l)").bitcast(F8)
+                out=raw[u][:].rearrange("p t l -> p (t l)"), in_=zb[u][:].rearrange("p t l -> p (t l)").bitcast(F8)
             )
 
-        def scale_interleave(u, parts):
-            gp, lo = u[1], u[2]
-            for part in parts:
-                a, b = part[2] - lo, part[3] - lo
-                nc.vector.tensor_tensor(
-                    out=il[u][:, 4 * a : 4 * b].rearrange("p (c i t) -> p c t i", i=4, t=4),
-                    in0=planes[part][:].rearrange("p t (c i) -> p c t i", i=4),
-                    in1=zs_psum[:, gp].unsqueeze(1).to_broadcast([P, (b - a) // 4, 4, 4]),
-                    op=MULT,
+        def step_tiles(k):
+            planes[k] = work.tile([P, 4, W + EDGE], BF16, name="planes", tag="planes", bufs=4, align_bytes=64)
+            il_v[k] = work.tile([P, 4 * W], BF16, name="il_v", tag="il_v", bufs=3, align_bytes=64)
+
+        def scale_interleave(k, part):
+            a = relief[k] + part[2] - cast_pieces[k][2]
+            nc.vector.tensor_tensor(
+                out=il_v[k][:, 4 * a : 4 * (a + width(part))].rearrange("p (c i t) -> p c t i", i=4, t=4),
+                in0=raw[part][:].rearrange("p t (c i) -> p c t i", i=4),
+                in1=zs_psum[:, part[1]].unsqueeze(1).to_broadcast([P, width(part) // 4, 4, 4]),
+                op=MULT,
+            )
+
+        def widen(k, u, first):
+            for t in range(4):
+                nc.scalar.activation(
+                    out=planes[k][:, t, first : first + width(u)],
+                    in_=zb[u][:, t, :].bitcast(F8),
+                    func=COPY,
+                    scale=zs[:, u[1], t : t + 1],
                 )
 
-        def plane_tile(u):
-            planes[u] = work.tile([P, 4, W], BF16, name="planes", tag="planes", bufs=3, align_bytes=64)
-
-        def widen_row(u, t):
-            nc.scalar.activation(
-                out=planes[u][:, t, 0 : width(u)], in_=zb[u][:, t, :].bitcast(F8), func=COPY, scale=zs[:, u[1], t : t + 1]
-            )
-
-        def widen_row_on_vector(u, t):
+        def widen_row_on_vector(t):
+            u = plane_pieces[0]
             nc.vector.tensor_scalar(
-                out=planes[u][:, t, :], in0=zb[u][:, t, :].bitcast(F8), scalar1=zs[:, u[1], t : t + 1], scalar2=None, op0=MULT
+                out=planes[0][:, t, 0:W], in0=zb[u][:, t, :].bitcast(F8), scalar1=zs[:, u[1], t : t + 1], scalar2=None, op0=MULT
             )
 
-        def edge_through_pe(u):
-            planes[u] = work.tile([P, 4, width(u)], BF16, name="edge_planes", tag="edge_planes", bufs=2, align_bytes=64)
-            for t in range(4):
-                widen_row(u, t)
-            by_pe = psum.tile([P, 4 * width(u)], BF16, name="by_pe", tag="by_pe", bufs=1)
-            nc.tensor.matmul(
-                by_pe[:].rearrange("p (l t) -> p l t", t=4),
-                lhsT=ident_bf[:],
-                rhs=planes[u][:].rearrange("p t l -> p l t"),
-                start=True,
-                stop=True,
-            )
+        def interleave_on_pe(k):
+            first, count = width(plane_pieces[k]) - relief[k], relief[k] + edge_width[k]
+            by_pe = psum.tile([P, 4 * count], BF16, name="by_pe", tag="by_pe", bufs=1)
+            for a in range(0, count, P):
+                b = min(a + P, count)
+                nc.tensor.matmul(
+                    by_pe[:, 4 * a : 4 * b].rearrange("p (l t) -> p l t", t=4),
+                    lhsT=ident_bf[:],
+                    rhs=planes[k][:, :, first + a : first + b].rearrange("p t l -> p l t"),
+                    start=True,
+                    stop=True,
+                )
             return by_pe
 
-        def interleave_on_gpsimd(u):
-            il[u] = work.tile([P, 4 * W], BF16, name="il_g", tag="il_g", bufs=1, align_bytes=64)
+        def by_pe_out(k, by_pe):
+            count = relief[k] + edge_width[k]
+            nc.scalar.copy(out=il_v[k][:, 0 : 4 * count].bitcast(F32), in_=by_pe[:].bitcast(F32))
+
+        def interleave_on_gpsimd(k):
+            count = width(plane_pieces[k]) - relief[k]
+            il_g[k] = work.tile([P, 4 * W], BF16, name="il_g", tag="il_g", bufs=1, align_bytes=64)
             nc.gpsimd.tensor_scalar(
-                out=il[u][:, 0 : 4 * width(u)].rearrange("p (c i t) -> p c t i", i=4, t=4),
-                in0=planes[u][:, :, 0 : width(u)].rearrange("p t (c i) -> p c t i", i=4),
+                out=il_g[k][:, 0 : 4 * count].rearrange("p (c i t) -> p c t i", i=4, t=4),
+                in0=planes[k][:, :, 0:count].rearrange("p t (c i) -> p c t i", i=4),
                 scalar1=1.0,
                 scalar2=0.0,
                 op0=MULT,
                 op1=ADD,
             )
 
-        def quantise(u, half=None):
-            if half != 1:
-                z_codes = work.tile([P, W], U32, name="z_codes", tag="z_codes", bufs=5, align_bytes=64)
-                z_scales = work.tile([P, W], U8, name="z_scales", tag="z_scales", bufs=5, align_bytes=64)
-                codes[u] = (z_codes, z_scales)
-            z_codes, z_scales = codes[u]
-            a, b = (0, width(u)) if half is None else (half * width(u) // 2, (half + 1) * width(u) // 2)
+        def code_tiles(k):
+            z_codes = work.tile([P, 2 * W], U32, name="z_codes", tag="z_codes", bufs=3, align_bytes=64)
+            z_scales = work.tile([P, 2 * W], U8, name="z_scales", tag="z_scales", bufs=3, align_bytes=64)
+            codes[k] = (z_codes, z_scales)
+
+        def quantise(k, src, first, a, b):
+            z_codes, z_scales = codes[k]
             nc.vector.quantize_mx(
-                out=z_codes[:, a:b].bitcast(FP8X4), scales=z_scales[:, a:b], in_=il[u][:, 4 * a : 4 * b]
+                out=z_codes[:, first + a : first + b].bitcast(FP8X4),
+                scales=z_scales[:, first + a : first + b],
+                in_=src[:, 4 * a : 4 * b],
             )
 
-        def kz_passes(u):
-            c, gp, lo, hi = u
-            z_codes, z_scales = codes[u]
+        def kz_passes(k):
+            z_codes, z_scales = codes[k]
             complete = []
-            for col in range(0, hi - lo, BLK):
-                h = (W * c + lo + col) // BLK
-                if h not in kz:
-                    kz[h] = psum.tile([P, BLK], F32, name="kz", tag="kz", bufs=4)
-                done = passes_done.get(h, 0)
-                passes_done[h] = done + 1
-                nc.tensor.matmul_mx(
-                    out=kz[h][:],
-                    lhsT=k_codes[:, gp, :].bitcast(FP8X4),
-                    lhsT_scale=k_scales[:, gp, :],
-                    rhs=z_codes[:, col : col + BLK].bitcast(FP8X4),
-                    rhs_scale=z_scales[:, col : col + BLK],
-                    start=(done == 0),
-                    stop=(done == PASSES - 1),
-                )
-                if done == PASSES - 1:
-                    complete.append(h)
+            for first, (c, gp, lo, hi) in ((0, plane_pieces[k]), (width(plane_pieces[k]), cast_pieces[k])):
+                for col in range(0, hi - lo, BLK):
+                    h = (W * c + lo + col) // BLK
+                    if h not in kz:
+                        kz[h] = psum.tile([P, BLK], F32, name="kz", tag="kz", bufs=4)
+                    done = passes_done.get(h, 0)
+                    passes_done[h] = done + 1
+                    nc.tensor.matmul_mx(
+                        out=kz[h][:],
+                        lhsT=k_codes[:, gp, :].bitcast(FP8X4),
+                        lhsT_scale=k_scales[:, gp, :],
+                        rhs=z_codes[:, first + col : first + col + BLK].bitcast(FP8X4),
+                        rhs_scale=z_scales[:, first + col : first + col + BLK],
+                        start=(done == 0),
+                        stop=(done == PASSES - 1),
+                    )
+                    if done == PASSES - 1:
+                        complete.append(h)
             return complete
 
         def kz_out(h, parts=((0, 4),)):
@@ -308,23 +327,22 @@ def tile_josephkalmanupdate_w_kernel(tc, s, z_bytes, z_scale, kgain, g, d, r, ou
             load(plane_pieces[0], rows=slice(1, 3))
             load(first_halves[1])
             load(plane_pieces[0], rows=slice(3, 4))
-            load(edge[cast_pieces[1]], "zb_edge", 4)
+            load(edges[1], "zb_edge", 4)
             load(plane_pieces[1], rows=slice(0, 2))
             load(plane_pieces[1], rows=slice(2, 4))
             load_kgain(0)
-            load(body[cast_pieces[1]])
+            load(bodies[1])
             load_step(2)
             load_kgain(1)
 
-            plane_tile(plane_pieces[0])
-            widen_row_on_vector(plane_pieces[0], 0)
+            step_tiles(0)
+            widen_row_on_vector(0)
             scales_to_psum()
             cast(first_halves[0])
             scales_turn()
             cast(first_halves[1])
             for t in range(1, 4):
-                widen_row_on_vector(plane_pieces[0], t)
-            il[cast_pieces[0]] = work.tile([P, 4 * W], BF16, name="il_v", tag="il_v", bufs=3, align_bytes=64)
+                widen_row_on_vector(t)
 
             complete, to_turn, products, j_due = [], [], [], None
             for k in range(steps):
@@ -337,31 +355,36 @@ def tile_josephkalmanupdate_w_kernel(tc, s, z_bytes, z_scale, kgain, g, d, r, ou
                     nc.sync.dma_start(out=g_sb[:], in_=g.rearrange("(h p t) -> p h t", p=P, t=4))
                     nc.sync.dma_start(out=d_sb[:], in_=d.rearrange("(h p t) -> p h t", p=P, t=4))
                     nc.sync.dma_start(out=s_rows[:], in_=s)
-                piece, beside = cast_pieces[k], plane_pieces[k]
-                interleave_on_gpsimd(beside)
+                interleave_on_gpsimd(k)
                 if k < K_QUARTERS:
                     k_bank = k_turn(k)
 
                 if k + 1 < steps:
-                    ahead = cast_pieces[k + 1]
-                    il[ahead] = work.tile([P, 4 * W], BF16, name="il_v", tag="il_v", bufs=3, align_bytes=64)
-                    by_pe = edge_through_pe(edge[ahead])
-                    plane_tile(plane_pieces[k + 1])
-                    for t in range(4):
-                        widen_row(plane_pieces[k + 1], t)
-                    cast(body[ahead])
-                    nc.scalar.copy(
-                        out=il[ahead][:, 4 * width(body[ahead]) : 4 * width(ahead)].bitcast(F32), in_=by_pe[:].bitcast(F32)
-                    )
+                    step_tiles(k + 1)
+                    widen(k + 1, edges[k + 1], width(plane_pieces[k + 1]))
+                if relief[k]:
+                    by_pe_out(k, by_pe)
+                if k + 1 < steps and not relief[k + 1]:
+                    by_pe = interleave_on_pe(k + 1)
+                if k >= 1:
+                    complete = complete + kz_passes(k - 1)
+                if k + 1 < steps:
+                    widen(k + 1, plane_pieces[k + 1], 0)
+                    if relief[k + 1]:
+                        by_pe = interleave_on_pe(k + 1)
+                    else:
+                        by_pe_out(k + 1, by_pe)
+                    cast(bodies[k + 1])
                 else:
                     s_turn(BLOCKS - 1, "kz", 4)
                     gain_products_on_scalar(BLOCKS - 2)
-                if complete:
+                if complete and k % 2 == 0:
                     h = complete.pop(0)
                     kz_out(h)
                     to_turn.append(h)
 
-                scale_interleave(piece, first_halves if k == 0 else [body[piece]])
+                for part in first_halves if k == 0 else [bodies[k]]:
+                    scale_interleave(k, part)
                 j_now, j_due = j_due, None
                 if k < K_QUARTERS:
                     k_out(k, k_bank)
@@ -384,16 +407,20 @@ def tile_josephkalmanupdate_w_kernel(tc, s, z_bytes, z_scale, kgain, g, d, r, ou
                     products = [(h, 0), (h, 1)] if h < BLOCKS - 2 else []
                 if j_now is not None:
                     j_pass(j_now)
-                quantise(piece, 0)
+                code_tiles(k)
+                by_g = width(plane_pieces[k]) - relief[k]
+                cut = relief[k] or width(cast_pieces[k]) // 2
+                quantise(k, il_v[k], by_g, 0, cut)
                 if k < K_QUARTERS:
                     quantise_k(k_il, k_codes, k_scales, 2 * k, 2 * k + 2)
                 if k == K_QUARTERS:
                     nc.vector.tensor_tensor(out=gd_f32[:], in0=g_sb[:], in1=d_sb[:], op=MULT)
                     nc.vector.tensor_copy(out=g_f32[:], in_=g_sb[:])
-                quantise(beside)
-                quantise(piece, 1)
-                complete = complete + kz_passes(beside) + kz_passes(piece)
+                for a, b in ((0, by_g - relief[k]), (by_g - relief[k], by_g)) if relief[k] else ((0, by_g),):
+                    quantise(k, il_g[k], 0, a, b)
+                quantise(k, il_v[k], by_g, cut, relief[k] + width(cast_pieces[k]))
 
+            kz_passes(steps - 1)
             kz_out(BLOCKS - 1, ((0, 2), (2, 4)))
             kz_turn(BLOCKS - 1)
             kr_product(4, PASSES)

@@ -24,8 +24,8 @@ BLOCKS = L // BLK
 W = 2 * BLK
 CHUNKS = L // W
 EDGE = 96
-EDGE_BESIDE_KZ = 64
-LATE_EDGE = 128
+DOUBLE_EDGE = 256
+LATE_EDGE = 192
 RELIEF = P
 K_QUARTERS = PASSES // 2
 
@@ -61,18 +61,16 @@ def tile_josephkalmanupdate_w_kernel(tc, s, z_bytes, z_scale, kgain, g, d, r, ou
         r_psum = factors[:, P:].bitcast(BF16).rearrange("p (g t) -> p g t", t=4)
 
         last_chunk = CHUNKS - 1
-        cast_pieces = [(c, gp, 0, W) for c in range(CHUNKS) for gp in range(0, PASSES, 2)][:-2]
-        cast_pieces = cast_pieces + [(last_chunk, gp, lo, lo + BLK) for lo in (0, BLK) for gp in (4, 6)]
-        plane_pieces = [(c, gp + 1, lo, hi) for c, gp, lo, hi in cast_pieces]
-        steps = len(cast_pieces)
-        first_halves = [(0, 0, lo, lo + BLK) for lo in (0, BLK)]
-        edge_width = [0] + [
-            LATE_EDGE if hi - lo < W else EDGE_BESIDE_KZ if k > K_QUARTERS and k % 2 else EDGE
-            for k, (c, gp, lo, hi) in enumerate(cast_pieces)
-        ][1:]
-        relief = [RELIEF if lo else 0 for c, gp, lo, hi in plane_pieces]
-        edges = [(c, gp, lo, lo + x) for (c, gp, lo, hi), x in zip(cast_pieces, edge_width)]
-        bodies = [(c, gp, lo + x, hi) for (c, gp, lo, hi), x in zip(cast_pieces, edge_width)]
+        casts = [[(c, gp, 0, W)] for c in range(CHUNKS) for gp in range(0, PASSES, 2)][:-2]
+        casts = casts + [[(last_chunk, gp, 0, BLK) for gp in (4, 6)]] + [[(last_chunk, gp, BLK, W)] for gp in (4, 6)]
+        odd = [[(c, gp + 1, lo, hi) for c, gp, lo, hi in pieces] for pieces in casts]
+        steps = len(casts)
+        columns = [sum(hi - lo for c, gp, lo, hi in pieces) for pieces in casts]
+        edge_width = [0] + [LATE_EDGE if columns[k] < W else EDGE if len(casts[k]) == 1 else DOUBLE_EDGE for k in range(1, steps)]
+        relief = [RELIEF if columns[k] < W else 0 for k in range(steps)]
+        edges = [pieces[0][:3] + (pieces[0][2] + x,) for pieces, x in zip(casts, edge_width)]
+        bodies = [[u[:2] + (u[3], pieces[0][3])] + pieces[1:] for u, pieces in zip(edges, casts)]
+        bodies[0] = [(0, 0, lo, lo + BLK) for lo in (0, BLK)]
 
         zb, raw, planes, il_v, il_g, codes, kz, neg_kz, turned, w_wd = {}, {}, {}, {}, {}, {}, {}, {}, {}, {}
         passes_done = {}
@@ -89,8 +87,8 @@ def tile_josephkalmanupdate_w_kernel(tc, s, z_bytes, z_scale, kgain, g, d, r, ou
 
         def load_step(k):
             load(edges[k], "zb_edge", 4)
-            load(plane_pieces[k])
-            load(bodies[k])
+            for u in odd[k] + bodies[k]:
+                load(u)
 
         def load_kgain(q):
             cols = slice(2 * K_PASS * q, 2 * K_PASS * (q + 1))
@@ -103,11 +101,10 @@ def tile_josephkalmanupdate_w_kernel(tc, s, z_bytes, z_scale, kgain, g, d, r, ou
             )
 
         def step_tiles(k):
-            planes[k] = work.tile([P, 4, W + EDGE], BF16, name="planes", tag="planes", bufs=4, align_bytes=64)
+            planes[k] = work.tile([P, 4, W + DOUBLE_EDGE], BF16, name="planes", tag="planes", bufs=4, align_bytes=64)
             il_v[k] = work.tile([P, 4 * W], BF16, name="il_v", tag="il_v", bufs=3, align_bytes=64)
 
-        def scale_interleave(k, part):
-            a = relief[k] + part[2] - cast_pieces[k][2]
+        def scale_interleave(k, part, a):
             nc.vector.tensor_tensor(
                 out=il_v[k][:, 4 * a : 4 * (a + width(part))].rearrange("p (c i t) -> p c t i", i=4, t=4),
                 in0=raw[part][:].rearrange("p t (c i) -> p c t i", i=4),
@@ -125,31 +122,37 @@ def tile_josephkalmanupdate_w_kernel(tc, s, z_bytes, z_scale, kgain, g, d, r, ou
                 )
 
         def widen_row_on_vector(t):
-            u = plane_pieces[0]
+            u = odd[0][0]
             nc.vector.tensor_scalar(
                 out=planes[0][:, t, 0:W], in0=zb[u][:, t, :].bitcast(F8), scalar1=zs[:, u[1], t : t + 1], scalar2=None, op0=MULT
             )
 
         def interleave_on_pe(k):
-            first, count = width(plane_pieces[k]) - relief[k], relief[k] + edge_width[k]
-            by_pe = psum.tile([P, 4 * count], BF16, name="by_pe", tag="by_pe", bufs=1)
+            first, count = columns[k] - relief[k], relief[k] + edge_width[k]
+            banks = []
             for a in range(0, count, P):
                 b = min(a + P, count)
+                if a % (2 * P) == 0:
+                    tag, bufs = ("kz", 4) if a else ("by_pe", 1)
+                    banks.append(psum.tile([P, 4 * min(2 * P, count - a)], BF16, name=tag, tag=tag, bufs=bufs))
+                into = a % (2 * P)
                 nc.tensor.matmul(
-                    by_pe[:, 4 * a : 4 * b].rearrange("p (l t) -> p l t", t=4),
+                    banks[-1][:, 4 * into : 4 * (into + b - a)].rearrange("p (l t) -> p l t", t=4),
                     lhsT=ident_bf[:],
                     rhs=planes[k][:, :, first + a : first + b].rearrange("p t l -> p l t"),
                     start=True,
                     stop=True,
                 )
-            return by_pe
+            return banks
 
-        def by_pe_out(k, by_pe):
+        def by_pe_out(k, banks):
             count = relief[k] + edge_width[k]
-            nc.scalar.copy(out=il_v[k][:, 0 : 4 * count].bitcast(F32), in_=by_pe[:].bitcast(F32))
+            for i, bank in enumerate(banks):
+                a, b = 2 * P * i, min(2 * P * (i + 1), count)
+                nc.scalar.copy(out=il_v[k][:, 4 * a : 4 * b].bitcast(F32), in_=bank[:].bitcast(F32))
 
         def interleave_on_gpsimd(k):
-            count = width(plane_pieces[k]) - relief[k]
+            count = columns[k] - relief[k]
             il_g[k] = work.tile([P, 4 * W], BF16, name="il_g", tag="il_g", bufs=1, align_bytes=64)
             nc.gpsimd.tensor_scalar(
                 out=il_g[k][:, 0 : 4 * count].rearrange("p (c i t) -> p c t i", i=4, t=4),
@@ -176,9 +179,9 @@ def tile_josephkalmanupdate_w_kernel(tc, s, z_bytes, z_scale, kgain, g, d, r, ou
         def kz_passes(k):
             z_codes, z_scales = codes[k]
             complete = []
-            for first, (c, gp, lo, hi) in ((0, plane_pieces[k]), (width(plane_pieces[k]), cast_pieces[k])):
-                for col in range(0, hi - lo, BLK):
-                    h = (W * c + lo + col) // BLK
+            col = 0
+            for c, gp, lo, hi in odd[k] + casts[k]:
+                for h in range((W * c + lo) // BLK, (W * c + hi) // BLK):
                     if h not in kz:
                         kz[h] = psum.tile([P, BLK], F32, name="kz", tag="kz", bufs=4)
                     done = passes_done.get(h, 0)
@@ -187,11 +190,12 @@ def tile_josephkalmanupdate_w_kernel(tc, s, z_bytes, z_scale, kgain, g, d, r, ou
                         out=kz[h][:],
                         lhsT=k_codes[:, gp, :].bitcast(FP8X4),
                         lhsT_scale=k_scales[:, gp, :],
-                        rhs=z_codes[:, first + col : first + col + BLK].bitcast(FP8X4),
-                        rhs_scale=z_scales[:, first + col : first + col + BLK],
+                        rhs=z_codes[:, col : col + BLK].bitcast(FP8X4),
+                        rhs_scale=z_scales[:, col : col + BLK],
                         start=(done == 0),
                         stop=(done == PASSES - 1),
                     )
+                    col += BLK
                     if done == PASSES - 1:
                         complete.append(h)
             return complete
@@ -201,6 +205,15 @@ def tile_josephkalmanupdate_w_kernel(tc, s, z_bytes, z_scale, kgain, g, d, r, ou
             src = kz[h][:].rearrange("n (p t) -> n t p", t=4)
             for a, b in parts:
                 nc.scalar.activation(out=neg_kz[h][:, a:b, :], in_=src[:, a:b, :], func=COPY, scale=-1.0)
+
+        def empty_block():
+            h = complete.pop(0)
+            kz_out(h)
+            if h < BLOCKS - 2:
+                to_turn.append(h)
+            else:
+                s_turn(h, "kz", 4)
+                kz_turn(h)
 
         def s_turn(h, tag, bufs):
             turned[h] = psum.tile([P, N, 4], F32, name=tag, tag=tag, bufs=bufs)
@@ -322,29 +335,29 @@ def tile_josephkalmanupdate_w_kernel(tc, s, z_bytes, z_scale, kgain, g, d, r, ou
             make_identity(nc, ident[:])
             nc.gpsimd.tensor_copy(out=ident_bf[:], in_=ident[:])
 
-            load(plane_pieces[0], rows=slice(0, 1))
-            load(first_halves[0])
-            load(plane_pieces[0], rows=slice(1, 3))
-            load(first_halves[1])
-            load(plane_pieces[0], rows=slice(3, 4))
+            load(odd[0][0], rows=slice(0, 1))
+            load(bodies[0][0])
+            load(odd[0][0], rows=slice(1, 3))
+            load(bodies[0][1])
+            load(odd[0][0], rows=slice(3, 4))
             load(edges[1], "zb_edge", 4)
-            load(plane_pieces[1], rows=slice(0, 2))
-            load(plane_pieces[1], rows=slice(2, 4))
+            load(odd[1][0], rows=slice(0, 2))
+            load(odd[1][0], rows=slice(2, 4))
             load_kgain(0)
-            load(bodies[1])
+            load(bodies[1][0])
             load_step(2)
             load_kgain(1)
 
             step_tiles(0)
             widen_row_on_vector(0)
             scales_to_psum()
-            cast(first_halves[0])
+            cast(bodies[0][0])
             scales_turn()
-            cast(first_halves[1])
+            cast(bodies[0][1])
             for t in range(1, 4):
                 widen_row_on_vector(t)
 
-            complete, to_turn, products, j_due = [], [], [], None
+            complete, to_turn, products, j_due, kr_done = [], [], [], [], 0
             for k in range(steps):
                 if k + 3 < steps:
                     load_step(k + 3)
@@ -359,71 +372,79 @@ def tile_josephkalmanupdate_w_kernel(tc, s, z_bytes, z_scale, kgain, g, d, r, ou
                 if k < K_QUARTERS:
                     k_bank = k_turn(k)
 
+                if len(casts[k]) > 1:
+                    empty_block()
                 if k + 1 < steps:
                     step_tiles(k + 1)
-                    widen(k + 1, edges[k + 1], width(plane_pieces[k + 1]))
+                    widen(k + 1, edges[k + 1], columns[k + 1])
                 if relief[k]:
                     by_pe_out(k, by_pe)
                 if k + 1 < steps and not relief[k + 1]:
                     by_pe = interleave_on_pe(k + 1)
                 if k >= 1:
-                    complete = complete + kz_passes(k - 1)
+                    complete.extend(kz_passes(k - 1))
                 if k + 1 < steps:
-                    widen(k + 1, plane_pieces[k + 1], 0)
-                    if relief[k + 1]:
-                        by_pe = interleave_on_pe(k + 1)
-                    else:
+                    for i, u in enumerate(odd[k + 1]):
+                        widen(k + 1, u, i * width(u))
+                    if not relief[k + 1]:
                         by_pe_out(k + 1, by_pe)
-                    cast(bodies[k + 1])
+                    elif len(casts[k]) == 1:
+                        by_pe = interleave_on_pe(k + 1)
+                    for u in bodies[k + 1]:
+                        cast(u)
                 else:
-                    s_turn(BLOCKS - 1, "kz", 4)
+                    s_turn(BLOCKS - 1, "turned", 1)
                     gain_products_on_scalar(BLOCKS - 2)
-                if complete and k % 2 == 0:
-                    h = complete.pop(0)
-                    kz_out(h)
-                    to_turn.append(h)
+                if complete and len(products) < 2 and not to_turn:
+                    empty_block()
 
-                for part in first_halves if k == 0 else [bodies[k]]:
-                    scale_interleave(k, part)
-                j_now, j_due = j_due, None
-                if k < K_QUARTERS:
-                    k_out(k, k_bank)
-                elif products:
-                    h, i = products.pop(0)
-                    gain_product(h, i)
-                    if i == 1:
-                        j_due = h
-                else:
-                    kr_done = 0 if k == K_QUARTERS else 2
-                    kr_product(kr_done, kr_done + 2)
+                col = relief[k] + edge_width[k]
+                for part in bodies[k]:
+                    j_now, j_due = j_now + j_due if part != bodies[k][0] else j_due, []
+                    scale_interleave(k, part, col)
+                    col += width(part)
+                    if part == bodies[0][0]:
+                        continue
+                    if k < K_QUARTERS:
+                        k_out(k, k_bank)
+                    elif products:
+                        h, i = products.pop(0)
+                        gain_product(h, i)
+                        j_due = [h] * i
+                    else:
+                        kr_product(kr_done, kr_done + 2)
+                        kr_done += 2
+                    if to_turn and not products:
+                        h = to_turn.pop(0)
+                        s_turn(h, "turned", 1)
+                        kz_turn(h)
+                        products.extend([(h, 0), (h, 1)])
+                if len(casts[k]) > 1:
+                    by_pe = interleave_on_pe(k + 1)
                 if k == K_QUARTERS - 1:
                     nc.tensor.matmul(
                         factors[:, P:].bitcast(BF16), lhsT=ident_bf[:], rhs=r_sb[:].rearrange("p g t -> p (g t)"), start=True, stop=True
                     )
-                if to_turn and not products:
-                    h = to_turn.pop(0)
-                    s_turn(h, "turned", 1)
-                    kz_turn(h)
-                    products = [(h, 0), (h, 1)] if h < BLOCKS - 2 else []
-                if j_now is not None:
-                    j_pass(j_now)
+                for h in j_now:
+                    j_pass(h)
                 code_tiles(k)
-                by_g = width(plane_pieces[k]) - relief[k]
-                cut = relief[k] or width(cast_pieces[k]) // 2
-                quantise(k, il_v[k], by_g, 0, cut)
+                by_g = columns[k] - relief[k]
+                cut = relief[k] or (0 if j_now else columns[k] // 2)
+                if cut:
+                    quantise(k, il_v[k], by_g, 0, cut)
                 if k < K_QUARTERS:
                     quantise_k(k_il, k_codes, k_scales, 2 * k, 2 * k + 2)
                 if k == K_QUARTERS:
                     nc.vector.tensor_tensor(out=gd_f32[:], in0=g_sb[:], in1=d_sb[:], op=MULT)
                     nc.vector.tensor_copy(out=g_f32[:], in_=g_sb[:])
-                for a, b in ((0, by_g - relief[k]), (by_g - relief[k], by_g)) if relief[k] else ((0, by_g),):
+                for a, b in ((0, 2 * P), (2 * P, by_g)) if relief[k] else ((0, by_g),):
                     quantise(k, il_g[k], 0, a, b)
-                quantise(k, il_v[k], by_g, cut, relief[k] + width(cast_pieces[k]))
+                quantise(k, il_v[k], by_g, cut, relief[k] + columns[k])
 
             kz_passes(steps - 1)
             kz_out(BLOCKS - 1, ((0, 2), (2, 4)))
             kz_turn(BLOCKS - 1)
-            kr_product(4, PASSES)
+            kr_product(kr_done, PASSES)
             j_pass(BLOCKS - 2)
             quantise_k(kr_il, kr_codes, kr_scales, 0, PASSES)
             q_passes()

@@ -24,7 +24,8 @@ BLOCKS = L // BLK
 W = 2 * BLK
 CHUNKS = L // W
 EDGE = 96
-DOUBLE_EDGE = 256
+EDGE_BESIDE_KZ = 64
+DOUBLE_EDGE = 224
 LATE_EDGE = 192
 RELIEF = P
 K_QUARTERS = PASSES // 2
@@ -66,7 +67,7 @@ def tile_josephkalmanupdate_w_kernel(tc, s, z_bytes, z_scale, kgain, g, d, r, ou
         odd = [[(c, gp + 1, lo, hi) for c, gp, lo, hi in pieces] for pieces in casts]
         steps = len(casts)
         columns = [sum(hi - lo for c, gp, lo, hi in pieces) for pieces in casts]
-        edge_width = [0] + [LATE_EDGE if columns[k] < W else EDGE if len(casts[k]) == 1 else DOUBLE_EDGE for k in range(1, steps)]
+        edge_width = [0] + [LATE_EDGE if columns[k] < W else DOUBLE_EDGE if len(casts[k]) > 1 else EDGE if k <= K_QUARTERS else EDGE_BESIDE_KZ for k in range(1, steps)]
         relief = [RELIEF if columns[k] < W else 0 for k in range(steps)]
         edges = [pieces[0][:3] + (pieces[0][2] + x,) for pieces, x in zip(casts, edge_width)]
         bodies = [[u[:2] + (u[3], pieces[0][3])] + pieces[1:] for u, pieces in zip(edges, casts)]
@@ -445,9 +446,10 @@ def tile_josephkalmanupdate_w_kernel(tc, s, z_bytes, z_scale, kgain, g, d, r, ou
             kz_out(BLOCKS - 1, ((0, 2), (2, 4)))
             kz_turn(BLOCKS - 1)
             kr_product(kr_done, PASSES)
-            j_pass(BLOCKS - 2)
-            quantise_k(kr_il, kr_codes, kr_scales, 0, PASSES)
+            quantise_k(kr_il, kr_codes, kr_scales, 0, kr_done)
+            quantise_k(kr_il, kr_codes, kr_scales, kr_done, PASSES)
             q_passes()
+            j_pass(BLOCKS - 2)
             for i in range(2):
                 gain_product(BLOCKS - 1, i)
             j_pass(BLOCKS - 1, ((0, 1), (1, 2)))

@@ -107,9 +107,9 @@ def tile_josephkalmanupdate_w_kernel(tc, s, z_bytes, z_scale, kgain, g, d, r, ou
 
         def scale_interleave(k, part, a):
             nc.vector.tensor_tensor(
-                out=il_v[k][:, 4 * a : 4 * (a + width(part))].rearrange("p (c i t) -> p c t i", i=4, t=4),
-                in0=raw[part][:].rearrange("p t (c i) -> p c t i", i=4),
-                in1=zs_psum[:, part[1]].unsqueeze(1).to_broadcast([P, width(part) // 4, 4, 4]),
+                out=il_v[k][:, 4 * a : 4 * (a + width(part))].rearrange("p (c i t) -> p c t i", i=8, t=4),
+                in0=raw[part][:].rearrange("p t (c i) -> p c t i", i=8),
+                in1=zs_psum[:, part[1], :, 0:1].unsqueeze(1).to_broadcast([P, width(part) // 8, 4, 8]),
                 op=MULT,
             )
 

@@ -156,8 +156,8 @@ def tile_josephkalmanupdate_w_kernel(tc, s, z_bytes, z_scale, kgain, g, d, r, ou
             count = columns[k] - relief[k]
             il_g[k] = work.tile([P, 4 * W], BF16, name="il_g", tag="il_g", bufs=1, align_bytes=64)
             nc.gpsimd.tensor_scalar(
-                out=il_g[k][:, 0 : 4 * count].rearrange("p (c i t) -> p c t i", i=4, t=4),
-                in0=planes[k][:, :, 0:count].rearrange("p t (c i) -> p c t i", i=4),
+                out=il_g[k][:, 0 : 4 * count].rearrange("p (c i t) -> p c t i", i=8, t=4),
+                in0=planes[k][:, :, 0:count].rearrange("p t (c i) -> p c t i", i=8),
                 scalar1=1.0,
                 scalar2=0.0,
                 op0=MULT,
@@ -202,7 +202,12 @@ def tile_josephkalmanupdate_w_kernel(tc, s, z_bytes, z_scale, kgain, g, d, r, ou
             return complete
 
         def kz_out(h, parts=((0, 4),)):
-            neg_kz[h] = work.tile([P, 4, P], F32, name="neg_kz", tag="neg_kz", bufs=2)
+            tile = work.tile([P, BLK], F32, name="neg_kz", tag="neg_kz", bufs=2)
+            if h < BLOCKS - 3:
+                neg_kz[h] = tile[:].rearrange("n (p t) -> n t p", t=4)
+                nc.scalar.activation(out=tile[:], in_=kz[h][:], func=COPY, scale=-1.0)
+                return
+            neg_kz[h] = tile[:].rearrange("n (t p) -> n t p", t=4)
             src = kz[h][:].rearrange("n (p t) -> n t p", t=4)
             for a, b in parts:
                 nc.scalar.activation(out=neg_kz[h][:, a:b, :], in_=src[:, a:b, :], func=COPY, scale=-1.0)

@@ -26,7 +26,7 @@ CHUNKS = L // W
 EDGE = 96
 EDGE_BESIDE_KZ = 64
 DOUBLE_EDGE = 224
-LATE_EDGE = 192
+LATE_EDGE = 224
 RELIEF = P
 K_QUARTERS = PASSES // 2
 
@@ -74,7 +74,7 @@ def tile_josephkalmanupdate_w_kernel(tc, s, z_bytes, z_scale, kgain, g, d, r, ou
         bodies[0] = [(0, 0, lo, lo + BLK) for lo in (0, BLK)]
 
         zb, raw, planes, il_v, il_g, codes, kz, neg_kz, turned, w_wd = {}, {}, {}, {}, {}, {}, {}, {}, {}, {}
-        passes_done = {}
+        passes_done, spare = {}, []
 
         def width(u):
             return u[3] - u[2]
@@ -96,14 +96,14 @@ def tile_josephkalmanupdate_w_kernel(tc, s, z_bytes, z_scale, kgain, g, d, r, ou
             nc.sync.dma_start(out=k_rows[:, cols], in_=kgain[:, cols])
 
         def cast(u):
-            raw[u] = work.tile([P, 4, width(u)], BF16, name="raw", tag="raw", bufs=3, align_bytes=64)
+            raw[u] = work.tile([P, 4, width(u)], BF16, name="raw", tag="raw", bufs=3, align_bytes=256)
             nc.scalar.copy(
                 out=raw[u][:].rearrange("p t l -> p (t l)"), in_=zb[u][:].rearrange("p t l -> p (t l)").bitcast(F8)
             )
 
         def step_tiles(k):
-            planes[k] = work.tile([P, 4, W + DOUBLE_EDGE], BF16, name="planes", tag="planes", bufs=4, align_bytes=64)
-            il_v[k] = work.tile([P, 4 * W], BF16, name="il_v", tag="il_v", bufs=3, align_bytes=64)
+            planes[k] = work.tile([P, 4, W + DOUBLE_EDGE], BF16, name="planes", tag="planes", bufs=4, align_bytes=256)
+            il_v[k] = work.tile([P, 4 * W], BF16, name="il_v", tag="il_v", bufs=3, align_bytes=256)
 
         def scale_interleave(k, part, a):
             nc.vector.tensor_tensor(
@@ -133,9 +133,12 @@ def tile_josephkalmanupdate_w_kernel(tc, s, z_bytes, z_scale, kgain, g, d, r, ou
             banks = []
             for a in range(0, count, P):
                 b = min(a + P, count)
-                if a % (2 * P) == 0:
-                    tag, bufs = ("kz", 4) if a else ("by_pe", 1)
-                    banks.append(psum.tile([P, 4 * min(2 * P, count - a)], BF16, name=tag, tag=tag, bufs=bufs))
+                if a == 0:
+                    banks.append(psum.tile([P, 4 * min(2 * P, count)], BF16, name="by_pe", tag="by_pe", bufs=1))
+                elif a == 2 * P:
+                    if not spare:
+                        spare.append(psum.tile([P, 4 * (count - a)], BF16, name="kz", tag="kz", bufs=4))
+                    banks.append(spare[0])
                 into = a % (2 * P)
                 nc.tensor.matmul(
                     banks[-1][:, 4 * into : 4 * (into + b - a)].rearrange("p (l t) -> p l t", t=4),
@@ -154,7 +157,7 @@ def tile_josephkalmanupdate_w_kernel(tc, s, z_bytes, z_scale, kgain, g, d, r, ou
 
         def interleave_on_gpsimd(k):
             count = columns[k] - relief[k]
-            il_g[k] = work.tile([P, 4 * W], BF16, name="il_g", tag="il_g", bufs=1, align_bytes=64)
+            il_g[k] = work.tile([P, 4 * W], BF16, name="il_g", tag="il_g", bufs=1, align_bytes=256)
             nc.gpsimd.tensor_scalar(
                 out=il_g[k][:, 0 : 4 * count].rearrange("p (c i t) -> p c t i", i=8, t=4),
                 in0=planes[k][:, :, 0:count].rearrange("p t (c i) -> p c t i", i=8),
@@ -165,8 +168,8 @@ def tile_josephkalmanupdate_w_kernel(tc, s, z_bytes, z_scale, kgain, g, d, r, ou
             )
 
         def code_tiles(k):
-            z_codes = work.tile([P, 2 * W], U32, name="z_codes", tag="z_codes", bufs=3, align_bytes=64)
-            z_scales = work.tile([P, 2 * W], U8, name="z_scales", tag="z_scales", bufs=3, align_bytes=64)
+            z_codes = work.tile([P, 2 * W], U32, name="z_codes", tag="z_codes", bufs=3, align_bytes=256)
+            z_scales = work.tile([P, 2 * W], U8, name="z_scales", tag="z_scales", bufs=3, align_bytes=256)
             codes[k] = (z_codes, z_scales)
 
         def quantise(k, src, first, a, b):
@@ -218,11 +221,12 @@ def tile_josephkalmanupdate_w_kernel(tc, s, z_bytes, z_scale, kgain, g, d, r, ou
             if h < BLOCKS - 2:
                 to_turn.append(h)
             else:
-                s_turn(h, "kz", 4)
                 kz_turn(h)
 
         def s_turn(h, tag, bufs):
-            turned[h] = psum.tile([P, N, 4], F32, name=tag, tag=tag, bufs=bufs)
+            bank = psum.tile([P, 4 * N], F32, name=tag, tag=tag, bufs=bufs)
+            order = "p (t n) -> p n t" if h == BLOCKS - 2 else "p (n t) -> p n t"
+            turned[h] = bank[:].rearrange(order, t=4)
             for t in range(4):
                 nc.tensor.matmul(
                     turned[h][:, :, t],
@@ -243,7 +247,7 @@ def tile_josephkalmanupdate_w_kernel(tc, s, z_bytes, z_scale, kgain, g, d, r, ou
                 w_wd[h] = work.tile([P, 2, BLK], BF16, name="w_wd", tag="w_wd", bufs=3, align_bytes=64)
             nc.vector.tensor_tensor(
                 out=w_wd[h][:, i, :].rearrange("p (n t) -> p n t", t=4),
-                in0=turned[h][:],
+                in0=turned[h],
                 in1=(g_sb, gd_f32)[i][:, h, :].unsqueeze(1).to_broadcast([P, N, 4]),
                 op=MULT,
             )
@@ -427,6 +431,7 @@ def tile_josephkalmanupdate_w_kernel(tc, s, z_bytes, z_scale, kgain, g, d, r, ou
                         products.extend([(h, 0), (h, 1)])
                 if len(casts[k]) > 1:
                     by_pe = interleave_on_pe(k + 1)
+                    s_turn(BLOCKS - 2, "kz", 4)
                 if k == K_QUARTERS - 1:
                     nc.tensor.matmul(
                         factors[:, P:].bitcast(BF16), lhsT=ident_bf[:], rhs=r_sb[:].rearrange("p g t -> p (g t)"), start=True, stop=True

@@ -28,6 +28,8 @@ EDGE_BESIDE_KZ = 64
 DOUBLE_EDGE = 224
 LATE_EDGE = 224
 RELIEF = P
+RUN = 8
+AHEAD = 3
 K_QUARTERS = PASSES // 2
 
 
@@ -40,14 +42,14 @@ def tile_josephkalmanupdate_w_kernel(tc, s, z_bytes, z_scale, kgain, g, d, r, ou
 
         ident = keep.tile([P, P], F32, name="ident")
         ident_bf = keep.tile([P, P], BF16, name="ident_bf")
-        zs = keep.tile([P, PASSES, 4], F32, name="zs")
-        zs_four = keep.tile([P, 4 * PASSES, 4], F32, name="zs_four")
+        zs = keep.tile([P, PASSES, 8], F32, name="zs")[:, :, 0:4]
+        zs_four = keep.tile([P, PASSES, 4, 4], F32, name="zs_four")
         zs_turned = keep.tile([P, P], F32, name="zs_turned")
         r_sb = keep.tile([P, PASSES, 4], BF16, name="r_sb")
         g_sb = keep.tile([P, BLOCKS, 4], BF16, name="g_sb")
         d_sb = keep.tile([P, BLOCKS, 4], BF16, name="d_sb")
         gd_f32 = keep.tile([P, BLOCKS, 4], F32, name="gd_f32")
-        g_f32 = keep.tile([P, BLOCKS, 4], F32, name="g_f32")
+        g_f32 = keep.tile([P, 4], F32, name="g_f32")
         k_rows = keep.tile([P, M], BF16, name="k_rows")
         k_il = keep.tile([P, PASSES, 4 * N], BF16, name="k_il", align_bytes=64)
         kr_il = keep.tile([P, PASSES, 4 * N], BF16, name="kr_il", align_bytes=64)
@@ -67,8 +69,17 @@ def tile_josephkalmanupdate_w_kernel(tc, s, z_bytes, z_scale, kgain, g, d, r, ou
         odd = [[(c, gp + 1, lo, hi) for c, gp, lo, hi in pieces] for pieces in casts]
         steps = len(casts)
         columns = [sum(hi - lo for c, gp, lo, hi in pieces) for pieces in casts]
-        edge_width = [0] + [LATE_EDGE if columns[k] < W else DOUBLE_EDGE if len(casts[k]) > 1 else EDGE if k <= K_QUARTERS else EDGE_BESIDE_KZ for k in range(1, steps)]
-        relief = [RELIEF if columns[k] < W else 0 for k in range(steps)]
+        double_step = steps - 3
+
+        def edge_of(k):
+            if k == 0:
+                return 0
+            if k >= double_step:
+                return DOUBLE_EDGE if k == double_step else LATE_EDGE
+            return EDGE if k <= K_QUARTERS or casts[k][0][1] == 0 else EDGE_BESIDE_KZ
+
+        edge_width = [edge_of(k) for k in range(steps)]
+        relief = [RELIEF if k > double_step else 0 for k in range(steps)]
         edges = [pieces[0][:3] + (pieces[0][2] + x,) for pieces, x in zip(casts, edge_width)]
         bodies = [[u[:2] + (u[3], pieces[0][3])] + pieces[1:] for u, pieces in zip(edges, casts)]
         bodies[0] = [(0, 0, lo, lo + BLK) for lo in (0, BLK)]
@@ -107,9 +118,9 @@ def tile_josephkalmanupdate_w_kernel(tc, s, z_bytes, z_scale, kgain, g, d, r, ou
 
         def scale_interleave(k, part, a):
             nc.vector.tensor_tensor(
-                out=il_v[k][:, 4 * a : 4 * (a + width(part))].rearrange("p (c i t) -> p c t i", i=8, t=4),
-                in0=raw[part][:].rearrange("p t (c i) -> p c t i", i=8),
-                in1=zs_psum[:, part[1], :, 0:1].unsqueeze(1).to_broadcast([P, width(part) // 8, 4, 8]),
+                out=il_v[k][:, 4 * a : 4 * (a + width(part))].rearrange("p (c i t) -> p c t i", i=RUN, t=4),
+                in0=raw[part][:].rearrange("p t (c i) -> p c t i", i=RUN),
+                in1=zs_psum[:, part[1], :, 0:1].unsqueeze(1).to_broadcast([P, width(part) // RUN, 4, RUN]),
                 op=MULT,
             )
 
@@ -125,7 +136,11 @@ def tile_josephkalmanupdate_w_kernel(tc, s, z_bytes, z_scale, kgain, g, d, r, ou
         def widen_row_on_vector(t):
             u = odd[0][0]
             nc.vector.tensor_scalar(
-                out=planes[0][:, t, 0:W], in0=zb[u][:, t, :].bitcast(F8), scalar1=zs[:, u[1], t : t + 1], scalar2=None, op0=MULT
+                out=planes[0][:, t, 0:W],
+                in0=zb[u][:, t, :].bitcast(F8),
+                scalar1=zs[:, u[1], t : t + 1],
+                scalar2=None,
+                op0=MULT,
             )
 
         def interleave_on_pe(k):
@@ -159,8 +174,8 @@ def tile_josephkalmanupdate_w_kernel(tc, s, z_bytes, z_scale, kgain, g, d, r, ou
             count = columns[k] - relief[k]
             il_g[k] = work.tile([P, 4 * W], BF16, name="il_g", tag="il_g", bufs=1, align_bytes=256)
             nc.gpsimd.tensor_scalar(
-                out=il_g[k][:, 0 : 4 * count].rearrange("p (c i t) -> p c t i", i=8, t=4),
-                in0=planes[k][:, :, 0:count].rearrange("p t (c i) -> p c t i", i=8),
+                out=il_g[k][:, 0 : 4 * count].rearrange("p (c i t) -> p c t i", i=RUN, t=4),
+                in0=planes[k][:, :, 0:count].rearrange("p t (c i) -> p c t i", i=RUN),
                 scalar1=1.0,
                 scalar2=0.0,
                 op0=MULT,
@@ -239,7 +254,12 @@ def tile_josephkalmanupdate_w_kernel(tc, s, z_bytes, z_scale, kgain, g, d, r, ou
         def kz_turn(h):
             for t in range(4):
                 nc.tensor.matmul(
-                    turned[h][:, :, t], lhsT=neg_kz[h][:, t, :], rhs=ident[:], is_transpose=True, start=False, stop=(t == 3)
+                    turned[h][:, :, t],
+                    lhsT=neg_kz[h][:, t, :],
+                    rhs=ident[:],
+                    is_transpose=True,
+                    start=False,
+                    stop=(t == 3),
                 )
 
         def gain_product(h, i):
@@ -255,10 +275,10 @@ def tile_josephkalmanupdate_w_kernel(tc, s, z_bytes, z_scale, kgain, g, d, r, ou
         def gain_products_on_scalar(h):
             w_wd[h] = work.tile([P, 2, BLK], BF16, name="w_wd", tag="w_wd", bufs=3, align_bytes=64)
             by_t = work.tile([P, 2, 4, N], BF16, name="by_t", tag="by_t", bufs=1)
-            for i, gain in enumerate((g_f32, gd_f32)):
+            for i, gain in enumerate((g_f32[:], gd_f32[:, h, :])):
                 for t in range(4):
                     nc.scalar.activation(
-                        out=by_t[:, i, t, :], in_=turned[h][:, :, t], func=COPY, scale=gain[:, h, t : t + 1]
+                        out=by_t[:, i, t, :], in_=turned[h][:, :, t], func=COPY, scale=gain[:, t : t + 1]
                     )
             for i in range(2):
                 nc.scalar.copy(
@@ -327,16 +347,25 @@ def tile_josephkalmanupdate_w_kernel(tc, s, z_bytes, z_scale, kgain, g, d, r, ou
                     stop=False,
                 )
 
-        def scales_to_psum():
+        def scales_four_times():
             nc.vector.tensor_copy(
-                out=zs_four[:], in_=zs[:].rearrange("p g t -> p (g t)").unsqueeze(2).to_broadcast([P, 4 * PASSES, 4])
+                out=zs_four[:], in_=zs.unsqueeze(3).to_broadcast([P, PASSES, 4, 4])
             )
 
-        def scales_turn():
+        def scales_to_psum():
             once = psum.tile([P, P], F32, name="by_pe", tag="by_pe", bufs=1)
-            nc.tensor.transpose(once[:], zs_four[:].rearrange("p x i -> p (x i)"), ident[:])
+            nc.tensor.transpose(once[:], zs_four[:].rearrange("p g t i -> p (g t i)"), ident[:])
             nc.scalar.copy(out=zs_turned[:], in_=once[:])
             nc.tensor.transpose(factors[:, 0:P], zs_turned[:], ident[:])
+
+        def r_to_psum():
+            nc.tensor.matmul(
+                factors[:, P:].bitcast(BF16),
+                lhsT=ident_bf[:],
+                rhs=r_sb[:].rearrange("p g t -> p (g t)"),
+                start=True,
+                stop=True,
+            )
 
         with tc.manual_schedule():
             zs_hbm = z_scale.rearrange("(g p t) o -> p g (t o)", p=P, t=4)
@@ -360,17 +389,17 @@ def tile_josephkalmanupdate_w_kernel(tc, s, z_bytes, z_scale, kgain, g, d, r, ou
 
             step_tiles(0)
             widen_row_on_vector(0)
-            scales_to_psum()
+            scales_four_times()
             cast(bodies[0][0])
-            scales_turn()
+            scales_to_psum()
             cast(bodies[0][1])
             for t in range(1, 4):
                 widen_row_on_vector(t)
 
             complete, to_turn, products, j_due, kr_done = [], [], [], [], 0
             for k in range(steps):
-                if k + 3 < steps:
-                    load_step(k + 3)
+                if k + AHEAD < steps:
+                    load_step(k + AHEAD)
                 if k + 2 < K_QUARTERS:
                     load_kgain(k + 2)
                 if k == 1:
@@ -382,8 +411,9 @@ def tile_josephkalmanupdate_w_kernel(tc, s, z_bytes, z_scale, kgain, g, d, r, ou
                 if k < K_QUARTERS:
                     k_bank = k_turn(k)
 
-                if len(casts[k]) > 1:
+                if k == double_step:
                     empty_block()
+                    nc.scalar.copy(out=g_f32[:], in_=g_sb[:, BLOCKS - 2, :])
                 if k + 1 < steps:
                     step_tiles(k + 1)
                     widen(k + 1, edges[k + 1], columns[k + 1])
@@ -398,7 +428,7 @@ def tile_josephkalmanupdate_w_kernel(tc, s, z_bytes, z_scale, kgain, g, d, r, ou
                         widen(k + 1, u, i * width(u))
                     if not relief[k + 1]:
                         by_pe_out(k + 1, by_pe)
-                    elif len(casts[k]) == 1:
+                    elif k != double_step:
                         by_pe = interleave_on_pe(k + 1)
                     for u in bodies[k + 1]:
                         cast(u)
@@ -408,9 +438,9 @@ def tile_josephkalmanupdate_w_kernel(tc, s, z_bytes, z_scale, kgain, g, d, r, ou
                 if complete and len(products) < 2 and not to_turn:
                     empty_block()
 
-                col = relief[k] + edge_width[k]
+                col, j_now = relief[k] + edge_width[k], []
                 for part in bodies[k]:
-                    j_now, j_due = j_now + j_due if part != bodies[k][0] else j_due, []
+                    j_now, j_due = j_now + j_due, []
                     scale_interleave(k, part, col)
                     col += width(part)
                     if part == bodies[0][0]:
@@ -420,7 +450,7 @@ def tile_josephkalmanupdate_w_kernel(tc, s, z_bytes, z_scale, kgain, g, d, r, ou
                     elif products:
                         h, i = products.pop(0)
                         gain_product(h, i)
-                        j_due = [h] * i
+                        j_due = [h] if i == 1 else []
                     else:
                         kr_product(kr_done, kr_done + 2)
                         kr_done += 2
@@ -429,13 +459,11 @@ def tile_josephkalmanupdate_w_kernel(tc, s, z_bytes, z_scale, kgain, g, d, r, ou
                         s_turn(h, "turned", 1)
                         kz_turn(h)
                         products.extend([(h, 0), (h, 1)])
-                if len(casts[k]) > 1:
+                if k == double_step:
                     by_pe = interleave_on_pe(k + 1)
                     s_turn(BLOCKS - 2, "kz", 4)
                 if k == K_QUARTERS - 1:
-                    nc.tensor.matmul(
-                        factors[:, P:].bitcast(BF16), lhsT=ident_bf[:], rhs=r_sb[:].rearrange("p g t -> p (g t)"), start=True, stop=True
-                    )
+                    r_to_psum()
                 for h in j_now:
                     j_pass(h)
                 code_tiles(k)
@@ -447,7 +475,6 @@ def tile_josephkalmanupdate_w_kernel(tc, s, z_bytes, z_scale, kgain, g, d, r, ou
                     quantise_k(k_il, k_codes, k_scales, 2 * k, 2 * k + 2)
                 if k == K_QUARTERS:
                     nc.vector.tensor_tensor(out=gd_f32[:], in0=g_sb[:], in1=d_sb[:], op=MULT)
-                    nc.vector.tensor_copy(out=g_f32[:], in_=g_sb[:])
                 for a, b in ((0, 2 * P), (2 * P, by_g)) if relief[k] else ((0, by_g),):
                     quantise(k, il_g[k], 0, a, b)
                 quantise(k, il_v[k], by_g, cut, relief[k] + columns[k])

@@ -29,6 +29,8 @@ DOUBLE_EDGE = 224
 LATE_EDGE = 224
 RELIEF = P
 RUN = 8
+HEAD_ROWS = 1
+ON_SCALAR = BLOCKS - 3
 AHEAD = 3
 K_QUARTERS = PASSES // 2
 
@@ -76,13 +78,12 @@ def tile_josephkalmanupdate_w_kernel(tc, s, z_bytes, z_scale, kgain, g, d, r, ou
                 return 0
             if k >= double_step:
                 return DOUBLE_EDGE if k == double_step else LATE_EDGE
-            return EDGE if k <= K_QUARTERS or casts[k][0][1] == 0 else EDGE_BESIDE_KZ
+            return EDGE if k <= K_QUARTERS + 1 else EDGE_BESIDE_KZ
 
         edge_width = [edge_of(k) for k in range(steps)]
         relief = [RELIEF if k > double_step else 0 for k in range(steps)]
         edges = [pieces[0][:3] + (pieces[0][2] + x,) for pieces, x in zip(casts, edge_width)]
         bodies = [[u[:2] + (u[3], pieces[0][3])] + pieces[1:] for u, pieces in zip(edges, casts)]
-        bodies[0] = [(0, 0, lo, lo + BLK) for lo in (0, BLK)]
 
         zb, raw, planes, il_v, il_g, codes, kz, neg_kz, turned, w_wd = {}, {}, {}, {}, {}, {}, {}, {}, {}, {}
         passes_done, spare = {}, []
@@ -106,26 +107,28 @@ def tile_josephkalmanupdate_w_kernel(tc, s, z_bytes, z_scale, kgain, g, d, r, ou
             cols = slice(2 * K_PASS * q, 2 * K_PASS * (q + 1))
             nc.sync.dma_start(out=k_rows[:, cols], in_=kgain[:, cols])
 
-        def cast(u):
-            raw[u] = work.tile([P, 4, width(u)], BF16, name="raw", tag="raw", bufs=3, align_bytes=256)
+        def cast(u, rows=slice(0, 4)):
+            if rows.start == 0:
+                raw[u] = work.tile([P, 4, width(u)], BF16, name="raw", tag="raw", bufs=3, align_bytes=256)
             nc.scalar.copy(
-                out=raw[u][:].rearrange("p t l -> p (t l)"), in_=zb[u][:].rearrange("p t l -> p (t l)").bitcast(F8)
+                out=raw[u][:, rows, :].rearrange("p t l -> p (t l)"),
+                in_=zb[u][:, rows, :].rearrange("p t l -> p (t l)").bitcast(F8),
             )
 
         def step_tiles(k):
             planes[k] = work.tile([P, 4, W + DOUBLE_EDGE], BF16, name="planes", tag="planes", bufs=4, align_bytes=256)
-            il_v[k] = work.tile([P, 4 * W], BF16, name="il_v", tag="il_v", bufs=3, align_bytes=256)
+            il_v[k] = work.tile([P, 4 * W], BF16, name="il_v", tag="il_v", bufs=2, align_bytes=256)
 
-        def scale_interleave(k, part, a):
+        def scale_interleave(dst, a, part, lo, hi):
             nc.vector.tensor_tensor(
-                out=il_v[k][:, 4 * a : 4 * (a + width(part))].rearrange("p (c i t) -> p c t i", i=RUN, t=4),
-                in0=raw[part][:].rearrange("p t (c i) -> p c t i", i=RUN),
-                in1=zs_psum[:, part[1], :, 0:1].unsqueeze(1).to_broadcast([P, width(part) // RUN, 4, RUN]),
+                out=dst[:, 4 * a : 4 * (a + hi - lo)].rearrange("p (c i t) -> p c t i", i=RUN, t=4),
+                in0=raw[part][:, :, lo:hi].rearrange("p t (c i) -> p c t i", i=RUN),
+                in1=zs_psum[:, part[1], :, 0:1].unsqueeze(1).to_broadcast([P, (hi - lo) // RUN, 4, RUN]),
                 op=MULT,
             )
 
-        def widen(k, u, first):
-            for t in range(4):
+        def widen(k, u, first, rows=range(4)):
+            for t in rows:
                 nc.scalar.activation(
                     out=planes[k][:, t, first : first + width(u)],
                     in_=zb[u][:, t, :].bitcast(F8),
@@ -133,10 +136,10 @@ def tile_josephkalmanupdate_w_kernel(tc, s, z_bytes, z_scale, kgain, g, d, r, ou
                     scale=zs[:, u[1], t : t + 1],
                 )
 
-        def widen_row_on_vector(t):
-            u = odd[0][0]
+        def widen_row_on_vector(k, t):
+            u = odd[k][0]
             nc.vector.tensor_scalar(
-                out=planes[0][:, t, 0:W],
+                out=planes[k][:, t, 0:W],
                 in0=zb[u][:, t, :].bitcast(F8),
                 scalar1=zs[:, u[1], t : t + 1],
                 scalar2=None,
@@ -152,7 +155,7 @@ def tile_josephkalmanupdate_w_kernel(tc, s, z_bytes, z_scale, kgain, g, d, r, ou
                     banks.append(psum.tile([P, 4 * min(2 * P, count)], BF16, name="by_pe", tag="by_pe", bufs=1))
                 elif a == 2 * P:
                     if not spare:
-                        spare.append(psum.tile([P, 4 * (count - a)], BF16, name="kz", tag="kz", bufs=4))
+                        spare.append(psum.tile([P, 8 * P], BF16, name="kz", tag="kz", bufs=4))
                     banks.append(spare[0])
                 into = a % (2 * P)
                 nc.tensor.matmul(
@@ -168,11 +171,15 @@ def tile_josephkalmanupdate_w_kernel(tc, s, z_bytes, z_scale, kgain, g, d, r, ou
             count = relief[k] + edge_width[k]
             for i, bank in enumerate(banks):
                 a, b = 2 * P * i, min(2 * P * (i + 1), count)
-                nc.scalar.copy(out=il_v[k][:, 4 * a : 4 * b].bitcast(F32), in_=bank[:].bitcast(F32))
+                nc.scalar.copy(out=il_v[k][:, 4 * a : 4 * b].bitcast(F32), in_=bank[:, 0 : 4 * (b - a)].bitcast(F32))
+
+        def g_buffer(k):
+            tag = ("il_g_even", "il_g_odd")[k % 2]
+            return work.tile([P, 4 * W], BF16, name=tag, tag=tag, bufs=1, align_bytes=256)
 
         def interleave_on_gpsimd(k):
             count = columns[k] - relief[k]
-            il_g[k] = work.tile([P, 4 * W], BF16, name="il_g", tag="il_g", bufs=1, align_bytes=256)
+            il_g[k] = g_buffer(min(k, double_step))
             nc.gpsimd.tensor_scalar(
                 out=il_g[k][:, 0 : 4 * count].rearrange("p (c i t) -> p c t i", i=RUN, t=4),
                 in0=planes[k][:, :, 0:count].rearrange("p t (c i) -> p c t i", i=RUN),
@@ -183,8 +190,8 @@ def tile_josephkalmanupdate_w_kernel(tc, s, z_bytes, z_scale, kgain, g, d, r, ou
             )
 
         def code_tiles(k):
-            z_codes = work.tile([P, 2 * W], U32, name="z_codes", tag="z_codes", bufs=3, align_bytes=256)
-            z_scales = work.tile([P, 2 * W], U8, name="z_scales", tag="z_scales", bufs=3, align_bytes=256)
+            z_codes = work.tile([P, 2 * W], U32, name="z_codes", tag="z_codes", bufs=4, align_bytes=256)
+            z_scales = work.tile([P, 2 * W], U8, name="z_scales", tag="z_scales", bufs=4, align_bytes=256)
             codes[k] = (z_codes, z_scales)
 
         def quantise(k, src, first, a, b):
@@ -195,11 +202,10 @@ def tile_josephkalmanupdate_w_kernel(tc, s, z_bytes, z_scale, kgain, g, d, r, ou
                 in_=src[:, 4 * a : 4 * b],
             )
 
-        def kz_passes(k):
+        def kz_passes(k, pieces, col):
             z_codes, z_scales = codes[k]
             complete = []
-            col = 0
-            for c, gp, lo, hi in odd[k] + casts[k]:
+            for c, gp, lo, hi in pieces:
                 for h in range((W * c + lo) // BLK, (W * c + hi) // BLK):
                     if h not in kz:
                         kz[h] = psum.tile([P, BLK], F32, name="kz", tag="kz", bufs=4)
@@ -230,17 +236,14 @@ def tile_josephkalmanupdate_w_kernel(tc, s, z_bytes, z_scale, kgain, g, d, r, ou
             for a, b in parts:
                 nc.scalar.activation(out=neg_kz[h][:, a:b, :], in_=src[:, a:b, :], func=COPY, scale=-1.0)
 
-        def empty_block():
-            h = complete.pop(0)
+        def turn(h, tag, bufs):
             kz_out(h)
-            if h < BLOCKS - 2:
-                to_turn.append(h)
-            else:
-                kz_turn(h)
+            s_turn(h, tag, bufs)
+            kz_turn(h)
 
         def s_turn(h, tag, bufs):
             bank = psum.tile([P, 4 * N], F32, name=tag, tag=tag, bufs=bufs)
-            order = "p (t n) -> p n t" if h == BLOCKS - 2 else "p (n t) -> p n t"
+            order = "p (t n) -> p n t" if h >= ON_SCALAR else "p (n t) -> p n t"
             turned[h] = bank[:].rearrange(order, t=4)
             for t in range(4):
                 nc.tensor.matmul(
@@ -265,10 +268,19 @@ def tile_josephkalmanupdate_w_kernel(tc, s, z_bytes, z_scale, kgain, g, d, r, ou
         def gain_product(h, i):
             if i == 0:
                 w_wd[h] = work.tile([P, 2, BLK], BF16, name="w_wd", tag="w_wd", bufs=3, align_bytes=64)
+            gain = (g_sb, gd_f32)[i][:, h, :].unsqueeze(1)
+            if h < ON_SCALAR:
+                nc.vector.tensor_tensor(
+                    out=w_wd[h][:, i, :].rearrange("p (n t) -> p n t", t=4),
+                    in0=turned[h],
+                    in1=gain.to_broadcast([P, N, 4]),
+                    op=MULT,
+                )
+                return
             nc.vector.tensor_tensor(
-                out=w_wd[h][:, i, :].rearrange("p (n t) -> p n t", t=4),
-                in0=turned[h],
-                in1=(g_sb, gd_f32)[i][:, h, :].unsqueeze(1).to_broadcast([P, N, 4]),
+                out=w_wd[h][:, i, :].rearrange("p (c j t) -> p c t j", j=RUN, t=4),
+                in0=turned[h].rearrange("p (c j) t -> p c t j", j=RUN),
+                in1=gain.unsqueeze(3).to_broadcast([P, N // RUN, 4, RUN]),
                 op=MULT,
             )
 
@@ -287,8 +299,8 @@ def tile_josephkalmanupdate_w_kernel(tc, s, z_bytes, z_scale, kgain, g, d, r, ou
                 )
 
         def j_pass(h, parts=((0, 2),)):
-            w_codes = work.tile([P, 2, N], U32, name="w_codes", tag="w_codes", bufs=2, align_bytes=64)
-            w_scales = work.tile([P, 2, N], U8, name="w_scales", tag="w_scales", bufs=2, align_bytes=64)
+            w_codes = work.tile([P, 2, N], U32, name="w_codes", tag="w_codes", bufs=3, align_bytes=64)
+            w_scales = work.tile([P, 2, N], U8, name="w_scales", tag="w_scales", bufs=3, align_bytes=64)
             for a, b in parts:
                 nc.vector.quantize_mx(
                     out=w_codes[:, a:b, :].rearrange("p i n -> p (i n)").bitcast(FP8X4),
@@ -372,15 +384,14 @@ def tile_josephkalmanupdate_w_kernel(tc, s, z_bytes, z_scale, kgain, g, d, r, ou
             nc.scalar.dma_start(out=zs[:, 0:2, :], in_=zs_hbm[:, 0:2, :])
             nc.scalar.dma_start(out=zs[:, 2:PASSES, :], in_=zs_hbm[:, 2:PASSES, :])
             make_identity(nc, ident[:])
-            nc.gpsimd.tensor_copy(out=ident_bf[:], in_=ident[:])
+            nc.vector.tensor_copy(out=ident_bf[:], in_=ident[:])
 
-            load(odd[0][0], rows=slice(0, 1))
-            load(bodies[0][0])
-            load(odd[0][0], rows=slice(1, 3))
-            load(bodies[0][1])
-            load(odd[0][0], rows=slice(3, 4))
+            for t in range(4):
+                load(odd[0][0], rows=slice(t, t + 1))
+                load(bodies[0][0], rows=slice(t, t + 1))
+            load(odd[1][0], rows=slice(0, 1))
             load(edges[1], "zb_edge", 4)
-            load(odd[1][0], rows=slice(0, 2))
+            load(odd[1][0], rows=slice(1, 2))
             load(odd[1][0], rows=slice(2, 4))
             load_kgain(0)
             load(bodies[1][0])
@@ -388,15 +399,20 @@ def tile_josephkalmanupdate_w_kernel(tc, s, z_bytes, z_scale, kgain, g, d, r, ou
             load_kgain(1)
 
             step_tiles(0)
-            widen_row_on_vector(0)
+            step_tiles(1)
+            widen_row_on_vector(0, 0)
             scales_four_times()
-            cast(bodies[0][0])
+            cast(bodies[0][0], slice(0, 1))
+            cast(bodies[0][0], slice(1, 2))
             scales_to_psum()
-            cast(bodies[0][1])
             for t in range(1, 4):
-                widen_row_on_vector(t)
+                widen_row_on_vector(0, t)
+            for t in range(HEAD_ROWS):
+                widen_row_on_vector(1, t)
+            for t in range(2, 4):
+                cast(bodies[0][0], slice(t, t + 1))
 
-            complete, to_turn, products, j_due, kr_done = [], [], [], [], 0
+            due, complete, products, j_due, kr_done = [], [], [], [], 0
             for k in range(steps):
                 if k + AHEAD < steps:
                     load_step(k + AHEAD)
@@ -411,82 +427,97 @@ def tile_josephkalmanupdate_w_kernel(tc, s, z_bytes, z_scale, kgain, g, d, r, ou
                 if k < K_QUARTERS:
                     k_bank = k_turn(k)
 
+                nxt = k + 1
                 if k == double_step:
-                    empty_block()
-                    nc.scalar.copy(out=g_f32[:], in_=g_sb[:, BLOCKS - 2, :])
-                if k + 1 < steps:
-                    step_tiles(k + 1)
-                    widen(k + 1, edges[k + 1], columns[k + 1])
-                if relief[k]:
+                    turn(ON_SCALAR, "kz", 4)
+                    nc.scalar.copy(out=g_f32[:], in_=g_sb[:, ON_SCALAR, :])
+                if nxt < steps:
+                    if k > 0:
+                        step_tiles(nxt)
+                    widen(nxt, edges[nxt], columns[nxt])
+                if k == double_step + 1:
                     by_pe_out(k, by_pe)
-                if k + 1 < steps and not relief[k + 1]:
-                    by_pe = interleave_on_pe(k + 1)
-                if k >= 1:
-                    complete.extend(kz_passes(k - 1))
-                if k + 1 < steps:
-                    for i, u in enumerate(odd[k + 1]):
-                        widen(k + 1, u, i * width(u))
-                    if not relief[k + 1]:
-                        by_pe_out(k + 1, by_pe)
-                    elif k != double_step:
-                        by_pe = interleave_on_pe(k + 1)
-                    for u in bodies[k + 1]:
-                        cast(u)
-                else:
-                    s_turn(BLOCKS - 1, "turned", 1)
-                    gain_products_on_scalar(BLOCKS - 2)
-                if complete and len(products) < 2 and not to_turn:
-                    empty_block()
-
-                col, j_now = relief[k] + edge_width[k], []
-                for part in bodies[k]:
-                    j_now, j_due = j_now + j_due, []
-                    scale_interleave(k, part, col)
-                    col += width(part)
-                    if part == bodies[0][0]:
-                        continue
-                    if k < K_QUARTERS:
-                        k_out(k, k_bank)
-                    elif products:
-                        h, i = products.pop(0)
-                        gain_product(h, i)
-                        j_due = [h] if i == 1 else []
+                while due and due[0][1][-1][1] < 2 * (k - 1):
+                    complete.extend(kz_passes(*due.pop(0)))
+                if nxt <= double_step:
+                    by_pe = interleave_on_pe(nxt)
+                if nxt < steps:
+                    for i, u in enumerate(odd[nxt]):
+                        widen(nxt, u, i * width(u), range(HEAD_ROWS if k == 0 else 0, 4))
+                    if nxt <= double_step:
+                        by_pe_out(nxt, by_pe)
                     else:
-                        kr_product(kr_done, kr_done + 2)
-                        kr_done += 2
-                    if to_turn and not products:
-                        h = to_turn.pop(0)
-                        s_turn(h, "turned", 1)
-                        kz_turn(h)
-                        products.extend([(h, 0), (h, 1)])
-                if k == double_step:
-                    by_pe = interleave_on_pe(k + 1)
-                    s_turn(BLOCKS - 2, "kz", 4)
+                        by_pe = interleave_on_pe(nxt)
+                    for u in reversed(bodies[nxt]):
+                        cast(u)
+
+                j_first, j_due = j_due, []
+                if k == 0:
+                    first_half = g_buffer(1)
+                    scale_interleave(first_half, 0, bodies[0][0], 0, BLK)
+                    scale_interleave(il_v[0], BLK, bodies[0][0], BLK, W)
+                    k_out(k, k_bank)
+                else:
+                    ends = relief[k] + columns[k]
+                    for part in reversed(bodies[k]):
+                        ends -= width(part)
+                        scale_interleave(il_v[k], ends, part, 0, width(part))
+                        if k < K_QUARTERS:
+                            k_out(k, k_bank)
+                        elif products and (k, part) != (double_step, bodies[k][-1]):
+                            h, i = products.pop(0)
+                            gain_product(h, i)
+                            j_due.extend([h] * i)
+                        else:
+                            kr_product(kr_done, kr_done + 2)
+                            kr_done += 2
                 if k == K_QUARTERS - 1:
                     r_to_psum()
-                for h in j_now:
+                if k < double_step and complete and not products:
+                    h = complete.pop(0)
+                    turn(h, "turned", 1)
+                    products.extend([(h, 0), (h, 1)])
+                if k == double_step + 1:
+                    turn(BLOCKS - 2, "turned", 1)
+                    by_pe_out(nxt, by_pe)
+                    gain_products_on_scalar(ON_SCALAR)
+
+                for h in j_first:
                     j_pass(h)
-                code_tiles(k)
-                by_g = columns[k] - relief[k]
-                cut = relief[k] or (0 if j_now else columns[k] // 2)
-                if cut:
-                    quantise(k, il_v[k], by_g, 0, cut)
-                if k < K_QUARTERS:
-                    quantise_k(k_il, k_codes, k_scales, 2 * k, 2 * k + 2)
+                if 1 <= k <= K_QUARTERS:
+                    quantise_k(k_il, k_codes, k_scales, 2 * k - 2, 2 * k)
                 if k == K_QUARTERS:
                     nc.vector.tensor_tensor(out=gd_f32[:], in0=g_sb[:], in1=d_sb[:], op=MULT)
-                for a, b in ((0, 2 * P), (2 * P, by_g)) if relief[k] else ((0, by_g),):
-                    quantise(k, il_g[k], 0, a, b)
-                quantise(k, il_v[k], by_g, cut, relief[k] + columns[k])
+                code_tiles(k)
+                by_g = columns[k] - relief[k]
+                if 1 <= k <= double_step:
+                    quantise(k - 1, il_g[k - 1], 0, 0, W)
+                    due.append((k - 1, odd[k - 1], 0))
+                if k == 0:
+                    quantise(k, first_half, W, 0, BLK)
+                    quantise(k, il_v[k], W, BLK, W)
+                elif k < double_step:
+                    quantise(k, il_v[k], W, 0, W)
+                else:
+                    if relief[k]:
+                        quantise(k, il_v[k], by_g, 0, relief[k])
+                    for a, b in ((0, 2 * P), (2 * P, by_g)) if relief[k] else ((0, by_g),):
+                        quantise(k, il_g[k], 0, a, b)
+                    quantise(k, il_v[k], by_g, relief[k], relief[k] + columns[k])
+                    due.append((k, odd[k], 0))
+                due.append((k, casts[k], columns[k]))
 
-            kz_passes(steps - 1)
+            s_turn(BLOCKS - 1, "kz", 4)
+            for passes in due:
+                kz_passes(*passes)
             kz_out(BLOCKS - 1, ((0, 2), (2, 4)))
             kz_turn(BLOCKS - 1)
-            kr_product(kr_done, PASSES)
-            quantise_k(kr_il, kr_codes, kr_scales, 0, kr_done)
-            quantise_k(kr_il, kr_codes, kr_scales, kr_done, PASSES)
+            for i in range(2):
+                gain_product(BLOCKS - 2, i)
+            quantise_k(kr_il, kr_codes, kr_scales, 0, PASSES)
             q_passes()
-            j_pass(BLOCKS - 2)
+            for h in range(ON_SCALAR, BLOCKS - 1):
+                j_pass(h)
             for i in range(2):
                 gain_product(BLOCKS - 1, i)
             j_pass(BLOCKS - 1, ((0, 1), (1, 2)))

@@ -24,7 +24,7 @@ BLOCKS = L // BLK
 W = 2 * BLK
 CHUNKS = L // W
 EDGE = 96
-EDGE_BESIDE_KZ = 64
+PAIR_EDGE = 192
 DOUBLE_EDGE = 224
 LATE_EDGE = 224
 RELIEF = P
@@ -50,8 +50,7 @@ def tile_josephkalmanupdate_w_kernel(tc, s, z_bytes, z_scale, kgain, g, d, r, ou
         r_sb = keep.tile([P, PASSES, 4], BF16, name="r_sb")
         g_sb = keep.tile([P, BLOCKS, 4], BF16, name="g_sb")
         d_sb = keep.tile([P, BLOCKS, 4], BF16, name="d_sb")
-        gd_f32 = keep.tile([P, BLOCKS, 4], F32, name="gd_f32")
-        g_f32 = keep.tile([P, 4], F32, name="g_f32")
+        gains = keep.tile([P, BLOCKS, 2, 4], F32, name="gains")
         k_rows = keep.tile([P, M], BF16, name="k_rows")
         k_il = keep.tile([P, PASSES, 4 * N], BF16, name="k_il", align_bytes=64)
         kr_il = keep.tile([P, PASSES, 4 * N], BF16, name="kr_il", align_bytes=64)
@@ -78,7 +77,9 @@ def tile_josephkalmanupdate_w_kernel(tc, s, z_bytes, z_scale, kgain, g, d, r, ou
                 return 0
             if k >= double_step:
                 return DOUBLE_EDGE if k == double_step else LATE_EDGE
-            return EDGE if k <= K_QUARTERS + 1 else EDGE_BESIDE_KZ
+            if k < K_QUARTERS:
+                return EDGE
+            return PAIR_EDGE if k % 2 == 0 else 0
 
         edge_width = [edge_of(k) for k in range(steps)]
         relief = [RELIEF if k > double_step else 0 for k in range(steps)]
@@ -99,7 +100,8 @@ def tile_josephkalmanupdate_w_kernel(tc, s, z_bytes, z_scale, kgain, g, d, r, ou
             nc.sync.dma_start(out=zb[u][:, rows, :], in_=src[:, rows, :])
 
         def load_step(k):
-            load(edges[k], "zb_edge", 4)
+            if edge_width[k]:
+                load(edges[k], "zb_edge", 4)
             for u in odd[k] + bodies[k]:
                 load(u)
 
@@ -268,7 +270,7 @@ def tile_josephkalmanupdate_w_kernel(tc, s, z_bytes, z_scale, kgain, g, d, r, ou
         def gain_product(h, i):
             if i == 0:
                 w_wd[h] = work.tile([P, 2, BLK], BF16, name="w_wd", tag="w_wd", bufs=3, align_bytes=64)
-            gain = (g_sb, gd_f32)[i][:, h, :].unsqueeze(1)
+            gain = gains[:, h, i, :].unsqueeze(1)
             if h < ON_SCALAR:
                 nc.vector.tensor_tensor(
                     out=w_wd[h][:, i, :].rearrange("p (n t) -> p n t", t=4),
@@ -284,13 +286,22 @@ def tile_josephkalmanupdate_w_kernel(tc, s, z_bytes, z_scale, kgain, g, d, r, ou
                 op=MULT,
             )
 
+        def both_gain_products(h):
+            w_wd[h] = work.tile([P, 2, BLK], BF16, name="w_wd", tag="w_wd", bufs=3, align_bytes=64)
+            nc.vector.tensor_tensor(
+                out=w_wd[h][:].rearrange("p i (n t) -> p i n t", t=4),
+                in0=turned[h].unsqueeze(1).to_broadcast([P, 2, N, 4]),
+                in1=gains[:, h].unsqueeze(2).to_broadcast([P, 2, N, 4]),
+                op=MULT,
+            )
+
         def gain_products_on_scalar(h):
             w_wd[h] = work.tile([P, 2, BLK], BF16, name="w_wd", tag="w_wd", bufs=3, align_bytes=64)
             by_t = work.tile([P, 2, 4, N], BF16, name="by_t", tag="by_t", bufs=1)
-            for i, gain in enumerate((g_f32[:], gd_f32[:, h, :])):
+            for i in range(2):
                 for t in range(4):
                     nc.scalar.activation(
-                        out=by_t[:, i, t, :], in_=turned[h][:, :, t], func=COPY, scale=gain[:, t : t + 1]
+                        out=by_t[:, i, t, :], in_=turned[h][:, :, t], func=COPY, scale=gains[:, h, i, t : t + 1]
                     )
             for i in range(2):
                 nc.scalar.copy(
@@ -430,11 +441,11 @@ def tile_josephkalmanupdate_w_kernel(tc, s, z_bytes, z_scale, kgain, g, d, r, ou
                 nxt = k + 1
                 if k == double_step:
                     turn(ON_SCALAR, "kz", 4)
-                    nc.scalar.copy(out=g_f32[:], in_=g_sb[:, ON_SCALAR, :])
                 if nxt < steps:
                     if k > 0:
                         step_tiles(nxt)
-                    widen(nxt, edges[nxt], columns[nxt])
+                    if edge_width[nxt]:
+                        widen(nxt, edges[nxt], columns[nxt])
                 if k == double_step + 1:
                     by_pe_out(k, by_pe)
                 while due and due[0][1][-1][1] < 2 * (k - 1):
@@ -464,6 +475,15 @@ def tile_josephkalmanupdate_w_kernel(tc, s, z_bytes, z_scale, kgain, g, d, r, ou
                         scale_interleave(il_v[k], ends, part, 0, width(part))
                         if k < K_QUARTERS:
                             k_out(k, k_bank)
+                        elif k < double_step:
+                            if k == K_QUARTERS:
+                                kr_product(0, PASSES // 2)
+                                kr_done = PASSES // 2
+                            elif products:
+                                h = products.pop(0)[0]
+                                products.pop(0)
+                                both_gain_products(h)
+                                j_due.append(h)
                         elif products and (k, part) != (double_step, bodies[k][-1]):
                             h, i = products.pop(0)
                             gain_product(h, i)
@@ -473,7 +493,7 @@ def tile_josephkalmanupdate_w_kernel(tc, s, z_bytes, z_scale, kgain, g, d, r, ou
                             kr_done += 2
                 if k == K_QUARTERS - 1:
                     r_to_psum()
-                if k < double_step and complete and not products:
+                if k < double_step and complete and k % 2 == 1:
                     h = complete.pop(0)
                     turn(h, "turned", 1)
                     products.extend([(h, 0), (h, 1)])
@@ -487,7 +507,8 @@ def tile_josephkalmanupdate_w_kernel(tc, s, z_bytes, z_scale, kgain, g, d, r, ou
                 if 1 <= k <= K_QUARTERS:
                     quantise_k(k_il, k_codes, k_scales, 2 * k - 2, 2 * k)
                 if k == K_QUARTERS:
-                    nc.vector.tensor_tensor(out=gd_f32[:], in0=g_sb[:], in1=d_sb[:], op=MULT)
+                    nc.vector.tensor_tensor(out=gains[:, :, 1, :], in0=g_sb[:], in1=d_sb[:], op=MULT)
+                    nc.vector.tensor_copy(out=gains[:, :, 0, :], in_=g_sb[:])
                 code_tiles(k)
                 by_g = columns[k] - relief[k]
                 if 1 <= k <= double_step:

@@ -24,10 +24,11 @@ BLOCKS = L // BLK
 W = 2 * BLK
 CHUNKS = L // W
 EDGE = 96
-PAIR_EDGE = 192
+PAIR_EDGE = 160
 DOUBLE_EDGE = 224
-LATE_EDGE = 224
-RELIEF = P
+LATE_EDGE = 256
+SPLIT_N = 104
+RELIEF = 2 * P
 RUN = 8
 HEAD_ROWS = 1
 ON_SCALAR = BLOCKS - 3
@@ -286,12 +287,13 @@ def tile_josephkalmanupdate_w_kernel(tc, s, z_bytes, z_scale, kgain, g, d, r, ou
                 op=MULT,
             )
 
-        def both_gain_products(h):
-            w_wd[h] = work.tile([P, 2, BLK], BF16, name="w_wd", tag="w_wd", bufs=3, align_bytes=64)
+        def both_gain_products(h, a, b):
+            if a == 0:
+                w_wd[h] = work.tile([P, 2, BLK], BF16, name="w_wd", tag="w_wd", bufs=3, align_bytes=64)
             nc.vector.tensor_tensor(
-                out=w_wd[h][:].rearrange("p i (n t) -> p i n t", t=4),
-                in0=turned[h].unsqueeze(1).to_broadcast([P, 2, N, 4]),
-                in1=gains[:, h].unsqueeze(2).to_broadcast([P, 2, N, 4]),
+                out=w_wd[h][:].rearrange("p i (n t) -> p i n t", t=4)[:, :, a:b, :],
+                in0=turned[h][:, a:b, :].unsqueeze(1).to_broadcast([P, 2, b - a, 4]),
+                in1=gains[:, h].unsqueeze(2).to_broadcast([P, 2, b - a, 4]),
                 op=MULT,
             )
 
@@ -395,7 +397,7 @@ def tile_josephkalmanupdate_w_kernel(tc, s, z_bytes, z_scale, kgain, g, d, r, ou
             nc.scalar.dma_start(out=zs[:, 0:2, :], in_=zs_hbm[:, 0:2, :])
             nc.scalar.dma_start(out=zs[:, 2:PASSES, :], in_=zs_hbm[:, 2:PASSES, :])
             make_identity(nc, ident[:])
-            nc.vector.tensor_copy(out=ident_bf[:], in_=ident[:])
+            nc.gpsimd.tensor_scalar(out=ident_bf[:], in0=ident[:], scalar1=1.0, scalar2=0.0, op0=MULT, op1=ADD)
 
             for t in range(4):
                 load(odd[0][0], rows=slice(t, t + 1))
@@ -476,14 +478,14 @@ def tile_josephkalmanupdate_w_kernel(tc, s, z_bytes, z_scale, kgain, g, d, r, ou
                         if k < K_QUARTERS:
                             k_out(k, k_bank)
                         elif k < double_step:
-                            if k == K_QUARTERS:
-                                kr_product(0, PASSES // 2)
-                                kr_done = PASSES // 2
-                            elif products:
-                                h = products.pop(0)[0]
-                                products.pop(0)
-                                both_gain_products(h)
-                                j_due.append(h)
+                            if products:
+                                h, i = products.pop(0)
+                                both_gain_products(h, *((0, SPLIT_N), (SPLIT_N, N))[i])
+                                j_due.extend([h] * i)
+                            else:
+                                more = 3 if edge_width[k] else 1
+                                kr_product(kr_done, kr_done + more)
+                                kr_done += more
                         elif products and (k, part) != (double_step, bodies[k][-1]):
                             h, i = products.pop(0)
                             gain_product(h, i)
@@ -522,8 +524,7 @@ def tile_josephkalmanupdate_w_kernel(tc, s, z_bytes, z_scale, kgain, g, d, r, ou
                 else:
                     if relief[k]:
                         quantise(k, il_v[k], by_g, 0, relief[k])
-                    for a, b in ((0, 2 * P), (2 * P, by_g)) if relief[k] else ((0, by_g),):
-                        quantise(k, il_g[k], 0, a, b)
+                    quantise(k, il_g[k], 0, 0, by_g)
                     quantise(k, il_v[k], by_g, relief[k], relief[k] + columns[k])
                     due.append((k, odd[k], 0))
                 due.append((k, casts[k], columns[k]))

@@ -23,12 +23,14 @@ BLK = 512
 BLOCKS = L // BLK
 W = 2 * BLK
 CHUNKS = L // W
-EDGE = 96
-PAIR_EDGE = 160
+EDGE = 64
+PAIR_EDGE = 128
 DOUBLE_EDGE = 224
-LATE_EDGE = 256
-SPLIT_N = 104
-RELIEF = 2 * P
+LATE_EDGE = 224
+SPLIT_N = 80
+RELIEF = 32
+PAIR_RELIEF = 64
+LATE_RELIEF = 192
 RUN = 8
 HEAD_ROWS = 1
 ON_SCALAR = BLOCKS - 3
@@ -59,6 +61,8 @@ def tile_josephkalmanupdate_w_kernel(tc, s, z_bytes, z_scale, kgain, g, d, r, ou
         k_scales = keep.tile([P, PASSES, N], U8, name="k_scales", align_bytes=64)
         kr_codes = keep.tile([P, PASSES, N], U32, name="kr_codes", align_bytes=64)
         kr_scales = keep.tile([P, PASSES, N], U8, name="kr_scales", align_bytes=64)
+        il_even = keep.tile([P, 8 * W], BF16, name="il_even", align_bytes=256)
+        il_odd = keep.tile([P, 8 * W], BF16, name="il_odd", align_bytes=256)
         s_rows = keep.tile([P, L], BF16, name="s_rows")
         jq = psum.tile([P, N], F32, name="jq", tag="jq", bufs=1)
         factors = psum.tile([P, P + 2 * PASSES], F32, name="factors", tag="factors", bufs=1)
@@ -83,12 +87,21 @@ def tile_josephkalmanupdate_w_kernel(tc, s, z_bytes, z_scale, kgain, g, d, r, ou
             return PAIR_EDGE if k % 2 == 0 else 0
 
         edge_width = [edge_of(k) for k in range(steps)]
-        relief = [RELIEF if k > double_step else 0 for k in range(steps)]
+        def relief_of(k):
+            if k > double_step:
+                return LATE_RELIEF
+            if k == double_step or 1 <= k < K_QUARTERS:
+                return RELIEF
+            return PAIR_RELIEF if edge_of(k) else 0
+
+        relief = [relief_of(k) for k in range(steps)]
         edges = [pieces[0][:3] + (pieces[0][2] + x,) for pieces, x in zip(casts, edge_width)]
         bodies = [[u[:2] + (u[3], pieces[0][3])] + pieces[1:] for u, pieces in zip(edges, casts)]
 
-        zb, raw, planes, il_v, il_g, codes, kz, neg_kz, turned, w_wd = {}, {}, {}, {}, {}, {}, {}, {}, {}, {}
+        zb, raw, planes, by_pe, codes, kz, neg_kz, turned, w_wd = {}, {}, {}, {}, {}, {}, {}, {}, {}
         passes_done, spare = {}, []
+
+        il = [(il_even, il_odd)[min(k, double_step) % 2] for k in range(steps)]
 
         def width(u):
             return u[3] - u[2]
@@ -120,7 +133,6 @@ def tile_josephkalmanupdate_w_kernel(tc, s, z_bytes, z_scale, kgain, g, d, r, ou
 
         def step_tiles(k):
             planes[k] = work.tile([P, 4, W + DOUBLE_EDGE], BF16, name="planes", tag="planes", bufs=4, align_bytes=256)
-            il_v[k] = work.tile([P, 4 * W], BF16, name="il_v", tag="il_v", bufs=2, align_bytes=256)
 
         def scale_interleave(dst, a, part, lo, hi):
             nc.vector.tensor_tensor(
@@ -149,42 +161,38 @@ def tile_josephkalmanupdate_w_kernel(tc, s, z_bytes, z_scale, kgain, g, d, r, ou
                 op0=MULT,
             )
 
-        def interleave_on_pe(k):
+        def interleave_on_pe(k, edge_alone):
             first, count = columns[k] - relief[k], relief[k] + edge_width[k]
-            banks = []
-            for a in range(0, count, P):
-                b = min(a + P, count)
-                if a == 0:
-                    banks.append(psum.tile([P, 4 * min(2 * P, count)], BF16, name="by_pe", tag="by_pe", bufs=1))
-                elif a == 2 * P:
+            if k not in by_pe:
+                by_pe[k] = [psum.tile([P, 8 * P], BF16, name="by_pe", tag="by_pe", bufs=1)]
+                if count > 2 * P:
                     if not spare:
                         spare.append(psum.tile([P, 8 * P], BF16, name="kz", tag="kz", bufs=4))
-                    banks.append(spare[0])
-                into = a % (2 * P)
-                nc.tensor.matmul(
-                    banks[-1][:, 4 * into : 4 * (into + b - a)].rearrange("p (l t) -> p l t", t=4),
-                    lhsT=ident_bf[:],
-                    rhs=planes[k][:, :, first + a : first + b].rearrange("p t l -> p l t"),
-                    start=True,
-                    stop=True,
-                )
-            return banks
+                    by_pe[k].append(spare[0])
+            for a in range(0, count, P):
+                if (a >= relief[k]) == edge_alone:
+                    b = min(a + P, count)
+                    into = a % (2 * P)
+                    nc.tensor.matmul(
+                        by_pe[k][a // (2 * P)][:, 4 * into : 4 * (into + b - a)].rearrange("p (l t) -> p l t", t=4),
+                        lhsT=ident_bf[:],
+                        rhs=planes[k][:, :, first + a : first + b].rearrange("p t l -> p l t"),
+                        start=True,
+                        stop=True,
+                    )
 
-        def by_pe_out(k, banks):
-            count = relief[k] + edge_width[k]
-            for i, bank in enumerate(banks):
+        def by_pe_out(k):
+            first, count = columns[k] - relief[k], relief[k] + edge_width[k]
+            for i, bank in enumerate(by_pe[k]):
                 a, b = 2 * P * i, min(2 * P * (i + 1), count)
-                nc.scalar.copy(out=il_v[k][:, 4 * a : 4 * b].bitcast(F32), in_=bank[:, 0 : 4 * (b - a)].bitcast(F32))
-
-        def g_buffer(k):
-            tag = ("il_g_even", "il_g_odd")[k % 2]
-            return work.tile([P, 4 * W], BF16, name=tag, tag=tag, bufs=1, align_bytes=256)
+                nc.scalar.copy(
+                    out=il[k][:, 4 * (first + a) : 4 * (first + b)].bitcast(F32), in_=bank[:, 0 : 4 * (b - a)].bitcast(F32)
+                )
 
         def interleave_on_gpsimd(k):
             count = columns[k] - relief[k]
-            il_g[k] = g_buffer(min(k, double_step))
             nc.gpsimd.tensor_scalar(
-                out=il_g[k][:, 0 : 4 * count].rearrange("p (c i t) -> p c t i", i=RUN, t=4),
+                out=il[k][:, 0 : 4 * count].rearrange("p (c i t) -> p c t i", i=RUN, t=4),
                 in0=planes[k][:, :, 0:count].rearrange("p t (c i) -> p c t i", i=RUN),
                 scalar1=1.0,
                 scalar2=0.0,
@@ -448,33 +456,38 @@ def tile_josephkalmanupdate_w_kernel(tc, s, z_bytes, z_scale, kgain, g, d, r, ou
                         step_tiles(nxt)
                     if edge_width[nxt]:
                         widen(nxt, edges[nxt], columns[nxt])
-                if k == double_step + 1:
-                    by_pe_out(k, by_pe)
                 while due and due[0][1][-1][1] < 2 * (k - 1):
                     complete.extend(kz_passes(*due.pop(0)))
-                if nxt <= double_step:
-                    by_pe = interleave_on_pe(nxt)
                 if nxt < steps:
                     for i, u in enumerate(odd[nxt]):
-                        widen(nxt, u, i * width(u), range(HEAD_ROWS if k == 0 else 0, 4))
-                    if nxt <= double_step:
-                        by_pe_out(nxt, by_pe)
-                    else:
-                        by_pe = interleave_on_pe(nxt)
+                        widen(nxt, u, i * width(u), range(HEAD_ROWS if k == 0 else 0, 2))
+                        if k in by_pe and i == 0:
+                            by_pe_out(k)
+                        if k == double_step + 1:
+                            interleave_on_pe(nxt, True)
+                        widen(nxt, u, i * width(u), range(2, 4))
+                    if edge_width[nxt]:
+                        if k != double_step + 1:
+                            interleave_on_pe(nxt, True)
+                        interleave_on_pe(nxt, False)
                     for u in reversed(bodies[nxt]):
                         cast(u)
 
-                j_first, j_due = j_due, []
+                if k == steps - 1:
+                    by_pe_out(k)
+                    gain_products_on_scalar(ON_SCALAR)
+
+                j_first = [j_due.pop(0)] if j_due and k != double_step else []
                 if k == 0:
-                    first_half = g_buffer(1)
-                    scale_interleave(first_half, 0, bodies[0][0], 0, BLK)
-                    scale_interleave(il_v[0], BLK, bodies[0][0], BLK, W)
+                    scale_interleave(il[1], 0, bodies[0][0], 0, BLK)
+                    scale_interleave(il[0], W + BLK, bodies[0][0], BLK, W)
                     k_out(k, k_bank)
                 else:
-                    ends = relief[k] + columns[k]
+                    ends = 2 * columns[k]
                     for part in reversed(bodies[k]):
                         ends -= width(part)
-                        scale_interleave(il_v[k], ends, part, 0, width(part))
+                        if k < steps - 1:
+                            scale_interleave(il[k], ends, part, 0, width(part))
                         if k < K_QUARTERS:
                             k_out(k, k_bank)
                         elif k < double_step:
@@ -493,6 +506,8 @@ def tile_josephkalmanupdate_w_kernel(tc, s, z_bytes, z_scale, kgain, g, d, r, ou
                         else:
                             kr_product(kr_done, kr_done + 2)
                             kr_done += 2
+                if k == steps - 1:
+                    scale_interleave(il[k], ends, part, 0, width(part))
                 if k == K_QUARTERS - 1:
                     r_to_psum()
                 if k < double_step and complete and k % 2 == 1:
@@ -501,8 +516,6 @@ def tile_josephkalmanupdate_w_kernel(tc, s, z_bytes, z_scale, kgain, g, d, r, ou
                     products.extend([(h, 0), (h, 1)])
                 if k == double_step + 1:
                     turn(BLOCKS - 2, "turned", 1)
-                    by_pe_out(nxt, by_pe)
-                    gain_products_on_scalar(ON_SCALAR)
 
                 for h in j_first:
                     j_pass(h)
@@ -512,21 +525,18 @@ def tile_josephkalmanupdate_w_kernel(tc, s, z_bytes, z_scale, kgain, g, d, r, ou
                     nc.vector.tensor_tensor(out=gains[:, :, 1, :], in0=g_sb[:], in1=d_sb[:], op=MULT)
                     nc.vector.tensor_copy(out=gains[:, :, 0, :], in_=g_sb[:])
                 code_tiles(k)
-                by_g = columns[k] - relief[k]
                 if 1 <= k <= double_step:
-                    quantise(k - 1, il_g[k - 1], 0, 0, W)
+                    quantise(k - 1, il[k - 1], 0, 0, W)
                     due.append((k - 1, odd[k - 1], 0))
                 if k == 0:
-                    quantise(k, first_half, W, 0, BLK)
-                    quantise(k, il_v[k], W, BLK, W)
-                elif k < double_step:
-                    quantise(k, il_v[k], W, 0, W)
-                else:
-                    if relief[k]:
-                        quantise(k, il_v[k], by_g, 0, relief[k])
-                    quantise(k, il_g[k], 0, 0, by_g)
-                    quantise(k, il_v[k], by_g, relief[k], relief[k] + columns[k])
+                    quantise(k, il[1], W, 0, BLK)
+                    quantise(k, il[0], 0, W + BLK, 2 * W)
+                    due.append((k, casts[k], columns[k]))
+                    continue
+                if k >= double_step:
+                    quantise(k, il[k], 0, 0, columns[k])
                     due.append((k, odd[k], 0))
+                quantise(k, il[k], 0, columns[k], 2 * columns[k])
                 due.append((k, casts[k], columns[k]))
 
             s_turn(BLOCKS - 1, "kz", 4)

@@ -23,13 +23,13 @@ BLK = 512
 BLOCKS = L // BLK
 W = 2 * BLK
 CHUNKS = L // W
-EDGE = 64
-PAIR_EDGE = 128
+EDGE = 96
+PAIR_EDGE = 160
 DOUBLE_EDGE = 224
-LATE_EDGE = 224
-SPLIT_N = 80
+LATE_EDGE = 256
+SPLIT_N = 104
 RELIEF = 32
-PAIR_RELIEF = 64
+PAIR_RELIEF = 16
 LATE_RELIEF = 192
 RUN = 8
 HEAD_ROWS = 1

@@ -24,16 +24,18 @@ BLOCKS = L // BLK
 W = 2 * BLK
 CHUNKS = L // W
 EDGE = 96
-PAIR_EDGE = 160
+PAIR_EDGE = 192
 DOUBLE_EDGE = 224
 LATE_EDGE = 256
-SPLIT_N = 104
+SPLIT_N = 112
+EARLY_RELIEF = 48
 RELIEF = 32
-PAIR_RELIEF = 16
+PAIR_RELIEF = 32
 LATE_RELIEF = 192
 RUN = 8
 HEAD_ROWS = 1
 ON_SCALAR = BLOCKS - 3
+ROW_STEPS = (1, 5)
 AHEAD = 3
 K_QUARTERS = PASSES // 2
 
@@ -78,20 +80,20 @@ def tile_josephkalmanupdate_w_kernel(tc, s, z_bytes, z_scale, kgain, g, d, r, ou
         double_step = steps - 3
 
         def edge_of(k):
-            if k == 0:
-                return 0
             if k >= double_step:
                 return DOUBLE_EDGE if k == double_step else LATE_EDGE
             if k < K_QUARTERS:
-                return EDGE
+                return 0
             return PAIR_EDGE if k % 2 == 0 else 0
 
         edge_width = [edge_of(k) for k in range(steps)]
         def relief_of(k):
             if k > double_step:
                 return LATE_RELIEF
-            if k == double_step or 1 <= k < K_QUARTERS:
+            if k == double_step:
                 return RELIEF
+            if k < K_QUARTERS:
+                return EARLY_RELIEF if k else 0
             return PAIR_RELIEF if edge_of(k) else 0
 
         relief = [relief_of(k) for k in range(steps)]
@@ -348,7 +350,7 @@ def tile_josephkalmanupdate_w_kernel(tc, s, z_bytes, z_scale, kgain, g, d, r, ou
             return k_bank
 
         def k_out(q, k_bank):
-            nc.vector.tensor_copy(
+            nc.scalar.copy(
                 out=k_il[:, 2 * q : 2 * q + 2, :].bitcast(F32).rearrange("p j (n u) -> p j n u", u=2),
                 in_=k_bank[:].rearrange("p j u n -> p j n u"),
             )
@@ -411,7 +413,6 @@ def tile_josephkalmanupdate_w_kernel(tc, s, z_bytes, z_scale, kgain, g, d, r, ou
                 load(odd[0][0], rows=slice(t, t + 1))
                 load(bodies[0][0], rows=slice(t, t + 1))
             load(odd[1][0], rows=slice(0, 1))
-            load(edges[1], "zb_edge", 4)
             load(odd[1][0], rows=slice(1, 2))
             load(odd[1][0], rows=slice(2, 4))
             load_kgain(0)
@@ -433,7 +434,7 @@ def tile_josephkalmanupdate_w_kernel(tc, s, z_bytes, z_scale, kgain, g, d, r, ou
             for t in range(2, 4):
                 cast(bodies[0][0], slice(t, t + 1))
 
-            due, complete, products, j_due, kr_done = [], [], [], [], 0
+            due, complete, products, j_due, kr_done, k_ready = [], [], [], [], 0, 0
             for k in range(steps):
                 if k + AHEAD < steps:
                     load_step(k + AHEAD)
@@ -452,21 +453,21 @@ def tile_josephkalmanupdate_w_kernel(tc, s, z_bytes, z_scale, kgain, g, d, r, ou
                 if k == double_step:
                     turn(ON_SCALAR, "kz", 4)
                 if nxt < steps:
-                    if k > 0:
+                    if nxt not in planes:
                         step_tiles(nxt)
                     if edge_width[nxt]:
                         widen(nxt, edges[nxt], columns[nxt])
-                while due and due[0][1][-1][1] < 2 * (k - 1):
+                while due and due[0][1][-1][1] < k_ready:
                     complete.extend(kz_passes(*due.pop(0)))
                 if nxt < steps:
                     for i, u in enumerate(odd[nxt]):
-                        widen(nxt, u, i * width(u), range(HEAD_ROWS if k == 0 else 0, 2))
+                        widen(nxt, u, i * width(u), range(1 if k == 0 or k - 1 in ROW_STEPS else 0, 2))
                         if k in by_pe and i == 0:
                             by_pe_out(k)
                         if k == double_step + 1:
                             interleave_on_pe(nxt, True)
                         widen(nxt, u, i * width(u), range(2, 4))
-                    if edge_width[nxt]:
+                    if relief[nxt]:
                         if k != double_step + 1:
                             interleave_on_pe(nxt, True)
                         interleave_on_pe(nxt, False)
@@ -477,11 +478,13 @@ def tile_josephkalmanupdate_w_kernel(tc, s, z_bytes, z_scale, kgain, g, d, r, ou
                     by_pe_out(k)
                     gain_products_on_scalar(ON_SCALAR)
 
+                if k < K_QUARTERS:
+                    k_out(k, k_bank)
+
                 j_first = [j_due.pop(0)] if j_due and k != double_step else []
                 if k == 0:
                     scale_interleave(il[1], 0, bodies[0][0], 0, BLK)
                     scale_interleave(il[0], W + BLK, bodies[0][0], BLK, W)
-                    k_out(k, k_bank)
                 else:
                     ends = 2 * columns[k]
                     for part in reversed(bodies[k]):
@@ -489,8 +492,8 @@ def tile_josephkalmanupdate_w_kernel(tc, s, z_bytes, z_scale, kgain, g, d, r, ou
                         if k < steps - 1:
                             scale_interleave(il[k], ends, part, 0, width(part))
                         if k < K_QUARTERS:
-                            k_out(k, k_bank)
-                        elif k < double_step:
+                            continue
+                        if k < double_step:
                             if products:
                                 h, i = products.pop(0)
                                 both_gain_products(h, *((0, SPLIT_N), (SPLIT_N, N))[i])
@@ -517,10 +520,14 @@ def tile_josephkalmanupdate_w_kernel(tc, s, z_bytes, z_scale, kgain, g, d, r, ou
                 if k == double_step + 1:
                     turn(BLOCKS - 2, "turned", 1)
 
+                if k in ROW_STEPS:
+                    step_tiles(k + 2)
+                    widen_row_on_vector(k + 2, 0)
                 for h in j_first:
                     j_pass(h)
-                if 1 <= k <= K_QUARTERS:
-                    quantise_k(k_il, k_codes, k_scales, 2 * k - 2, 2 * k)
+                if k in (K_QUARTERS // 2, K_QUARTERS):
+                    quantise_k(k_il, k_codes, k_scales, 2 * k - K_QUARTERS, 2 * k)
+                    k_ready = 2 * k
                 if k == K_QUARTERS:
                     nc.vector.tensor_tensor(out=gains[:, :, 1, :], in0=g_sb[:], in1=d_sb[:], op=MULT)
                     nc.vector.tensor_copy(out=gains[:, :, 0, :], in_=g_sb[:])

@@ -49,9 +49,9 @@ def tile_josephkalmanupdate_w_kernel(tc, s, z_bytes, z_scale, kgain, g, d, r, ou
 
         ident = keep.tile([P, P], F32, name="ident")
         ident_bf = keep.tile([P, P], BF16, name="ident_bf")
-        zs = keep.tile([P, PASSES, 8], F32, name="zs")[:, :, 0:4]
-        zs_four = keep.tile([P, PASSES, 4, 4], F32, name="zs_four")
-        zs_turned = keep.tile([P, P], F32, name="zs_turned")
+        zs = keep.tile([P, PASSES, 4], F32, name="zs")
+        zs_rows = keep.tile([P, K_PASS], F32, name="zs_rows")
+        zs_first = keep.tile([P, 2, 8], F32, name="zs_first")[:, :, 0:4]
         r_sb = keep.tile([P, PASSES, 4], BF16, name="r_sb")
         g_sb = keep.tile([P, BLOCKS, 4], BF16, name="g_sb")
         d_sb = keep.tile([P, BLOCKS, 4], BF16, name="d_sb")
@@ -67,9 +67,9 @@ def tile_josephkalmanupdate_w_kernel(tc, s, z_bytes, z_scale, kgain, g, d, r, ou
         il_odd = keep.tile([P, 8 * W], BF16, name="il_odd", align_bytes=256)
         s_rows = keep.tile([P, L], BF16, name="s_rows")
         jq = psum.tile([P, N], F32, name="jq", tag="jq", bufs=1)
-        factors = psum.tile([P, P + 2 * PASSES], F32, name="factors", tag="factors", bufs=1)
-        zs_psum = factors[:, 0:P].rearrange("p (g t i) -> p g t i", t=4, i=4)
-        r_psum = factors[:, P:].bitcast(BF16).rearrange("p (g t) -> p g t", t=4)
+        factors = psum.tile([P, 4 * P], F32, name="factors", tag="factors", bufs=1)
+        zs_psum = factors[:, 0 : 4 * PASSES].rearrange("p (g t) -> p g t", t=4)
+        r_psum = factors[:, 4 * PASSES : 6 * PASSES].bitcast(BF16)
 
         last_chunk = CHUNKS - 1
         casts = [[(c, gp, 0, W)] for c in range(CHUNKS) for gp in range(0, PASSES, 2)][:-2]
@@ -140,9 +140,14 @@ def tile_josephkalmanupdate_w_kernel(tc, s, z_bytes, z_scale, kgain, g, d, r, ou
             nc.vector.tensor_tensor(
                 out=dst[:, 4 * a : 4 * (a + hi - lo)].rearrange("p (c i t) -> p c t i", i=RUN, t=4),
                 in0=raw[part][:, :, lo:hi].rearrange("p t (c i) -> p c t i", i=RUN),
-                in1=zs_psum[:, part[1], :, 0:1].unsqueeze(1).to_broadcast([P, (hi - lo) // RUN, 4, RUN]),
+                in1=zs_psum[:, part[1], :].unsqueeze(1).unsqueeze(3).to_broadcast([P, (hi - lo) // RUN, 4, RUN]),
                 op=MULT,
             )
+
+        def scale_of(u, t):
+            if u in (odd[0][0], odd[1][0]):
+                return zs_first[:, u[1] // 2, t : t + 1]
+            return zs[:, u[1], t : t + 1]
 
         def widen(k, u, first, rows=range(4)):
             for t in rows:
@@ -150,7 +155,7 @@ def tile_josephkalmanupdate_w_kernel(tc, s, z_bytes, z_scale, kgain, g, d, r, ou
                     out=planes[k][:, t, first : first + width(u)],
                     in_=zb[u][:, t, :].bitcast(F8),
                     func=COPY,
-                    scale=zs[:, u[1], t : t + 1],
+                    scale=scale_of(u, t),
                 )
 
         def widen_row_on_vector(k, t):
@@ -158,7 +163,7 @@ def tile_josephkalmanupdate_w_kernel(tc, s, z_bytes, z_scale, kgain, g, d, r, ou
             nc.vector.tensor_scalar(
                 out=planes[k][:, t, 0:W],
                 in0=zb[u][:, t, :].bitcast(F8),
-                scalar1=zs[:, u[1], t : t + 1],
+                scalar1=scale_of(u, t),
                 scalar2=None,
                 op0=MULT,
             )
@@ -366,7 +371,7 @@ def tile_josephkalmanupdate_w_kernel(tc, s, z_bytes, z_scale, kgain, g, d, r, ou
             nc.vector.tensor_tensor(
                 out=kr_il[:, a:b, :].rearrange("p g (n t) -> p g n t", t=4),
                 in0=k_il[:, a:b, :].rearrange("p g (n t) -> p g n t", t=4),
-                in1=r_psum[:, a:b, :].unsqueeze(2).to_broadcast([P, b - a, N, 4]),
+                in1=r_psum.rearrange("p (g t) -> p g t", t=4)[:, a:b, :].unsqueeze(2).to_broadcast([P, b - a, N, 4]),
                 op=MULT,
             )
 
@@ -382,20 +387,13 @@ def tile_josephkalmanupdate_w_kernel(tc, s, z_bytes, z_scale, kgain, g, d, r, ou
                     stop=False,
                 )
 
-        def scales_four_times():
-            nc.vector.tensor_copy(
-                out=zs_four[:], in_=zs.unsqueeze(3).to_broadcast([P, PASSES, 4, 4])
-            )
-
         def scales_to_psum():
-            once = psum.tile([P, P], F32, name="by_pe", tag="by_pe", bufs=1)
-            nc.tensor.transpose(once[:], zs_four[:].rearrange("p g t i -> p (g t i)"), ident[:])
-            nc.scalar.copy(out=zs_turned[:], in_=once[:])
-            nc.tensor.transpose(factors[:, 0:P], zs_turned[:], ident[:])
+            for t in range(4):
+                nc.tensor.transpose(factors[:, t : 4 * P : 4], zs_rows[:, t:K_PASS:4], ident[:])
 
         def r_to_psum():
             nc.tensor.matmul(
-                factors[:, P:].bitcast(BF16),
+                r_psum,
                 lhsT=ident_bf[:],
                 rhs=r_sb[:].rearrange("p g t -> p (g t)"),
                 start=True,
@@ -403,15 +401,16 @@ def tile_josephkalmanupdate_w_kernel(tc, s, z_bytes, z_scale, kgain, g, d, r, ou
             )
 
         with tc.manual_schedule():
-            zs_hbm = z_scale.rearrange("(g p t) o -> p g (t o)", p=P, t=4)
-            nc.scalar.dma_start(out=zs[:, 0:2, :], in_=zs_hbm[:, 0:2, :])
-            nc.scalar.dma_start(out=zs[:, 2:PASSES, :], in_=zs_hbm[:, 2:PASSES, :])
+            nc.scalar.dma_start(out=zs_first, in_=z_scale.rearrange("(g p t) o -> p g (t o)", p=P, t=4)[:, 1:4:2, :])
+            nc.vector.memset(zs_rows[:], 0.0)
             make_identity(nc, ident[:])
-            nc.gpsimd.tensor_scalar(out=ident_bf[:], in0=ident[:], scalar1=1.0, scalar2=0.0, op0=MULT, op1=ADD)
+            nc.vector.tensor_copy(out=ident_bf[:], in_=ident[:])
 
             for t in range(4):
                 load(odd[0][0], rows=slice(t, t + 1))
                 load(bodies[0][0], rows=slice(t, t + 1))
+                if t == 1:
+                    nc.sync.dma_start(out=zs_rows[0:PASSES, :], in_=z_scale.rearrange("(g m) o -> g (m o)", g=PASSES))
             load(odd[1][0], rows=slice(0, 1))
             load(odd[1][0], rows=slice(1, 2))
             load(odd[1][0], rows=slice(2, 4))
@@ -422,17 +421,12 @@ def tile_josephkalmanupdate_w_kernel(tc, s, z_bytes, z_scale, kgain, g, d, r, ou
 
             step_tiles(0)
             step_tiles(1)
-            widen_row_on_vector(0, 0)
-            scales_four_times()
-            cast(bodies[0][0], slice(0, 1))
-            cast(bodies[0][0], slice(1, 2))
             scales_to_psum()
-            for t in range(1, 4):
+            for t in range(4):
                 widen_row_on_vector(0, t)
-            for t in range(HEAD_ROWS):
-                widen_row_on_vector(1, t)
-            for t in range(2, 4):
                 cast(bodies[0][0], slice(t, t + 1))
+            widen_row_on_vector(1, 0)
+            nc.scalar.copy(out=zs[:], in_=zs_psum)
 
             due, complete, products, j_due, kr_done, k_ready = [], [], [], [], 0, 0
             for k in range(steps):

@@ -23,21 +23,19 @@ BLK = 512
 BLOCKS = L // BLK
 W = 2 * BLK
 CHUNKS = L // W
-EDGE = 96
-PAIR_EDGE = 192
-DOUBLE_EDGE = 224
-LATE_EDGE = 256
-SPLIT_N = 112
-EARLY_RELIEF = 48
-RELIEF = 32
-PAIR_RELIEF = 32
-LATE_RELIEF = 192
+PAIRS = PASSES // 2
+WIDE_STEPS = range(2, 2 * CHUNKS)
+DOUBLE_STEP = 2 * CHUNKS
+STEPS = DOUBLE_STEP + 3
+EDGES = (192, 160)
+DOUBLE_EDGE = 448
+LATE_EDGE = 320
+BEYOND = (32, 64)
+DOUBLE_BEYOND = -192
+LATE_BEYOND = -128
+HELP = {0: (2, 0, 512), 4: (5, 0, 640), 6: (7, 0, 640)}
 RUN = 8
-HEAD_ROWS = 1
-ON_SCALAR = BLOCKS - 3
-ROW_STEPS = (1, 5)
-AHEAD = 3
-K_QUARTERS = PASSES // 2
+LATE = BLOCKS - 3
 
 
 def tile_josephkalmanupdate_w_kernel(tc, s, z_bytes, z_scale, kgain, g, d, r, out):
@@ -63,143 +61,157 @@ def tile_josephkalmanupdate_w_kernel(tc, s, z_bytes, z_scale, kgain, g, d, r, ou
         k_scales = keep.tile([P, PASSES, N], U8, name="k_scales", align_bytes=64)
         kr_codes = keep.tile([P, PASSES, N], U32, name="kr_codes", align_bytes=64)
         kr_scales = keep.tile([P, PASSES, N], U8, name="kr_scales", align_bytes=64)
-        il_even = keep.tile([P, 8 * W], BF16, name="il_even", align_bytes=256)
-        il_odd = keep.tile([P, 8 * W], BF16, name="il_odd", align_bytes=256)
+        il = keep.tile([P, 5 * 4 * W], BF16, name="il", align_bytes=256)
         s_rows = keep.tile([P, L], BF16, name="s_rows")
         jq = psum.tile([P, N], F32, name="jq", tag="jq", bufs=1)
         factors = psum.tile([P, 4 * P], F32, name="factors", tag="factors", bufs=1)
         zs_psum = factors[:, 0 : 4 * PASSES].rearrange("p (g t) -> p g t", t=4)
         r_psum = factors[:, 4 * PASSES : 6 * PASSES].bitcast(BF16)
 
-        last_chunk = CHUNKS - 1
-        casts = [[(c, gp, 0, W)] for c in range(CHUNKS) for gp in range(0, PASSES, 2)][:-2]
-        casts = casts + [[(last_chunk, gp, 0, BLK) for gp in (4, 6)]] + [[(last_chunk, gp, BLK, W)] for gp in (4, 6)]
-        odd = [[(c, gp + 1, lo, hi) for c, gp, lo, hi in pieces] for pieces in casts]
-        steps = len(casts)
-        columns = [sum(hi - lo for c, gp, lo, hi in pieces) for pieces in casts]
-        double_step = steps - 3
+        casts = []
+        for k in range(DOUBLE_STEP):
+            casts.append([(2 * (k % PAIRS), W * max(0, k // 2 - 1), W * (k // 2 + 1))])
+        casts.append([(gp, L - W, L - BLK) for gp in (0, 2)])
+        casts.extend([[(gp, L - BLK, L)] for gp in (0, 2)])
+        odd = [[(gp + 1, lo, hi) for gp, lo, hi in pieces] for pieces in casts]
+        columns = [sum(hi - lo for gp, lo, hi in pieces) for pieces in casts]
+        edge = [0, 0] + [EDGES[k % 2] for k in WIDE_STEPS] + [DOUBLE_EDGE, LATE_EDGE, LATE_EDGE]
+        beyond = [0, 0] + [BEYOND[k % 2] for k in WIDE_STEPS] + [DOUBLE_BEYOND, LATE_BEYOND, LATE_BEYOND]
+        bodies = []
+        for pieces, x in zip(casts, edge):
+            parts = [(gp, a, min(a + W, hi)) for gp, lo, hi in pieces for a in range(lo, hi, W)]
+            bodies.append([(parts[0][0], parts[0][1] + x, parts[0][2])] + parts[1:])
+        plane_at = [0, 3 * W] + [2 * W * (k % 2) for k in WIDE_STEPS]
+        cast_at = [[3 * W], [W]] + [((2 * W, 3 * W), (4 * W, 0))[k % 2] for k in WIDE_STEPS]
+        cast_end = W
+        for k in range(DOUBLE_STEP, STEPS):
+            plane_at.append(cast_end - columns[k] - beyond[k])
+            cast_at.append([plane_at[k] + columns[k] + BLK * i for i in range(len(casts[k]))])
+            cast_end = plane_at[k] + 2 * columns[k]
 
-        def edge_of(k):
-            if k >= double_step:
-                return DOUBLE_EDGE if k == double_step else LATE_EDGE
-            if k < K_QUARTERS:
-                return 0
-            return PAIR_EDGE if k % 2 == 0 else 0
+        zb, raw, planes, by_pe, kz, neg_kz, turned, w_wd = {}, {}, {}, {}, {}, {}, {}, {}
+        passes_done, waiting = {}, []
+        helped = {(k, t): count for k, t, count in HELP.values()}
+        helped[1, 0] = W
 
-        edge_width = [edge_of(k) for k in range(steps)]
-        def relief_of(k):
-            if k > double_step:
-                return LATE_RELIEF
-            if k == double_step:
-                return RELIEF
-            if k < K_QUARTERS:
-                return EARLY_RELIEF if k else 0
-            return PAIR_RELIEF if edge_of(k) else 0
+        def load(key, pieces, bufs, rows=slice(0, 4)):
+            if key not in zb:
+                count = sum(hi - lo for gp, lo, hi in pieces)
+                zb[key] = work.tile([P, 4, count], U8, name=key[0], tag=key[0], bufs=bufs)
+            at = 0
+            for gp, lo, hi in pieces:
+                src = z_bytes[K_PASS * gp : K_PASS * (gp + 1), lo:hi].rearrange("(p t) w -> p t w", t=4)
+                nc.sync.dma_start(out=zb[key][:, rows, at : at + hi - lo], in_=src[:, rows, :])
+                at += hi - lo
 
-        relief = [relief_of(k) for k in range(steps)]
-        edges = [pieces[0][:3] + (pieces[0][2] + x,) for pieces, x in zip(casts, edge_width)]
-        bodies = [[u[:2] + (u[3], pieces[0][3])] + pieces[1:] for u, pieces in zip(edges, casts)]
+        def load_plane(k, rows=slice(0, 4)):
+            load(("zb_plane", k), odd[k], 2, rows)
 
-        zb, raw, planes, by_pe, codes, kz, neg_kz, turned, w_wd = {}, {}, {}, {}, {}, {}, {}, {}, {}
-        passes_done, spare = {}, []
-
-        il = [(il_even, il_odd)[min(k, double_step) % 2] for k in range(steps)]
-
-        def width(u):
-            return u[3] - u[2]
-
-        def load(u, tag="zb", bufs=8, rows=slice(0, 4)):
-            c, gp, lo, hi = u
-            if rows.start == 0:
-                zb[u] = work.tile([P, 4, hi - lo], U8, name=tag, tag=tag, bufs=bufs)
-            src = z_bytes[K_PASS * gp : K_PASS * (gp + 1), W * c + lo : W * c + hi].rearrange("(p t) w -> p t w", t=4)
-            nc.sync.dma_start(out=zb[u][:, rows, :], in_=src[:, rows, :])
+        def load_body(k, i, rows=slice(0, 4)):
+            load(("zb_body", k, i), [bodies[k][i]], 4, rows)
 
         def load_step(k):
-            if edge_width[k]:
-                load(edges[k], "zb_edge", 4)
-            for u in odd[k] + bodies[k]:
-                load(u)
+            if edge[k]:
+                gp, lo, hi = casts[k][0]
+                load(("zb_edge", k), [(gp, lo, lo + edge[k])], 2)
+            load_plane(k)
+            for i in range(len(bodies[k])):
+                load_body(k, i)
 
         def load_kgain(q):
             cols = slice(2 * K_PASS * q, 2 * K_PASS * (q + 1))
             nc.sync.dma_start(out=k_rows[:, cols], in_=kgain[:, cols])
 
-        def cast(u, rows=slice(0, 4)):
+        def cast(k, i, rows=slice(0, 4)):
             if rows.start == 0:
-                raw[u] = work.tile([P, 4, width(u)], BF16, name="raw", tag="raw", bufs=3, align_bytes=256)
+                gp, lo, hi = bodies[k][i]
+                raw[k, i] = work.tile([P, 4, hi - lo], BF16, name="raw", tag="raw", bufs=3, align_bytes=256)
             nc.scalar.copy(
-                out=raw[u][:, rows, :].rearrange("p t l -> p (t l)"),
-                in_=zb[u][:, rows, :].rearrange("p t l -> p (t l)").bitcast(F8),
+                out=raw[k, i][:, rows, :].rearrange("p t l -> p (t l)"),
+                in_=zb["zb_body", k, i][:, rows, :].rearrange("p t l -> p (t l)").bitcast(F8),
             )
 
-        def step_tiles(k):
-            planes[k] = work.tile([P, 4, W + DOUBLE_EDGE], BF16, name="planes", tag="planes", bufs=4, align_bytes=256)
+        def plane_tile(k):
+            planes[k] = work.tile([P, 4, 2 * W + max(EDGES)], BF16, name="planes", tag="planes", bufs=2, align_bytes=256)
 
-        def scale_interleave(dst, a, part, lo, hi):
+        def scale_interleave(k, i):
+            gp, lo, hi = bodies[k][i]
+            first = cast_at[k][i] + (0 if i else edge[k])
             nc.vector.tensor_tensor(
-                out=dst[:, 4 * a : 4 * (a + hi - lo)].rearrange("p (c i t) -> p c t i", i=RUN, t=4),
-                in0=raw[part][:, :, lo:hi].rearrange("p t (c i) -> p c t i", i=RUN),
-                in1=zs_psum[:, part[1], :].unsqueeze(1).unsqueeze(3).to_broadcast([P, (hi - lo) // RUN, 4, RUN]),
+                out=il[:, 4 * first : 4 * (first + hi - lo)].rearrange("p (c i t) -> p c t i", i=RUN, t=4),
+                in0=raw[k, i][:].rearrange("p t (c i) -> p c t i", i=RUN),
+                in1=zs_psum[:, gp, :].unsqueeze(1).unsqueeze(3).to_broadcast([P, (hi - lo) // RUN, 4, RUN]),
                 op=MULT,
             )
 
-        def scale_of(u, t):
-            if u in (odd[0][0], odd[1][0]):
-                return zs_first[:, u[1] // 2, t : t + 1]
-            return zs[:, u[1], t : t + 1]
+        def products(k):
+            for i in range(len(bodies[k])):
+                scale_interleave(k, i)
 
-        def widen(k, u, first, rows=range(4)):
-            for t in rows:
+        def scale_of(k, gp, t):
+            if k < 2 and gp % 2:
+                return zs_first[:, k, t : t + 1]
+            return zs[:, gp, t : t + 1]
+
+        def widen(k, i, t, first=0):
+            gp, lo, hi = odd[k][i]
+            cols = slice(i * (hi - lo) + first, (i + 1) * (hi - lo))
+            nc.scalar.activation(
+                out=planes[k][:, t, cols], in_=zb["zb_plane", k][:, t, cols].bitcast(F8), func=COPY, scale=scale_of(k, gp, t)
+            )
+
+        def widen_rows(k, i):
+            for t in range(4):
+                if helped.get((k, t), 0) < columns[k]:
+                    widen(k, i, t, helped.get((k, t), 0))
+
+        def widen_edge(k):
+            for t in range(4):
                 nc.scalar.activation(
-                    out=planes[k][:, t, first : first + width(u)],
-                    in_=zb[u][:, t, :].bitcast(F8),
+                    out=planes[k][:, t, columns[k] : columns[k] + edge[k]],
+                    in_=zb["zb_edge", k][:, t, :].bitcast(F8),
                     func=COPY,
-                    scale=scale_of(u, t),
+                    scale=scale_of(k, casts[k][0][0], t),
                 )
 
-        def widen_row_on_vector(k, t):
-            u = odd[k][0]
+        def widen_on_vector(k, t, count):
             nc.vector.tensor_scalar(
-                out=planes[k][:, t, 0:W],
-                in0=zb[u][:, t, :].bitcast(F8),
-                scalar1=scale_of(u, t),
+                out=planes[k][:, t, 0:count],
+                in0=zb["zb_plane", k][:, t, 0:count].bitcast(F8),
+                scalar1=scale_of(k, odd[k][0][0], t),
                 scalar2=None,
                 op0=MULT,
             )
 
-        def interleave_on_pe(k, edge_alone):
-            first, count = columns[k] - relief[k], relief[k] + edge_width[k]
-            if k not in by_pe:
-                by_pe[k] = [psum.tile([P, 8 * P], BF16, name="by_pe", tag="by_pe", bufs=1)]
-                if count > 2 * P:
-                    if not spare:
-                        spare.append(psum.tile([P, 8 * P], BF16, name="kz", tag="kz", bufs=4))
-                    by_pe[k].append(spare[0])
-            for a in range(0, count, P):
-                if (a >= relief[k]) == edge_alone:
-                    b = min(a + P, count)
-                    into = a % (2 * P)
-                    nc.tensor.matmul(
-                        by_pe[k][a // (2 * P)][:, 4 * into : 4 * (into + b - a)].rearrange("p (l t) -> p l t", t=4),
-                        lhsT=ident_bf[:],
-                        rhs=planes[k][:, :, first + a : first + b].rearrange("p t l -> p l t"),
-                        start=True,
-                        stop=True,
-                    )
-
-        def by_pe_out(k):
-            first, count = columns[k] - relief[k], relief[k] + edge_width[k]
-            for i, bank in enumerate(by_pe[k]):
-                a, b = 2 * P * i, min(2 * P * (i + 1), count)
-                nc.scalar.copy(
-                    out=il[k][:, 4 * (first + a) : 4 * (first + b)].bitcast(F32), in_=bank[:, 0 : 4 * (b - a)].bitcast(F32)
+        def interleave_on_pe(k, first, end, bank):
+            by_pe.setdefault(k, []).append((bank, end - first, plane_at[k] + first))
+            for t in (0, 2):
+                nc.tensor.matmul(
+                    bank[:, 0 : 4 * (end - first)].rearrange("p (l t) -> p l t", t=4)[:, :, t : t + 2],
+                    lhsT=ident_bf[:],
+                    rhs=planes[k][:, t : t + 2, first:end].rearrange("p t l -> p l t"),
+                    start=True,
+                    stop=True,
                 )
 
+        def pe_bank(tag, bufs):
+            return psum.tile([P, 8 * P], BF16, name=tag, tag=tag, bufs=bufs)
+
+        def edge_on_pe(k):
+            end = columns[k] + edge[k]
+            interleave_on_pe(k, max(columns[k] + beyond[k], end - 2 * P), end, pe_bank("by_pe", 1))
+
+        def rest_on_pe(k, bank):
+            interleave_on_pe(k, columns[k] + beyond[k], columns[k] + edge[k] - 2 * P, bank)
+
+        def by_pe_out(k):
+            for bank, count, into in by_pe.pop(k, []):
+                nc.scalar.copy(out=il[:, 4 * into : 4 * (into + count)].bitcast(F32), in_=bank[:, 0 : 4 * count].bitcast(F32))
+
         def interleave_on_gpsimd(k):
-            count = columns[k] - relief[k]
+            first, count = plane_at[k], columns[k] + beyond[k]
             nc.gpsimd.tensor_scalar(
-                out=il[k][:, 0 : 4 * count].rearrange("p (c i t) -> p c t i", i=RUN, t=4),
+                out=il[:, 4 * first : 4 * (first + count)].rearrange("p (c i t) -> p c t i", i=RUN, t=4),
                 in0=planes[k][:, :, 0:count].rearrange("p t (c i) -> p c t i", i=RUN),
                 scalar1=1.0,
                 scalar2=0.0,
@@ -207,45 +219,44 @@ def tile_josephkalmanupdate_w_kernel(tc, s, z_bytes, z_scale, kgain, g, d, r, ou
                 op1=ADD,
             )
 
-        def code_tiles(k):
-            z_codes = work.tile([P, 2 * W], U32, name="z_codes", tag="z_codes", bufs=4, align_bytes=256)
-            z_scales = work.tile([P, 2 * W], U8, name="z_scales", tag="z_scales", bufs=4, align_bytes=256)
-            codes[k] = (z_codes, z_scales)
-
-        def quantise(k, src, first, a, b):
-            z_codes, z_scales = codes[k]
+        def quantise(pieces, first, part):
+            units = [(gp, h) for gp, lo, hi in pieces for h in range(lo // BLK, hi // BLK)][2 * part : 2 * part + 2]
+            count = BLK * len(units)
+            z_codes = work.tile([P, count], U32, name="z_codes", tag="z_codes", bufs=7, align_bytes=256)
+            z_scales = work.tile([P, count], U8, name="z_scales", tag="z_scales", bufs=7, align_bytes=256)
             nc.vector.quantize_mx(
-                out=z_codes[:, first + a : first + b].bitcast(FP8X4),
-                scales=z_scales[:, first + a : first + b],
-                in_=src[:, 4 * a : 4 * b],
+                out=z_codes[:].bitcast(FP8X4), scales=z_scales[:], in_=il[:, 4 * first : 4 * (first + count)]
             )
+            return z_codes, z_scales, units
 
-        def kz_passes(k, pieces, col):
-            z_codes, z_scales = codes[k]
-            complete = []
-            for c, gp, lo, hi in pieces:
-                for h in range((W * c + lo) // BLK, (W * c + hi) // BLK):
-                    if h not in kz:
-                        kz[h] = psum.tile([P, BLK], F32, name="kz", tag="kz", bufs=4)
-                    done = passes_done.get(h, 0)
-                    passes_done[h] = done + 1
-                    nc.tensor.matmul_mx(
-                        out=kz[h][:],
-                        lhsT=k_codes[:, gp, :].bitcast(FP8X4),
-                        lhsT_scale=k_scales[:, gp, :],
-                        rhs=z_codes[:, col : col + BLK].bitcast(FP8X4),
-                        rhs_scale=z_scales[:, col : col + BLK],
-                        start=(done == 0),
-                        stop=(done == PASSES - 1),
-                    )
-                    col += BLK
-                    if done == PASSES - 1:
-                        complete.append(h)
-            return complete
+        def kz_passes(z_codes, z_scales, units):
+            for i, (gp, h) in enumerate(units):
+                if h not in kz:
+                    kz[h] = psum.tile([P, BLK], F32, name="kz", tag="kz", bufs=4)
+                done = passes_done.get(h, 0)
+                passes_done[h] = done + 1
+                nc.tensor.matmul_mx(
+                    out=kz[h][:],
+                    lhsT=k_codes[:, gp, :].bitcast(FP8X4),
+                    lhsT_scale=k_scales[:, gp, :],
+                    rhs=z_codes[:, BLK * i : BLK * (i + 1)].bitcast(FP8X4),
+                    rhs_scale=z_scales[:, BLK * i : BLK * (i + 1)],
+                    start=(done == 0),
+                    stop=(done == PASSES - 1),
+                )
+
+        def quantise_step(k, k_ready, items=slice(0, 4)):
+            order = [(casts[k], cast_at[k][0], 0), (odd[k], plane_at[k], 0)]
+            if k in WIDE_STEPS:
+                order.extend([(casts[k], cast_at[k][1], 1), (odd[k], plane_at[k] + W, 1)])
+            for item in order[items]:
+                waiting.append(quantise(*item))
+                while waiting and waiting[0][2][-1][0] < k_ready:
+                    kz_passes(*waiting.pop(0))
 
         def kz_out(h, parts=((0, 4),)):
             tile = work.tile([P, BLK], F32, name="neg_kz", tag="neg_kz", bufs=2)
-            if h < BLOCKS - 3:
+            if h < LATE:
                 neg_kz[h] = tile[:].rearrange("n (p t) -> n t p", t=4)
                 nc.scalar.activation(out=tile[:], in_=kz[h][:], func=COPY, scale=-1.0)
                 return
@@ -254,14 +265,9 @@ def tile_josephkalmanupdate_w_kernel(tc, s, z_bytes, z_scale, kgain, g, d, r, ou
             for a, b in parts:
                 nc.scalar.activation(out=neg_kz[h][:, a:b, :], in_=src[:, a:b, :], func=COPY, scale=-1.0)
 
-        def turn(h, tag, bufs):
-            kz_out(h)
-            s_turn(h, tag, bufs)
-            kz_turn(h)
-
         def s_turn(h, tag, bufs):
             bank = psum.tile([P, 4 * N], F32, name=tag, tag=tag, bufs=bufs)
-            order = "p (t n) -> p n t" if h >= ON_SCALAR else "p (n t) -> p n t"
+            order = "p (t n) -> p n t" if h >= LATE else "p (n t) -> p n t"
             turned[h] = bank[:].rearrange(order, t=4)
             for t in range(4):
                 nc.tensor.matmul(
@@ -283,11 +289,15 @@ def tile_josephkalmanupdate_w_kernel(tc, s, z_bytes, z_scale, kgain, g, d, r, ou
                     stop=(t == 3),
                 )
 
+        def turn(h, tag, bufs):
+            s_turn(h, tag, bufs)
+            kz_turn(h)
+
         def gain_product(h, i):
             if i == 0:
-                w_wd[h] = work.tile([P, 2, BLK], BF16, name="w_wd", tag="w_wd", bufs=3, align_bytes=64)
+                w_wd[h] = work.tile([P, 2, BLK], BF16, name="w_wd", tag="w_wd", bufs=4, align_bytes=64)
             gain = gains[:, h, i, :].unsqueeze(1)
-            if h < ON_SCALAR:
+            if h < LATE:
                 nc.vector.tensor_tensor(
                     out=w_wd[h][:, i, :].rearrange("p (n t) -> p n t", t=4),
                     in0=turned[h],
@@ -302,24 +312,23 @@ def tile_josephkalmanupdate_w_kernel(tc, s, z_bytes, z_scale, kgain, g, d, r, ou
                 op=MULT,
             )
 
-        def both_gain_products(h, a, b):
-            if a == 0:
-                w_wd[h] = work.tile([P, 2, BLK], BF16, name="w_wd", tag="w_wd", bufs=3, align_bytes=64)
+        def both_gain_products(h):
+            w_wd[h] = work.tile([P, 2, BLK], BF16, name="w_wd", tag="w_wd", bufs=4, align_bytes=64)
             nc.vector.tensor_tensor(
-                out=w_wd[h][:].rearrange("p i (n t) -> p i n t", t=4)[:, :, a:b, :],
-                in0=turned[h][:, a:b, :].unsqueeze(1).to_broadcast([P, 2, b - a, 4]),
-                in1=gains[:, h].unsqueeze(2).to_broadcast([P, 2, b - a, 4]),
+                out=w_wd[h][:].rearrange("p i (n t) -> p i n t", t=4),
+                in0=turned[h].unsqueeze(1).to_broadcast([P, 2, N, 4]),
+                in1=gains[:, h].unsqueeze(2).to_broadcast([P, 2, N, 4]),
                 op=MULT,
             )
 
-        def gain_products_on_scalar(h):
-            w_wd[h] = work.tile([P, 2, BLK], BF16, name="w_wd", tag="w_wd", bufs=3, align_bytes=64)
-            by_t = work.tile([P, 2, 4, N], BF16, name="by_t", tag="by_t", bufs=1)
-            for i in range(2):
-                for t in range(4):
-                    nc.scalar.activation(
-                        out=by_t[:, i, t, :], in_=turned[h][:, :, t], func=COPY, scale=gains[:, h, i, t : t + 1]
-                    )
+        def gain_rows_on_scalar(h, i, by_t):
+            for t in range(4):
+                nc.scalar.activation(
+                    out=by_t[:, i, t, :], in_=turned[h][:, :, t], func=COPY, scale=gains[:, h, i, t : t + 1]
+                )
+
+        def interleave_on_scalar(h, by_t):
+            w_wd[h] = work.tile([P, 2, BLK], BF16, name="w_wd", tag="w_wd", bufs=4, align_bytes=64)
             for i in range(2):
                 nc.scalar.copy(
                     out=w_wd[h][:, i, :].rearrange("p (c j t) -> p c t j", j=4, t=4),
@@ -355,7 +364,7 @@ def tile_josephkalmanupdate_w_kernel(tc, s, z_bytes, z_scale, kgain, g, d, r, ou
             return k_bank
 
         def k_out(q, k_bank):
-            nc.scalar.copy(
+            nc.vector.tensor_copy(
                 out=k_il[:, 2 * q : 2 * q + 2, :].bitcast(F32).rearrange("p j (n u) -> p j n u", u=2),
                 in_=k_bank[:].rearrange("p j u n -> p j n u"),
             )
@@ -406,151 +415,153 @@ def tile_josephkalmanupdate_w_kernel(tc, s, z_bytes, z_scale, kgain, g, d, r, ou
             make_identity(nc, ident[:])
             nc.vector.tensor_copy(out=ident_bf[:], in_=ident[:])
 
+            first_two = work.tile([P, 2, 4, W], U8, name="zb_plane", tag="zb_plane", bufs=2)
+            zb["zb_plane", 0], zb["zb_plane", 1] = first_two[:, 0], first_two[:, 1]
             for t in range(4):
-                load(odd[0][0], rows=slice(t, t + 1))
-                load(bodies[0][0], rows=slice(t, t + 1))
+                load_plane(0, slice(t, t + 1))
+                load_body(0, 0, slice(t, t + 1))
                 if t == 1:
                     nc.sync.dma_start(out=zs_rows[0:PASSES, :], in_=z_scale.rearrange("(g m) o -> g (m o)", g=PASSES))
-            load(odd[1][0], rows=slice(0, 1))
-            load(odd[1][0], rows=slice(1, 2))
-            load(odd[1][0], rows=slice(2, 4))
+            for rows in (slice(0, 1), slice(1, 2), slice(2, 4)):
+                load_plane(1, rows)
             load_kgain(0)
-            load(bodies[1][0])
-            load_step(2)
-            load_kgain(1)
+            load_body(1, 0)
 
-            step_tiles(0)
-            step_tiles(1)
+            plane_tile(0)
+            plane_tile(1)
             scales_to_psum()
             for t in range(4):
-                widen_row_on_vector(0, t)
-                cast(bodies[0][0], slice(t, t + 1))
-            widen_row_on_vector(1, 0)
+                widen_on_vector(0, t, W)
+                cast(0, 0, slice(t, t + 1))
+            widen_on_vector(1, 0, W)
             nc.scalar.copy(out=zs[:], in_=zs_psum)
+            k_bank = k_turn(0)
 
-            due, complete, products, j_due, kr_done, k_ready = [], [], [], [], 0, 0
-            for k in range(steps):
-                if k + AHEAD < steps:
-                    load_step(k + AHEAD)
-                if k + 2 < K_QUARTERS:
-                    load_kgain(k + 2)
-                if k == 1:
+            for k in range(DOUBLE_STEP):
+                nxt = k + 1
+                if nxt < PAIRS:
+                    load_kgain(nxt)
+                load_step(k + 2)
+                if k == 0:
                     nc.sync.dma_start(out=r_sb[:], in_=r.rearrange("(g p t) -> p g t", p=P, t=4))
+                if k == 1:
                     nc.sync.dma_start(out=g_sb[:], in_=g.rearrange("(h p t) -> p h t", p=P, t=4))
                     nc.sync.dma_start(out=d_sb[:], in_=d.rearrange("(h p t) -> p h t", p=P, t=4))
                     nc.sync.dma_start(out=s_rows[:], in_=s)
                 interleave_on_gpsimd(k)
-                if k < K_QUARTERS:
-                    k_bank = k_turn(k)
 
-                nxt = k + 1
-                if k == double_step:
-                    turn(ON_SCALAR, "kz", 4)
-                if nxt < steps:
-                    if nxt not in planes:
-                        step_tiles(nxt)
-                    if edge_width[nxt]:
-                        widen(nxt, edges[nxt], columns[nxt])
-                while due and due[0][1][-1][1] < k_ready:
-                    complete.extend(kz_passes(*due.pop(0)))
-                if nxt < steps:
-                    for i, u in enumerate(odd[nxt]):
-                        widen(nxt, u, i * width(u), range(1 if k == 0 or k - 1 in ROW_STEPS else 0, 2))
-                        if k in by_pe and i == 0:
-                            by_pe_out(k)
-                        if k == double_step + 1:
-                            interleave_on_pe(nxt, True)
-                        widen(nxt, u, i * width(u), range(2, 4))
-                    if relief[nxt]:
-                        if k != double_step + 1:
-                            interleave_on_pe(nxt, True)
-                        interleave_on_pe(nxt, False)
-                    for u in reversed(bodies[nxt]):
-                        cast(u)
-
-                if k == steps - 1:
+                block = k - PAIRS
+                if k in WIDE_STEPS:
+                    cast(k, 1)
                     by_pe_out(k)
-                    gain_products_on_scalar(ON_SCALAR)
+                if block in (0, 2):
+                    kz_out(block)
+                    kz_out(block + 1)
 
-                if k < K_QUARTERS:
+                if 0 < k < PAIRS:
                     k_out(k, k_bank)
-
-                j_first = [j_due.pop(0)] if j_due and k != double_step else []
+                if k in (2, 3):
+                    kr_product(2 * (k - 2), 2 * (k - 1))
+                if k == PAIRS:
+                    kr_product(PAIRS, PASSES)
+                if block > 0:
+                    both_gain_products(block - 1)
+                products(k)
                 if k == 0:
-                    scale_interleave(il[1], 0, bodies[0][0], 0, BLK)
-                    scale_interleave(il[0], W + BLK, bodies[0][0], BLK, W)
-                else:
-                    ends = 2 * columns[k]
-                    for part in reversed(bodies[k]):
-                        ends -= width(part)
-                        if k < steps - 1:
-                            scale_interleave(il[k], ends, part, 0, width(part))
-                        if k < K_QUARTERS:
-                            continue
-                        if k < double_step:
-                            if products:
-                                h, i = products.pop(0)
-                                both_gain_products(h, *((0, SPLIT_N), (SPLIT_N, N))[i])
-                                j_due.extend([h] * i)
-                            else:
-                                more = 3 if edge_width[k] else 1
-                                kr_product(kr_done, kr_done + more)
-                                kr_done += more
-                        elif products and (k, part) != (double_step, bodies[k][-1]):
-                            h, i = products.pop(0)
-                            gain_product(h, i)
-                            j_due.extend([h] * i)
-                        else:
-                            kr_product(kr_done, kr_done + 2)
-                            kr_done += 2
-                if k == steps - 1:
-                    scale_interleave(il[k], ends, part, 0, width(part))
-                if k == K_QUARTERS - 1:
+                    k_out(k, k_bank)
+                if k == 1:
                     r_to_psum()
-                if k < double_step and complete and k % 2 == 1:
-                    h = complete.pop(0)
-                    turn(h, "turned", 1)
-                    products.extend([(h, 0), (h, 1)])
-                if k == double_step + 1:
-                    turn(BLOCKS - 2, "turned", 1)
+                if nxt < PAIRS:
+                    k_bank = k_turn(nxt)
+                if block >= 0:
+                    turn(block, "turned", 1)
 
-                if k in ROW_STEPS:
-                    step_tiles(k + 2)
-                    widen_row_on_vector(k + 2, 0)
-                for h in j_first:
-                    j_pass(h)
-                if k in (K_QUARTERS // 2, K_QUARTERS):
-                    quantise_k(k_il, k_codes, k_scales, 2 * k - K_QUARTERS, 2 * k)
-                    k_ready = 2 * k
-                if k == K_QUARTERS:
+                if nxt not in planes:
+                    plane_tile(nxt)
+                if edge[nxt]:
+                    widen_edge(nxt)
+                    edge_on_pe(nxt)
+                widen_rows(nxt, 0)
+                if nxt == DOUBLE_STEP:
+                    by_pe_out(nxt)
+                    interleave_on_pe(nxt, W, W + edge[nxt] - 2 * P, pe_bank("by_pe", 1))
+                    widen_rows(nxt, 1)
+                    by_pe_out(nxt)
+                    interleave_on_pe(nxt, W + beyond[nxt], W, pe_bank("by_pe", 1))
+                cast(nxt, 0)
+
+                if k in HELP:
+                    if HELP[k][0] not in planes:
+                        plane_tile(HELP[k][0])
+                    widen_on_vector(*HELP[k])
+                if k in (1, 3):
+                    quantise_k(k_il, k_codes, k_scales, 2 * k - 2, 2 * k + 2)
+                if k == 2:
                     nc.vector.tensor_tensor(out=gains[:, :, 1, :], in0=g_sb[:], in1=d_sb[:], op=MULT)
                     nc.vector.tensor_copy(out=gains[:, :, 0, :], in_=g_sb[:])
-                code_tiles(k)
-                if 1 <= k <= double_step:
-                    quantise(k - 1, il[k - 1], 0, 0, W)
-                    due.append((k - 1, odd[k - 1], 0))
-                if k == 0:
-                    quantise(k, il[1], W, 0, BLK)
-                    quantise(k, il[0], 0, W + BLK, 2 * W)
-                    due.append((k, casts[k], columns[k]))
-                    continue
-                if k >= double_step:
-                    quantise(k, il[k], 0, 0, columns[k])
-                    due.append((k, odd[k], 0))
-                quantise(k, il[k], 0, columns[k], 2 * columns[k])
-                due.append((k, casts[k], columns[k]))
+                if block > 0:
+                    j_pass(block - 1)
+                quantise_step(k, PAIRS * ((k + 1) // 2), slice(0, 2 if nxt == DOUBLE_STEP else 4))
 
+            first_short, last = DOUBLE_STEP + 1, DOUBLE_STEP + 2
+            load_step(last)
+            cast(DOUBLE_STEP, 1)
+            by_pe_out(DOUBLE_STEP)
+            plane_tile(first_short)
+            planes[last] = planes[first_short][:, :, W:]
+            widen_edge(first_short)
+            edge_on_pe(first_short)
+            quantise_step(DOUBLE_STEP - 1, PASSES, slice(2, 4))
+
+            interleave_on_gpsimd(DOUBLE_STEP)
+            kz_out(LATE - 1)
+            widen_rows(first_short, 0)
+            kz_out(LATE)
+            by_pe_out(first_short)
+            both_gain_products(LATE - 2)
+            products(DOUBLE_STEP)
+            turn(LATE - 1, "turned", 1)
+            spare = pe_bank("kz", 4)
+            rest_on_pe(first_short, spare)
+            widen_edge(last)
+            edge_on_pe(last)
+            cast(first_short, 0)
+            by_pe_out(first_short)
+            j_pass(LATE - 2)
+            quantise_step(DOUBLE_STEP, PASSES)
+
+            interleave_on_gpsimd(first_short)
+            turn(LATE, "kz", 4)
+            for t in range(4):
+                widen(last, 0, t)
+                if t == 2:
+                    kz_out(LATE + 1)
+            products(first_short)
+            both_gain_products(LATE - 1)
+            turn(LATE + 1, "turned", 1)
+            cast(last, 0)
+            by_pe_out(last)
+            rest_on_pe(last, spare)
+            quantise_step(first_short, PASSES)
+
+            interleave_on_gpsimd(last)
+            by_t = work.tile([P, 2, 4, N], BF16, name="by_t", tag="by_t", bufs=1)
+            gain_rows_on_scalar(LATE, 0, by_t)
+            by_pe_out(last)
+            gain_rows_on_scalar(LATE, 1, by_t)
+            interleave_on_scalar(LATE, by_t)
+            products(last)
+            for i in range(2):
+                gain_product(LATE + 1, i)
             s_turn(BLOCKS - 1, "kz", 4)
-            for passes in due:
-                kz_passes(*passes)
+            quantise_step(last, PASSES)
+
             kz_out(BLOCKS - 1, ((0, 2), (2, 4)))
             kz_turn(BLOCKS - 1)
-            for i in range(2):
-                gain_product(BLOCKS - 2, i)
             quantise_k(kr_il, kr_codes, kr_scales, 0, PASSES)
-            q_passes()
-            for h in range(ON_SCALAR, BLOCKS - 1):
+            for h in range(LATE - 1, BLOCKS - 1):
                 j_pass(h)
+            q_passes()
             for i in range(2):
                 gain_product(BLOCKS - 1, i)
             j_pass(BLOCKS - 1, ((0, 1), (1, 2)))

@@ -27,13 +27,13 @@ PAIRS = PASSES // 2
 WIDE_STEPS = range(2, 2 * CHUNKS)
 DOUBLE_STEP = 2 * CHUNKS
 STEPS = DOUBLE_STEP + 3
-EDGES = (192, 160)
-DOUBLE_EDGE = 448
-LATE_EDGE = 320
-BEYOND = (32, 64)
-DOUBLE_BEYOND = -192
+EDGES = (160, 160)
+DOUBLE_EDGE = 416
+LATE_EDGE = 352
+BEYOND = (16, 16)
+DOUBLE_BEYOND = -208
 LATE_BEYOND = -128
-HELP = {0: (2, 0, 512), 4: (5, 0, 640), 6: (7, 0, 640)}
+HELP = {0: (2, 0, 256), 4: (5, 0, 640)}
 RUN = 8
 LATE = BLOCKS - 3
 
@@ -531,24 +531,22 @@ def tile_josephkalmanupdate_w_kernel(tc, s, z_bytes, z_scale, kgain, g, d, r, ou
             quantise_step(DOUBLE_STEP, PASSES)
 
             interleave_on_gpsimd(first_short)
-            turn(LATE, "kz", 4)
-            for t in range(4):
-                widen(last, 0, t)
-                if t == 2:
-                    kz_out(LATE + 1)
-            products(first_short)
-            both_gain_products(LATE - 1)
-            turn(LATE + 1, "turned", 1)
+            s_turn(LATE + 1, "kz", 4)
+            widen_rows(last, 0)
+            rest_on_pe(last, spare)
+            kz_out(LATE + 1)
+            kz_turn(LATE + 1)
             cast(last, 0)
             by_pe_out(last)
-            rest_on_pe(last, spare)
+            products(first_short)
+            both_gain_products(LATE - 1)
+            turn(LATE, "turned", 1)
             quantise_step(first_short, PASSES)
 
             interleave_on_gpsimd(last)
             by_t = work.tile([P, 2, 4, N], BF16, name="by_t", tag="by_t", bufs=1)
-            gain_rows_on_scalar(LATE, 0, by_t)
-            by_pe_out(last)
-            gain_rows_on_scalar(LATE, 1, by_t)
+            for i in range(2):
+                gain_rows_on_scalar(LATE, i, by_t)
             interleave_on_scalar(LATE, by_t)
             products(last)
             for i in range(2):

@@ -27,11 +27,11 @@ PAIRS = PASSES // 2
 WIDE_STEPS = range(2, 2 * CHUNKS)
 DOUBLE_STEP = 2 * CHUNKS
 STEPS = DOUBLE_STEP + 3
-EDGES = (160, 160)
-DOUBLE_EDGE = 416
+EDGES = (160, 192)
+DOUBLE_EDGE = 384
 LATE_EDGE = 352
-BEYOND = (16, 16)
-DOUBLE_BEYOND = -208
+BEYOND = (40, 8)
+DOUBLE_BEYOND = -192
 LATE_BEYOND = -128
 HELP = {0: (2, 0, 256), 4: (5, 0, 640)}
 RUN = 8

@@ -355,18 +355,18 @@ def tile_josephkalmanupdate_w_kernel(tc, s, z_bytes, z_scale, kgain, g, d, r, ou
             )
 
         def k_turn(q):
-            k_bank = psum.tile([P, 2, 2, N], F32, name="turned", tag="turned", bufs=1)
+            k_bank = psum.tile([P, 2, N, 2], F32, name="turned", tag="turned", bufs=1)
             words = k_rows[:].bitcast(F32)
             for j in range(2):
                 for u in range(2):
                     first = K_PASS // 2 * (2 * q + j)
-                    nc.tensor.transpose(k_bank[:, j, u, :], words[:, first + u : first + K_PASS // 2 : 2], ident[:])
+                    nc.tensor.transpose(k_bank[:, j, :, u], words[:, first + u : first + K_PASS // 2 : 2], ident[:])
             return k_bank
 
         def k_out(q, k_bank):
             nc.vector.tensor_copy(
-                out=k_il[:, 2 * q : 2 * q + 2, :].bitcast(F32).rearrange("p j (n u) -> p j n u", u=2),
-                in_=k_bank[:].rearrange("p j u n -> p j n u"),
+                out=k_il[:, 2 * q : 2 * q + 2, :].rearrange("p j x -> p (j x)").bitcast(F32),
+                in_=k_bank[:].rearrange("p j n u -> p (j n u)"),
             )
 
         def quantise_k(src, dst_codes, dst_scales, a, b):

from contextlib import ExitStack

import concourse.mybir as mybir
from concourse.masks import make_identity

N, M, L = 128, 4096, 4096
FLOPS = 2 * N * M * L + 4 * N * N * L

F32 = mybir.dt.float32
BF16 = mybir.dt.bfloat16
U32 = mybir.dt.uint32
U8 = mybir.dt.uint8
F8 = mybir.dt.float8_e4m3fn
FP8X4 = mybir.dt.float8_e4m3fn_x4
MULT = mybir.AluOpType.mult
ADD = mybir.AluOpType.add
COPY = mybir.ActivationFunctionType.Copy

P = 128
K_PASS = 4 * P
PASSES = M // K_PASS
BLK = 512
BLOCKS = L // BLK
W = 2 * BLK
CHUNKS = L // W
PAIRS = PASSES // 2
WIDE_STEPS = range(2, 2 * CHUNKS)
DOUBLE_STEP = 2 * CHUNKS
STEPS = DOUBLE_STEP + 3
EDGES = (160, 192)
DOUBLE_EDGE = 384
LATE_EDGE = 352
BEYOND = (40, 8)
DOUBLE_BEYOND = -192
LATE_BEYOND = -128
HELP = {0: (2, 0, 256), 4: (5, 0, 640)}
RUN = 8
LATE = BLOCKS - 3


def tile_josephkalmanupdate_w_kernel(tc, s, z_bytes, z_scale, kgain, g, d, r, out):
    nc = tc.nc
    with ExitStack() as ctx:
        keep = ctx.enter_context(tc.tile_pool(name="keep", bufs=1))
        work = ctx.enter_context(tc.tile_pool(name="work", bufs=1))
        psum = ctx.enter_context(tc.psum_pool(name="psum", bufs=1))

        ident = keep.tile([P, P], F32, name="ident")
        ident_bf = keep.tile([P, P], BF16, name="ident_bf")
        zs = keep.tile([P, PASSES, 4], F32, name="zs")
        zs_rows = keep.tile([P, K_PASS], F32, name="zs_rows")
        zs_first = keep.tile([P, 2, 8], F32, name="zs_first")[:, :, 0:4]
        r_sb = keep.tile([P, PASSES, 4], BF16, name="r_sb")
        g_sb = keep.tile([P, BLOCKS, 4], BF16, name="g_sb")
        d_sb = keep.tile([P, BLOCKS, 4], BF16, name="d_sb")
        gains = keep.tile([P, BLOCKS, 2, 4], F32, name="gains")
        k_rows = keep.tile([P, M], BF16, name="k_rows")
        k_il = keep.tile([P, PASSES, 4 * N], BF16, name="k_il", align_bytes=64)
        kr_il = keep.tile([P, PASSES, 4 * N], BF16, name="kr_il", align_bytes=64)
        k_codes = keep.tile([P, PASSES, N], U32, name="k_codes", align_bytes=64)
        k_scales = keep.tile([P, PASSES, N], U8, name="k_scales", align_bytes=64)
        kr_codes = keep.tile([P, PASSES, N], U32, name="kr_codes", align_bytes=64)
        kr_scales = keep.tile([P, PASSES, N], U8, name="kr_scales", align_bytes=64)
        il = keep.tile([P, 5 * 4 * W], BF16, name="il", align_bytes=256)
        s_rows = keep.tile([P, L], BF16, name="s_rows")
        jq = psum.tile([P, N], F32, name="jq", tag="jq", bufs=1)
        factors = psum.tile([P, 4 * P], F32, name="factors", tag="factors", bufs=1)
        zs_psum = factors[:, 0 : 4 * PASSES].rearrange("p (g t) -> p g t", t=4)
        r_psum = factors[:, 4 * PASSES : 6 * PASSES].bitcast(BF16)

        casts = []
        for k in range(DOUBLE_STEP):
            casts.append([(2 * (k % PAIRS), W * max(0, k // 2 - 1), W * (k // 2 + 1))])
        casts.append([(gp, L - W, L - BLK) for gp in (0, 2)])
        casts.extend([[(gp, L - BLK, L)] for gp in (0, 2)])
        odd = [[(gp + 1, lo, hi) for gp, lo, hi in pieces] for pieces in casts]
        columns = [sum(hi - lo for gp, lo, hi in pieces) for pieces in casts]
        edge = [0, 0] + [EDGES[k % 2] for k in WIDE_STEPS] + [DOUBLE_EDGE, LATE_EDGE, LATE_EDGE]
        beyond = [0, 0] + [BEYOND[k % 2] for k in WIDE_STEPS] + [DOUBLE_BEYOND, LATE_BEYOND, LATE_BEYOND]
        bodies = []
        for pieces, x in zip(casts, edge):
            parts = [(gp, a, min(a + W, hi)) for gp, lo, hi in pieces for a in range(lo, hi, W)]
            bodies.append([(parts[0][0], parts[0][1] + x, parts[0][2])] + parts[1:])
        plane_at = [0, 3 * W] + [2 * W * (k % 2) for k in WIDE_STEPS]
        cast_at = [[3 * W], [W]] + [((2 * W, 3 * W), (4 * W, 0))[k % 2] for k in WIDE_STEPS]
        cast_end = W
        for k in range(DOUBLE_STEP, STEPS):
            plane_at.append(cast_end - columns[k] - beyond[k])
            cast_at.append([plane_at[k] + columns[k] + BLK * i for i in range(len(casts[k]))])
            cast_end = plane_at[k] + 2 * columns[k]

        zb, raw, planes, by_pe, kz, neg_kz, turned, w_wd = {}, {}, {}, {}, {}, {}, {}, {}
        passes_done, waiting = {}, []
        helped = {(k, t): count for k, t, count in HELP.values()}
        helped[1, 0] = W

        def load(key, pieces, bufs, rows=slice(0, 4)):
            if key not in zb:
                count = sum(hi - lo for gp, lo, hi in pieces)
                zb[key] = work.tile([P, 4, count], U8, name=key[0], tag=key[0], bufs=bufs)
            at = 0
            for gp, lo, hi in pieces:
                src = z_bytes[K_PASS * gp : K_PASS * (gp + 1), lo:hi].rearrange("(p t) w -> p t w", t=4)
                nc.sync.dma_start(out=zb[key][:, rows, at : at + hi - lo], in_=src[:, rows, :])
                at += hi - lo

        def load_plane(k, rows=slice(0, 4)):
            load(("zb_plane", k), odd[k], 2, rows)

        def load_body(k, i, rows=slice(0, 4)):
            load(("zb_body", k, i), [bodies[k][i]], 4, rows)

        def load_step(k):
            if edge[k]:
                gp, lo, hi = casts[k][0]
                load(("zb_edge", k), [(gp, lo, lo + edge[k])], 2)
            load_plane(k)
            for i in range(len(bodies[k])):
                load_body(k, i)

        def load_kgain(q):
            cols = slice(2 * K_PASS * q, 2 * K_PASS * (q + 1))
            nc.sync.dma_start(out=k_rows[:, cols], in_=kgain[:, cols])

        def cast(k, i, rows=slice(0, 4)):
            if rows.start == 0:
                gp, lo, hi = bodies[k][i]
                raw[k, i] = work.tile([P, 4, hi - lo], BF16, name="raw", tag="raw", bufs=3, align_bytes=256)
            nc.scalar.copy(
                out=raw[k, i][:, rows, :].rearrange("p t l -> p (t l)"),
                in_=zb["zb_body", k, i][:, rows, :].rearrange("p t l -> p (t l)").bitcast(F8),
            )

        def plane_tile(k):
            planes[k] = work.tile([P, 4, 2 * W + max(EDGES)], BF16, name="planes", tag="planes", bufs=2, align_bytes=256)

        def scale_interleave(k, i):
            gp, lo, hi = bodies[k][i]
            first = cast_at[k][i] + (0 if i else edge[k])
            nc.vector.tensor_tensor(
                out=il[:, 4 * first : 4 * (first + hi - lo)].rearrange("p (c i t) -> p c t i", i=RUN, t=4),
                in0=raw[k, i][:].rearrange("p t (c i) -> p c t i", i=RUN),
                in1=zs_psum[:, gp, :].unsqueeze(1).unsqueeze(3).to_broadcast([P, (hi - lo) // RUN, 4, RUN]),
                op=MULT,
            )

        def products(k):
            for i in range(len(bodies[k])):
                scale_interleave(k, i)

        def scale_of(k, gp, t):
            if k < 2 and gp % 2:
                return zs_first[:, k, t : t + 1]
            return zs[:, gp, t : t + 1]

        def widen(k, i, t, first=0):
            gp, lo, hi = odd[k][i]
            cols = slice(i * (hi - lo) + first, (i + 1) * (hi - lo))
            nc.scalar.activation(
                out=planes[k][:, t, cols], in_=zb["zb_plane", k][:, t, cols].bitcast(F8), func=COPY, scale=scale_of(k, gp, t)
            )

        def widen_rows(k, i):
            for t in range(4):
                if helped.get((k, t), 0) < columns[k]:
                    widen(k, i, t, helped.get((k, t), 0))

        def widen_edge(k):
            for t in range(4):
                nc.scalar.activation(
                    out=planes[k][:, t, columns[k] : columns[k] + edge[k]],
                    in_=zb["zb_edge", k][:, t, :].bitcast(F8),
                    func=COPY,
                    scale=scale_of(k, casts[k][0][0], t),
                )

        def widen_on_vector(k, t, count):
            nc.vector.tensor_scalar(
                out=planes[k][:, t, 0:count],
                in0=zb["zb_plane", k][:, t, 0:count].bitcast(F8),
                scalar1=scale_of(k, odd[k][0][0], t),
                scalar2=None,
                op0=MULT,
            )

        def interleave_on_pe(k, first, end, bank):
            by_pe.setdefault(k, []).append((bank, end - first, plane_at[k] + first))
            for t in (0, 2):
                nc.tensor.matmul(
                    bank[:, 0 : 4 * (end - first)].rearrange("p (l t) -> p l t", t=4)[:, :, t : t + 2],
                    lhsT=ident_bf[:],
                    rhs=planes[k][:, t : t + 2, first:end].rearrange("p t l -> p l t"),
                    start=True,
                    stop=True,
                )

        def pe_bank(tag, bufs):
            return psum.tile([P, 8 * P], BF16, name=tag, tag=tag, bufs=bufs)

        def edge_on_pe(k):
            end = columns[k] + edge[k]
            interleave_on_pe(k, max(columns[k] + beyond[k], end - 2 * P), end, pe_bank("by_pe", 1))

        def rest_on_pe(k, bank):
            interleave_on_pe(k, columns[k] + beyond[k], columns[k] + edge[k] - 2 * P, bank)

        def by_pe_out(k):
            for bank, count, into in by_pe.pop(k, []):
                nc.scalar.copy(out=il[:, 4 * into : 4 * (into + count)].bitcast(F32), in_=bank[:, 0 : 4 * count].bitcast(F32))

        def interleave_on_gpsimd(k):
            first, count = plane_at[k], columns[k] + beyond[k]
            nc.gpsimd.tensor_scalar(
                out=il[:, 4 * first : 4 * (first + count)].rearrange("p (c i t) -> p c t i", i=RUN, t=4),
                in0=planes[k][:, :, 0:count].rearrange("p t (c i) -> p c t i", i=RUN),
                scalar1=1.0,
                scalar2=0.0,
                op0=MULT,
                op1=ADD,
            )

        def quantise(pieces, first, part):
            units = [(gp, h) for gp, lo, hi in pieces for h in range(lo // BLK, hi // BLK)][2 * part : 2 * part + 2]
            count = BLK * len(units)
            z_codes = work.tile([P, count], U32, name="z_codes", tag="z_codes", bufs=7, align_bytes=256)
            z_scales = work.tile([P, count], U8, name="z_scales", tag="z_scales", bufs=7, align_bytes=256)
            nc.vector.quantize_mx(
                out=z_codes[:].bitcast(FP8X4), scales=z_scales[:], in_=il[:, 4 * first : 4 * (first + count)]
            )
            return z_codes, z_scales, units

        def kz_passes(z_codes, z_scales, units):
            for i, (gp, h) in enumerate(units):
                if h not in kz:
                    kz[h] = psum.tile([P, BLK], F32, name="kz", tag="kz", bufs=4)
                done = passes_done.get(h, 0)
                passes_done[h] = done + 1
                nc.tensor.matmul_mx(
                    out=kz[h][:],
                    lhsT=k_codes[:, gp, :].bitcast(FP8X4),
                    lhsT_scale=k_scales[:, gp, :],
                    rhs=z_codes[:, BLK * i : BLK * (i + 1)].bitcast(FP8X4),
                    rhs_scale=z_scales[:, BLK * i : BLK * (i + 1)],
                    start=(done == 0),
                    stop=(done == PASSES - 1),
                )

        def quantise_step(k, k_ready, items=slice(0, 4)):
            order = [(casts[k], cast_at[k][0], 0), (odd[k], plane_at[k], 0)]
            if k in WIDE_STEPS:
                order.extend([(casts[k], cast_at[k][1], 1), (odd[k], plane_at[k] + W, 1)])
            for item in order[items]:
                waiting.append(quantise(*item))
                while waiting and waiting[0][2][-1][0] < k_ready:
                    kz_passes(*waiting.pop(0))

        def kz_out(h, parts=((0, 4),)):
            tile = work.tile([P, BLK], F32, name="neg_kz", tag="neg_kz", bufs=2)
            if h < LATE:
                neg_kz[h] = tile[:].rearrange("n (p t) -> n t p", t=4)
                nc.scalar.activation(out=tile[:], in_=kz[h][:], func=COPY, scale=-1.0)
                return
            neg_kz[h] = tile[:].rearrange("n (t p) -> n t p", t=4)
            src = kz[h][:].rearrange("n (p t) -> n t p", t=4)
            for a, b in parts:
                nc.scalar.activation(out=neg_kz[h][:, a:b, :], in_=src[:, a:b, :], func=COPY, scale=-1.0)

        def s_turn(h, tag, bufs):
            bank = psum.tile([P, 4 * N], F32, name=tag, tag=tag, bufs=bufs)
            order = "p (t n) -> p n t" if h >= LATE else "p (n t) -> p n t"
            turned[h] = bank[:].rearrange(order, t=4)
            for t in range(4):
                nc.tensor.matmul(
                    turned[h][:, :, t],
                    lhsT=s_rows[:, BLK * h + t : BLK * (h + 1) : 4],
                    rhs=ident_bf[:],
                    start=(t == 0),
                    stop=False,
                )

        def kz_turn(h):
            for t in range(4):
                nc.tensor.matmul(
                    turned[h][:, :, t],
                    lhsT=neg_kz[h][:, t, :],
                    rhs=ident[:],
                    is_transpose=True,
                    start=False,
                    stop=(t == 3),
                )

        def turn(h, tag, bufs):
            s_turn(h, tag, bufs)
            kz_turn(h)

        def gain_product(h, i):
            if i == 0:
                w_wd[h] = work.tile([P, 2, BLK], BF16, name="w_wd", tag="w_wd", bufs=4, align_bytes=64)
            gain = gains[:, h, i, :].unsqueeze(1)
            if h < LATE:
                nc.vector.tensor_tensor(
                    out=w_wd[h][:, i, :].rearrange("p (n t) -> p n t", t=4),
                    in0=turned[h],
                    in1=gain.to_broadcast([P, N, 4]),
                    op=MULT,
                )
                return
            nc.vector.tensor_tensor(
                out=w_wd[h][:, i, :].rearrange("p (c j t) -> p c t j", j=RUN, t=4),
                in0=turned[h].rearrange("p (c j) t -> p c t j", j=RUN),
                in1=gain.unsqueeze(3).to_broadcast([P, N // RUN, 4, RUN]),
                op=MULT,
            )

        def both_gain_products(h):
            w_wd[h] = work.tile([P, 2, BLK], BF16, name="w_wd", tag="w_wd", bufs=4, align_bytes=64)
            nc.vector.tensor_tensor(
                out=w_wd[h][:].rearrange("p i (n t) -> p i n t", t=4),
                in0=turned[h].unsqueeze(1).to_broadcast([P, 2, N, 4]),
                in1=gains[:, h].unsqueeze(2).to_broadcast([P, 2, N, 4]),
                op=MULT,
            )

        def gain_rows_on_scalar(h, i, by_t):
            for t in range(4):
                nc.scalar.activation(
                    out=by_t[:, i, t, :], in_=turned[h][:, :, t], func=COPY, scale=gains[:, h, i, t : t + 1]
                )

        def interleave_on_scalar(h, by_t):
            w_wd[h] = work.tile([P, 2, BLK], BF16, name="w_wd", tag="w_wd", bufs=4, align_bytes=64)
            for i in range(2):
                nc.scalar.copy(
                    out=w_wd[h][:, i, :].rearrange("p (c j t) -> p c t j", j=4, t=4),
                    in_=by_t[:, i].rearrange("p t (c j) -> p c t j", j=4),
                )

        def j_pass(h, parts=((0, 2),)):
            w_codes = work.tile([P, 2, N], U32, name="w_codes", tag="w_codes", bufs=3, align_bytes=64)
            w_scales = work.tile([P, 2, N], U8, name="w_scales", tag="w_scales", bufs=3, align_bytes=64)
            for a, b in parts:
                nc.vector.quantize_mx(
                    out=w_codes[:, a:b, :].rearrange("p i n -> p (i n)").bitcast(FP8X4),
                    scales=w_scales[:, a:b, :].rearrange("p i n -> p (i n)"),
                    in_=w_wd[h][:, a:b, :].rearrange("p i x -> p (i x)"),
                )
            nc.tensor.matmul_mx(
                out=jq[:],
                lhsT=w_codes[:, 1, :].bitcast(FP8X4),
                lhsT_scale=w_scales[:, 1, :],
                rhs=w_codes[:, 0, :].bitcast(FP8X4),
                rhs_scale=w_scales[:, 0, :],
                start=(h == 0),
                stop=(h == BLOCKS - 1),
            )

        def k_turn(q):
            k_bank = psum.tile([P, 2, N, 2], F32, name="turned", tag="turned", bufs=1)
            words = k_rows[:].bitcast(F32)
            for j in range(2):
                for u in range(2):
                    first = K_PASS // 2 * (2 * q + j)
                    nc.tensor.transpose(k_bank[:, j, :, u], words[:, first + u : first + K_PASS // 2 : 2], ident[:])
            return k_bank

        def k_out(q, k_bank):
            nc.vector.tensor_copy(
                out=k_il[:, 2 * q : 2 * q + 2, :].rearrange("p j x -> p (j x)").bitcast(F32),
                in_=k_bank[:].rearrange("p j n u -> p (j n u)"),
            )

        def quantise_k(src, dst_codes, dst_scales, a, b):
            nc.vector.quantize_mx(
                out=dst_codes[:, a:b, :].rearrange("p g n -> p (g n)").bitcast(FP8X4),
                scales=dst_scales[:, a:b, :].rearrange("p g n -> p (g n)"),
                in_=src[:, a:b, :].rearrange("p g x -> p (g x)"),
            )

        def kr_product(a, b):
            nc.vector.tensor_tensor(
                out=kr_il[:, a:b, :].rearrange("p g (n t) -> p g n t", t=4),
                in0=k_il[:, a:b, :].rearrange("p g (n t) -> p g n t", t=4),
                in1=r_psum.rearrange("p (g t) -> p g t", t=4)[:, a:b, :].unsqueeze(2).to_broadcast([P, b - a, N, 4]),
                op=MULT,
            )

        def q_passes():
            for gp in range(PASSES):
                nc.tensor.matmul_mx(
                    out=jq[:],
                    lhsT=kr_codes[:, gp, :].bitcast(FP8X4),
                    lhsT_scale=kr_scales[:, gp, :],
                    rhs=k_codes[:, gp, :].bitcast(FP8X4),
                    rhs_scale=k_scales[:, gp, :],
                    start=False,
                    stop=False,
                )

        def scales_to_psum():
            for t in range(4):
                nc.tensor.transpose(factors[:, t : 4 * P : 4], zs_rows[:, t:K_PASS:4], ident[:])

        def r_to_psum():
            nc.tensor.matmul(
                r_psum,
                lhsT=ident_bf[:],
                rhs=r_sb[:].rearrange("p g t -> p (g t)"),
                start=True,
                stop=True,
            )

        with tc.manual_schedule():
            nc.scalar.dma_start(out=zs_first, in_=z_scale.rearrange("(g p t) o -> p g (t o)", p=P, t=4)[:, 1:4:2, :])
            nc.vector.memset(zs_rows[:], 0.0)
            make_identity(nc, ident[:])
            nc.vector.tensor_copy(out=ident_bf[:], in_=ident[:])

            first_two = work.tile([P, 2, 4, W], U8, name="zb_plane", tag="zb_plane", bufs=2)
            zb["zb_plane", 0], zb["zb_plane", 1] = first_two[:, 0], first_two[:, 1]
            for t in range(4):
                load_plane(0, slice(t, t + 1))
                load_body(0, 0, slice(t, t + 1))
                if t == 1:
                    nc.sync.dma_start(out=zs_rows[0:PASSES, :], in_=z_scale.rearrange("(g m) o -> g (m o)", g=PASSES))
            for rows in (slice(0, 1), slice(1, 2), slice(2, 4)):
                load_plane(1, rows)
            load_kgain(0)
            load_body(1, 0)

            plane_tile(0)
            plane_tile(1)
            scales_to_psum()
            for t in range(4):
                widen_on_vector(0, t, W)
                cast(0, 0, slice(t, t + 1))
            widen_on_vector(1, 0, W)
            nc.scalar.copy(out=zs[:], in_=zs_psum)
            k_bank = k_turn(0)

            for k in range(DOUBLE_STEP):
                nxt = k + 1
                if nxt < PAIRS:
                    load_kgain(nxt)
                load_step(k + 2)
                if k == 0:
                    nc.sync.dma_start(out=r_sb[:], in_=r.rearrange("(g p t) -> p g t", p=P, t=4))
                if k == 1:
                    nc.sync.dma_start(out=g_sb[:], in_=g.rearrange("(h p t) -> p h t", p=P, t=4))
                    nc.sync.dma_start(out=d_sb[:], in_=d.rearrange("(h p t) -> p h t", p=P, t=4))
                    nc.sync.dma_start(out=s_rows[:], in_=s)
                interleave_on_gpsimd(k)

                block = k - PAIRS
                if k in WIDE_STEPS:
                    cast(k, 1)
                    by_pe_out(k)
                if block in (0, 2):
                    kz_out(block)
                    kz_out(block + 1)

                if 0 < k < PAIRS:
                    k_out(k, k_bank)
                if k in (2, 3):
                    kr_product(2 * (k - 2), 2 * (k - 1))
                if k == PAIRS:
                    kr_product(PAIRS, PASSES)
                if block > 0:
                    both_gain_products(block - 1)
                products(k)
                if k == 0:
                    k_out(k, k_bank)
                if k == 1:
                    r_to_psum()
                if nxt < PAIRS:
                    k_bank = k_turn(nxt)
                if block >= 0:
                    turn(block, "turned", 1)

                if nxt not in planes:
                    plane_tile(nxt)
                if edge[nxt]:
                    widen_edge(nxt)
                    edge_on_pe(nxt)
                widen_rows(nxt, 0)
                if nxt == DOUBLE_STEP:
                    by_pe_out(nxt)
                    interleave_on_pe(nxt, W, W + edge[nxt] - 2 * P, pe_bank("by_pe", 1))
                    widen_rows(nxt, 1)
                    by_pe_out(nxt)
                    interleave_on_pe(nxt, W + beyond[nxt], W, pe_bank("by_pe", 1))
                cast(nxt, 0)

                if k in HELP:
                    if HELP[k][0] not in planes:
                        plane_tile(HELP[k][0])
                    widen_on_vector(*HELP[k])
                if k in (1, 3):
                    quantise_k(k_il, k_codes, k_scales, 2 * k - 2, 2 * k + 2)
                if k == 2:
                    nc.vector.tensor_tensor(out=gains[:, :, 1, :], in0=g_sb[:], in1=d_sb[:], op=MULT)
                    nc.vector.tensor_copy(out=gains[:, :, 0, :], in_=g_sb[:])
                if block > 0:
                    j_pass(block - 1)
                quantise_step(k, PAIRS * ((k + 1) // 2), slice(0, 2 if nxt == DOUBLE_STEP else 4))

            first_short, last = DOUBLE_STEP + 1, DOUBLE_STEP + 2
            load_step(last)
            cast(DOUBLE_STEP, 1)
            by_pe_out(DOUBLE_STEP)
            plane_tile(first_short)
            planes[last] = planes[first_short][:, :, W:]
            widen_edge(first_short)
            edge_on_pe(first_short)
            quantise_step(DOUBLE_STEP - 1, PASSES, slice(2, 4))

            interleave_on_gpsimd(DOUBLE_STEP)
            kz_out(LATE - 1)
            widen_rows(first_short, 0)
            kz_out(LATE)
            by_pe_out(first_short)
            both_gain_products(LATE - 2)
            products(DOUBLE_STEP)
            turn(LATE - 1, "turned", 1)
            spare = pe_bank("kz", 4)
            rest_on_pe(first_short, spare)
            widen_edge(last)
            edge_on_pe(last)
            cast(first_short, 0)
            by_pe_out(first_short)
            j_pass(LATE - 2)
            quantise_step(DOUBLE_STEP, PASSES)

            interleave_on_gpsimd(first_short)
            s_turn(LATE + 1, "kz", 4)
            widen_rows(last, 0)
            rest_on_pe(last, spare)
            kz_out(LATE + 1)
            kz_turn(LATE + 1)
            cast(last, 0)
            by_pe_out(last)
            products(first_short)
            both_gain_products(LATE - 1)
            turn(LATE, "turned", 1)
            quantise_step(first_short, PASSES)

            interleave_on_gpsimd(last)
            by_t = work.tile([P, 2, 4, N], BF16, name="by_t", tag="by_t", bufs=1)
            for i in range(2):
                gain_rows_on_scalar(LATE, i, by_t)
            interleave_on_scalar(LATE, by_t)
            products(last)
            for i in range(2):
                gain_product(LATE + 1, i)
            s_turn(BLOCKS - 1, "kz", 4)
            quantise_step(last, PASSES)

            kz_out(BLOCKS - 1, ((0, 2), (2, 4)))
            kz_turn(BLOCKS - 1)
            quantise_k(kr_il, kr_codes, kr_scales, 0, PASSES)
            for h in range(LATE - 1, BLOCKS - 1):
                j_pass(h)
            q_passes()
            for i in range(2):
                gain_product(BLOCKS - 1, i)
            j_pass(BLOCKS - 1, ((0, 1), (1, 2)))
            result = work.tile([P, N], F32, name="result", tag="result", bufs=1)
            nc.vector.tensor_copy(out=result[:], in_=jq[:])
            nc.sync.dma_start(out=out, in_=result[:])
